import numpy as np, ml_dtypes
CORES = [13,21,141,149]
N = 4
BF = ml_dtypes.bfloat16
def gentries(a):
    return np.ascontiguousarray(a.reshape(8, 16, -1).transpose(0, 2, 1)).reshape(8, -1)
def gtable(e):
    e = np.asarray(e); return np.ascontiguousarray(e.reshape(8, -1, 16).transpose(0, 2, 1)).reshape(128, -1).astype(np.int32)
W0, P, S, R, A, W = 2048, 256, 2, 4, 512, 3072
WT = [1, 64, 5, 83, 17, 131, 29, 211, 43, 157, 61, 239, 71, 113, 97, 199]
def parts(rng):
    x = rng.integers(0, 64, (N, 8, 16, W0)); rich = rng.permutation(8)[:3]; x[:, rich] = 48 + (x[:, rich] >> 2)
    fr = rng.integers(0, A, (N, 8, W0))
    hot = np.argsort(rng.random((N, 8, W0)), axis=-1)[..., :256]
    often = np.take_along_axis(hot, rng.integers(0, 256, (N, 8, A * 16)), 2).reshape(N, 8, A, 16)
    C = np.where(rng.random((N, 8, A, 16)) < 0.4, often, rng.integers(0, W0, (N, 8, A, 16)))
    return x, fr, C, rng.integers(0, 64, (N, 8, P, 16)), rng.integers(0, A, (N, 8, P))
def pack(x, fr, C, z, b):
    return {"x0": np.ascontiguousarray(x.reshape(N, 128, W0)).astype(np.float32).astype(BF), "fr0": np.ascontiguousarray(fr).astype(np.int32),
            "pl": np.ascontiguousarray(C.transpose(0, 1, 3, 2).reshape(N, 128, A)).astype(np.int32),
            "z0": np.ascontiguousarray(z.transpose(0, 1, 3, 2).reshape(N, 128, P)).astype(np.float32).astype(BF), "b0": np.stack([gtable(a) for a in b])}
def setup_inputs(rng):
    return pack(*parts(rng))
def setup_inputs_spread(rng):
    x, fr, C, z, b = parts(rng)
    x = (np.exp2(6 * rng.random((N, 8, 1, W0))) * rng.random((N, 8, 16, W0))).astype(np.int64)
    z = (np.exp2(6 * rng.random((N, 8, P, 1))) * rng.random((N, 8, P, 16))).astype(np.int64)
    fr[:, ::2] = (A * rng.random((N, 4, W0)) ** 3).astype(np.int64)
    C = (W0 * rng.random((N, 8, A, 16)) ** 2).astype(np.int64); b = (A * rng.random((N, 8, P)) ** 2).astype(np.int64)
    return pack(x, fr, C, z, b)
def setup_inputs_ends(rng):
    x, fr, C, z, b = parts(rng)
    sd = rng.integers(0, 2, (N, 8, W0)); sd[..., 0] = 0; sd[..., W0 - 1] = 1; sd[:, 7, 1] = 1; fr = sd * (A - 1)
    kd = rng.random((N, 8, 1, W0)); mix = 63 * rng.integers(0, 2, (N, 8, 16, W0))
    less = 63 - (np.arange(16)[:, None] == rng.integers(0, 16, (N, 8, 1, W0)))
    x = np.where(kd < 0.45, 63, np.where(kd < 0.6, less, np.where(kd < 0.75, 0, mix)))
    x[:, 0::2, :, 0] = 0; x[:, 0::2, :, W0 - 1] = 0; x[:, 1::2, :, 0] = 63; x[:, 1::2, :, W0 - 1] = 63
    x[:, 7, :, 1] = 63; x[:, 7, 5, 1] = 62
    ps = rng.integers(0, 2, (N, 8, A)); ps[..., 0] = 0; ps[..., A - 1] = 1; ps = ps[..., None]
    by = np.argsort(sd + 0.5 * rng.random((N, 8, W0)), axis=-1); c1 = np.sum(sd, axis=-1)[:, :, None, None]; u = rng.random((N, 8, A, 16))
    ix = np.where(ps == 1, W0 - c1 + (u * c1).astype(np.int64), (u * (W0 - c1)).astype(np.int64))
    some = np.take_along_axis(by, ix.reshape(N, 8, A * 16), 2).reshape(N, 8, A, 16)
    C = np.where(rng.random((N, 8, A, 16)) < 0.68, ps * (W0 - 1), some)
    kz = rng.random((N, 8, P, 1))
    z = np.where(kz < 0.3, 63, np.where(kz < 0.4, 0, 63 * rng.integers(0, 2, (N, 8, P, 16))))
    b = np.where(rng.random((N, 8, P)) < 0.7, (A - 1) * rng.integers(0, 2, (N, 8, P)), b)
    for a in (A - S, A - 1):
        C[:, 7, a, :15] = 1; C[:, 7, a, 15] = W0 - 1
    z[:, 7, P - 1] = 63; b[:, 7, P - 1] = A - 1
    return pack(x, fr, C, z, b)
def setup_inputs_corners(rng):
    x, fr, C, z, b = parts(rng); o = [int(v) for v in rng.permutation(8)]
    fr[:, o[0]] = (fr[:, o[0]] // N) * N + np.arange(N)[:, None]
    fr[:, o[1]] = int(rng.integers(0, A))
    g = o[2]; zz = rng.integers(0, 64, (N, P, 16)); zz[..., :2] = 0; want = S * np.arange(P)
    need = (want[None, :] - np.sum(zz * np.array(WT), axis=-1)) & (A - 1); zz[..., 0] = need & 63; zz[..., 1] = need >> 6
    x[:, g] = 0; fr[:, g, :A] = np.arange(A); C[:, g, :, 0] = np.arange(A); z[:, g] = zz; b[:, g] = want
    g = o[3]; few = np.argsort(rng.random((N, W0)), axis=-1)[:, :320]; few[:, 0] = 0; few[:, 319] = W0 - 1
    x[:, g] = 63; C[:, g] = np.take_along_axis(few, rng.integers(0, 320, (N, A * 16)), 1).reshape(N, A, 16)
    g = o[4]; C[:, g] = rng.integers(0, W0, (N, A, 1)); C[:, g, ::7] = 0; C[:, g, A - 1] = W0 - 1
    fr[:, g] = rng.integers(0, 8, (N, W0))
    g = o[5]; own = np.arange(A)[:, None] + np.zeros((1, 16), np.int64); kd = rng.integers(0, 4, (N, A, 16))
    C[:, g] = np.where(kd == 0, 0, np.where(kd == 1, W0 - 1, np.where(kd == 2, own, C[:, g])))
    x[:, g] = 63 * rng.integers(0, 2, (N, 1, W0)); b[:, g] = np.where(rng.random((N, P)) < 0.5, np.arange(P) * S, b[:, g])
    g = o[6]; z[:, g, ::2] = 0; z[:, g, 1::2] = 63; x[::2, g] = 0
    g = o[7]; bl = np.arange(P // 4); ev = (bl & 1) == 0; od = ~ev; e8 = np.arange(8); amt = 8 * rng.integers(1, 4, P // 4)
    pt = S * (4 * bl[:, None] + (e8 >> 1)[None, :]) + (e8 & 1)[None, :]
    kind = np.zeros((P // 4, 8, 4), np.int64) + np.array([1, 2, 2, 7, 5, 7, 7, 7])[None, :, None]
    kind[:, 0, 0] = 6; kind[:, 3, 0] = 6; kind[ev, 3, 1] = 3; kind[ev, 4, 0] = 6; kind[ev, 4, 1] = 3; kind[ev, 7, :3] = 3; kind[od, 6, 0] = 3
    nme = np.zeros((A, 4), np.int64); nme[pt] = pt[bl[:, None, None], kind]
    bal = np.zeros((A, 4), np.int64); bal[pt[od, 0], 0] = 2 * amt[od]; bal[pt[od, 3], 0] = amt[od]; bal[pt[od, 6], 0] = amt[od]
    pm = np.argsort(rng.random((N, W0)), axis=-1)[:, :4 * A]; rk = np.arange(N)[:, None]
    fr[rk, g, pm] = nme.reshape(-1)[None, :]; x[:, g] = 0; x[rk, g, 1, pm] = bal.reshape(-1)[None, :]
    C[:, g] = pm[:, 4 * np.arange(A)[:, None] + np.minimum(np.arange(16), 3)[None, :]]
    want = pt[:, [3, 4, 2, 0]].reshape(P); zz = rng.integers(0, 64, (N, P, 16)); zz[..., 0] = 0; zz[..., 10] = 0; zz[..., 1] = np.repeat(amt, 4)
    need = (want[None, :] - np.sum(zz * np.array(WT), axis=-1)) & (A - 1); zz[..., 10] = need // WT[10]; zz[..., 0] = need - WT[10] * zz[..., 10]
    z[:, g] = zz; b[:, g] = want
    return pack(x, fr, C, z, b)
def setup_inputs_crowd(rng):
    x, fr, C, z, b = parts(rng); o = [int(v) for v in rng.permutation(8)]
    for j in (0, 1):
        g = o[j]; one = np.argsort(rng.random((N, W0)), axis=-1)[:, :16]
        fr[:, g] = int(rng.integers(0, A)); x[:, g] = rng.integers(0, 41, (N, 16, W0)); z[:, g] = rng.integers(41, 64, (N, P, 16))
        for r in range(N):
            other = C[r, g, 0].copy(); C[r, g] = one[r]; x[r, g, :, int(one[r, int(rng.integers(0, 16))])] = 63
            if j == 1: C[r, g, S * int(rng.integers(0, P))] = other
    for j in (2, 3):
        g = o[j]; B = int(rng.integers(0, A))
        fr[:, g] = int(rng.integers(0, A)); x[:, g] = rng.integers(0, 41, (N, 16, W0)); z[:, g] = rng.integers(41, 64, (N, P, 16))
        C[:, g] = np.arange(A)[:, None] + A * (np.arange(16)[None, :] % (W0 // A)); x[:, g, :, B] = 63; b[:, g] = B
        if j == 3:
            for r in range(N): b[r, g, int(rng.integers(0, P))] = (B + 1) % A
    g = o[4]; fr[:, g] = (A - 1) * rng.integers(0, 2, (N, W0))
    pay = np.arange(A) // S; pn = np.arange(P); rk = np.arange(N)[:, None]
    for j in (5, 6):
        g = o[j]; bal = np.zeros((A, 4), np.int64)
        if j == 5:
            am = 8 * rng.integers(1, 4, P); nxt = S * ((pn + 1) % P); nme = (S * pay)[:, None] + np.zeros((1, 4), np.int64)
            nme[S * pn, 0] = nxt; nme[S * pn, 1:] = (S * pn + 1)[:, None]; bal[S * pn, 0] = am; bal[S * pn, 1:] = 2 * am[:, None]
            bal[S * pn + 1, 1:] = np.roll(am, 1)[:, None]; want = nxt + 1; z1 = 2 * am
        else:
            bl = np.arange(P // 4); ev = (bl & 1) == 0; am = 8 * rng.integers(1, 3, P // 4); p0, p1, p2, p3 = [S * (4 * bl + v) for v in range(4)]
            nme = np.repeat(np.stack([p0 + 1, p1 + 1, p2, p2 + 1], axis=1).reshape(P), S)[:, None] + np.zeros((1, 4), np.int64)
            up = np.where(ev, p2 + 2 % S, p2 + 1)
            nme[p0, 0] = p1; nme[p1 + 1, 0] = p3 + 1; nme[up, 0] = p3 + 1; nme[p3 + 1] = p1[:, None]
            bal[p0, 0] = 3 * am; bal[p1 + 1, 0] = am; bal[up, 0] = am; bal[p3 + 1, 1:] = 3 * am[:, None]
            want = np.stack([p3 + 1, p0, p0, p1 + 1], axis=1).reshape(P)
            z1 = np.stack([3 * am + np.where(ev, 0, 8), am, am * np.where(ev, 1, 2), am], axis=1).reshape(P)
        pm = np.argsort(rng.random((N, W0)), axis=-1)[:, :4 * A]
        fr[rk, g, pm] = nme.reshape(-1)[None, :]; x[:, g] = 0; x[rk, g, 1, pm] = bal.reshape(-1)[None, :]
        C[:, g] = pm[:, 4 * np.arange(A)[:, None] + np.minimum(np.arange(16), 3)[None, :]]
        zz = rng.integers(0, 64, (N, P, 16)); zz[..., 0] = 0; zz[..., 10] = 0; zz[..., 1] = z1
        need = (want[None, :] - np.sum(zz * np.array(WT), axis=-1)) & (A - 1); zz[..., 10] = need // WT[10]; zz[..., 0] = need - WT[10] * zz[..., 10]
        z[:, g] = zz; b[:, g] = want
    g = o[7]; pm = np.argsort(rng.random((N, W0)), axis=-1)[:, :2 * A]
    nme = np.zeros((A, 2), np.int64); nme[:, 0] = 1; nme[S * pn, 0] = 0; nme[:, 1] = A - 1
    fr[rk, g, pm] = nme.reshape(-1)[None, :]
    for r in range(N):
        x[r, g] = 63 * rng.integers(0, 2, (1, W0)); x[r, g][:, pm[r, 0::2]] = 63; x[r, g][:, pm[r, 1::2]] = 0
    C[:, g] = pm[:, 2 * np.arange(A)[:, None] + (np.arange(16) == 15).astype(np.int64)[None, :]]
    z[:, g] = 63; b[:, g] = S * pn + 1
    return pack(x, fr, C, z, b)
def setup_inputs_ties(rng):
    x, fr, C, z, b = parts(rng)
    x = rng.integers(2, 5, (N, 8, 1, W0)) + np.zeros((1, 1, 16, 1), np.int64); z = rng.integers(2, 4, (N, 8, P, 16)); z[:, :, ::3] = 3
    fr[:, ::2] = rng.integers(0, 24, (N, 4, W0))
    return pack(x, fr, C, z, b)
def check_inputs(d):
    bad = []
    for k, lo, hi in (("x0", 0, 63), ("fr0", 0, A - 1), ("pl", 0, W0 - 1), ("z0", 0, 63), ("b0", 0, A - 1)):
        a = np.asarray(d[k]).astype(np.float64)
        if not (np.min(a) >= lo and np.max(a) <= hi): bad.append("range of " + k)
        elif not np.all(a == np.floor(a)): bad.append("whole numbers in " + k)
    return bad
def first(key):
    ok = np.zeros(len(key), bool); ok[np.unique(key, return_index=True)[1]] = True
    return ok
def reference(x0, fr0, pl, z0, b0):
    X = np.zeros((N, 8, W, 16), np.int32); X[:, :, :W0] = x0.astype(np.float32).astype(np.int32).reshape(N, 8, 16, W0).transpose(0, 1, 3, 2)
    nm = np.zeros((N, 8, W), np.int64); nm[:, :, :W0] = fr0
    sup = np.zeros((N, 8, 2, R * P), np.int64)
    C = np.ascontiguousarray(pl.astype(np.int64).reshape(N, 8, 16, A).transpose(0, 1, 3, 2))
    z = np.ascontiguousarray(z0.astype(np.float32).astype(np.int32).reshape(N, 8, 16, P).transpose(0, 1, 3, 2))
    b = np.stack([gentries(a) for a in b0]).astype(np.int64)
    g2 = np.arange(8)[:, None]; g3 = g2[:, :, None]; pi = np.arange(P)[None, :]; wt = np.array(WT)
    for t in range(R):
        s = t % S; base = X.copy(); took = np.zeros_like(X); back = np.zeros_like(X); D = C.copy(); made = []
        for r in range(N):
            q = (r + 1 + s) % N
            La = C[r][:, s::S]; Ma = C[q][g2, b[r]]
            y = X[r][g3, La]; h = X[q][g3, Ma]
            fk = np.add.reduce(np.minimum(y, z[r][:, :, None, :]), axis=3); hl = np.add.reduce(np.minimum(h, z[r][:, :, None, :]), axis=3)
            fits = nm[r][g3, La][:, :, :, None] == nm[q][g3, Ma][:, :, None, :]
            score = np.where(fits, fk[:, :, :, None] + hl[:, :, None, :], -1).reshape(8, P, 256)
            best = np.argmax(score, axis=2); found = np.max(score, axis=2) >= 0
            k = np.where(found, best >> 4, np.argmin(fk, axis=2)); l = best & 15
            c = La[g2, pi, k]; m = Ma[g2, pi, l]; yk = y[g2, pi, k]
            v = np.minimum(np.minimum(yk, z[r]), h[g2, pi, l])
            gb, ib = np.nonzero(found)
            ok = first(gb * W + c[gb, ib]); gb, ib = gb[ok], ib[ok]
            ok = first(gb * W + m[gb, ib]); gb, ib = gb[ok], ib[ok]
            j = P * t + ib; cb, mb, vb = c[gb, ib], m[gb, ib], v[gb, ib]
            took[r, gb, cb] += vb; took[q, gb, mb] += vb
            made.append((r, gb, W0 + j, vb)); nm[r, gb, W0 + j] = b[r][gb, ib]
            sup[r, gb, 0, j] = cb; sup[r, gb, 1, j] = mb; D[r, gb, S * ib + s, k[gb, ib]] = W0 + j
            gc, ic = np.nonzero(~found & (c >= W0)); n = c[gc, ic] - W0; w = yk[gc, ic]
            base[r, gc, W0 + n] = 0
            np.add.at(back[r], (gc, sup[r, gc, 0, n]), w); np.add.at(back[q], (gc, sup[r, gc, 1, n]), w)
            D[r, gc, S * ic + s, k[gc, ic]] = sup[r, gc, 0, n]
            if t < R - 1:
                z[r] = np.abs(z[r] - yk); b[r] = np.add.reduce(z[r] * wt, axis=2) & (A - 1)
        X = np.minimum(63, np.maximum(base - took, 0) + back); C = D
        for r, gb, n, vb in made: X[r, gb, n] = vb
    rec = np.concatenate([nm[:, :, W0:], sup[:, :, 0], sup[:, :, 1]], axis=1)
    return {"xo": np.ascontiguousarray(X.transpose(0, 1, 3, 2)).reshape(N, 128, W).astype(np.float32).astype(BF),
            "co": np.ascontiguousarray(C.transpose(0, 1, 3, 2)).reshape(N, 128, A).astype(np.float32), "rec": rec.astype(np.float32)}

@@ -1,0 +1,785 @@
+from concourse.bass import DstId, RemoteDMATransfer
+from concourse.mybir import AluOpType, AxisListType, ActivationFunctionType
+
+OP = AluOpType
+AF = ActivationFunctionType
+NR, W0, P, R = 4, 2048, 256, 4
+WT = [1, 64, 5, 83, 17, 131, 29, 211, 43, 157, 61, 239, 71, 113, 97, 199]
+XW = 3328
+PIECE = 704
+MID = 1536.0
+NDVE = 2
+ZACT = 8
+
+F, H16, B16, I32, U16 = "float32", "float16", "bfloat16", "int32", "uint16"
+SCRATCH = {
+    "X": ("sbuf", [128, XW], B16), "XF0": ("sbuf", [128, XW], B16), "XF1": ("sbuf", [128, XW], B16),
+    "LH": ("sbuf", [128, 2304], B16), "LB": ("sbuf", [128, 192], U16), "TV": ("sbuf", [128, 768], B16),
+    "NB": ("sbuf", [128, 512], B16), "NV": ("sbuf", [128, 768], B16), "TP": ("sbuf", [128, 768], B16),
+    "TB": ("sbuf", [128, 1024], F), "TF0": ("sbuf", [128, 1024], F), "TF1": ("sbuf", [128, 1024], F),
+    "PL": ("sbuf", [128, 512], I32), "FR": ("sbuf", [128, 128], I32), "FR16": ("sbuf", [128, 128], H16),
+    "FW": ("sbuf", [128, 2048], F), "NG": ("sbuf", [128, 4096], H16), "N0": ("sbuf", [128, 256], H16),
+    "MY": ("sbuf", [128, 4096], H16), "MH": ("sbuf", [128, 4096], H16), "ZR": ("sbuf", [128, 4096], B16),
+    "ZB": ("sbuf", [128, 512], B16),
+    "LO": ("sbuf", [128, 512], U16), "MO": ("sbuf", [128, 256], U16), "BO16": ("sbuf", [128, 16], U16),
+    "BI": ("sbuf", [128, 64], I32), "BH": ("sbuf", [128, 16], H16),
+    "CM": ("sbuf", [128, 512], H16), "NL": ("sbuf", [128, 256], H16), "NM": ("sbuf", [128, 256], H16),
+    "FS": ("sbuf", [128, 256], H16), "HS": ("sbuf", [128, 256], H16),
+    "NFK": ("sbuf", [128, 256], F), "KN": ("sbuf", [128, 16], F), "KI": ("sbuf", [128, 64], I32),
+    "RR": ("sbuf", [128, 16], F), "VA": ("sbuf", [128, 32], H16), "VB": ("sbuf", [128, 32], H16),
+    "VT": ("sbuf", [128, 128], H16), "WK": ("sbuf", [128, 1024], H16), "KB": ("sbuf", [128, 512], H16),
+    "LM": ("sbuf", [128, 32], U16), "EE": ("sbuf", [128, 2176], H16), "E2": ("sbuf", [128, 2176], H16),
+    "ST": ("sbuf", [128, 256], H16), "BD": ("sbuf", [128, 256], H16),
+    "M1": ("sbuf", [128, 256], B16), "VY": ("sbuf", [128, 1024], B16), "TM": ("sbuf", [128, 768], B16),
+    "RV": ("sbuf", [128, 96], F), "DM": ("sbuf", [128, 128], F), "G2": ("sbuf", [128, 96], F),
+    "OH": ("sbuf", [128, 32], U16), "OF": ("sbuf", [128, 128], U16),
+    "LV": ("sbuf", [128, 1536], B16), "LF": ("sbuf", [128, 128], U16),
+    "RC": ("sbuf", [128, 48], F), "RH": ("sbuf", [128, 48], H16), "RO": ("sbuf", [8, 768], F),
+    "T1": ("sbuf", [128, 256], F), "T2": ("sbuf", [128, 768], H16), "MK": ("sbuf", [128, 256], H16),
+    "CO": ("sbuf", [128, 512], F),
+    "PI": ("sbuf", [128, 8], I32), "PC": ("sbuf", [128, 8], F),
+    "IOX": ("sbuf", [128, 256], F), "IOA": ("sbuf", [128, 512], F), "IOB": ("sbuf", [128, 512], F),
+    "RK": ("sbuf", [128, 512], H16), "RL": ("sbuf", [128, 512], H16), "ID": ("sbuf", [128, 256], H16),
+    "IB": ("sbuf", [128, 256], B16),
+    "U1": ("sbuf", [128, 144], H16), "US": ("sbuf", [128, 144], H16), "UW": ("sbuf", [128, 144], B16),
+    "BK": ("sbuf", [128, 640], H16), "SJ": ("sbuf", [128, 2048], H16), "DG": ("sbuf", [128, 16], F),
+    "WR": ("sbuf", [128, 32], F), "WC": ("sbuf", [128, 2], F), "SG": ("sbuf", [128, 768], F),
+    "THR": ("sbuf", [128, 256], F), "TIE": ("sbuf", [128, 768], H16), "DUM": ("sbuf", [128, 16], F),
+}
+for _b in range(8):
+    SCRATCH["P%d" % _b] = ("psum", [128, 512], F)
+
+MSGS = ["c0", "x0", "n0", "u1"] + ["v%d" % t for t in range(R)] + ["o%d" % t for t in range(R)] + \
+       ["x1", "x2", "x3", "tb0", "tb1"] + [m + str(t) for m in ("a", "ao", "b", "bo", "ta") for t in range(R - 1)]
+HAND = [0, 512, 1024]
+NDMA = 16
+SEMAPHORES = ["sv", "sa", "sp", "sg"] + ["d%d" % i for i in range(NDMA)] + \
+             ["arr_" + m for m in MSGS] + ["snt_" + m for m in MSGS]
+ENG_SEM = {"v": "sv", "a": "sa", "p": "sp", "g": "sg"}
+LAND = [0, 256, 512, 1024]
+
+
+def reg(name, a=None, b=None, step=1, p0=0, p1=128, off=None):
+    if a is None:
+        a, b = 0, SCRATCH[name][1][1]
+    return {"n": name, "a": a, "b": b, "s": step, "p0": p0, "p1": p1, "off": off}
+
+
+def ap(T, r):
+    if not isinstance(r, dict):
+        return r
+    t = T[r["n"]]
+    if r["off"] is not None:
+        return t[:, r["a"]:r["b"]].indirect(ap(T, r["off"]))
+    if r["s"] == 1:
+        return t[r["p0"]:r["p1"], r["a"]:r["b"]]
+    return t[r["p0"]:r["p1"], r["a"]:r["b"]:r["s"]]
+
+
+def spans(rs):
+    return [(r["n"], r["a"], r["b"], r["s"]) for r in rs if isinstance(r, dict)]
+
+
+def routes(T, topo, src, dst, mode):
+    other = T.cores[(T.rank_of(src) + 1) % NR]
+    ports = [c for c in topo.cores_of(src) if T.rank_of(c) is None and topo.may_write(c, dst) and topo.may_write(c, other)]
+    near = [c for c in ports if topo.die(c) == topo.die(src)]
+    far = [c for c in ports if topo.die(c) != topo.die(src)]
+    if topo.may_write(src, dst):
+        near = [None, None]
+    return {"near": near[:2], "near2": near[1:2], "far": far[:2], "all": near[:2] + far[:2]}[mode]
+
+
+def messages(T, topo):
+    ms = []
+
+    def xship(t):
+        w = (W0 + P * max(t - 1, 0)) // 4
+        xf = "XF%d" % (t % 2)
+        return ("x%d" % t, -1 - t % 2, "all",
+                [(reg("X", j * w, (j + 1) * w), reg("X", t * PIECE, t * PIECE + w), reg(xf, j * w, (j + 1) * w)) for j in range(4)])
+
+    def tab(name, step, cols, stage, mode="far", w=256):
+        tf = "TF%d" % (-step - 1)
+        return (name, step, mode, [(reg("TB", c, c + w), reg(stage[0], stage[1], stage[1] + w), reg(tf, c, c + w)) for c in cols])
+
+    def plain(name, step, mode, pairs):
+        return (name, step, mode, [(a, b, b) for a, b in pairs])
+
+    ms += [tab("c0", -1, [0, 256], ("TB", 0)), xship(0), tab("n0", -1, [512, 640, 768, 896], ("TB", 256), "all", 128),
+           tab("u1", -2, [256, 768], ("TB", 512)), xship(1)]
+    for t in range(R):
+        s, wx = t % 2, W0 + P * t
+        w, n = (128, 16) if t < 2 else (256, 32)
+        s0, l0, h0 = 512 * s, LAND[t], HAND[t % 3]
+        ms.append(plain("v%d" % t, 1 + s, "near", [(reg("VY", s0 + j * w, s0 + (j + 1) * w), reg("LV", l0 + j * w, l0 + (j + 1) * w)) for j in range(2)]))
+        ms.append(plain("o%d" % t, 1 + s, "near", [(reg("OF", 32 * t, 32 * t + n), reg("LF", 32 * t, 32 * t + n))]))
+        if t == R - 1:
+            break
+        xf = "XF%d" % (1 - s)
+        ms.append(plain("ao%d" % t, s - 2, "near2", [(reg("OH", 0, n), reg("LB", 64 * t, 64 * t + n))]))
+        ms.append(plain("a%d" % t, s - 2, "near", [(reg("TM", 512, 768), reg("LH", h0, h0 + 256)), (reg("NB", 0, 256), reg(xf, wx, wx + 256))] +
+                        ([(reg("NB", 256, 512), reg("LH", h0 + 1024, h0 + 1280))] if t >= 2 else [])))
+        ms.append(tab("ta%d" % t, s - 2, [256 * s, 512 + 256 * s, 256 * s + 128, 640 + 256 * s], [("TB", 768), ("TF0", 0), ("TF0", 256)][t], "all", 128))
+        ms.append(plain("bo%d" % t, s - 2, "near2", [(reg("LF", 32 * t, 32 * t + n), reg("LB", 64 * t + 32, 64 * t + 32 + n))]))
+        if t < 2:
+            ms.append(plain("b%d" % t, s - 2, "near", [(reg("TV", 128 * j, 128 * j + 128), reg("LH", h0 + 256 + 128 * j, h0 + 384 + 128 * j)) for j in range(2)]))
+            ms.append(xship(t + 2))
+            ms.append(tab("tb%d" % t, -1 - s, [256 * s, 512 + 256 * s], ("TF0", 512 + 256 * t)))
+        else:
+            ms.append(plain("b%d" % t, s - 2, "near", [(reg("TV", 384 * j, 384 * j + 384), reg("LH", h0 + 256 + 384 * j, h0 + 640 + 384 * j)) for j in range(2)]))
+    return ms
+
+
+def mask_of(engs):
+    m = 0
+    for e in engs:
+        m |= 1 << e
+    return m
+
+
+def plan_message(T, topo, src, msg):
+    name, step, mode, pieces = msg
+    dst = T.cores[(T.rank_of(src) + step) % NR]
+    ways = routes(T, topo, src, dst, mode)
+    way = [ways[j % len(ways)] for j in range(len(pieces))]
+    direct = [j for j in range(len(pieces)) if way[j] is None]
+    handed = [j for j in range(len(pieces)) if way[j] is not None]
+    engs, used, total = {}, [], 0
+    if direct:
+        engs.update(deal(topo.engines(src, dst), direct))
+        used = topo.engines(src, dst)
+        total += sum(len(engs[j]) for j in direct)
+    if handed:
+        engs.update(deal([e for e in topo.engines(src, way[handed[0]]) if e not in used], handed))
+        for c in set(way[j] for j in handed):
+            second = deal(topo.engines(c, dst), [j for j in handed if way[j] == c])
+            total += sum(len(e) for e in second.values())
+    return dst, way, engs, total
+
+
+def deal(pool, items):
+    n = 1
+    while 2 * n * len(items) <= len(pool):
+        n *= 2
+    return {j: pool[q * n:(q + 1) * n] for q, j in enumerate(items)}
+
+
+def write(g, T, topo, core, name, trs):
+    arr, snt = T.sem["arr_" + name], T.sem["snt_" + name]
+    if len(trs) == 1:
+        to, engs, a, b = trs[0]
+        rid, pid = topo.addr(to, core)
+        g.remote_dma(ap(T, b), ap(T, a), arr, snt, pid, rid, mask_of(engs))
+    else:
+        g.remote_dma_fused([RemoteDMATransfer(dst_ids=[DstId(rid=topo.addr(to, core)[0], pnc=topo.addr(to, core)[1])], dma_engine_mask=mask_of(engs),
+                                              remote_sem=arr, src=ap(T, a), dst=ap(T, b)) for to, engs, a, b in trs], local_sem=snt)
+
+
+def carrier_program(g, core, T, topo):
+    owners = [c for c in topo.cores_of(core) if T.rank_of(c) is not None]
+    if not owners:
+        return
+    src = owners[0]
+    sent = []
+    for msg in messages(T, topo):
+        dst, way, engs, total = plan_message(T, topo, src, msg)
+        mine = [j for j in range(len(way)) if way[j] == core]
+        if mine:
+            second = deal(topo.engines(core, dst), mine)
+            g.wait_ge(T.sem["arr_" + msg[0]], sum(len(engs[j]) for j in mine))
+            write(g, T, topo, core, msg[0], [(dst, second[j], msg[3][j][1], msg[3][j][2]) for j in mine])
+            sent.append((msg[0], sum(len(e) for e in second.values())))
+    for name, n in sent:
+        g.wait_ge(T.sem["snt_" + name], n)
+
+
+def rank_program(g, core, T, topo):
+    rank = T.rank_of(core)
+    if rank is None:
+        carrier_program(g, core, T, topo)
+        return
+    ops = []
+    ndma = [0]
+    msgs = {m[0]: m for m in messages(T, topo)}
+    queue = {"v": g.vector, "a": g.scalar, "p": g.tensor, "g": g, "s": g.sync}
+
+    def add(eng, fn, outs, ins, sem=None):
+        rd, wr = spans(ins), spans(outs)
+        for r in list(ins) + list(outs):
+            if isinstance(r, dict) and r["off"] is not None:
+                rd += spans([r["off"]])
+        ops.append({"e": eng, "f": fn, "r": rd, "w": wr, "sem": sem})
+
+    A = lambda r: ap(T, r)
+
+    def copy(out, in_):
+        add("v", lambda: g.vector.tensor_copy(A(out), A(in_)), [out], [in_])
+
+    def tt(out, a, b, op):
+        add("v", lambda: g.vector.tensor_tensor(A(out), A(a), A(b), op), [out], [a, b])
+
+    def ts(out, a, s1, op0, s2=None, op1=None):
+        if op1 is None:
+            add("v", lambda: g.vector.tensor_scalar(A(out), A(a), A(s1), None, op0), [out], [a, s1])
+        else:
+            add("v", lambda: g.vector.tensor_scalar(A(out), A(a), A(s1), A(s2), op0, op1), [out], [a, s1, s2])
+
+    def fill(out, c):
+        add("v", lambda: g.vector.memset(A(out), c), [out], [])
+
+    def red(out, a, op, absolute=False):
+        add("v", lambda: g.vector.tensor_reduce(A(out), A(a), AxisListType.X, op, apply_absolute_value=absolute), [out], [a])
+
+    def scan(out, d0, d1, init, op0, op1):
+        add("v", lambda: g.vector.tensor_tensor_scan(A(out), A(d0), A(d1), init, op0, op1), [out], [d0, d1])
+
+    def act(out, a, func=AF.Identity, bias=0.0, scale=1.0):
+        add("a", lambda: g.scalar.activation(A(out), A(a), func, bias=A(bias), scale=A(scale)), [out], [a, bias, scale])
+
+    def mm(out, lhs, rhs, start, stop):
+        add("p", lambda: g.tensor.matmul(A(out), A(lhs), A(rhs), start, stop), [out], [lhs, rhs])
+
+    def total(out, terms):
+        for q, (lhs, rhs) in enumerate(terms):
+            mm(out, lhs, rhs, q == 0, q == len(terms) - 1)
+
+    def iota(out, pattern, base, cm):
+        if SCRATCH[out["n"]][2] == I32:
+            add("g", lambda: g.iota(A(out), pattern, base, cm), [out], [])
+        else:
+            add("g", lambda: g.iota(A(out), pattern, base, cm, allow_small_or_imprecise_dtypes=True), [out], [])
+
+    def dma(eng, pairs):
+        name = "d%d" % ndma[0]
+        ndma[0] += 1
+
+        def fn():
+            for out, in_ in pairs:
+                queue[eng].dma_start(A(out), A(in_)).then_inc(T.sem[name], 16)
+        add(eng, fn, [p[0] for p in pairs], [p[1] for p in pairs], sem=(name, 16 * len(pairs)))
+
+    def send(name, after=()):
+        msg = msgs[name]
+        dst, way, engs, _ = plan_message(T, topo, core, msg)
+        trs = [(dst, engs[j], p[0], p[2]) if way[j] is None else (way[j], engs[j], p[0], p[1]) for j, p in enumerate(msg[3])]
+        add("g", lambda: write(g, T, topo, core, name, trs), [], [p[0] for p in msg[3]] + list(after),
+            sem=("snt_" + name, sum(len(e) for e in engs.values())))
+
+    def arrive(name):
+        msg = msgs[name]
+        src = T.cores[(rank - msg[1]) % NR]
+        add("x", None, [p[2] for p in msg[3]], [], sem=("arr_" + name, plan_message(T, topo, src, msg)[3]))
+
+    def bank(b, a=0, e=512, step=1, p1=128):
+        return reg("P%d" % b, a, e, step, 0, p1)
+
+    col = lambda n, c: reg(n, c, c + 1)
+    P16, P32, PG, PP, PG16 = [col("PC", c) for c in range(5)]
+    BO, BOM, BO128, BOBIG, BOW = [reg("BK", 128 * j, 128 * j + 128) for j in range(5)]
+    ID, NID, IDB, NIDB = reg("ID", 0, 128), reg("ID", 128, 256), reg("IB", 0, 128), reg("IB", 128, 256)
+
+    def to_slots(out, src, a):
+        total(out, [(reg("U1", 15 - k, 143 - k), reg(src, a + k, a + 2048, 16)) for k in range(16)])
+
+    def to_list(out, sel, src, a, n):
+        total(out, [(reg(sel, 15 - j, 143 - j), reg(src, a + j, a + n, 16)) for j in range(16)])
+
+    def payee(t):
+        ts(reg("BI", 16, 32), reg("BI", 0, 16), 513.0, OP.mult)
+        copy(reg("RV", 48 * (t % 2), 48 * (t % 2) + 16), reg("BI", 0, 16))
+        ts(reg("BI", 32, 48), reg("BI", 16, 32), 1, OP.logical_shift_right, 511, OP.bitwise_and)
+        if t < R - 1:
+            ts(reg("BH"), reg("BI", 0, 16), 16.0, OP.mult)
+        copy(reg("BO16"), reg("BI", 32, 48))
+
+    dma("s", [(reg("FR"), T.fr0[:])])
+    dma("a", [(reg("ZB", 0, 256), T.z0[:])])
+    dma("a", [(reg("PL"), T.pl[:])])
+    dma("s", [(reg("X", 0, 1024), T.x0[:, 0:1024])])
+    dma("a", [(reg("X", 1024, 2048), T.x0[:, 1024:2048])])
+    dma("s", [(reg("BI", 0, 16), T.b0[:])])
+    iota(col("PI", 0), [[0, 1]], 0, 1)
+    iota(reg("IOA", 0, 128), [[1, 8], [0, 16]], 0, 0)
+    iota(reg("IOX"), [[1, 256]], 0, 0)
+    fill(reg("X", W0, XW), 0.0)
+    ts(col("PI", 1), col("PI", 0), 15, OP.bitwise_and)
+    ts(col("PI", 2), col("PI", 0), 31, OP.bitwise_and)
+    ts(col("PI", 3), col("PI", 0), 4, OP.logical_shift_right)
+    ts(col("PI", 5), col("PI", 0), 112, OP.bitwise_and)
+    copy(col("PI", 4), col("PI", 0))
+    copy(reg("PC", 0, 5), reg("PI", 1, 6))
+    ts(BO, reg("IOA", 0, 128), PG, OP.is_equal)
+    ts(reg("DG"), reg("IOX", 0, 16), P16, OP.is_equal)
+    for j in range(16):
+        if j % 4 == 3:
+            act(reg("SJ", 128 * j, 128 * j + 128), BO, AF.Copy, scale=col("DG", j))
+        else:
+            ts(reg("SJ", 128 * j, 128 * j + 128), BO, col("DG", j), OP.mult)
+    iota(reg("IOA", 128, 512), [[1, 24], [0, 16]], 8, 0)
+    ts(reg("U1"), reg("IOX", 0, 144), 15.0, OP.subtract, PG16, OP.is_equal)
+    copy(reg("FR16"), reg("FR"))
+    copy(reg("TB", 0, 256), reg("PL", 0, 512, 2))
+    copy(reg("TB", 256, 512), reg("PL", 1, 512, 2))
+    send("c0")
+    send("x0")
+    iota(reg("IOB"), [[16, 2], [0, 16], [1, 16]], 0, 0)
+    for k in range(ZACT):
+        act(reg("ZR", k, 4096, 16), reg("ZB", 0, 256), AF.Copy)
+    for j in range(16):
+        mm(bank(j // 4, 128 * (j % 4), 128 * (j % 4) + 128), reg("SJ", 128 * j, 128 * j + 128), reg("FR16"), True, True)
+    copy(reg("LO"), reg("TB", 0, 512))
+    act(reg("FW", 0, 512), bank(0), AF.Copy)
+    copy(reg("FW", 512, 1024), bank(1))
+    act(reg("FW", 1024, 1536), bank(2), AF.Copy)
+    copy(reg("FW", 1536, 2048), bank(3))
+    for e in range(16):
+        iota(col("WR", e), [[0, 1]], WT[e], 0)
+
+    def name_gather(c, eng):
+        buf, a = ("NG" if eng == "a" else "MH"), 2048 * (c % 2)
+        w = reg("FW", off=reg("LO", 128 * c, 128 * c + 128))
+        if eng == "a":
+            act(reg(buf, a, a + 2048), w, AF.Copy)
+        else:
+            copy(reg(buf, a, a + 2048), w)
+        return buf, a
+
+    def name_out(c):
+        act(reg("TB", 512 + 128 * c, 640 + 128 * c), bank(4 + c, 0, 128), AF.Copy)
+
+    on_v, on_a = list(range(4 - NDVE, 4)), list(range(4 - NDVE))
+    place, done = {}, []
+    for q in range(max(len(on_a), len(on_v))):
+        for lst, eng in ((on_a, "a"), (on_v, "v")):
+            if q < len(lst):
+                place[lst[q]] = name_gather(lst[q], eng)
+        for c in done:
+            name_out(c)
+        done = [lst[q] for lst in (on_a, on_v) if q < len(lst)]
+        for c in done:
+            to_slots(bank(4 + c, 0, 128), place[c][0], place[c][1])
+    for k in range(ZACT, 16):
+        copy(reg("ZR", k, 4096, 16), reg("ZB", 0, 256))
+    for c in done:
+        name_out(c)
+    send("n0")
+    for m in ("c0", "x0", "n0"):
+        arrive(m)
+    send("u1", after=[reg("TF0", 512, 1024)])
+    send("x1")
+    payee(0)
+    act(reg("NL"), reg("TB", 512, 768), AF.Copy, scale=-1.0)
+
+    def late_constants():
+        ts(reg("RK"), reg("IOA"), P32, OP.is_equal)
+        ts(reg("RL"), reg("IOB"), P32, OP.is_equal)
+        ts(ID, reg("IOX", 0, 128), PP, OP.is_equal)
+        ts(reg("SG", 0, 256), reg("IOB", 0, 256), 0.0, OP.is_gt)
+        for h in range(2):
+            act(reg("TIE", 256 * h, 256 * h + 256), reg("IOX"), AF.Copy, scale=1.0 / 256)
+        act(reg("TIE", 512, 640), reg("IOB", 0, 128), bias=15.0 / 16, scale=-1.0 / 16)
+        act(reg("TIE", 640, 768), reg("IOX", 0, 128), bias=1.0 / 256, scale=0.0)
+
+    def later_constants():
+        act(reg("CM", 0, 256), reg("TB", 0, 256), bias=-MID)
+        act(reg("N0"), reg("TB", 512, 768), AF.Copy)
+        act(reg("SG", 256, 512), reg("SG", 0, 256), AF.Copy, scale=0.5)
+        act(reg("SG", 512, 768), reg("SG", 0, 256), bias=256.0, scale=-256.0)
+        act(BOM, BO, AF.Copy, scale=-2048.0)
+        act(BO128, BO, AF.Copy, scale=-128.0)
+        act(BOBIG, BO, AF.Copy, scale=256.0)
+        act(reg("US"), reg("U1"), AF.Copy, scale=1.0 / 16)
+        act(NID, ID, AF.Copy, scale=-1.0)
+        act(IDB, ID, AF.Copy)
+        act(NIDB, ID, AF.Copy, scale=-1.0)
+
+    def last_constants():
+        scan(reg("T1"), reg("SG", 256, 512), reg("SG", 512, 768), 0.0, OP.mult, OP.add)
+        tt(reg("WR", 16, 32), reg("WR", 0, 16), reg("DG"), OP.mult)
+        ts(reg("DUM"), reg("IOX", 0, 256, 16), P16, OP.add, 3072.0, OP.add)
+        red(col("WC", 0), reg("WR", 16, 32), OP.add)
+        tt(reg("WR", 0, 16), reg("T1", 0, 16), reg("DG"), OP.mult)
+        act(reg("THR"), reg("T1"), bias=-2048.0)
+        act(reg("UW"), reg("U1"), AF.Copy, scale=col("WC", 0))
+        red(col("WC", 1), reg("WR", 0, 16), OP.add)
+        ts(BOW, BO, col("WC", 1), OP.mult, 0.5, OP.mult)
+
+    def follow_home(t):
+        xf, h0, wx = "XF%d" % (1 - t % 2), HAND[t], W0 + P * t
+        for m in ("x%d" % (t + 1), "ao%d" % t, "a%d" % t):
+            arrive(m)
+        if t >= 2:
+            copy(reg(xf, wx - 512, wx - 256), reg("LH", h0 + 1024, h0 + 1280))
+        copy(reg(xf, off=reg("LB", 64 * t, 64 * t + 16)), reg("LH", h0, h0 + 256))
+
+    def follow_far(t):
+        xf, h0 = "XF%d" % (1 - t % 2), HAND[t]
+        arrive("bo%d" % t)
+        arrive("b%d" % t)
+        if t < 2:
+            send("x%d" % (t + 2), after=[reg("LH", h0 + 256, h0 + 512)])
+            send("tb%d" % t)
+        for q, o in enumerate([32, 16, 48][:1 if t < 2 else 3]):
+            copy(reg(xf, off=reg("LB", 64 * t + o, 64 * t + o + 16)), reg("LH", h0 + 256 * (q + 1), h0 + 256 * (q + 2)))
+
+    for t in range(R):
+        s = t % 2
+        wx = W0 + P * t
+        XF, TF = "XF%d" % s, "TF%d" % s
+        z = reg("ZB", 256 * s, 256 * s + 256)
+        zn = reg("ZB", 256 * (1 - s), 256 * (1 - s) + 256)
+        C, Nn = reg("TB", 256 * s, 256 * s + 256), reg("TB", 512 + 256 * s, 768 + 256 * s)
+        zb = [0, 1, 2, 3, 4, 5, 6, 0]
+
+        def zpass(q, kind, start=False, stop=False):
+            h, p0 = q // 4, 32 * (q % 4)
+            if kind == "tie":
+                mm(bank(zb[q]), reg("TIE", 640, 768, 1, p0, p0 + 1), reg("TIE", 0, 512, 1, p0, p0 + 1), start, stop)
+                return
+            src, sel = {"nl": ("NL", "RK"), "nm": ("NM", "RL"), "f": ("FS", "RK"), "h": ("HS", "RL")}[kind]
+            mm(bank(zb[q]), reg(src, 128 * h, 128 * h + 128, 1, p0, p0 + 32), reg(sel, 0, 512, 1, p0, p0 + 32), start, stop)
+
+        def znames(q):
+            if q == 7:
+                zpass(q, "nl", start=True)
+            zpass(q, "nm")
+            zpass(q, "tie")
+
+        def gather(dst, win, off, h, a):
+            tt(reg(dst, 2048 * h, 2048 * h + 2048), reg(win, 0, wx, off=reg(off, a + 128 * h, a + 128 * h + 128)),
+               reg("ZR", 2048 * h, 2048 * h + 2048), OP.min)
+
+        def sums(src, dst, h, a):
+            to_slots(bank(7, a, a + 128), src, 2048 * h)
+            act(reg(dst, 128 * h, 128 * h + 128), bank(7, a, a + 128), bias=1008.0 / 256, scale=-1.0 / 256)
+
+        def far_names():
+            act(reg("NM"), reg(TF, 512, 1024, off=reg("BO16")), AF.Copy)
+
+        def far_entries():
+            act(reg("CM", 256, 512), reg(TF, 0, 512, off=reg("BO16")), bias=-MID)
+
+        if t > 0:
+            arrive("ta%d" % (t - 1))
+            arrive("u1" if t == 1 else "tb%d" % (t - 2))
+
+        gather("MY", "X", "LO", 0, 256 * s)
+        if t == 0:
+            late_constants()
+            sums("MY", "FS", 0, 0)
+            later_constants()
+        for q in range(7):
+            zpass(q, "nl", start=True)
+        if t > 0:
+            sums("MY", "FS", 0, 0)
+            far_names()
+            far_entries()
+            for q in range(4):
+                znames(q)
+        gather("MY", "X", "LO", 1, 256 * s)
+        copy(reg("MO"), reg(TF, 0, 512, off=reg("BO16")))
+        if t > 0:
+            if s == 0:
+                follow_home(t - 1)
+            follow_far(t - 1)
+        sums("MY", "FS", 1, 128)
+        if t == 0:
+            last_constants()
+            far_entries()
+            far_names()
+        for h in range(2):
+            total(bank(7, 128 * h, 128 * h + 128), [(reg("FS", 128 * h, 128 * h + 128), ID), (reg("TIE", 640, 768, p1=1), reg("TIE", 512, 640, p1=1))])
+        if t == 0:
+            for q in range(4):
+                znames(q)
+        for q in range(4):
+            zpass(q, "f")
+        if t > 0:
+            for q in (4, 5, 6):
+                znames(q)
+                zpass(q, "f")
+        gather("MH", XF, "MO", 0, 0)
+        scan(reg("NFK"), reg("SG", 0, 256), bank(7, 0, 256), 0.0, OP.mult, OP.max)
+        sums("MH", "HS", 0, 256)
+        for q in range(4):
+            zpass(q, "h", stop=True)
+        if t == 0:
+            for q in (4, 5):
+                znames(q)
+                zpass(q, "f")
+        ts(reg("KI", 32, 48), reg("NFK", 15, 256, 16), 4096.0, OP.mult)
+        gather("MH", XF, "MO", 1, 0)
+        ts(reg("KI", 48, 64), reg("KI", 32, 48), 15, OP.bitwise_and)
+        sums("MH", "HS", 1, 384)
+        for q in range(8):
+            if q == 1:
+                ts(reg("KN"), reg("KI", 48, 64), -1.0 / 16, OP.mult, 15.0 / 16, OP.add)
+                for q2 in (4, 5, 6):
+                    if t == 0 and q2 == 6:
+                        znames(q2)
+                        zpass(q2, "f")
+                    zpass(q2, "h", stop=True)
+                znames(7)
+                zpass(7, "f")
+                zpass(7, "h", stop=True)
+            if q == 7:
+                mm(bank(5), ID, reg("CM"), True, True)
+            for g2 in range(2):
+                red(col("RR", 8 * (q // 4) + 2 * (q % 4) + g2), bank(zb[q], 256 * g2, 256 * g2 + 256), OP.min, True)
+
+        ts(reg("KI", 32, 48), reg("RR"), 8.0, OP.min, 65536.0, OP.mult)
+        ts(reg("VB", 16, 32), reg("RR"), 8.0, OP.is_ge, 16.0, OP.mult)
+        ts(reg("KI", 0, 16), reg("KI", 32, 48), 4, OP.logical_shift_right, 15, OP.bitwise_and)
+        ts(reg("KI", 16, 32), reg("KI", 32, 48), 15, OP.bitwise_and)
+        tt(reg("VB", 0, 16), reg("VB", 16, 32), reg("KN"), OP.mult)
+        copy(reg("VA"), reg("KI", 0, 32))
+        total(bank(1, 0, 128, p1=32), [(reg("VB"), ID), (reg("VA"), ID)])
+        copy(reg("VT", p1=32), bank(1, 0, 128, p1=32))
+        for q in range(4):
+            mm(bank(2, 128 * q, 128 * q + 128), reg("RK", 128 * q, 128 * q + 128, p1=32), reg("VT", p1=32), True, True)
+        dn = bank(0, 0, 256)
+        if t < R - 1:
+            mm(dn, ID, reg("NL"), True, False)
+            for j in range(16):
+                mm(bank(0, j, 256, 16), reg("SJ", 128 * j, 128 * j + 128), reg("BH"), False, j == 15)
+        if t == 2:
+            total(bank(6, 256, 512), [(NID, reg("NL")), (NID, reg("N0"))])
+            act(reg("T2", 512, 768), bank(6, 256, 512), AF.Copy)
+        ts(reg("WK", 0, 512), bank(2), P16, OP.is_equal)
+        tt(reg("WK", 512, 1024), reg("WK", 0, 512), bank(5), OP.mult)
+        mm(bank(4, 0, 256), BO, reg("WK", 512, 768), True, True)
+        to_list(bank(3, 0, 48), "U1", "WK", 256, 768)
+        mm(bank(5, 0, 256), BO, reg("WK", 768, 1024), True, True)
+        mm(bank(6, 0, 256), BOM, reg("WK", 256, 512), True, False)
+        act(reg("KB", 0, 256), bank(4, 0, 256), AF.Copy)
+        if t >= 2:
+            total(bank(7, 0, 256), [(BO, reg("WK", 512, 768)), (BOM, reg("WK", 256, 512))])
+        ts(reg("LM"), bank(3, 16, 48), MID, OP.add)
+        offL, offM = reg("LM", 0, 16), reg("LM", 16, 32)
+        v = reg("VY", 512 * s, 512 * s + 256)
+        yk = reg("VY", 512 * s + 256, 512 * s + 512)
+        act(yk, reg("X", 0, wx, off=offL), AF.Copy)
+        act(reg("KB", 256, 512), bank(5, 0, 256), AF.Copy)
+        nrow = bank(1, 256, 512)
+        act(nrow, reg("IOX"), bias=float(wx))
+
+        def first_of(ebuf, key, kcol, flag, cnt):
+            offs, o = [], 0
+            for h in range(16):
+                offs.append(o)
+                o += 256 - 16 * h
+            for grp in ([0, 1, 2], [3, 4, 5, 6], [7, 8, 9, 10, 11], [12, 13, 14, 15]):
+                for h in grp:
+                    ts(reg(ebuf, offs[h], offs[h] + 256 - 16 * h), reg("KB", key + 16 * h, key + 256), kcol(h), OP.is_equal, flag(h), OP.mult)
+                for h in reversed(grp):
+                    mm(bank(cnt, 16 * h, 16 * h + 16), BOW, reg(ebuf, offs[h], offs[h] + 16), False, False)
+                    if h < 15:
+                        mm(bank(cnt, 16 * h + 16, 256), BOBIG, reg(ebuf, offs[h] + 16, offs[h] + 256 - 16 * h), False, h == 12)
+
+        first_of("EE", 0, lambda h: bank(3, 16 + h, 17 + h), lambda h: bank(3, h, h + 1), 6)
+        if t < R - 1:
+            total(bank(4, 256, 512), [(IDB, yk), (NIDB, z)])
+            act(zn, bank(4, 256, 512), AF.Abs)
+        tt(reg("M1"), reg("X", 0, wx, off=offL), z, OP.min)
+        tt(reg("ST"), bank(6, 0, 256), reg("THR"), OP.is_lt)
+        to_list(bank(1, 0, 16), "US", "ST", 0, 256)
+        mm(bank(2, 0, 256), BO128, reg("ST"), True, False)
+        tt(v, reg(XF, 0, wx, off=offM), reg("M1"), OP.min)
+        send("v%d" % t)
+        rv, dm = 48 * s, 32 * t
+        ts(reg("RV", rv + 16, rv + 48), bank(3, 16, 48), MID, OP.add)
+        if t < R - 1:
+            for k in range(8):
+                act(reg("ZR", k, 4096, 16), zn, AF.Copy)
+        first_of("E2", 256, lambda h: bank(3, 32 + h, 33 + h), lambda h: bank(1, h, h + 1), 2)
+        total(bank(6, 0, 256), [(IDB, yk), (NIDB, v)])
+        act(reg("TM", 512, 768), bank(6, 0, 256), AF.Copy)
+        if t < R - 1:
+            for k in range(8, 16):
+                act(reg("ZR", k, 4096, 16), zn, AF.Copy)
+        keep = bank(7, 256, 512)
+        tt(reg("DM", dm + 16, dm + 32), reg("RV", rv + 32, rv + 48), reg("DUM"), OP.subtract)
+        tt(reg("DM", dm, dm + 16), reg("RV", rv + 16, rv + 32), reg("DUM"), OP.subtract)
+        if t >= 2:
+            ts(keep, bank(7, 0, 256), 512.0, OP.is_lt)
+            ts(reg("G2", 64, 80), bank(3, 0, 16), -4096.0, OP.mult)
+        tt(reg("BD"), bank(2, 0, 256), reg("THR"), OP.is_lt)
+        build = bank(2, 256, 512)
+        if t < 2:
+            mm(build, ID, reg("BD"), True, True)
+        to_list(bank(5, 0, 16), "US", "BD", 0, 256)
+        if t >= 2:
+            mm(build, ID, reg("BD"), True, True)
+        if t < R - 1:
+            to_list(bank(4, 0, 16), "UW", "ZB", 256 * (1 - s), 256)
+        if t < 2:
+            tt(reg("NB", 0, 256), v, build, OP.mult)
+            tt(reg("MK"), reg("WK", 0, 256), build, OP.mult)
+        if t >= 2:
+            tt(reg("G2", 64, 80), reg("G2", 64, 80), reg("RV", rv + 16, rv + 32), OP.add)
+            old = reg("X", wx - 512, wx - 256)
+            tt(reg("NB", 256, 512) if t < R - 1 else old, old, keep, OP.mult)
+            ts(reg("G2", 80, 96), reg("G2", 64, 80), 2048.0, OP.is_ge)
+            if t < R - 1:
+                copy(old, reg("NB", 256, 512))
+            tt(reg("G2", 48, 64), reg("G2", 80, 96), reg("DM", dm - 48, dm - 32), OP.mult)
+        tt(reg("G2", 16, 32), bank(5, 0, 16), reg("DM", dm + 16, dm + 32), OP.mult)
+        tt(reg("G2", 0, 16), bank(5, 0, 16), reg("DM", dm, dm + 16), OP.mult)
+        if t >= 2:
+            tt(reg("G2", 48, 64), reg("G2", 48, 64), reg("DUM"), OP.add)
+        tt(reg("G2", 16, 32), reg("G2", 16, 32), reg("DUM"), OP.add)
+        tt(reg("G2", 0, 16), reg("G2", 0, 16), reg("DUM"), OP.add)
+        if t >= 2:
+            copy(reg("OF", 32 * t + 16, 32 * t + 32), reg("G2", 48, 64))
+        copy(reg("OF", 32 * t, 32 * t + 16), reg("G2", 16, 32))
+        send("o%d" % t)
+        if t >= 2:
+            tt(reg("G2", 32, 48), reg("G2", 80, 96), reg("DM", dm - 64, dm - 48), OP.mult)
+            tt(reg("NB", 0, 256) if t < R - 1 else reg("X", wx, wx + 256), v, build, OP.mult)
+            tt(reg("G2", 32, 48), reg("G2", 32, 48), reg("DUM"), OP.add)
+        copy(reg("OH", 0, 16), reg("G2", 0, 16))
+        if t >= 2:
+            copy(reg("OH", 16, 32), reg("G2", 32, 48))
+        if t < R - 1:
+            send("ao%d" % t)
+            send("a%d" % t)
+
+        if t >= 2:
+            tt(reg("MK"), reg("WK", 0, 256), build, OP.mult)
+            tt(C, C, keep, OP.mult)
+        if t == 2:
+            tt(reg("T2", 256, 512), reg("T2", 512, 768), keep, OP.mult)
+        if t < R - 1:
+            tt(reg("T2", 0, 256), reg("MK"), dn, OP.mult)
+            base = [(NID, reg("NL"))] if t < 2 else [(ID, reg("N0")), (ID, reg("T2", 256, 512))]
+            total(bank(0, 256, 512), base + [(ID, reg("T2", 0, 256))])
+            act(Nn, bank(0, 256, 512), AF.Copy)
+        arrive("v%d" % t)
+        fv, fw = reg("LV", LAND[t], LAND[t] + 256), reg("LV", LAND[t] + 256, LAND[t] + 512)
+        act(reg("NV", 0, 256), fv, AF.Copy, scale=-1.0)
+        if t >= 2:
+            act(reg("NV", 256, 512), yk, bias=63.0, scale=-1.0)
+            act(reg("NV", 512, 768), fw, bias=63.0, scale=-1.0)
+
+        def lists_end():
+            tt(nrow, reg("MK"), nrow, OP.mult)
+            if t >= 2:
+                tt(C, C, reg("PL", s, 512, 2), OP.max)
+            tt(C, C, nrow, OP.max)
+            if t == R - 1:
+                act(reg("CO", s, 512, 2), C, AF.Copy)
+                dma("s", [(T.co[:], reg("CO"))])
+
+        if t < R - 1:
+            lists_end()
+            send("ta%d" % t)
+            copy(reg("X", wx, wx + 256), reg("NB", 0, 256))
+        copy(reg("X", off=reg("OH", 0, 16)), reg("TM", 512, 768))
+        if t < R - 1:
+            copy(reg("BI", 48, 64), bank(4, 0, 16))
+            ts(reg("BI", 0, 16), reg("BI", 48, 64), 511, OP.bitwise_and)
+        for q in range(3):
+            tt(reg("RC", 16 * q, 16 * q + 16), bank(5, 0, 16), reg("RV", rv + 16 * q, rv + 16 * q + 16), OP.mult)
+        if t < R - 1:
+            payee(t + 1)
+            c2 = 256 * (1 - s)
+            act(reg("NL"), reg("TB", 512 + c2, 768 + c2), AF.Copy, scale=-1.0)
+            act(reg("CM", 0, 256), reg("TB", c2, c2 + 256), bias=-MID)
+        ts(reg("RH"), reg("RC"), MID, OP.subtract)
+        for j in range(16):
+            mm(bank(6, j, 512, 16, p1=8), reg("ID", j, 128, 16), reg("RH", 0, 32), True, True)
+        for j in range(16):
+            mm(bank(3, 256 + j, 512, 16, p1=8), reg("ID", j, 128, 16), reg("RH", 32, 48), True, True)
+        act(reg("RO", 0, 512, p1=8), bank(6, 0, 512, p1=8), bias=MID)
+        act(reg("RO", 512, 768, p1=8), bank(3, 256, 512, p1=8), bias=MID)
+        dma("s", [(T.rec[8 * q:8 * q + 8, P * t:P * t + P], reg("RO", 256 * q, 256 * q + 256, p1=8)) for q in range(3)])
+        if t == 2:
+            act(reg("CO", s, 512, 2), C, AF.Copy)
+        arrive("o%d" % t)
+
+        def change(q, off, bound, op, step):
+            part = reg("TP", 256 * q, 256 * q + 256)
+            tt(part, reg("X", off=off), bound, op)
+            tt(reg("X", off=off), part, step, OP.add)
+            if t < R - 1:
+                total(bank(4 + q, 0, 256), [(IDB, part), (IDB, step)])
+                act(reg("TV", 256 * q, 256 * q + 256), bank(4 + q, 0, 256), AF.Copy)
+
+        if t < R - 1:
+            send("bo%d" % t)
+            if t < 2:
+                copy(reg("LO", 256 * s, 256 * s + 256), C)
+            if s == 0:
+                follow_home(t)
+        change(0, reg("LF", 32 * t, 32 * t + 16), fv, OP.max, reg("NV", 0, 256))
+        if t >= 2:
+            change(1, reg("OH", 16, 32), reg("NV", 256, 512), OP.min, yk)
+            change(2, reg("LF", 32 * t + 16, 32 * t + 32), reg("NV", 512, 768), OP.min, fw)
+        if t < R - 1:
+            send("b%d" % t)
+        else:
+            dma("s", [(T.xo[:, 0:1536], reg("X", 0, 1536))])
+            dma("a", [(T.xo[:, 1536:3072], reg("X", 1536, 3072))])
+            lists_end()
+
+    emit(g, T, ops, queue)
+
+
+def emit(g, T, ops, queue):
+    n = len(ops)
+    hist = {}
+    waits = [[] for _ in range(n)]
+    clock = [None] * n
+    known = {e: {} for e in queue}
+    marked = [False] * n
+    key = lambda j: ops[j]["sem"][0] if ops[j]["sem"] else ops[j]["e"]
+    for i, op in enumerate(ops):
+        e = op["e"]
+        deps = set()
+        for kind, lst in (("r", op["r"]), ("w", op["w"])):
+            for name, a, b, st in lst:
+                psum = SCRATCH[name][0] == "psum"
+                for j, k2, a2, b2, st2 in hist.get(name, []):
+                    same = ops[j]["e"] == e and not ops[j]["sem"] and not op["sem"]
+                    over = a < b2 and a2 < b and not (st == st2 and (a - a2) % st)
+                    if same:
+                        if over and e != "p" and (kind == "w" or k2 == "w"):
+                            deps.add(j)
+                    elif psum or (over and (kind == "w" or k2 == "w")):
+                        deps.add(j)
+        if e != "x":
+            for j in sorted(deps, reverse=True):
+                if known[e].get(key(j), -1) >= j:
+                    continue
+                waits[i].append(j)
+                marked[j] = True
+                for k, val in clock[j].items():
+                    if known[e].get(k, -1) < val:
+                        known[e][k] = val
+            clock[i] = dict(known[e])
+        else:
+            clock[i] = {}
+        clock[i][key(i)] = i
+        for kind, lst in (("r", op["r"]), ("w", op["w"])):
+            for name, a, b, st in lst:
+                hist.setdefault(name, []).append((i, kind, a, b, st))
+    count, value = {e: 0 for e in ENG_SEM}, [None] * n
+    waited = {}
+    for i, op in enumerate(ops):
+        if op["sem"]:
+            value[i] = op["sem"]
+        elif marked[i]:
+            count[op["e"]] += 1
+            value[i] = (ENG_SEM[op["e"]], count[op["e"]])
+        if op["e"] == "x":
+            continue
+        for j in waits[i]:
+            queue[op["e"]].wait_ge(T.sem[value[j][0]], value[j][1])
+            waited[value[j][0]] = 1
+        ins = op["f"]()
+        if marked[i] and not op["sem"]:
+            ins.then_inc(T.sem[value[i][0]], 1)
+    for op in ops:
+        if op["sem"] and op["sem"][0] not in waited:
+            g.wait_ge(T.sem[op["sem"][0]], op["sem"][1])

@@ -14,7 +14,7 @@ ZACT = 8
 F, H16, B16, I32, U16 = "float32", "float16", "bfloat16", "int32", "uint16"
 SCRATCH = {
     "X": ("sbuf", [128, XW], B16), "XF0": ("sbuf", [128, XW], B16), "XF1": ("sbuf", [128, XW], B16),
-    "LH": ("sbuf", [128, 2304], B16), "LB": ("sbuf", [128, 192], U16), "TV": ("sbuf", [128, 768], B16),
+    "LH": ("sbuf", [128, 2048], B16), "LN": ("sbuf", [128, 1024], B16), "LB": ("sbuf", [128, 192], U16), "TV": ("sbuf", [128, 768], B16),
     "NB": ("sbuf", [128, 512], B16), "NV": ("sbuf", [128, 768], B16), "TP": ("sbuf", [128, 768], B16),
     "TB": ("sbuf", [128, 1024], F), "TF0": ("sbuf", [128, 1024], F), "TF1": ("sbuf", [128, 1024], F),
     "PL": ("sbuf", [128, 512], I32), "FR": ("sbuf", [128, 128], I32), "FR16": ("sbuf", [128, 128], H16),
@@ -24,7 +24,8 @@ SCRATCH = {
     "LO": ("sbuf", [128, 512], U16), "MO": ("sbuf", [128, 256], U16), "BO16": ("sbuf", [128, 16], U16),
     "BI": ("sbuf", [128, 64], I32), "BH": ("sbuf", [128, 16], H16),
     "CM": ("sbuf", [128, 512], H16), "NL": ("sbuf", [128, 256], H16), "NM": ("sbuf", [128, 256], H16),
-    "FS": ("sbuf", [128, 256], H16), "HS": ("sbuf", [128, 256], H16),
+    "FS": ("sbuf", [128, 256], H16), "FH": ("sbuf", [128, 512], H16), "NS": ("sbuf", [128, 512], H16), "SW": ("sbuf", [128, 128], H16),
+    "YG": ("sbuf", [128, 2048], B16), "SEL": ("sbuf", [128, 2048], H16), "U2": ("sbuf", [128, 144], H16), "NBO": ("sbuf", [128, 128], B16),
     "NFK": ("sbuf", [128, 256], F), "KN": ("sbuf", [128, 16], F), "KI": ("sbuf", [128, 64], I32),
     "RR": ("sbuf", [128, 16], F), "VA": ("sbuf", [128, 32], H16), "VB": ("sbuf", [128, 32], H16),
     "VT": ("sbuf", [128, 128], H16), "WK": ("sbuf", [128, 1024], H16), "KB": ("sbuf", [128, 512], H16),
@@ -33,7 +34,7 @@ SCRATCH = {
     "M1": ("sbuf", [128, 256], B16), "VY": ("sbuf", [128, 1024], B16), "TM": ("sbuf", [128, 768], B16),
     "RV": ("sbuf", [128, 96], F), "DM": ("sbuf", [128, 128], F), "G2": ("sbuf", [128, 96], F),
     "OH": ("sbuf", [128, 32], U16), "OF": ("sbuf", [128, 128], U16),
-    "LV": ("sbuf", [128, 1536], B16), "LF": ("sbuf", [128, 128], U16),
+    "LV": ("sbuf", [128, 1536], B16), "LF": ("sbuf", [128, 128], U16), "LG": ("sbuf", [128, 64], U16),
     "RC": ("sbuf", [128, 48], F), "RH": ("sbuf", [128, 48], H16), "RO": ("sbuf", [8, 768], F),
     "T1": ("sbuf", [128, 256], F), "T2": ("sbuf", [128, 768], H16), "MK": ("sbuf", [128, 256], H16),
     "CO": ("sbuf", [128, 512], F),
@@ -49,8 +50,8 @@ SCRATCH = {
 for _b in range(8):
     SCRATCH["P%d" % _b] = ("psum", [128, 512], F)
 
-MSGS = ["c0", "x0", "n0", "u1"] + ["v%d" % t for t in range(R)] + ["o%d" % t for t in range(R)] + \
-       ["x1", "x2", "x3", "tb0", "tb1"] + [m + str(t) for m in ("a", "ao", "b", "bo", "ta") for t in range(R - 1)]
+MSGS = ["c0", "x0", "n0", "u1"] + ["v%d" % t for t in range(R)] + ["m%d" % t for t in range(R)] + ["o%d" % t for t in range(R)] + \
+       ["x1", "x2", "x3", "tb0", "tb1", "b3", "b4"] + [m + str(t) for m in ("a", "at", "ao", "b", "bo", "ta", "tn") for t in range(R - 1)]
 HAND = [0, 512, 1024]
 NDMA = 16
 SEMAPHORES = ["sv", "sa", "sp", "sg"] + ["d%d" % i for i in range(NDMA)] + \
@@ -77,7 +78,7 @@ def ap(T, r):
 
 
 def spans(rs):
-    return [(r["n"], r["a"], r["b"], r["s"]) for r in rs if isinstance(r, dict)]
+    return [(r["n"], r["a"], r["b"], r["s"], r["p0"], r["p1"]) for r in rs if isinstance(r, dict)]
 
 
 def routes(T, topo, src, dst, mode):
@@ -87,7 +88,7 @@ def routes(T, topo, src, dst, mode):
     far = [c for c in ports if topo.die(c) != topo.die(src)]
     if topo.may_write(src, dst):
         near = [None, None]
-    return {"near": near[:2], "near2": near[1:2], "far": far[:2], "all": near[:2] + far[:2]}[mode]
+    return {"near": near[:2], "near1": near[:1], "near2": near[1:2], "far1": far[:1], "far": far[:2], "all": near[:2] + far[:2]}[mode]
 
 
 def messages(T, topo):
@@ -112,22 +113,25 @@ def messages(T, topo):
         s, wx = t % 2, W0 + P * t
         w, n = (128, 16) if t < 2 else (256, 32)
         s0, l0, h0 = 512 * s, LAND[t], HAND[t % 3]
+        ms.append(plain("m%d" % t, 1 + s, "near1", [(reg("LM", 16, 32), reg("LG", 16 * t, 16 * t + 16))]))
         ms.append(plain("v%d" % t, 1 + s, "near", [(reg("VY", s0 + j * w, s0 + (j + 1) * w), reg("LV", l0 + j * w, l0 + (j + 1) * w)) for j in range(2)]))
-        ms.append(plain("o%d" % t, 1 + s, "near", [(reg("OF", 32 * t, 32 * t + n), reg("LF", 32 * t, 32 * t + n))]))
+        if t < R - 1:
+            ms.append(plain("at%d" % t, s - 2, "near", [(reg("TM", 512 + 128 * j, 640 + 128 * j), reg("LH", h0 + 128 * j, h0 + 128 + 128 * j)) for j in range(2)]))
+        ms.append(plain("o%d" % t, 1 + s, "near" if s else "far1", [(reg("OF", 32 * t, 32 * t + n), reg("LF", 32 * t, 32 * t + n))]))
         if t == R - 1:
             break
-        xf = "XF%d" % (1 - s)
+        ms.append(plain("bo%d" % t, 2 * s - 1, "near1", [(reg("OF", 32 * t, 32 * t + n), reg("LB", 64 * t + 32, 64 * t + 32 + n))]))
         ms.append(plain("ao%d" % t, s - 2, "near2", [(reg("OH", 0, n), reg("LB", 64 * t, 64 * t + n))]))
-        ms.append(plain("a%d" % t, s - 2, "near", [(reg("TM", 512, 768), reg("LH", h0, h0 + 256)), (reg("NB", 0, 256), reg(xf, wx, wx + 256))] +
-                        ([(reg("NB", 256, 512), reg("LH", h0 + 1024, h0 + 1280))] if t >= 2 else [])))
-        ms.append(tab("ta%d" % t, s - 2, [256 * s, 512 + 256 * s, 256 * s + 128, 640 + 256 * s], [("TB", 768), ("TF0", 0), ("TF0", 256)][t], "all", 128))
-        ms.append(plain("bo%d" % t, s - 2, "near2", [(reg("LF", 32 * t, 32 * t + n), reg("LB", 64 * t + 32, 64 * t + 32 + n))]))
+        ms.append(plain("a%d" % t, s - 2, "far", [(reg("NB", 256 * j, 256 * j + 256), reg("LN", 256 * (t + j), 256 * (t + j + 1))) for j in range(1 + t // 2)]))
+        stage = [("TB", 768), ("TF0", 0), ("TF0", 256)][t]
+        ms.append(tab("ta%d" % t, s - 2, [256 * s, 256 * s + 128], stage, "near", 128))
+        ms.append(tab("tn%d" % t, s - 2, [512 + 256 * s, 640 + 256 * s], stage, "far", 128))
+        for q in range(1 if t < 2 else 3):
+            c, l = 256 * q, h0 + 256 * (q + 1)
+            ms.append(plain("b%d" % (t + q), s - 2, "near", [(reg("TV", c + 128 * j, c + 128 * j + 128), reg("LH", l + 128 * j, l + 128 * j + 128)) for j in range(2)]))
         if t < 2:
-            ms.append(plain("b%d" % t, s - 2, "near", [(reg("TV", 128 * j, 128 * j + 128), reg("LH", h0 + 256 + 128 * j, h0 + 384 + 128 * j)) for j in range(2)]))
             ms.append(xship(t + 2))
             ms.append(tab("tb%d" % t, -1 - s, [256 * s, 512 + 256 * s], ("TF0", 512 + 256 * t)))
-        else:
-            ms.append(plain("b%d" % t, s - 2, "near", [(reg("TV", 384 * j, 384 * j + 384), reg("LH", h0 + 256 + 384 * j, h0 + 640 + 384 * j)) for j in range(2)]))
     return ms
 
 
@@ -139,41 +143,54 @@ def mask_of(engs):
 
 
 def plan_message(T, topo, src, msg):
-    name, step, mode, pieces = msg
-    dst = T.cores[(T.rank_of(src) + step) % NR]
-    ways = routes(T, topo, src, dst, mode)
-    way = [ways[j % len(ways)] for j in range(len(pieces))]
-    direct = [j for j in range(len(pieces)) if way[j] is None]
-    handed = [j for j in range(len(pieces)) if way[j] is not None]
-    engs, used, total = {}, [], 0
-    if direct:
-        engs.update(deal(topo.engines(src, dst), direct))
-        used = topo.engines(src, dst)
-        total += sum(len(engs[j]) for j in direct)
+    dsts, ways, direct, handed, used = {}, {}, [], [], []
+    for name, step, mode, pieces in [m for m in messages(T, topo) if call_of(m[0]) == call_of(msg[0])]:
+        dsts[name] = T.cores[(T.rank_of(src) + step) % NR]
+        rt = routes(T, topo, src, dsts[name], mode)
+        ways[name] = [rt[j % len(rt)] for j in range(len(pieces))]
+        direct += [(name, j) for j in range(len(pieces)) if ways[name][j] is None]
+        handed += [(name, j) for j in range(len(pieces)) if ways[name][j] is not None]
+        if topo.may_write(src, dsts[name]):
+            used = topo.engines(src, dsts[name])
+    share = deal(used, direct)
     if handed:
-        engs.update(deal([e for e in topo.engines(src, way[handed[0]]) if e not in used], handed))
-        for c in set(way[j] for j in handed):
-            second = deal(topo.engines(c, dst), [j for j in handed if way[j] == c])
-            total += sum(len(e) for e in second.values())
+        share.update(deal([e for e in topo.engines(src, ways[handed[0][0]][handed[0][1]]) if e not in used], handed))
+    dst, way = dsts[msg[0]], ways[msg[0]]
+    engs = {j: share[(msg[0], j)] for j in range(len(way))}
+    total = sum(len(engs[j]) for j in engs if way[j] is None)
+    for c in set(way) - {None}:
+        total += sum(len(e) for e in deal(topo.engines(c, dst), [j for j in engs if way[j] == c]).values())
     return dst, way, engs, total
 
 
+def call_of(name):
+    return {"bo": "o", "tn": "ta"}.get(name[:-1], name[:-1]) + name[-1]
+
+
 def deal(pool, items):
+    if not items:
+        return {}
     n = 1
     while 2 * n * len(items) <= len(pool):
         n *= 2
-    return {j: pool[q * n:(q + 1) * n] for q, j in enumerate(items)}
+    more = (len(pool) - n * len(items)) // n
+    out, at = {}, 0
+    for q, j in enumerate(items):
+        w = 2 * n if q < more else n
+        out[j] = pool[at:at + w]
+        at += w
+    return out
 
 
 def write(g, T, topo, core, name, trs):
-    arr, snt = T.sem["arr_" + name], T.sem["snt_" + name]
+    snt = T.sem["snt_" + name]
     if len(trs) == 1:
-        to, engs, a, b = trs[0]
+        m, to, engs, a, b = trs[0]
         rid, pid = topo.addr(to, core)
-        g.remote_dma(ap(T, b), ap(T, a), arr, snt, pid, rid, mask_of(engs))
+        g.remote_dma(ap(T, b), ap(T, a), T.sem["arr_" + m], snt, pid, rid, mask_of(engs))
     else:
         g.remote_dma_fused([RemoteDMATransfer(dst_ids=[DstId(rid=topo.addr(to, core)[0], pnc=topo.addr(to, core)[1])], dma_engine_mask=mask_of(engs),
-                                              remote_sem=arr, src=ap(T, a), dst=ap(T, b)) for to, engs, a, b in trs], local_sem=snt)
+                                              remote_sem=T.sem["arr_" + m], src=ap(T, a), dst=ap(T, b)) for m, to, engs, a, b in trs], local_sem=snt)
 
 
 def carrier_program(g, core, T, topo):
@@ -188,7 +205,7 @@ def carrier_program(g, core, T, topo):
         if mine:
             second = deal(topo.engines(core, dst), mine)
             g.wait_ge(T.sem["arr_" + msg[0]], sum(len(engs[j]) for j in mine))
-            write(g, T, topo, core, msg[0], [(dst, second[j], msg[3][j][1], msg[3][j][2]) for j in mine])
+            write(g, T, topo, core, msg[0], [(msg[0], dst, second[j], msg[3][j][1], msg[3][j][2]) for j in mine])
             sent.append((msg[0], sum(len(e) for e in second.values())))
     for name, n in sent:
         g.wait_ge(T.sem["snt_" + name], n)
@@ -260,11 +277,12 @@ def rank_program(g, core, T, topo):
         add(eng, fn, [p[0] for p in pairs], [p[1] for p in pairs], sem=(name, 16 * len(pairs)))
 
     def send(name, after=()):
-        msg = msgs[name]
-        dst, way, engs, _ = plan_message(T, topo, core, msg)
-        trs = [(dst, engs[j], p[0], p[2]) if way[j] is None else (way[j], engs[j], p[0], p[1]) for j, p in enumerate(msg[3])]
-        add("g", lambda: write(g, T, topo, core, name, trs), [], [p[0] for p in msg[3]] + list(after),
-            sem=("snt_" + name, sum(len(e) for e in engs.values())))
+        trs = []
+        for msg in [m for m in msgs.values() if call_of(m[0]) == name]:
+            dst, way, engs, _ = plan_message(T, topo, core, msg)
+            trs += [(msg[0], dst, engs[j], p[0], p[2]) if way[j] is None else (msg[0], way[j], engs[j], p[0], p[1]) for j, p in enumerate(msg[3])]
+        add("g", lambda: write(g, T, topo, core, name, trs), [], [tr[3] for tr in trs] + list(after),
+            sem=("snt_" + name, sum(len(tr[2]) for tr in trs)))
 
     def arrive(name):
         msg = msgs[name]
@@ -308,7 +326,8 @@ def rank_program(g, core, T, topo):
     ts(col("PI", 3), col("PI", 0), 4, OP.logical_shift_right)
     ts(col("PI", 5), col("PI", 0), 112, OP.bitwise_and)
     copy(col("PI", 4), col("PI", 0))
-    copy(reg("PC", 0, 5), reg("PI", 1, 6))
+    ts(col("PI", 6), col("PI", 0), 5, OP.logical_shift_right, 1, OP.bitwise_and)
+    copy(reg("PC", 0, 6), reg("PI", 1, 7))
     ts(BO, reg("IOA", 0, 128), PG, OP.is_equal)
     ts(reg("DG"), reg("IOX", 0, 16), P16, OP.is_equal)
     for j in range(16):
@@ -318,6 +337,7 @@ def rank_program(g, core, T, topo):
             ts(reg("SJ", 128 * j, 128 * j + 128), BO, col("DG", j), OP.mult)
     iota(reg("IOA", 128, 512), [[1, 24], [0, 16]], 8, 0)
     ts(reg("U1"), reg("IOX", 0, 144), 15.0, OP.subtract, PG16, OP.is_equal)
+    ts(ID, reg("IOX", 0, 128), PP, OP.is_equal)
     copy(reg("FR16"), reg("FR"))
     copy(reg("TB", 0, 256), reg("PL", 0, 512, 2))
     copy(reg("TB", 256, 512), reg("PL", 1, 512, 2))
@@ -369,12 +389,23 @@ def rank_program(g, core, T, topo):
     send("u1", after=[reg("TF0", 512, 1024)])
     send("x1")
     payee(0)
-    act(reg("NL"), reg("TB", 512, 768), AF.Copy, scale=-1.0)
+
+    def home_names(c):
+        act(reg("NL"), reg("TB", c, c + 256), AF.Copy, scale=-1.0)
+        act(reg("NS", 0, 256, 1, 0, 64), reg("TB", c, c + 256, 1, 0, 64), AF.Copy, scale=-1.0)
+        act(reg("NS", 256, 512, 1, 64, 128), reg("TB", c, c + 256, 1, 64, 128), AF.Copy, scale=-1.0)
+
+    home_names(512)
+    act(reg("SW", 0, 64), reg("ID", 64, 128), AF.Copy)
+    act(reg("SW", 64, 128), reg("ID", 0, 64), AF.Copy)
 
     def late_constants():
         ts(reg("RK"), reg("IOA"), P32, OP.is_equal)
         ts(reg("RL"), reg("IOB"), P32, OP.is_equal)
-        ts(ID, reg("IOX", 0, 128), PP, OP.is_equal)
+        act(IDB, ID, AF.Copy)
+        act(NIDB, ID, AF.Copy, scale=-1.0)
+        act(reg("NBO"), BO, AF.Copy, scale=-1.0)
+        act(col("PC", 6), col("PC", 5), bias=1.0, scale=-1.0)
         ts(reg("SG", 0, 256), reg("IOB", 0, 256), 0.0, OP.is_gt)
         for h in range(2):
             act(reg("TIE", 256 * h, 256 * h + 256), reg("IOX"), AF.Copy, scale=1.0 / 256)
@@ -391,8 +422,15 @@ def rank_program(g, core, T, topo):
         act(BOBIG, BO, AF.Copy, scale=256.0)
         act(reg("US"), reg("U1"), AF.Copy, scale=1.0 / 16)
         act(NID, ID, AF.Copy, scale=-1.0)
-        act(IDB, ID, AF.Copy)
-        act(NIDB, ID, AF.Copy, scale=-1.0)
+
+    def stacked_selectors():
+        for p0, a, b, n in ((0, 64, 0, 80), (0, 0, 80, 64), (64, 0, 64, 80), (64, 80, 0, 64)):
+            act(reg("U2", a, a + n, 1, p0, p0 + 64), reg("U1", b, b + n, 1, p0, p0 + 64), AF.Copy)
+        for j in range(4):
+            for p0 in (0, 64):
+                src = "RK" if (p0 == 0) == (j < 2) else "RL"
+                act(reg("SEL", 512 * j, 512 * j + 512, 1, p0, p0 + 64), reg(src, 0, 512, 1, p0, p0 + 64), AF.Copy,
+                    scale=reg("PC", 6 - j % 2, 7 - j % 2, 1, p0, p0 + 64))
 
     def last_constants():
         scan(reg("T1"), reg("SG", 256, 512), reg("SG", 512, 768), 0.0, OP.mult, OP.add)
@@ -406,17 +444,20 @@ def rank_program(g, core, T, topo):
         ts(BOW, BO, col("WC", 1), OP.mult, 0.5, OP.mult)
 
     def follow_home(t):
-        xf, h0, wx = "XF%d" % (1 - t % 2), HAND[t], W0 + P * t
-        for m in ("x%d" % (t + 1), "ao%d" % t, "a%d" % t):
+        xf, h0 = "XF%d" % (1 - t % 2), HAND[t]
+        for m in ("x%d" % (t + 1), "ao%d" % t, "at%d" % t):
             arrive(m)
-        if t >= 2:
-            copy(reg(xf, wx - 512, wx - 256), reg("LH", h0 + 1024, h0 + 1280))
         copy(reg(xf, off=reg("LB", 64 * t, 64 * t + 16)), reg("LH", h0, h0 + 256))
 
     def follow_far(t):
-        xf, h0 = "XF%d" % (1 - t % 2), HAND[t]
+        xf, h0, wx = "XF%d" % (1 - t % 2), HAND[t], W0 + P * t
+        arrive("a%d" % t)
+        copy(reg(xf, wx, wx + 256), reg("LN", 256 * t, 256 * t + 256))
+        if t >= 2:
+            copy(reg(xf, wx - 512, wx - 256), reg("LN", 256 * t + 256, 256 * t + 512))
         arrive("bo%d" % t)
-        arrive("b%d" % t)
+        for q in range(1 if t < 2 else 3):
+            arrive("b%d" % (t + q))
         if t < 2:
             send("x%d" % (t + 2), after=[reg("LH", h0 + 256, h0 + 512)])
             send("tb%d" % t)
@@ -433,26 +474,56 @@ def rank_program(g, core, T, topo):
         zb = [0, 1, 2, 3, 4, 5, 6, 0]
 
         def zpass(q, kind, start=False, stop=False):
-            h, p0 = q // 4, 32 * (q % 4)
+            h, j = q // 4, q % 4
+            p0 = 32 * j
             if kind == "tie":
                 mm(bank(zb[q]), reg("TIE", 640, 768, 1, p0, p0 + 1), reg("TIE", 0, 512, 1, p0, p0 + 1), start, stop)
-                return
-            src, sel = {"nl": ("NL", "RK"), "nm": ("NM", "RL"), "f": ("FS", "RK"), "h": ("HS", "RL")}[kind]
-            mm(bank(zb[q]), reg(src, 128 * h, 128 * h + 128, 1, p0, p0 + 32), reg(sel, 0, 512, 1, p0, p0 + 32), start, stop)
+            else:
+                a = 256 * (j // 2) + 128 * h
+                mm(bank(zb[q]), reg("FH" if kind == "fh" else "NS", a, a + 128), reg("SEL", 512 * j, 512 * j + 512), start, stop)
 
         def znames(q):
-            if q == 7:
-                zpass(q, "nl", start=True)
-            zpass(q, "nm")
+            zpass(q, "names", start=True)
             zpass(q, "tie")
+
+        def stack_names():
+            mm(bank(3, 0, 256), reg("SW"), reg("NM"), True, True)
+            act(reg("NS", 0, 256, 1, 64, 128), reg("P3", 0, 256, 1, 64, 128), AF.Copy)
+            act(reg("NS", 256, 512, 1, 0, 64), reg("P3", 0, 256, 1, 0, 64), AF.Copy)
 
         def gather(dst, win, off, h, a):
             tt(reg(dst, 2048 * h, 2048 * h + 2048), reg(win, 0, wx, off=reg(off, a + 128 * h, a + 128 * h + 128)),
                reg("ZR", 2048 * h, 2048 * h + 2048), OP.min)
 
-        def sums(src, dst, h, a):
-            to_slots(bank(7, a, a + 128), src, 2048 * h)
-            act(reg(dst, 128 * h, 128 * h + 128), bank(7, a, a + 128), bias=1008.0 / 256, scale=-1.0 / 256)
+        def halves(h, b, a, sign, low, high):
+            for p0, tile in ((0, low), (64, high)):
+                act(reg("FH", 256 * tile + 128 * h, 256 * tile + 128 * h + 128, 1, p0, p0 + 64), reg("P%d" % b, a, a + 128, 1, p0, p0 + 64),
+                    bias=1008.0 / 256, scale=sign / 256)
+
+        def home_sums(h):
+            helped = h == 1 and t > 0
+            a, sign = 128 * h, 1.0 if helped else -1.0
+            terms = [(reg("U1", 15 - k, 143 - k), reg("MY", 2048 * h + k, 2048 * h + 2048, 16)) for k in range(16)]
+            if helped:
+                terms = [(reg("NBO"), reg("ZB", 256 * s + 128, 256 * s + 256))] + terms
+            total(bank(7 - h, a, a + 128), terms)
+            halves(h, 7 - h, a, sign, 0, 1)
+            act(reg("FS", a, a + 128), bank(7 - h, a, a + 128), bias=1008.0 / 256, scale=sign / 256)
+
+        def far_sums(h):
+            a = 256 + 128 * h
+            total(bank(7, a, a + 128), [(reg("U2", 15 - k, 143 - k), reg("MH", 2048 * h + k, 2048 * h + 2048, 16)) for k in range(16)])
+            halves(h, 7, a, -1.0, 1, 0)
+
+        def fetch(c):
+            a = 256 * s + 128 + 64 * c
+            act(reg("YG", 1024 * c, 1024 * c + 1024), reg("X", 0, wx, off=reg("LO", a, a + 64)), AF.Copy)
+
+        def short(c):
+            total(bank(4 + c % 3), [(IDB, reg("ZR", 2048 + 512 * c, 2560 + 512 * c)), (NIDB, reg("YG", 512 * c, 512 * c + 512))])
+
+        def short_out(c):
+            act(reg("MY", 2048 + 512 * c, 2560 + 512 * c), bank(4 + c % 3), AF.Relu)
 
         def far_names():
             act(reg("NM"), reg(TF, 512, 1024, off=reg("BO16")), AF.Copy)
@@ -462,67 +533,73 @@ def rank_program(g, core, T, topo):
 
         if t > 0:
             arrive("ta%d" % (t - 1))
+            arrive("tn%d" % (t - 1))
             arrive("u1" if t == 1 else "tb%d" % (t - 2))
 
         gather("MY", "X", "LO", 0, 256 * s)
         if t == 0:
             late_constants()
-            sums("MY", "FS", 0, 0)
+            home_sums(0)
+            stacked_selectors()
             later_constants()
-        for q in range(7):
-            zpass(q, "nl", start=True)
-        if t > 0:
-            sums("MY", "FS", 0, 0)
-            far_names()
+            gather("MY", "X", "LO", 1, 256 * s)
+            copy(reg("MO"), reg(TF, 0, 512, off=reg("BO16")))
+            home_sums(1)
             far_entries()
+            far_names()
+            stack_names()
             for q in range(4):
                 znames(q)
-        gather("MY", "X", "LO", 1, 256 * s)
-        copy(reg("MO"), reg(TF, 0, 512, off=reg("BO16")))
-        if t > 0:
+        else:
+            fetch(0)
+            fetch(1)
+            short(0)
+            short(1)
+            short_out(0)
+            short_out(1)
+            home_sums(0)
+            short(2)
+            short(3)
+            far_names()
+            short_out(2)
+            stack_names()
+            short_out(3)
             if s == 0:
                 follow_home(t - 1)
+            copy(reg("MO"), reg(TF, 0, 512, off=reg("BO16")))
             follow_far(t - 1)
-        sums("MY", "FS", 1, 128)
-        if t == 0:
-            last_constants()
-            far_entries()
-            far_names()
-        for h in range(2):
-            total(bank(7, 128 * h, 128 * h + 128), [(reg("FS", 128 * h, 128 * h + 128), ID), (reg("TIE", 640, 768, p1=1), reg("TIE", 512, 640, p1=1))])
-        if t == 0:
             for q in range(4):
                 znames(q)
-        for q in range(4):
-            zpass(q, "f")
-        if t > 0:
-            for q in (4, 5, 6):
-                znames(q)
-                zpass(q, "f")
+            home_sums(1)
+            far_entries()
         gather("MH", XF, "MO", 0, 0)
-        scan(reg("NFK"), reg("SG", 0, 256), bank(7, 0, 256), 0.0, OP.mult, OP.max)
-        sums("MH", "HS", 0, 256)
-        for q in range(4):
-            zpass(q, "h", stop=True)
+        znames(4)
+        far_sums(0)
         if t == 0:
-            for q in (4, 5):
-                znames(q)
-                zpass(q, "f")
-        ts(reg("KI", 32, 48), reg("NFK", 15, 256, 16), 4096.0, OP.mult)
+            last_constants()
+        znames(5)
+        for q in range(4):
+            zpass(q, "fh", stop=True)
         gather("MH", XF, "MO", 1, 0)
-        ts(reg("KI", 48, 64), reg("KI", 32, 48), 15, OP.bitwise_and)
-        sums("MH", "HS", 1, 384)
+        far_sums(1)
+        for h in range(2):
+            total(bank(6, 128 * h, 128 * h + 128), [(reg("FS", 128 * h, 128 * h + 128), ID), (reg("TIE", 640, 768, p1=1), reg("TIE", 512, 640, p1=1))])
         for q in range(8):
             if q == 1:
-                ts(reg("KN"), reg("KI", 48, 64), -1.0 / 16, OP.mult, 15.0 / 16, OP.add)
-                for q2 in (4, 5, 6):
-                    if t == 0 and q2 == 6:
-                        znames(q2)
-                        zpass(q2, "f")
-                    zpass(q2, "h", stop=True)
                 znames(7)
-                zpass(7, "f")
-                zpass(7, "h", stop=True)
+                zpass(4, "fh", stop=True)
+                zpass(5, "fh", stop=True)
+            if q == 3:
+                scan(reg("NFK"), reg("SG", 0, 256), bank(6, 0, 256), 0.0, OP.mult, OP.max)
+                znames(6)
+                zpass(6, "fh", stop=True)
+                zpass(7, "fh", stop=True)
+            if q == 4:
+                ts(reg("KI", 32, 48), reg("NFK", 15, 256, 16), 4096.0, OP.mult)
+            if q == 5:
+                ts(reg("KI", 48, 64), reg("KI", 32, 48), 15, OP.bitwise_and)
+            if q == 6:
+                ts(reg("KN"), reg("KI", 48, 64), -1.0 / 16, OP.mult, 15.0 / 16, OP.add)
             if q == 7:
                 mm(bank(5), ID, reg("CM"), True, True)
             for g2 in range(2):
@@ -556,6 +633,7 @@ def rank_program(g, core, T, topo):
         if t >= 2:
             total(bank(7, 0, 256), [(BO, reg("WK", 512, 768)), (BOM, reg("WK", 256, 512))])
         ts(reg("LM"), bank(3, 16, 48), MID, OP.add)
+        send("m%d" % t)
         offL, offM = reg("LM", 0, 16), reg("LM", 16, 32)
         v = reg("VY", 512 * s, 512 * s + 256)
         yk = reg("VY", 512 * s + 256, 512 * s + 512)
@@ -589,12 +667,13 @@ def rank_program(g, core, T, topo):
         send("v%d" % t)
         rv, dm = 48 * s, 32 * t
         ts(reg("RV", rv + 16, rv + 48), bank(3, 16, 48), MID, OP.add)
+        total(bank(6, 0, 256), [(IDB, yk), (NIDB, v)])
+        act(reg("TM", 512, 768), bank(6, 0, 256), AF.Copy)
         if t < R - 1:
+            send("at%d" % t)
             for k in range(8):
                 act(reg("ZR", k, 4096, 16), zn, AF.Copy)
         first_of("E2", 256, lambda h: bank(3, 32 + h, 33 + h), lambda h: bank(1, h, h + 1), 2)
-        total(bank(6, 0, 256), [(IDB, yk), (NIDB, v)])
-        act(reg("TM", 512, 768), bank(6, 0, 256), AF.Copy)
         if t < R - 1:
             for k in range(8, 16):
                 act(reg("ZR", k, 4096, 16), zn, AF.Copy)
@@ -676,6 +755,18 @@ def rank_program(g, core, T, topo):
             send("ta%d" % t)
             copy(reg("X", wx, wx + 256), reg("NB", 0, 256))
         copy(reg("X", off=reg("OH", 0, 16)), reg("TM", 512, 768))
+
+        def look(q, win, bound, op, step):
+            part = reg("TP", 256 * q, 256 * q + 256)
+            tt(part, win, bound, op)
+            if t < R - 1:
+                total(bank([7, 4, 5][q], 256, 512), [(IDB, part), (IDB, step)])
+                act(reg("TV", 256 * q, 256 * q + 256), bank([7, 4, 5][q], 256, 512), AF.Copy)
+                send("b%d" % (t + q))
+
+        def put(q, off, step):
+            tt(reg("X", off=off), reg("TP", 256 * q, 256 * q + 256), step, OP.add)
+
         if t < R - 1:
             copy(reg("BI", 48, 64), bank(4, 0, 16))
             ts(reg("BI", 0, 16), reg("BI", 48, 64), 511, OP.bitwise_and)
@@ -684,9 +775,11 @@ def rank_program(g, core, T, topo):
         if t < R - 1:
             payee(t + 1)
             c2 = 256 * (1 - s)
-            act(reg("NL"), reg("TB", 512 + c2, 768 + c2), AF.Copy, scale=-1.0)
+            home_names(512 + c2)
             act(reg("CM", 0, 256), reg("TB", c2, c2 + 256), bias=-MID)
         ts(reg("RH"), reg("RC"), MID, OP.subtract)
+        arrive("m%d" % t)
+        look(0, reg("X", 0, wx, off=reg("LG", 16 * t, 16 * t + 16)), fv, OP.max, reg("NV", 0, 256))
         for j in range(16):
             mm(bank(6, j, 512, 16, p1=8), reg("ID", j, 128, 16), reg("RH", 0, 32), True, True)
         for j in range(16):
@@ -699,26 +792,19 @@ def rank_program(g, core, T, topo):
         arrive("o%d" % t)
 
         def change(q, off, bound, op, step):
-            part = reg("TP", 256 * q, 256 * q + 256)
-            tt(part, reg("X", off=off), bound, op)
-            tt(reg("X", off=off), part, step, OP.add)
-            if t < R - 1:
-                total(bank(4 + q, 0, 256), [(IDB, part), (IDB, step)])
-                act(reg("TV", 256 * q, 256 * q + 256), bank(4 + q, 0, 256), AF.Copy)
+            look(q, reg("X", off=off), bound, op, step)
+            put(q, off, step)
 
         if t < R - 1:
-            send("bo%d" % t)
             if t < 2:
                 copy(reg("LO", 256 * s, 256 * s + 256), C)
             if s == 0:
                 follow_home(t)
-        change(0, reg("LF", 32 * t, 32 * t + 16), fv, OP.max, reg("NV", 0, 256))
+        put(0, reg("LF", 32 * t, 32 * t + 16), reg("NV", 0, 256))
         if t >= 2:
             change(1, reg("OH", 16, 32), reg("NV", 256, 512), OP.min, yk)
             change(2, reg("LF", 32 * t + 16, 32 * t + 32), reg("NV", 512, 768), OP.min, fw)
-        if t < R - 1:
-            send("b%d" % t)
-        else:
+        if t == R - 1:
             dma("s", [(T.xo[:, 0:1536], reg("X", 0, 1536))])
             dma("a", [(T.xo[:, 1536:3072], reg("X", 1536, 3072))])
             lists_end()
@@ -738,11 +824,11 @@ def emit(g, T, ops, queue):
         e = op["e"]
         deps = set()
         for kind, lst in (("r", op["r"]), ("w", op["w"])):
-            for name, a, b, st in lst:
+            for name, a, b, st, p0, p1 in lst:
                 psum = SCRATCH[name][0] == "psum"
-                for j, k2, a2, b2, st2 in hist.get(name, []):
+                for j, k2, a2, b2, st2, q0, q1 in hist.get(name, []):
                     same = ops[j]["e"] == e and not ops[j]["sem"] and not op["sem"]
-                    over = a < b2 and a2 < b and not (st == st2 and (a - a2) % st)
+                    over = a < b2 and a2 < b and p0 < q1 and q0 < p1 and not (st == st2 and (a - a2) % st)
                     if same:
                         if over and e != "p" and (kind == "w" or k2 == "w"):
                             deps.add(j)
@@ -762,8 +848,8 @@ def emit(g, T, ops, queue):
             clock[i] = {}
         clock[i][key(i)] = i
         for kind, lst in (("r", op["r"]), ("w", op["w"])):
-            for name, a, b, st in lst:
-                hist.setdefault(name, []).append((i, kind, a, b, st))
+            for name, a, b, st, p0, p1 in lst:
+                hist.setdefault(name, []).append((i, kind, a, b, st, p0, p1))
     count, value = {e: 0 for e in ENG_SEM}, [None] * n
     waited = {}
     for i, op in enumerate(ops):

@@ -8,14 +8,15 @@ WT = [1, 64, 5, 83, 17, 131, 29, 211, 43, 157, 61, 239, 71, 113, 97, 199]
 XW = 3328
 PIECE = 704
 MID = 1536.0
-NDVE = 2
+SHARE = [(64, 32, 32, 32), (64, 64, 0, 32), (64, 32, 32, 32), (96, 64, 0, 32)]
+HELPED = 3
 ZACT = 8
 
 F, H16, B16, I32, U16 = "float32", "float16", "bfloat16", "int32", "uint16"
 SCRATCH = {
     "X": ("sbuf", [128, XW], B16), "XF0": ("sbuf", [128, XW], B16), "XF1": ("sbuf", [128, XW], B16),
     "LH": ("sbuf", [128, 2048], B16), "LN": ("sbuf", [128, 1024], B16), "LB": ("sbuf", [128, 192], U16), "TV": ("sbuf", [128, 768], B16),
-    "NB": ("sbuf", [128, 512], B16), "NV": ("sbuf", [128, 768], B16), "TP": ("sbuf", [128, 768], B16),
+    "NB": ("sbuf", [128, 256], B16), "NV": ("sbuf", [128, 1280], B16), "TP": ("sbuf", [128, 768], B16),
     "TB": ("sbuf", [128, 1024], F), "TF0": ("sbuf", [128, 1024], F), "TF1": ("sbuf", [128, 1024], F),
     "PL": ("sbuf", [128, 512], I32), "FR": ("sbuf", [128, 128], I32), "FR16": ("sbuf", [128, 128], H16),
     "FW": ("sbuf", [128, 2048], F), "NG": ("sbuf", [128, 4096], H16), "N0": ("sbuf", [128, 256], H16),
@@ -23,41 +24,47 @@ SCRATCH = {
     "ZB": ("sbuf", [128, 512], B16),
     "LO": ("sbuf", [128, 512], U16), "MO": ("sbuf", [128, 256], U16), "BO16": ("sbuf", [128, 16], U16),
     "BI": ("sbuf", [128, 64], I32), "BH": ("sbuf", [128, 16], H16),
-    "CM": ("sbuf", [128, 512], H16), "NL": ("sbuf", [128, 256], H16), "NM": ("sbuf", [128, 256], H16),
-    "FS": ("sbuf", [128, 256], H16), "FH": ("sbuf", [128, 512], H16), "NS": ("sbuf", [128, 512], H16), "SW": ("sbuf", [128, 128], H16),
-    "YG": ("sbuf", [128, 2048], B16), "SEL": ("sbuf", [128, 2048], H16), "U2": ("sbuf", [128, 144], H16), "NBO": ("sbuf", [128, 128], B16),
-    "NFK": ("sbuf", [128, 256], F), "KN": ("sbuf", [128, 16], F), "KI": ("sbuf", [128, 64], I32),
-    "RR": ("sbuf", [128, 16], F), "VA": ("sbuf", [128, 32], H16), "VB": ("sbuf", [128, 32], H16),
+    "CM": ("sbuf", [128, 768], H16), "NL": ("sbuf", [128, 256], H16),
+    "TS": ("sbuf", [128, 512], H16), "FH": ("sbuf", [128, 512], H16), "NS": ("sbuf", [128, 512], H16), "PM": ("sbuf", [128, 512], H16),
+    "YG": ("sbuf", [128, 8192], B16), "SN": ("sbuf", [128, 1024], H16), "SC": ("sbuf", [128, 1024], H16), "SF": ("sbuf", [128, 64], H16),
+    "R0": ("sbuf", [128, 1024], H16), "IA": ("sbuf", [128, 704], B16), "TIE": ("sbuf", [2, 576], F),
+    "NFK": ("sbuf", [128, 256], F), "KI": ("sbuf", [128, 48], I32), "PD": ("sbuf", [128, 24], F),
+    "RR": ("sbuf", [128, 2048], F), "AB": ("sbuf", [128, 2048], F), "VA": ("sbuf", [128, 32], H16), "FL": ("sbuf", [128, 32], F),
+    "BB": ("sbuf", [128, 256], B16), "BW": ("sbuf", [128, 2048], B16), "SL": ("sbuf", [128, 768], B16),
     "VT": ("sbuf", [128, 128], H16), "WK": ("sbuf", [128, 1024], H16), "KB": ("sbuf", [128, 512], H16),
-    "LM": ("sbuf", [128, 32], U16), "EE": ("sbuf", [128, 2176], H16), "E2": ("sbuf", [128, 2176], H16),
-    "ST": ("sbuf", [128, 256], H16), "BD": ("sbuf", [128, 256], H16),
-    "M1": ("sbuf", [128, 256], B16), "VY": ("sbuf", [128, 1024], B16), "TM": ("sbuf", [128, 768], B16),
+    "LM": ("sbuf", [128, 48], U16), "EE": ("sbuf", [128, 2176], B16), "E2": ("sbuf", [128, 2176], B16),
+    "ST": ("sbuf", [128, 256], B16), "BD": ("sbuf", [128, 256], B16),
+    "VY": ("sbuf", [128, 1024], B16), "TM": ("sbuf", [128, 256], B16),
     "RV": ("sbuf", [128, 96], F), "DM": ("sbuf", [128, 128], F), "G2": ("sbuf", [128, 96], F),
-    "OH": ("sbuf", [128, 32], U16), "OF": ("sbuf", [128, 128], U16),
-    "LV": ("sbuf", [128, 1536], B16), "LF": ("sbuf", [128, 128], U16), "LG": ("sbuf", [128, 64], U16),
+    "OH": ("sbuf", [128, 64], U16),
+    "LV": ("sbuf", [128, 2048], B16), "LF": ("sbuf", [128, 64], U16), "LG": ("sbuf", [128, 128], U16),
     "RC": ("sbuf", [128, 48], F), "RH": ("sbuf", [128, 48], H16), "RO": ("sbuf", [8, 768], F),
-    "T1": ("sbuf", [128, 256], F), "T2": ("sbuf", [128, 768], H16), "MK": ("sbuf", [128, 256], H16),
+    "T2": ("sbuf", [128, 768], H16), "MK": ("sbuf", [128, 256], H16),
     "CO": ("sbuf", [128, 512], F),
-    "PI": ("sbuf", [128, 8], I32), "PC": ("sbuf", [128, 8], F),
-    "IOX": ("sbuf", [128, 256], F), "IOA": ("sbuf", [128, 512], F), "IOB": ("sbuf", [128, 512], F),
-    "RK": ("sbuf", [128, 512], H16), "RL": ("sbuf", [128, 512], H16), "ID": ("sbuf", [128, 256], H16),
+    "PI": ("sbuf", [128, 16], I32), "PC": ("sbuf", [128, 16], F),
+    "IOX": ("sbuf", [128, 256], F), "IOA": ("sbuf", [128, 512], F), "IOB": ("sbuf", [128, 256], F),
+    "RK": ("sbuf", [128, 512], H16), "ID": ("sbuf", [128, 256], H16),
     "IB": ("sbuf", [128, 256], B16),
     "U1": ("sbuf", [128, 144], H16), "US": ("sbuf", [128, 144], H16), "UW": ("sbuf", [128, 144], B16),
-    "BK": ("sbuf", [128, 640], H16), "SJ": ("sbuf", [128, 2048], H16), "DG": ("sbuf", [128, 16], F),
-    "WR": ("sbuf", [128, 32], F), "WC": ("sbuf", [128, 2], F), "SG": ("sbuf", [128, 768], F),
-    "THR": ("sbuf", [128, 256], F), "TIE": ("sbuf", [128, 768], H16), "DUM": ("sbuf", [128, 16], F),
+    "BK": ("sbuf", [128, 256], H16), "SJ": ("sbuf", [128, 2048], H16), "DG": ("sbuf", [128, 16], F),
+    "WR": ("sbuf", [128, 32], F), "WC": ("sbuf", [128, 4], F), "SG": ("sbuf", [128, 512], F),
+    "THR": ("sbuf", [128, 256], F), "DUM": ("sbuf", [128, 32], F),
 }
 for _b in range(8):
     SCRATCH["P%d" % _b] = ("psum", [128, 512], F)
 
-MSGS = ["c0", "x0", "n0", "u1"] + ["v%d" % t for t in range(R)] + ["m%d" % t for t in range(R)] + ["o%d" % t for t in range(R)] + \
+MSGS = ["c0", "x0", "n0", "u1"] + [m + str(t) for m in ("v", "m", "o") for t in range(R)] + \
        ["x1", "x2", "x3", "tb0", "tb1", "b3", "b4"] + [m + str(t) for m in ("a", "at", "ao", "b", "bo", "ta", "tn") for t in range(R - 1)]
 HAND = [0, 512, 1024]
 NDMA = 16
 SEMAPHORES = ["sv", "sa", "sp", "sg"] + ["d%d" % i for i in range(NDMA)] + \
              ["arr_" + m for m in MSGS] + ["snt_" + m for m in MSGS]
 ENG_SEM = {"v": "sv", "a": "sa", "p": "sp", "g": "sg"}
-LAND = [0, 256, 512, 1024]
+LAND = [0, 512, 1024, 1536]
+CYCLE, TENSOR_CYCLE, GATHER, SCATTER, WAKE = 0.9, 0.45, 1.56, 3.8, 150.0
+ISSUE = {"g": 400.0, "s": 60.0, "a": 60.0, "x": 0.0}
+PASSES, SLACK = 2, 3000.0
+HOP, LOAD, BYTE = 2600.0, 2000.0, 1.0
 
 
 def reg(name, a=None, b=None, step=1, p0=0, p1=128, off=None):
@@ -79,6 +86,28 @@ def ap(T, r):
 
 def spans(rs):
     return [(r["n"], r["a"], r["b"], r["s"], r["p0"], r["p1"]) for r in rs if isinstance(r, dict)]
+
+
+def width(r):
+    return 16 * width(r["off"]) if r["off"] is not None else len(range(r["a"], r["b"], r["s"]))
+
+
+def row_bytes(r):
+    return width(r) * (4 if SCRATCH[r["n"]][2] in (F, I32) else 2)
+
+
+def duration(eng, out, ins, per):
+    full = [r for r in [out] + list(ins) if isinstance(r, dict)]
+    n = max(width(r) for r in full[:2])
+    if eng == "p":
+        return TENSOR_CYCLE * max(64, width(out))
+    if eng == "g":
+        return 130 + 2 * CYCLE * n
+    if any(r["off"] is not None for r in full):
+        return 60 + CYCLE * n * (SCATTER if out["off"] is not None else GATHER)
+    if per is None:
+        per = 0.5 if all(SCRATCH[r["n"]][2] in (H16, B16, U16) for r in full if width(r) == n) else 1.0
+    return CYCLE * max(64, per * n) + (70 if eng == "a" else 0)
 
 
 def routes(T, topo, src, dst, mode):
@@ -113,22 +142,22 @@ def messages(T, topo):
         s, wx = t % 2, W0 + P * t
         w, n = (128, 16) if t < 2 else (256, 32)
         s0, l0, h0 = 512 * s, LAND[t], HAND[t % 3]
-        ms.append(plain("m%d" % t, 1 + s, "near1", [(reg("LM", 16, 32), reg("LG", 16 * t, 16 * t + 16))]))
-        ms.append(plain("v%d" % t, 1 + s, "near", [(reg("VY", s0 + j * w, s0 + (j + 1) * w), reg("LV", l0 + j * w, l0 + (j + 1) * w)) for j in range(2)]))
+        ms.append(plain("m%d" % t, 1 + s, "near1", [(reg("LM", 16, 16 + n), reg("LG", 32 * t, 32 * t + n))]))
+        ms.append(plain("v%d" % t, 1 + s, "near", [(reg("VY", s0 + j * w, s0 + (j + 1 + s) * w), reg("LV", l0 + j * w, l0 + (j + 1 + s) * w)) for j in range(2 - s)]))
         if t < R - 1:
-            ms.append(plain("at%d" % t, s - 2, "near", [(reg("TM", 512 + 128 * j, 640 + 128 * j), reg("LH", h0 + 128 * j, h0 + 128 + 128 * j)) for j in range(2)]))
-        ms.append(plain("o%d" % t, 1 + s, "near" if s else "far1", [(reg("OF", 32 * t, 32 * t + n), reg("LF", 32 * t, 32 * t + n))]))
+            ms.append(plain("at%d" % t, s - 2, "near1", [(reg("TM"), reg("LH", h0, h0 + 256))]))
+            ms.append(plain("a%d" % t, s - 2, "far", [(reg("VY", s0, s0 + 256), reg("LN", 256 * t, 256 * t + 256)), (reg("NB"), reg("LN", 768, 1024))][:1 + t // 2]))
+        ms.append(plain("o%d" % t, 1 + s, "near" if s else "far1", [(reg("OH", 0, 16), reg("LF", 16 * t, 16 * t + 16))]))
         if t == R - 1:
             break
-        ms.append(plain("bo%d" % t, 2 * s - 1, "near1", [(reg("OF", 32 * t, 32 * t + n), reg("LB", 64 * t + 32, 64 * t + 32 + n))]))
-        ms.append(plain("ao%d" % t, s - 2, "near2", [(reg("OH", 0, n), reg("LB", 64 * t, 64 * t + n))]))
-        ms.append(plain("a%d" % t, s - 2, "far", [(reg("NB", 256 * j, 256 * j + 256), reg("LN", 256 * (t + j), 256 * (t + j + 1))) for j in range(1 + t // 2)]))
+        ms.append(plain("bo%d" % t, 2 * s - 1, "near1", [(reg("OH", 0, 16), reg("LB", 64 * t, 64 * t + 16))]))
+        ms.append(plain("ao%d" % t, s - 2, "near2", [(reg("OH", 16, 2 * n), reg("LB", 64 * t + 16, 64 * t + 2 * n))]))
         stage = [("TB", 768), ("TF0", 0), ("TF0", 256)][t]
         ms.append(tab("ta%d" % t, s - 2, [256 * s, 256 * s + 128], stage, "near", 128))
         ms.append(tab("tn%d" % t, s - 2, [512 + 256 * s, 640 + 256 * s], stage, "far", 128))
-        for q in range(1 if t < 2 else 3):
+        for q in [0] if t < 2 else [1, 2, 0]:
             c, l = 256 * q, h0 + 256 * (q + 1)
-            ms.append(plain("b%d" % (t + q), s - 2, "near", [(reg("TV", c + 128 * j, c + 128 * j + 128), reg("LH", l + 128 * j, l + 128 * j + 128)) for j in range(2)]))
+            ms.append(plain("b%d" % (t + q), s - 2, "near", [(reg("TV", c + 128 * j, c + 128 * j + 256 - 128 * s), reg("LH", l + 128 * j, l + 128 * j + 256 - 128 * s)) for j in range(1 + s)]))
         if t < 2:
             ms.append(xship(t + 2))
             ms.append(tab("tb%d" % t, -1 - s, [256 * s, 512 + 256 * s], ("TF0", 512 + 256 * t)))
@@ -164,7 +193,7 @@ def plan_message(T, topo, src, msg):
 
 
 def call_of(name):
-    return {"bo": "o", "tn": "ta"}.get(name[:-1], name[:-1]) + name[-1]
+    return {"bo": "o", "tn": "ta", "a": "at"}.get(name[:-1], "o" if name == "ao1" else name[:-1]) + name[-1]
 
 
 def deal(pool, items):
@@ -217,39 +246,42 @@ def rank_program(g, core, T, topo):
         carrier_program(g, core, T, topo)
         return
     ops = []
-    ndma = [0]
+    ndma, queued = [0], [0.0]
+    ahead = [0.0]
     msgs = {m[0]: m for m in messages(T, topo)}
     queue = {"v": g.vector, "a": g.scalar, "p": g.tensor, "g": g, "s": g.sync}
 
-    def add(eng, fn, outs, ins, sem=None):
+    def add(eng, fn, outs, ins, sem=None, per=1.0, lands=0.0, msg=None):
         rd, wr = spans(ins), spans(outs)
         for r in list(ins) + list(outs):
             if isinstance(r, dict) and r["off"] is not None:
                 rd += spans([r["off"]])
-        ops.append({"e": eng, "f": fn, "r": rd, "w": wr, "sem": sem})
+        ops.append({"e": eng, "f": fn, "r": rd, "w": wr, "sem": sem, "msg": msg, "lands": lands, "ahead": ahead[0],
+                    "busy": ISSUE[eng] if sem else duration(eng, outs[0], ins, per)})
 
     A = lambda r: ap(T, r)
 
     def copy(out, in_):
-        add("v", lambda: g.vector.tensor_copy(A(out), A(in_)), [out], [in_])
+        add("v", lambda: g.vector.tensor_copy(A(out), A(in_)), [out], [in_], per=None)
 
     def tt(out, a, b, op):
-        add("v", lambda: g.vector.tensor_tensor(A(out), A(a), A(b), op), [out], [a, b])
+        both = SCRATCH[a["n"]][0] == SCRATCH[b["n"]][0]
+        add("v", lambda: g.vector.tensor_tensor(A(out), A(a), A(b), op), [out], [a, b], per=2.0 if both else 1.0)
 
     def ts(out, a, s1, op0, s2=None, op1=None):
         if op1 is None:
-            add("v", lambda: g.vector.tensor_scalar(A(out), A(a), A(s1), None, op0), [out], [a, s1])
+            add("v", lambda: g.vector.tensor_scalar(A(out), A(a), A(s1), None, op0), [out], [a, s1], per=None)
         else:
-            add("v", lambda: g.vector.tensor_scalar(A(out), A(a), A(s1), A(s2), op0, op1), [out], [a, s1, s2])
+            add("v", lambda: g.vector.tensor_scalar(A(out), A(a), A(s1), A(s2), op0, op1), [out], [a, s1, s2], per=None)
 
     def fill(out, c):
-        add("v", lambda: g.vector.memset(A(out), c), [out], [])
+        add("v", lambda: g.vector.memset(A(out), c), [out], [], per=None)
 
     def red(out, a, op, absolute=False):
         add("v", lambda: g.vector.tensor_reduce(A(out), A(a), AxisListType.X, op, apply_absolute_value=absolute), [out], [a])
 
     def scan(out, d0, d1, init, op0, op1):
-        add("v", lambda: g.vector.tensor_tensor_scan(A(out), A(d0), A(d1), init, op0, op1), [out], [d0, d1])
+        add("v", lambda: g.vector.tensor_tensor_scan(A(out), A(d0), A(d1), A(init), op0, op1), [out], [d0, d1, init], per=None)
 
     def act(out, a, func=AF.Identity, bias=0.0, scale=1.0):
         add("a", lambda: g.scalar.activation(A(out), A(a), func, bias=A(bias), scale=A(scale)), [out], [a, bias, scale])
@@ -274,7 +306,8 @@ def rank_program(g, core, T, topo):
         def fn():
             for out, in_ in pairs:
                 queue[eng].dma_start(A(out), A(in_)).then_inc(T.sem[name], 16)
-        add(eng, fn, [p[0] for p in pairs], [p[1] for p in pairs], sem=(name, 16 * len(pairs)))
+        queued[0] = (queued[0] if ahead[0] else 0.0) + sum(250 + 0.35 * row_bytes(r) for p in pairs for r in p if isinstance(r, dict))
+        add(eng, fn, [p[0] for p in pairs], [p[1] for p in pairs], sem=(name, 16 * len(pairs)), lands=LOAD + queued[0])
 
     def send(name, after=()):
         trs = []
@@ -282,23 +315,28 @@ def rank_program(g, core, T, topo):
             dst, way, engs, _ = plan_message(T, topo, core, msg)
             trs += [(msg[0], dst, engs[j], p[0], p[2]) if way[j] is None else (msg[0], way[j], engs[j], p[0], p[1]) for j, p in enumerate(msg[3])]
         add("g", lambda: write(g, T, topo, core, name, trs), [], [tr[3] for tr in trs] + list(after),
-            sem=("snt_" + name, sum(len(tr[2]) for tr in trs)))
+            sem=("snt_" + name, sum(len(tr[2]) for tr in trs)), msg=name, lands=HOP + BYTE * sum(row_bytes(tr[3]) for tr in trs))
 
     def arrive(name):
         msg = msgs[name]
         src = T.cores[(rank - msg[1]) % NR]
-        add("x", None, [p[2] for p in msg[3]], [], sem=("arr_" + name, plan_message(T, topo, src, msg)[3]))
+        dst, way, engs, count = plan_message(T, topo, src, msg)
+        hops = 2 if set(way) - {None} else 1
+        add("x", None, [p[2] for p in msg[3]], [], sem=("arr_" + name, count), msg=(call_of(name), msg[1]),
+            lands=hops * (HOP + 2 * BYTE * sum(row_bytes(p[0]) for p in msg[3]) / len(set(way))))
 
     def bank(b, a=0, e=512, step=1, p1=128):
         return reg("P%d" % b, a, e, step, 0, p1)
 
     col = lambda n, c: reg(n, c, c + 1)
-    P16, P32, PG, PP, PG16 = [col("PC", c) for c in range(5)]
-    BO, BOM, BO128, BOBIG, BOW = [reg("BK", 128 * j, 128 * j + 128) for j in range(5)]
+    P16, PG, PP, PG16, PPAIR, PODD, P24, P3, P4 = [col("PC", c) for c in range(9)]
+    BO, BOM = [reg("BK", 128 * j, 128 * j + 128) for j in range(2)]
+    BIG, NBIG = [reg("BB", 128 * j, 128 * j + 128) for j in range(2)]
+    ROW, CROW, NCROW, KROW, BIAS, PP2, NFC = [col("PD", c) for c in (0, 4, 5, 6, 7, 8, 9)]
     ID, NID, IDB, NIDB = reg("ID", 0, 128), reg("ID", 128, 256), reg("IB", 0, 128), reg("IB", 128, 256)
-
-    def to_slots(out, src, a):
-        total(out, [(reg("U1", 15 - k, 143 - k), reg(src, a + k, a + 2048, 16)) for k in range(16)])
+    START, MINUS8 = reg("R0", 0, 256), reg("R0", 128, 136)
+    sign = lambda n: {0: 1.0, 128: -1.0}.get(n, col("PD", 12 + n // 32))
+    times = lambda c: reg("R0", *{-1: (128, 256), 2: (256, 384), -2: (384, 512), 1: (512, 640), 3: (640, 768)}[c])
 
     def to_list(out, sel, src, a, n):
         total(out, [(reg(sel, 15 - j, 143 - j), reg(src, a + j, a + n, 16)) for j in range(16)])
@@ -311,39 +349,43 @@ def rank_program(g, core, T, topo):
             ts(reg("BH"), reg("BI", 0, 16), 16.0, OP.mult)
         copy(reg("BO16"), reg("BI", 32, 48))
 
+    ahead[0] = 20000.0
     dma("s", [(reg("FR"), T.fr0[:])])
-    dma("a", [(reg("ZB", 0, 256), T.z0[:])])
     dma("a", [(reg("PL"), T.pl[:])])
+    dma("s", [(reg("BI", 0, 16), T.b0[:])])
+    dma("a", [(reg("ZB", 0, 256), T.z0[:])])
     dma("s", [(reg("X", 0, 1024), T.x0[:, 0:1024])])
     dma("a", [(reg("X", 1024, 2048), T.x0[:, 1024:2048])])
-    dma("s", [(reg("BI", 0, 16), T.b0[:])])
     iota(col("PI", 0), [[0, 1]], 0, 1)
     iota(reg("IOA", 0, 128), [[1, 8], [0, 16]], 0, 0)
     iota(reg("IOX"), [[1, 256]], 0, 0)
+    iota(reg("IA", 576, 704), [[0, 16], [1, 8]], 0, 0)
+    iota(reg("IA", 0, 512, 1, 0, 64), [[1, 2], [4, 16], [0, 16]], 0, 0)
+    iota(reg("IA", 0, 512, 1, 64, 128), [[1, 2], [0, 16], [4, 16]], 64, 0)
     fill(reg("X", W0, XW), 0.0)
-    ts(col("PI", 1), col("PI", 0), 15, OP.bitwise_and)
-    ts(col("PI", 2), col("PI", 0), 31, OP.bitwise_and)
-    ts(col("PI", 3), col("PI", 0), 4, OP.logical_shift_right)
-    ts(col("PI", 5), col("PI", 0), 112, OP.bitwise_and)
-    copy(col("PI", 4), col("PI", 0))
-    ts(col("PI", 6), col("PI", 0), 5, OP.logical_shift_right, 1, OP.bitwise_and)
-    copy(reg("PC", 0, 6), reg("PI", 1, 7))
+    for c, (shift, bits) in enumerate([(0, 15), (4, 7), (0, 127), (0, 112), (5, 3), (4, 1), (0, 24), (0, 3), (2, 1)]):
+        ts(col("PI", 1 + c), col("PI", 0), shift, OP.logical_shift_right, bits, OP.bitwise_and)
+    copy(reg("PC", 0, 9), reg("PI", 1, 10))
     ts(BO, reg("IOA", 0, 128), PG, OP.is_equal)
     ts(reg("DG"), reg("IOX", 0, 16), P16, OP.is_equal)
     for j in range(16):
-        if j % 4 == 3:
+        if j % 2:
             act(reg("SJ", 128 * j, 128 * j + 128), BO, AF.Copy, scale=col("DG", j))
         else:
             ts(reg("SJ", 128 * j, 128 * j + 128), BO, col("DG", j), OP.mult)
-    iota(reg("IOA", 128, 512), [[1, 24], [0, 16]], 8, 0)
+    copy(reg("FR16"), reg("FR"))
     ts(reg("U1"), reg("IOX", 0, 144), 15.0, OP.subtract, PG16, OP.is_equal)
     ts(ID, reg("IOX", 0, 128), PP, OP.is_equal)
-    copy(reg("FR16"), reg("FR"))
     copy(reg("TB", 0, 256), reg("PL", 0, 512, 2))
     copy(reg("TB", 256, 512), reg("PL", 1, 512, 2))
     send("c0")
     send("x0")
-    iota(reg("IOB"), [[16, 2], [0, 16], [1, 16]], 0, 0)
+    ahead[0] = 10000.0
+    iota(reg("TIE", 0, 512, p1=2), [[0, 2], [32, 16], [1, 16]], 0, 0)
+    iota(reg("TIE", 512, 576, p1=2), [[0, 4], [32, 16]], 16, 0)
+    iota(reg("IA", 512, 576), [[1, 4], [4, 16]], 0, 0)
+    iota(reg("IOB"), [[0, 16], [1, 16]], 0, 0)
+    iota(reg("IOA", 128, 512), [[1, 24], [0, 16]], 8, 0)
     for k in range(ZACT):
         act(reg("ZR", k, 4096, 16), reg("ZB", 0, 256), AF.Copy)
     for j in range(16):
@@ -356,34 +398,22 @@ def rank_program(g, core, T, topo):
     for e in range(16):
         iota(col("WR", e), [[0, 1]], WT[e], 0)
 
-    def name_gather(c, eng):
-        buf, a = ("NG" if eng == "a" else "MH"), 2048 * (c % 2)
-        w = reg("FW", off=reg("LO", 128 * c, 128 * c + 128))
-        if eng == "a":
-            act(reg(buf, a, a + 2048), w, AF.Copy)
-        else:
-            copy(reg(buf, a, a + 2048), w)
-        return buf, a
-
-    def name_out(c):
+    pieces = {"a": [(0, 128), (128, 192), (192, 256)], "v": [(256, 384), (384, 448), (448, 512)]}
+    for q in range(3):
+        for eng, buf in (("a", "NG"), ("v", "MH")):
+            a, b = pieces[eng][q]
+            out, w = reg(buf, 16 * (a % 256), 16 * (a % 256) + 16 * (b - a)), reg("FW", off=reg("LO", a, b))
+            if eng == "a":
+                act(out, w, AF.Copy)
+            else:
+                copy(out, w)
+            total(bank(4 + a // 128, a % 128, a % 128 + b - a), [(reg("U1", 15 - k, 143 - k), reg(buf, out["a"] + k, out["b"], 16)) for k in range(16)])
+    for c in (0, 2, 1, 3):
         act(reg("TB", 512 + 128 * c, 640 + 128 * c), bank(4 + c, 0, 128), AF.Copy)
-
-    on_v, on_a = list(range(4 - NDVE, 4)), list(range(4 - NDVE))
-    place, done = {}, []
-    for q in range(max(len(on_a), len(on_v))):
-        for lst, eng in ((on_a, "a"), (on_v, "v")):
-            if q < len(lst):
-                place[lst[q]] = name_gather(lst[q], eng)
-        for c in done:
-            name_out(c)
-        done = [lst[q] for lst in (on_a, on_v) if q < len(lst)]
-        for c in done:
-            to_slots(bank(4 + c, 0, 128), place[c][0], place[c][1])
+    send("n0")
+    ahead[0] = 0.0
     for k in range(ZACT, 16):
         copy(reg("ZR", k, 4096, 16), reg("ZB", 0, 256))
-    for c in done:
-        name_out(c)
-    send("n0")
     for m in ("c0", "x0", "n0"):
         arrive(m)
     send("u1", after=[reg("TF0", 512, 1024)])
@@ -392,62 +422,81 @@ def rank_program(g, core, T, topo):
 
     def home_names(c):
         act(reg("NL"), reg("TB", c, c + 256), AF.Copy, scale=-1.0)
-        act(reg("NS", 0, 256, 1, 0, 64), reg("TB", c, c + 256, 1, 0, 64), AF.Copy, scale=-1.0)
-        act(reg("NS", 256, 512, 1, 64, 128), reg("TB", c, c + 256, 1, 64, 128), AF.Copy, scale=-1.0)
 
-    home_names(512)
-    act(reg("SW", 0, 64), reg("ID", 64, 128), AF.Copy)
-    act(reg("SW", 64, 128), reg("ID", 0, 64), AF.Copy)
-
-    def late_constants():
-        ts(reg("RK"), reg("IOA"), P32, OP.is_equal)
-        ts(reg("RL"), reg("IOB"), P32, OP.is_equal)
+    def sum_constants():
+        parts = sorted({n for sh in SHARE for n in sh} - {0, 128})
+        ts(times(-1), reg("IA", 576, 704), PG, OP.is_equal, -1.0, OP.mult)
+        for n in parts:
+            ts(col("PD", 16 + n // 32), PP, float(n), OP.is_ge, 2.0, OP.mult)
+        for n in parts:
+            ts(sign(n), col("PD", 16 + n // 32), 1.0, OP.subtract)
         act(IDB, ID, AF.Copy)
         act(NIDB, ID, AF.Copy, scale=-1.0)
-        act(reg("NBO"), BO, AF.Copy, scale=-1.0)
-        act(col("PC", 6), col("PC", 5), bias=1.0, scale=-1.0)
-        ts(reg("SG", 0, 256), reg("IOB", 0, 256), 0.0, OP.is_gt)
-        for h in range(2):
-            act(reg("TIE", 256 * h, 256 * h + 256), reg("IOX"), AF.Copy, scale=1.0 / 256)
-        act(reg("TIE", 512, 640), reg("IOB", 0, 128), bias=15.0 / 16, scale=-1.0 / 16)
-        act(reg("TIE", 640, 768), reg("IOX", 0, 128), bias=1.0 / 256, scale=0.0)
+        act(reg("R0", 0, 8), MINUS8, AF.Copy, scale=0.0)
+        act(reg("R0", 8, 128), reg("R0", 136, 256), AF.Copy, scale=-1.0)
+        for c in (2, -2, 1, 3):
+            act(times(c), times(-1), AF.Copy, scale=-float(c))
+        act(reg("R0", 768, 1024), reg("R0", 0, 256), AF.Copy, scale=0.0)
+        act(reg("R0", 896, 904), MINUS8, AF.Copy)
+
+    def pair_constants():
+        ts(ROW, P16, 4.0, OP.mult, PPAIR, OP.add)
+        ts(col("PD", 3), PODD, 8.0, OP.mult)
+        ts(col("PD", 2), PODD, -8.0, OP.mult, 8.0, OP.add)
+        ts(CROW, PP, 4.0, OP.is_ge, 512.0, OP.mult)
+        ts(NCROW, PP, 4.0, OP.is_ge, -512.0, OP.mult)
+        ts(KROW, P3, 2.0, OP.mult, P24, OP.add)
+        ts(PP2, PP, 2.0, OP.subtract)
+        ts(col("PD", 10), PP, 64.0, OP.is_ge, 2016.0, OP.mult)
+        ts(col("PD", 11), PP, 1.0, OP.is_equal, 1024.0, OP.mult)
+        ts(NFC, PP, 1.0, OP.is_equal, 1528.0, OP.mult)
+        ts(col("PD", 1), ROW, 64.0, OP.add)
+        ts(KROW, KROW, P4, OP.add)
+        ts(BIAS, PP, 0.0, OP.is_equal, col("PD", 10), OP.add)
+        for j, c in enumerate((PP, PP2)):
+            ts(reg("SN", 512 * j, 512 * j + 512), reg("IA", 0, 512), c, OP.is_equal, 32768.0, OP.mult)
+            ts(reg("SC", 512 * j, 512 * j + 512), reg("IA", 0, 512), c, OP.is_equal, CROW, OP.mult)
+            act(reg("SC", 512 * j, 512 * j + 512, p1=2), reg("TIE", 0, 512, p1=2), AF.Copy, scale=reg("DG", 0, 1, p1=2))
+        ts(BIAS, BIAS, col("PD", 11), OP.add)
+        for side in range(2):
+            for odd in range(2):
+                ts(reg("PM", 256 * side + 128 * odd, 256 * side + 128 * odd + 128), reg("IOX", 0, 128), col("PD", side), OP.is_equal, col("PD", 2 + odd), OP.mult)
+        ts(reg("SF"), reg("IA", 512, 576), PP, OP.is_equal, NCROW, OP.mult)
+        ts(reg("SG", 0, 256), reg("IOB"), 0.0, OP.is_equal, 2.0 ** 23, OP.mult)
+        ts(reg("SF", p1=2), reg("TIE", 512, 576, p1=2), reg("DG", 0, 1, p1=2), OP.mult, reg("PD", 9, 10, p1=2), OP.add)
 
     def later_constants():
         act(reg("CM", 0, 256), reg("TB", 0, 256), bias=-MID)
         act(reg("N0"), reg("TB", 512, 768), AF.Copy)
-        act(reg("SG", 256, 512), reg("SG", 0, 256), AF.Copy, scale=0.5)
-        act(reg("SG", 512, 768), reg("SG", 0, 256), bias=256.0, scale=-256.0)
+        act(reg("SG", 256, 512), reg("SG", 0, 256), bias=0.5, scale=2.0 ** -24)
         act(BOM, BO, AF.Copy, scale=-2048.0)
-        act(BO128, BO, AF.Copy, scale=-128.0)
-        act(BOBIG, BO, AF.Copy, scale=256.0)
-        act(reg("US"), reg("U1"), AF.Copy, scale=1.0 / 16)
+        act(reg("SL", 0, 256), reg("SG", 0, 256), bias=1.0, scale=-2.0 ** -23)
         act(NID, ID, AF.Copy, scale=-1.0)
 
-    def stacked_selectors():
-        for p0, a, b, n in ((0, 64, 0, 80), (0, 0, 80, 64), (64, 0, 64, 80), (64, 80, 0, 64)):
-            act(reg("U2", a, a + n, 1, p0, p0 + 64), reg("U1", b, b + n, 1, p0, p0 + 64), AF.Copy)
-        for j in range(4):
-            for p0 in (0, 64):
-                src = "RK" if (p0 == 0) == (j < 2) else "RL"
-                act(reg("SEL", 512 * j, 512 * j + 512, 1, p0, p0 + 64), reg(src, 0, 512, 1, p0, p0 + 64), AF.Copy,
-                    scale=reg("PC", 6 - j % 2, 7 - j % 2, 1, p0, p0 + 64))
-
     def last_constants():
-        scan(reg("T1"), reg("SG", 256, 512), reg("SG", 512, 768), 0.0, OP.mult, OP.add)
+        ts(col("WC", 2), PP, 0.0, OP.mult, 2.0 ** 61, OP.add)
+        ts(reg("RK"), reg("IOA"), KROW, OP.is_equal)
         tt(reg("WR", 16, 32), reg("WR", 0, 16), reg("DG"), OP.mult)
-        ts(reg("DUM"), reg("IOX", 0, 256, 16), P16, OP.add, 3072.0, OP.add)
+        ts(col("WC", 3), col("WC", 2), 2.0 ** 60, OP.mult)
+        for a in (0, 16):
+            ts(reg("DUM", a, a + 16), reg("IOX", 0, 256, 16), P16, OP.add, 3072.0, OP.add)
         red(col("WC", 0), reg("WR", 16, 32), OP.add)
-        tt(reg("WR", 0, 16), reg("T1", 0, 16), reg("DG"), OP.mult)
-        act(reg("THR"), reg("T1"), bias=-2048.0)
+        scan(reg("THR"), reg("SG", 256, 512), reg("X", 3072, XW), col("WC", 3), OP.mult, OP.add)
+        ts(BIG, BO, col("WC", 3), OP.mult, 2.0, OP.mult)
+        ts(reg("NFK"), reg("IOB"), P16, OP.is_equal)
         act(reg("UW"), reg("U1"), AF.Copy, scale=col("WC", 0))
-        red(col("WC", 1), reg("WR", 0, 16), OP.add)
-        ts(BOW, BO, col("WC", 1), OP.mult, 0.5, OP.mult)
+        act(NBIG, BIG, AF.Copy, scale=-1.0)
+        tt(reg("THR"), reg("THR"), reg("NFK"), OP.mult)
+        scan(reg("NFK"), reg("SL", 0, 256), reg("THR"), 0.0, OP.mult, OP.max)
+        act(reg("FL", 0, 16), reg("NFK", 15, 256, 16), AF.Copy, scale=0.5)
+        for h in range(16):
+            act(reg("BW", 128 * h, 128 * h + 128), BO, AF.Copy, scale=col("FL", h))
 
     def follow_home(t):
         xf, h0 = "XF%d" % (1 - t % 2), HAND[t]
         for m in ("x%d" % (t + 1), "ao%d" % t, "at%d" % t):
             arrive(m)
-        copy(reg(xf, off=reg("LB", 64 * t, 64 * t + 16)), reg("LH", h0, h0 + 256))
+        copy(reg(xf, off=reg("LB", 64 * t + 16, 64 * t + 32)), reg("LH", h0, h0 + 256))
 
     def follow_far(t):
         xf, h0, wx = "XF%d" % (1 - t % 2), HAND[t], W0 + P * t
@@ -461,7 +510,7 @@ def rank_program(g, core, T, topo):
         if t < 2:
             send("x%d" % (t + 2), after=[reg("LH", h0 + 256, h0 + 512)])
             send("tb%d" % t)
-        for q, o in enumerate([32, 16, 48][:1 if t < 2 else 3]):
+        for q, o in [(0, 0)] if t < 2 else [(1, 32), (2, 48), (0, 0)]:
             copy(reg(xf, off=reg("LB", 64 * t + o, 64 * t + o + 16)), reg("LH", h0 + 256 * (q + 1), h0 + 256 * (q + 2)))
 
     for t in range(R):
@@ -471,147 +520,166 @@ def rank_program(g, core, T, topo):
         z = reg("ZB", 256 * s, 256 * s + 256)
         zn = reg("ZB", 256 * (1 - s), 256 * (1 - s) + 256)
         C, Nn = reg("TB", 256 * s, 256 * s + 256), reg("TB", 512 + 256 * s, 768 + 256 * s)
-        zb = [0, 1, 2, 3, 4, 5, 6, 0]
+        zb = [1, 2, 3, 0, 6, 7, 4, 1]
+        HOME, FAR = 0, 1
+        share = lambda side, h: SHARE[t][2 * side + h]
+        window = lambda side, h, a, b: reg(["X", XF][side], 0, wx, off=reg(["LO", "MO"][side], [256 * s, 0][side] + 128 * h + a, [256 * s, 0][side] + 128 * h + b))
+        mins = ["MY", "MH"]
+        ready, staged, free = [], [], [6, 7, 1, 2, 3]
 
-        def zpass(q, kind, start=False, stop=False):
-            h, j = q // 4, q % 4
-            p0 = 32 * j
-            if kind == "tie":
-                mm(bank(zb[q]), reg("TIE", 640, 768, 1, p0, p0 + 1), reg("TIE", 0, 512, 1, p0, p0 + 1), start, stop)
-            else:
-                a = 256 * (j // 2) + 128 * h
-                mm(bank(zb[q]), reg("FH" if kind == "fh" else "NS", a, a + 128), reg("SEL", 512 * j, 512 * j + 512), start, stop)
+        def gather(side, h):
+            n = share(side, h)
+            if n < 128:
+                a, b = 2048 * h + 16 * n, 2048 * h + 2048
+                tt(reg(mins[side], a, b), window(side, h, n, 128), reg("ZR", a, b), OP.min)
 
-        def znames(q):
-            zpass(q, "names", start=True)
-            zpass(q, "tie")
+        def fetch(side, h, a, b):
+            b = min(b, share(side, h))
+            if a < b:
+                c = 4096 * side + 2048 * h
+                act(reg("YG", c + 16 * a, c + 16 * b), window(side, h, a, b), AF.Copy)
+                ready.extend((side, 2048 * h + 16 * q) for q in range(a, b, 32))
 
-        def stack_names():
-            mm(bank(3, 0, 256), reg("SW"), reg("NM"), True, True)
-            act(reg("NS", 0, 256, 1, 64, 128), reg("P3", 0, 256, 1, 64, 128), AF.Copy)
-            act(reg("NS", 256, 512, 1, 0, 64), reg("P3", 0, 256, 1, 0, 64), AF.Copy)
+        def stage():
+            while ready and free:
+                (side, c), b = ready.pop(0), free.pop(0)
+                total(bank(b), [(IDB, reg("ZR", c, c + 512)), (NIDB, reg("YG", 4096 * side + c, 4096 * side + c + 512))])
+                staged.append((side, c, b))
 
-        def gather(dst, win, off, h, a):
-            tt(reg(dst, 2048 * h, 2048 * h + 2048), reg(win, 0, wx, off=reg(off, a + 128 * h, a + 128 * h + 128)),
-               reg("ZR", 2048 * h, 2048 * h + 2048), OP.min)
+        def short(n=1):
+            for _ in range(n):
+                if staged:
+                    side, c, b = staged.pop(0)
+                    act(reg(mins[side], c, c + 512), bank(b), AF.Relu)
+                    free.append(b)
+                    stage()
 
-        def halves(h, b, a, sign, low, high):
-            for p0, tile in ((0, low), (64, high)):
-                act(reg("FH", 256 * tile + 128 * h, 256 * tile + 128 * h + 128, 1, p0, p0 + 64), reg("P%d" % b, a, a + 128, 1, p0, p0 + 64),
-                    bias=1008.0 / 256, scale=sign / 256)
+        def home_sums(h, first):
+            c, nh, nf = 2048 * h, share(HOME, h), share(FAR, h)
+            mm(bank(4 + h, 0, 256), reg("MY", c, c + 2048, 16), START, first, False)
+            for n, y0, z0 in ([(nh, 2, -1), (nf, -2, 3)] if nf <= nh else [(nf, 2, 1), (nh, -2, 1)]):
+                if n:
+                    mm(bank(4 + h, 128, 256, p1=n), reg("MY", c, c + 16 * n, 16), times(y0), False, False)
+                    mm(bank(4 + h, 128, 256, p1=n), reg("ZB", 256 * s + 128 * h, 256 * s + 128 * h + n), times(z0), False, False)
+            for k in range(1, 16):
+                mm(bank(4 + h, 8 * k, 8 * k + 8), reg("MY", c + k, c + 2048, 16), MINUS8, False, k == 15 and not first)
 
-        def home_sums(h):
-            helped = h == 1 and t > 0
-            a, sign = 128 * h, 1.0 if helped else -1.0
-            terms = [(reg("U1", 15 - k, 143 - k), reg("MY", 2048 * h + k, 2048 * h + 2048, 16)) for k in range(16)]
-            if helped:
-                terms = [(reg("NBO"), reg("ZB", 256 * s + 128, 256 * s + 256))] + terms
-            total(bank(7 - h, a, a + 128), terms)
-            halves(h, 7 - h, a, sign, 0, 1)
-            act(reg("FS", a, a + 128), bank(7 - h, a, a + 128), bias=1008.0 / 256, scale=sign / 256)
+        def far_sums(h, first):
+            if first:
+                mm(bank(4 + h, 0, 256), reg("MH", 2048 * h, 2048 * h + 2048, 16), reg("R0", 768, 1024), True, False)
+            for l in range(1 if first else 0, 16):
+                mm(bank(4 + h, 128 + 8 * l, 136 + 8 * l), reg("MH", 2048 * h + l, 2048 * h + 2048, 16), MINUS8, False, l == 15 and not first)
 
-        def far_sums(h):
-            a = 256 + 128 * h
-            total(bank(7, a, a + 128), [(reg("U2", 15 - k, 143 - k), reg("MH", 2048 * h + k, 2048 * h + 2048, 16)) for k in range(16)])
-            halves(h, 7, a, -1.0, 1, 0)
+        def turn(h):
+            nh, nf = share(HOME, h), share(FAR, h)
+            for a, b, n in ([(0, 256, nh)] if nh == nf else [(0, 128, nh), (128, 256, nf)]):
+                act(reg("TS", 256 * h + a, 256 * h + b), bank(4 + h, a, b), AF.Copy, scale=sign(n))
+            for odd in range(2):
+                mm(bank(4 + h, 256 + 128 * odd, 384 + 128 * odd), reg("TS", 256 * h + odd, 256 * h + 256, 2), ID, True, True)
 
-        def fetch(c):
-            a = 256 * s + 128 + 64 * c
-            act(reg("YG", 1024 * c, 1024 * c + 1024), reg("X", 0, wx, off=reg("LO", a, a + 64)), AF.Copy)
+        def stack(h):
+            act(reg("FH", 256 * h, 256 * h + 256), bank(4 + h, 256, 512), bias=BIAS)
 
-        def short(c):
-            total(bank(4 + c % 3), [(IDB, reg("ZR", 2048 + 512 * c, 2560 + 512 * c)), (NIDB, reg("YG", 512 * c, 512 * c + 512))])
+        def least(h):
+            for odd in range(2):
+                a = 128 * h + 64 * odd
+                mm(bank(5, a, a + 64), reg("FH", 256 * h + 128 * odd, 256 * h + 128 * odd + 128), reg("SF"), True, True)
 
-        def short_out(c):
-            act(reg("MY", 2048 + 512 * c, 2560 + 512 * c), bank(4 + c % 3), AF.Relu)
+        def names(*qs):
+            for q in qs:
+                a = 256 * (q % 4 // 2) + 128 * (q // 4)
+                mm(bank(zb[q]), reg("NS", a, a + 128), reg("SN", 512 * (q % 2), 512 * (q % 2) + 512), True, False)
+
+        def costs(*qs):
+            for q in qs:
+                a = 128 * (q // 2)
+                mm(bank(zb[q]), reg("FH", a, a + 128), reg("SC", 512 * (q % 2), 512 * (q % 2) + 512), False, True)
+
+        def best(*qs):
+            for q in qs:
+                if q >= 8 - HELPED:
+                    act(reg("AB", 512 * (7 - q), 512 * (8 - q)), bank(zb[q]), AF.Abs)
+                for g2 in range(2):
+                    a, b = 128 * (2 * q + g2), 512 * (7 - q) + 256 * g2
+                    if q >= 8 - HELPED:
+                        scan(reg("RR", a, a + 128), reg("AB", b, b + 128), reg("AB", b + 128, b + 256), 2.0 ** 23, OP.min, OP.min)
+                    else:
+                        red(col("RR", a + 127), bank(zb[q], 256 * g2, 256 * g2 + 256), OP.min, True)
+
+        def far_offsets():
+            copy(reg("MO"), reg(TF, 0, 512, off=reg("BO16")))
 
         def far_names():
-            act(reg("NM"), reg(TF, 512, 1024, off=reg("BO16")), AF.Copy)
+            act(reg("CM", 512, 768), reg(TF, 512, 1024, off=reg("BO16")), AF.Copy)
 
         def far_entries():
             act(reg("CM", 256, 512), reg(TF, 0, 512, off=reg("BO16")), bias=-MID)
 
-        if t > 0:
+        def stack_names():
+            for odd in range(2):
+                total(bank(0, 256 * odd, 256 * odd + 256), [(reg("PM", 128 * odd, 128 * odd + 128), reg("NL")), (reg("PM", 256 + 128 * odd, 384 + 128 * odd), reg("CM", 512, 768))])
+            act(reg("NS"), bank(0), AF.Copy)
+            names(0, 1, 2, 3)
+
+        def slots(side):
+            for h in range(2):
+                gather(side, h)
+                fetch(side, h, 0, 64)
+                fetch(side, h, 64, 128)
+            stage()
+
+        if t == 0:
+            sum_constants()
+            pair_constants()
+            home_names(512)
+            later_constants()
+            last_constants()
+        else:
             arrive("ta%d" % (t - 1))
             arrive("tn%d" % (t - 1))
             arrive("u1" if t == 1 else "tb%d" % (t - 2))
-
-        gather("MY", "X", "LO", 0, 256 * s)
-        if t == 0:
-            late_constants()
-            home_sums(0)
-            stacked_selectors()
-            later_constants()
-            gather("MY", "X", "LO", 1, 256 * s)
-            copy(reg("MO"), reg(TF, 0, 512, off=reg("BO16")))
-            home_sums(1)
-            far_entries()
-            far_names()
-            stack_names()
-            for q in range(4):
-                znames(q)
-        else:
-            fetch(0)
-            fetch(1)
-            short(0)
-            short(1)
-            short_out(0)
-            short_out(1)
-            home_sums(0)
-            short(2)
-            short(3)
-            far_names()
-            short_out(2)
-            stack_names()
-            short_out(3)
-            if s == 0:
-                follow_home(t - 1)
-            copy(reg("MO"), reg(TF, 0, 512, off=reg("BO16")))
-            follow_far(t - 1)
-            for q in range(4):
-                znames(q)
-            home_sums(1)
-            far_entries()
-        gather("MH", XF, "MO", 0, 0)
-        znames(4)
-        far_sums(0)
-        if t == 0:
-            last_constants()
-        znames(5)
-        for q in range(4):
-            zpass(q, "fh", stop=True)
-        gather("MH", XF, "MO", 1, 0)
-        far_sums(1)
+        slots(HOME)
         for h in range(2):
-            total(bank(6, 128 * h, 128 * h + 128), [(reg("FS", 128 * h, 128 * h + 128), ID), (reg("TIE", 640, 768, p1=1), reg("TIE", 512, 640, p1=1))])
-        for q in range(8):
-            if q == 1:
-                znames(7)
-                zpass(4, "fh", stop=True)
-                zpass(5, "fh", stop=True)
-            if q == 3:
-                scan(reg("NFK"), reg("SG", 0, 256), bank(6, 0, 256), 0.0, OP.mult, OP.max)
-                znames(6)
-                zpass(6, "fh", stop=True)
-                zpass(7, "fh", stop=True)
-            if q == 4:
-                ts(reg("KI", 32, 48), reg("NFK", 15, 256, 16), 4096.0, OP.mult)
-            if q == 5:
-                ts(reg("KI", 48, 64), reg("KI", 32, 48), 15, OP.bitwise_and)
-            if q == 6:
-                ts(reg("KN"), reg("KI", 48, 64), -1.0 / 16, OP.mult, 15.0 / 16, OP.add)
-            if q == 7:
-                mm(bank(5), ID, reg("CM"), True, True)
-            for g2 in range(2):
-                red(col("RR", 8 * (q // 4) + 2 * (q % 4) + g2), bank(zb[q], 256 * g2, 256 * g2 + 256), OP.min, True)
+            short(share(HOME, h) // 32)
+            home_sums(h, True)
+        if t == 2:
+            follow_home(t - 1)
+        far_offsets()
+        if t > 0:
+            follow_far(t - 1)
+        free[:] = [6, 7]
+        far_names()
+        stack_names()
+        slots(FAR)
+        short(share(FAR, 0) // 32)
+        far_sums(0, False)
+        turn(0)
+        stack(0)
+        short(4)
+        costs(0, 1, 2, 3)
+        far_sums(1, False)
+        turn(1)
+        names(4, 5, 6)
+        stack(1)
+        far_entries()
+        best(0, 1, 2, 3)
+        costs(4, 5)
+        least(0)
+        least(1)
+        costs(6)
+        names(7)
+        costs(7)
+        best(4)
+        scan(reg("NFK"), reg("SG", 0, 256), bank(5, 0, 256), 0.0, OP.add, OP.min)
+        best(5, 6)
+        mm(bank(5), ID, reg("CM", 0, 512), True, True)
+        best(7)
 
-        ts(reg("KI", 32, 48), reg("RR"), 8.0, OP.min, 65536.0, OP.mult)
-        ts(reg("VB", 16, 32), reg("RR"), 8.0, OP.is_ge, 16.0, OP.mult)
-        ts(reg("KI", 0, 16), reg("KI", 32, 48), 4, OP.logical_shift_right, 15, OP.bitwise_and)
-        ts(reg("KI", 16, 32), reg("KI", 32, 48), 15, OP.bitwise_and)
-        tt(reg("VB", 0, 16), reg("VB", 16, 32), reg("KN"), OP.mult)
+        tt(reg("KI", 32, 48), reg("RR", 127, 2048, 128), reg("NFK", 15, 256, 16), OP.min)
+        ts(reg("KI", 0, 16), reg("KI", 32, 48), 5, OP.logical_shift_right, 15, OP.bitwise_and)
+        ts(reg("KI", 16, 32), reg("KI", 32, 48), 31, OP.bitwise_and)
         copy(reg("VA"), reg("KI", 0, 32))
-        total(bank(1, 0, 128, p1=32), [(reg("VB"), ID), (reg("VA"), ID)])
+        mm(bank(1, 0, 128, p1=32), reg("VA"), ID, True, True)
         copy(reg("VT", p1=32), bank(1, 0, 128, p1=32))
         for q in range(4):
             mm(bank(2, 128 * q, 128 * q + 128), reg("RK", 128 * q, 128 * q + 128, p1=32), reg("VT", p1=32), True, True)
@@ -625,108 +693,105 @@ def rank_program(g, core, T, topo):
             act(reg("T2", 512, 768), bank(6, 256, 512), AF.Copy)
         ts(reg("WK", 0, 512), bank(2), P16, OP.is_equal)
         tt(reg("WK", 512, 1024), reg("WK", 0, 512), bank(5), OP.mult)
+        mm(bank(6, 0, 256), BIG, reg("WK", 0, 256), True, False)
+        mm(bank(6, 0, 256), NBIG, reg("WK", 256, 512), False, False)
         mm(bank(4, 0, 256), BO, reg("WK", 512, 768), True, True)
         to_list(bank(3, 0, 48), "U1", "WK", 256, 768)
         mm(bank(5, 0, 256), BO, reg("WK", 768, 1024), True, True)
-        mm(bank(6, 0, 256), BOM, reg("WK", 256, 512), True, False)
         act(reg("KB", 0, 256), bank(4, 0, 256), AF.Copy)
         if t >= 2:
             total(bank(7, 0, 256), [(BO, reg("WK", 512, 768)), (BOM, reg("WK", 256, 512))])
-        ts(reg("LM"), bank(3, 16, 48), MID, OP.add)
+        ts(reg("LM", 0, 32), bank(3, 16, 48), MID, OP.add)
+        rv, dm = 48 * s, 32 * t
+        ts(reg("RV", rv + 16, rv + 48), bank(3, 16, 48), MID, OP.add)
+        keep, old = bank(7, 256, 512), reg("X", wx - 512, wx - 256)
+        if t >= 2:
+            ts(reg("G2", 64, 80), bank(3, 0, 16), -4096.0, OP.mult)
+            tt(reg("G2", 64, 80), reg("G2", 64, 80), reg("RV", rv + 16, rv + 32), OP.add)
+            ts(reg("G2", 80, 96), reg("G2", 64, 80), 2048.0, OP.is_ge)
+            tt(reg("G2", 48, 64), reg("G2", 80, 96), reg("DM", dm - 48, dm - 32), OP.mult)
+            tt(reg("G2", 32, 48), reg("G2", 80, 96), reg("DM", dm - 64, dm - 48), OP.mult)
+            tt(reg("G2", 32, 64), reg("G2", 32, 64), reg("DUM"), OP.add)
+            copy(reg("LM", 32, 48), reg("G2", 48, 64))
+            copy(reg("OH", 32, 48), reg("G2", 32, 48))
         send("m%d" % t)
         offL, offM = reg("LM", 0, 16), reg("LM", 16, 32)
         v = reg("VY", 512 * s, 512 * s + 256)
         yk = reg("VY", 512 * s + 256, 512 * s + 512)
-        act(yk, reg("X", 0, wx, off=offL), AF.Copy)
+        if t < R - 1:
+            act(yk, reg("X", 0, wx, off=offL), AF.Copy)
+        else:
+            act(reg("TM"), reg("X", 0, wx, off=offL), AF.Relu, bias=63.0, scale=-1.0)
+            act(yk, reg("TM"), bias=63.0, scale=-1.0)
         act(reg("KB", 256, 512), bank(5, 0, 256), AF.Copy)
         nrow = bank(1, 256, 512)
         act(nrow, reg("IOX"), bias=float(wx))
 
         def first_of(ebuf, key, kcol, flag, cnt):
-            offs, o = [], 0
+            o = 0
             for h in range(16):
-                offs.append(o)
+                e = reg(ebuf, o, o + 256 - 16 * h)
+                ts(e, reg("KB", key + 16 * h, key + 256), bank(3, kcol + h, kcol + h + 1), OP.is_equal, flag(h), OP.mult)
+                mm(bank(cnt, 16 * h, 256), reg("BW", 128 * h, 128 * h + 128), e, False, h == 15)
                 o += 256 - 16 * h
-            for grp in ([0, 1, 2], [3, 4, 5, 6], [7, 8, 9, 10, 11], [12, 13, 14, 15]):
-                for h in grp:
-                    ts(reg(ebuf, offs[h], offs[h] + 256 - 16 * h), reg("KB", key + 16 * h, key + 256), kcol(h), OP.is_equal, flag(h), OP.mult)
-                for h in reversed(grp):
-                    mm(bank(cnt, 16 * h, 16 * h + 16), BOW, reg(ebuf, offs[h], offs[h] + 16), False, False)
-                    if h < 15:
-                        mm(bank(cnt, 16 * h + 16, 256), BOBIG, reg(ebuf, offs[h] + 16, offs[h] + 256 - 16 * h), False, h == 12)
 
-        first_of("EE", 0, lambda h: bank(3, 16 + h, 17 + h), lambda h: bank(3, h, h + 1), 6)
-        if t < R - 1:
-            total(bank(4, 256, 512), [(IDB, yk), (NIDB, z)])
-            act(zn, bank(4, 256, 512), AF.Abs)
-        tt(reg("M1"), reg("X", 0, wx, off=offL), z, OP.min)
-        tt(reg("ST"), bank(6, 0, 256), reg("THR"), OP.is_lt)
-        to_list(bank(1, 0, 16), "US", "ST", 0, 256)
-        mm(bank(2, 0, 256), BO128, reg("ST"), True, False)
-        tt(v, reg(XF, 0, wx, off=offM), reg("M1"), OP.min)
+        def firsts(out, cnt, a):
+            tt(reg(out), bank(cnt, 0, 256), reg("THR"), OP.is_lt)
+            scan(a, reg("SL", 0, 256), reg(out), 0.0, OP.mult, OP.max)
+
+        first_of("EE", 0, 16, lambda h: bank(3, h, h + 1), 6)
+        mm(bank(2, 0, 256), BIG, reg("WK", 0, 256), True, False)
+        over, more, xm = [reg("TP", 256 * q, 256 * q + 256) for q in range(3)]
+        act(xm, reg(XF, 0, wx, off=offM), AF.Copy)
+        total(bank(4, 256, 512), [(IDB, yk), (NIDB, z)])
+        act(over, bank(4, 256, 512), AF.Relu)
+        total(bank(5, 256, 512), [(IDB, yk), (NIDB, xm), (NIDB, over)])
+        act(more, bank(5, 256, 512), AF.Relu)
+        total(bank(5, 0, 256), [(IDB, yk), (NIDB, over), (NIDB, more)])
+        act(v, bank(5, 0, 256), AF.Copy)
         send("v%d" % t)
-        rv, dm = 48 * s, 32 * t
-        ts(reg("RV", rv + 16, rv + 48), bank(3, 16, 48), MID, OP.add)
-        total(bank(6, 0, 256), [(IDB, yk), (NIDB, v)])
-        act(reg("TM", 512, 768), bank(6, 0, 256), AF.Copy)
         if t < R - 1:
-            send("at%d" % t)
-            for k in range(8):
-                act(reg("ZR", k, 4096, 16), zn, AF.Copy)
-        first_of("E2", 256, lambda h: bank(3, 32 + h, 33 + h), lambda h: bank(1, h, h + 1), 2)
-        if t < R - 1:
-            for k in range(8, 16):
-                act(reg("ZR", k, 4096, 16), zn, AF.Copy)
-        keep = bank(7, 256, 512)
-        tt(reg("DM", dm + 16, dm + 32), reg("RV", rv + 32, rv + 48), reg("DUM"), OP.subtract)
-        tt(reg("DM", dm, dm + 16), reg("RV", rv + 16, rv + 32), reg("DUM"), OP.subtract)
-        if t >= 2:
-            ts(keep, bank(7, 0, 256), 512.0, OP.is_lt)
-            ts(reg("G2", 64, 80), bank(3, 0, 16), -4096.0, OP.mult)
-        tt(reg("BD"), bank(2, 0, 256), reg("THR"), OP.is_lt)
-        build = bank(2, 256, 512)
-        if t < 2:
-            mm(build, ID, reg("BD"), True, True)
-        to_list(bank(5, 0, 16), "US", "BD", 0, 256)
-        if t >= 2:
-            mm(build, ID, reg("BD"), True, True)
+            act(zn, bank(4, 256, 512), AF.Abs)
+        total(bank(4, 256, 512), [(IDB, over), (IDB, more)])
+        act(reg("TM"), bank(4, 256, 512), AF.Copy)
         if t < R - 1:
             to_list(bank(4, 0, 16), "UW", "ZB", 256 * (1 - s), 256)
-        if t < 2:
-            tt(reg("NB", 0, 256), v, build, OP.mult)
-            tt(reg("MK"), reg("WK", 0, 256), build, OP.mult)
+        firsts("ST", 6, reg("NFK"))
+        mm(bank(2, 0, 256), NBIG, reg("ST"), False, False)
         if t >= 2:
-            tt(reg("G2", 64, 80), reg("G2", 64, 80), reg("RV", rv + 16, rv + 32), OP.add)
-            old = reg("X", wx - 512, wx - 256)
-            tt(reg("NB", 256, 512) if t < R - 1 else old, old, keep, OP.mult)
-            ts(reg("G2", 80, 96), reg("G2", 64, 80), 2048.0, OP.is_ge)
-            if t < R - 1:
-                copy(old, reg("NB", 256, 512))
-            tt(reg("G2", 48, 64), reg("G2", 80, 96), reg("DM", dm - 48, dm - 32), OP.mult)
-        tt(reg("G2", 16, 32), bank(5, 0, 16), reg("DM", dm + 16, dm + 32), OP.mult)
-        tt(reg("G2", 0, 16), bank(5, 0, 16), reg("DM", dm, dm + 16), OP.mult)
-        if t >= 2:
-            tt(reg("G2", 48, 64), reg("G2", 48, 64), reg("DUM"), OP.add)
-        tt(reg("G2", 16, 32), reg("G2", 16, 32), reg("DUM"), OP.add)
-        tt(reg("G2", 0, 16), reg("G2", 0, 16), reg("DUM"), OP.add)
-        if t >= 2:
-            copy(reg("OF", 32 * t + 16, 32 * t + 32), reg("G2", 48, 64))
-        copy(reg("OF", 32 * t, 32 * t + 16), reg("G2", 16, 32))
-        send("o%d" % t)
-        if t >= 2:
-            tt(reg("G2", 32, 48), reg("G2", 80, 96), reg("DM", dm - 64, dm - 48), OP.mult)
-            tt(reg("NB", 0, 256) if t < R - 1 else reg("X", wx, wx + 256), v, build, OP.mult)
-            tt(reg("G2", 32, 48), reg("G2", 32, 48), reg("DUM"), OP.add)
-        copy(reg("OH", 0, 16), reg("G2", 0, 16))
-        if t >= 2:
-            copy(reg("OH", 16, 32), reg("G2", 32, 48))
+            ts(keep, bank(7, 0, 256), 512.0, OP.is_lt)
+            tt(reg("NB") if t < R - 1 else old, old, keep, OP.mult)
+        if t == 2:
+            copy(old, reg("NB"))
         if t < R - 1:
+            send("at%d" % t)
+            for k in range(16):
+                act(reg("ZR", k, 4096, 16), zn, AF.Copy)
+        first_of("E2", 256, 32, lambda h: col("NFK", 16 * h + 15), 2)
+        tt(reg("DM", dm, dm + 32), reg("RV", rv + 16, rv + 48), reg("DUM"), OP.subtract)
+        firsts("BD", 2, reg("SL", 256, 512))
+        build, builds = bank(2, 256, 512), reg("SL", 256 + 15, 512, 16)
+        mm(build, BO, reg("BD"), True, True)
+        tt(reg("G2", 0, 16), builds, reg("DM", dm + 16, dm + 32), OP.mult)
+        tt(reg("G2", 16, 32), builds, reg("DM", dm, dm + 16), OP.mult)
+        tt(reg("G2", 0, 32), reg("G2", 0, 32), reg("DUM"), OP.add)
+        copy(reg("OH", 0, 32), reg("G2", 0, 32))
+        send("o%d" % t)
+        arrive("m%d" % t)
+        chosen, given = reg("LG", 32 * t, 32 * t + 16), reg("LG", 32 * t + 16, 32 * t + 32)
+        if t == 2:
+            copy(reg("OH", 48, 64), given)
+        if s == 0:
             send("ao%d" % t)
-            send("a%d" % t)
+        tt(reg("MK"), reg("WK", 0, 256), build, OP.mult)
+        if t < R - 1:
+            copy(reg("BI", 48, 64), bank(4, 0, 16))
+            ts(reg("BI", 0, 16), reg("BI", 48, 64), 511, OP.bitwise_and)
+            payee(t + 1)
 
         if t >= 2:
-            tt(reg("MK"), reg("WK", 0, 256), build, OP.mult)
             tt(C, C, keep, OP.mult)
+            tt(C, C, reg("PL", s, 512, 2), OP.max)
         if t == 2:
             tt(reg("T2", 256, 512), reg("T2", 512, 768), keep, OP.mult)
         if t < R - 1:
@@ -734,52 +799,50 @@ def rank_program(g, core, T, topo):
             base = [(NID, reg("NL"))] if t < 2 else [(ID, reg("N0")), (ID, reg("T2", 256, 512))]
             total(bank(0, 256, 512), base + [(ID, reg("T2", 0, 256))])
             act(Nn, bank(0, 256, 512), AF.Copy)
+        tt(nrow, reg("MK"), nrow, OP.mult)
+        tt(C, C, nrow, OP.max)
+        if t >= 2:
+            act(reg("CO", s, 512, 2), C, AF.Copy)
+        if t < R - 1:
+            send("ta%d" % t)
+        else:
+            dma("s", [(T.co[:], reg("CO"))])
+
         arrive("v%d" % t)
         fv, fw = reg("LV", LAND[t], LAND[t] + 256), reg("LV", LAND[t] + 256, LAND[t] + 512)
-        act(reg("NV", 0, 256), fv, AF.Copy, scale=-1.0)
+        before, left, after = [reg("NV", 256 * q, 256 * q + 256) for q in range(3)]
+        taken = reg("TV", 0, 256)
+        tt(reg("X", wx, wx + 256), v, build, OP.mult)
+        copy(reg("X", off=reg("OH", 16, 32)), reg("TM"))
+        act(before, reg("X", 0, wx, off=chosen), AF.Copy)
+        if t == R - 1:
+            act(after, before, AF.Relu, bias=-63.0)
+        total(bank(5, 0, 256), [(IDB, before), (NIDB, fv)] + [(NIDB, after)] * (t == R - 1))
+        act(left if t >= 2 else taken, bank(5, 0, 256), AF.Relu)
         if t >= 2:
-            act(reg("NV", 256, 512), yk, bias=63.0, scale=-1.0)
-            act(reg("NV", 512, 768), fw, bias=63.0, scale=-1.0)
-
-        def lists_end():
-            tt(nrow, reg("MK"), nrow, OP.mult)
-            if t >= 2:
-                tt(C, C, reg("PL", s, 512, 2), OP.max)
-            tt(C, C, nrow, OP.max)
+            for q, off, w in ((1, reg("OH", 32, 48), yk), (2, given, fw)):
+                held = reg("NV", 512 + 256 * q, 768 + 256 * q)
+                act(held, reg("X", off=off), AF.Copy)
+                tt(reg("X", off=off), held, w, OP.add)
+                if t < R - 1:
+                    total(bank(4, 256, 512), [(IDB, held), (IDB, w)])
+                    act(reg("TV", 256 * q, 256 * q + 256), bank(4, 256, 512), AF.Copy)
+                    send("b%d" % (t + q))
+            act(after, reg("X", 0, wx, off=chosen), AF.Copy)
+            total(bank(5, 0, 256), [(IDB, left), (NIDB, before), (IDB, after)])
             if t == R - 1:
-                act(reg("CO", s, 512, 2), C, AF.Copy)
-                dma("s", [(T.co[:], reg("CO"))])
-
+                ts(reg("X", 0, wx - 512), reg("X", 0, wx - 512), 63.0, OP.min)
+            ts(taken, bank(5, 0, 256), 63.0, OP.min)
         if t < R - 1:
-            lists_end()
-            send("ta%d" % t)
-            copy(reg("X", wx, wx + 256), reg("NB", 0, 256))
-        copy(reg("X", off=reg("OH", 0, 16)), reg("TM", 512, 768))
+            send("b%d" % t)
 
-        def look(q, win, bound, op, step):
-            part = reg("TP", 256 * q, 256 * q + 256)
-            tt(part, win, bound, op)
-            if t < R - 1:
-                total(bank([7, 4, 5][q], 256, 512), [(IDB, part), (IDB, step)])
-                act(reg("TV", 256 * q, 256 * q + 256), bank([7, 4, 5][q], 256, 512), AF.Copy)
-                send("b%d" % (t + q))
-
-        def put(q, off, step):
-            tt(reg("X", off=off), reg("TP", 256 * q, 256 * q + 256), step, OP.add)
-
-        if t < R - 1:
-            copy(reg("BI", 48, 64), bank(4, 0, 16))
-            ts(reg("BI", 0, 16), reg("BI", 48, 64), 511, OP.bitwise_and)
         for q in range(3):
-            tt(reg("RC", 16 * q, 16 * q + 16), bank(5, 0, 16), reg("RV", rv + 16 * q, rv + 16 * q + 16), OP.mult)
+            tt(reg("RC", 16 * q, 16 * q + 16), builds, reg("RV", rv + 16 * q, rv + 16 * q + 16), OP.mult)
         if t < R - 1:
-            payee(t + 1)
             c2 = 256 * (1 - s)
             home_names(512 + c2)
             act(reg("CM", 0, 256), reg("TB", c2, c2 + 256), bias=-MID)
         ts(reg("RH"), reg("RC"), MID, OP.subtract)
-        arrive("m%d" % t)
-        look(0, reg("X", 0, wx, off=reg("LG", 16 * t, 16 * t + 16)), fv, OP.max, reg("NV", 0, 256))
         for j in range(16):
             mm(bank(6, j, 512, 16, p1=8), reg("ID", j, 128, 16), reg("RH", 0, 32), True, True)
         for j in range(16):
@@ -787,34 +850,113 @@ def rank_program(g, core, T, topo):
         act(reg("RO", 0, 512, p1=8), bank(6, 0, 512, p1=8), bias=MID)
         act(reg("RO", 512, 768, p1=8), bank(3, 256, 512, p1=8), bias=MID)
         dma("s", [(T.rec[8 * q:8 * q + 8, P * t:P * t + P], reg("RO", 256 * q, 256 * q + 256, p1=8)) for q in range(3)])
-        if t == 2:
-            act(reg("CO", s, 512, 2), C, AF.Copy)
         arrive("o%d" % t)
-
-        def change(q, off, bound, op, step):
-            look(q, reg("X", off=off), bound, op, step)
-            put(q, off, step)
-
-        if t < R - 1:
-            if t < 2:
-                copy(reg("LO", 256 * s, 256 * s + 256), C)
-            if s == 0:
-                follow_home(t)
-        put(0, reg("LF", 32 * t, 32 * t + 16), reg("NV", 0, 256))
-        if t >= 2:
-            change(1, reg("OH", 16, 32), reg("NV", 256, 512), OP.min, yk)
-            change(2, reg("LF", 32 * t + 16, 32 * t + 32), reg("NV", 512, 768), OP.min, fw)
+        if t < 2:
+            copy(reg("LO", 256 * s, 256 * s + 256), C)
+        if s == 0:
+            follow_home(t)
+        copy(reg("X", off=reg("LF", 16 * t, 16 * t + 16)), taken)
         if t == R - 1:
             dma("s", [(T.xo[:, 0:1536], reg("X", 0, 1536))])
             dma("a", [(T.xo[:, 1536:3072], reg("X", 1536, 3072))])
-            lists_end()
 
     emit(g, T, ops, queue)
 
 
-def emit(g, T, ops, queue):
+def depend(ops):
+    hist, sent, last = {}, {}, {}
+    reach = []
+    for i, op in enumerate(ops):
+        e = op["e"]
+        need, after = set(), set()
+        for kind, lst in (("r", op["r"]), ("w", op["w"])):
+            for name, a, b, st, p0, p1 in lst:
+                psum = SCRATCH[name][0] == "psum"
+                for j, k2, a2, b2, st2, q0, q1 in hist.get(name, []):
+                    same = ops[j]["e"] == e and not ops[j]["sem"] and not op["sem"]
+                    over = a < b2 and a2 < b and p0 < q1 and q0 < p1 and not (st == st2 and (a - a2) % st)
+                    if same and e == "p":
+                        if psum:
+                            after.add(j)
+                    elif (psum and not same) or (over and (kind == "w" or k2 == "w")):
+                        need.add(j)
+        if e == "g" and not op["sem"]:
+            if "c" in last and (op["w"][0][4] or ops[last["c"]]["w"][0][4]):
+                need.add(last["c"])
+            last["c"] = i
+        if e in "gs":
+            after |= {last[e]} if e in last else set()
+            last[e] = i
+        if e == "x":
+            call, step = op["msg"]
+            gate = reach[sent[call]][-step % NR]
+            for j in need:
+                assert j < gate or ops[j]["e"] == "x"
+                if j < gate:
+                    ops[gate]["need"].add(j)
+            known = [-1] * NR
+            for o in range(NR):
+                known[(o + step) % NR] = reach[sent[call]][o]
+            known[step % NR] = sent[call]
+            need, after = set(), {sent[call]}
+        else:
+            known = [max([-1] + [reach[j][o] for j in need | (after if e == "g" else set())]) for o in range(NR)]
+            if op["msg"]:
+                sent[op["msg"]] = i
+        reach.append(known)
+        op["need"], op["after"] = need, after
+        for kind, lst in (("r", op["r"]), ("w", op["w"])):
+            for name, a, b, st, p0, p1 in lst:
+                hist.setdefault(name, []).append((i, kind, a, b, st, p0, p1))
+
+
+def schedule(ops):
     n = len(ops)
-    hist = {}
+    busy = [op["busy"] for op in ops]
+    pred, succ = [[] for _ in range(n)], [[] for _ in range(n)]
+    for i, op in enumerate(ops):
+        edges = [(j, max(busy[j], ops[j]["lands"] if ops[j]["e"] != "x" else 0.0) + WAKE) for j in op["need"]]
+        edges += [(j, op["lands"] if op["e"] == "x" else busy[j]) for j in op["after"] - op["need"]]
+        for j, d in edges:
+            pred[i].append((j, d))
+            succ[j].append((i, d + busy[i] - busy[j]))
+
+    def place(order, before, first):
+        start, taken = [0.0] * n, {e: [] for e in "vapgsx"}
+        for i in order:
+            t = max([first[i]] + [start[j] + d for j, d in before[i]])
+            slots = taken[ops[i]["e"]]
+            q = len(slots)
+            while q and slots[q - 1][1] > t:
+                q -= 1
+            while q < len(slots) and t + busy[i] > slots[q][0]:
+                t = max(t, slots[q][1])
+                q += 1
+            slots.insert(q, (t, t + busy[i]))
+            start[i] = t
+        return start
+
+    tail = [max(0.0, op["lands"] - op["busy"]) if op["e"] != "x" else 0.0 for op in ops]
+    start = place(range(n), pred, [0.0] * n)
+    for last in [False] * (PASSES - 1) + [True]:
+        back = place(sorted(range(n), key=lambda i: (-start[i] - busy[i], -i)), succ, tail)
+        end = max(back[i] + busy[i] for i in range(n))
+        room = [max(0.0, end - back[i] - busy[i] - start[i]) for i in range(n)]
+        late = [start[i] + (min(SLACK, room[i]) if ops[i]["e"] == "x" else min(400.0, room[i] / 2)) if last and ops[i]["e"] in "xpva" else 0.0 for i in range(n)]
+        due = [-back[i] - busy[i] - ops[i]["ahead"] for i in range(n)]
+        for i in reversed(range(n)):
+            for j, d in pred[i]:
+                due[j] = min(due[j], due[i] - d)
+        start = place(sorted(range(n), key=lambda i: (due[i], i)), pred, late)
+    return sorted(range(n), key=lambda i: (start[i], i))
+
+
+def emit(g, T, program, queue):
+    depend(program)
+    order = schedule(program)
+    place = {j: i for i, j in enumerate(order)}
+    ops = [program[j] for j in order]
+    n = len(ops)
     waits = [[] for _ in range(n)]
     clock = [None] * n
     known = {e: {} for e in queue}
@@ -822,20 +964,8 @@ def emit(g, T, ops, queue):
     key = lambda j: ops[j]["sem"][0] if ops[j]["sem"] else ops[j]["e"]
     for i, op in enumerate(ops):
         e = op["e"]
-        deps = set()
-        for kind, lst in (("r", op["r"]), ("w", op["w"])):
-            for name, a, b, st, p0, p1 in lst:
-                psum = SCRATCH[name][0] == "psum"
-                for j, k2, a2, b2, st2, q0, q1 in hist.get(name, []):
-                    same = ops[j]["e"] == e and not ops[j]["sem"] and not op["sem"]
-                    over = a < b2 and a2 < b and p0 < q1 and q0 < p1 and not (st == st2 and (a - a2) % st)
-                    if same:
-                        if over and e != "p" and (kind == "w" or k2 == "w"):
-                            deps.add(j)
-                    elif psum or (over and (kind == "w" or k2 == "w")):
-                        deps.add(j)
         if e != "x":
-            for j in sorted(deps, reverse=True):
+            for j in sorted((place[j] for j in op["need"]), reverse=True):
                 if known[e].get(key(j), -1) >= j:
                     continue
                 waits[i].append(j)
@@ -847,9 +977,6 @@ def emit(g, T, ops, queue):
         else:
             clock[i] = {}
         clock[i][key(i)] = i
-        for kind, lst in (("r", op["r"]), ("w", op["w"])):
-            for name, a, b, st, p0, p1 in lst:
-                hist.setdefault(name, []).append((i, kind, a, b, st, p0, p1))
     count, value = {e: 0 for e in ENG_SEM}, [None] * n
     waited = {}
     for i, op in enumerate(ops):

@@ -8,28 +8,35 @@ WT = [1, 64, 5, 83, 17, 131, 29, 211, 43, 157, 61, 239, 71, 113, 97, 199]
 XW = 3328
 PIECE = 704
 MID = 1536.0
-SHARE = [(64, 32, 32, 32), (64, 64, 0, 32), (64, 32, 32, 32), (96, 64, 0, 32)]
-HELPED = 3
-ZACT = 8
+SHARE = [(64, 64, 32, 0)] * 4
+HELPED = [(3, 5, 7)] * 4
+HALVES = (1, 3)
+BWACT = 10
+BLOCKS = (0, 2, 4, 6, 8, 11, 14, 16)
+NAMES = [("a", 0, 128), ("v", 384, 512), ("a", 128, 256), ("v", 304, 384), ("a", 256, 304)]
+ZACT = (2, 16, 16, 16)
 
 F, H16, B16, I32, U16 = "float32", "float16", "bfloat16", "int32", "uint16"
 SCRATCH = {
     "X": ("sbuf", [128, XW], B16), "XF0": ("sbuf", [128, XW], B16), "XF1": ("sbuf", [128, XW], B16),
-    "LH": ("sbuf", [128, 2048], B16), "LN": ("sbuf", [128, 1024], B16), "LB": ("sbuf", [128, 192], U16), "TV": ("sbuf", [128, 768], B16),
-    "NB": ("sbuf", [128, 256], B16), "NV": ("sbuf", [128, 1280], B16), "TP": ("sbuf", [128, 768], B16),
-    "TB": ("sbuf", [128, 1024], F), "TF0": ("sbuf", [128, 1024], F), "TF1": ("sbuf", [128, 1024], F),
+    "LH": ("sbuf", [128, 768], B16), "LN": ("sbuf", [128, 1024], B16), "LB": ("sbuf", [128, 192], U16), "TV": ("sbuf", [128, 512], B16),
+    "LW": ("sbuf", [128, 1024], B16), "LK": ("sbuf", [128, 96], U16), "NW": ("sbuf", [128, 1280], B16),
+    "NV": ("sbuf", [128, 1280], B16), "TP": ("sbuf", [128, 256], B16), "HL": ("sbuf", [128, 96], B16), "K1": ("sbuf", [128, 32], F),
+    "TB": ("sbuf", [128, 512], F), "TF0": ("sbuf", [128, 512], F), "TF1": ("sbuf", [128, 512], F),
+    "TN": ("sbuf", [128, 512], B16), "NF0": ("sbuf", [128, 512], B16), "NF1": ("sbuf", [128, 512], B16),
+    "PL16": ("sbuf", [128, 512], H16), "NR": ("sbuf", [128, 256], H16), "SK": ("sbuf", [128, 256], B16), "D0": ("sbuf", [128, 256], B16),
     "PL": ("sbuf", [128, 512], I32), "FR": ("sbuf", [128, 128], I32), "FR16": ("sbuf", [128, 128], H16),
     "FW": ("sbuf", [128, 2048], F), "NG": ("sbuf", [128, 4096], H16), "N0": ("sbuf", [128, 256], H16),
     "MY": ("sbuf", [128, 4096], H16), "MH": ("sbuf", [128, 4096], H16), "ZR": ("sbuf", [128, 4096], B16),
     "ZB": ("sbuf", [128, 512], B16),
-    "LO": ("sbuf", [128, 512], U16), "MO": ("sbuf", [128, 256], U16), "BO16": ("sbuf", [128, 16], U16),
+    "LO": ("sbuf", [128, 512], U16), "LC": ("sbuf", [128, 768], U16), "MO": ("sbuf", [128, 256], U16), "BO16": ("sbuf", [128, 16], U16),
     "BI": ("sbuf", [128, 64], I32), "BH": ("sbuf", [128, 16], H16),
-    "CM": ("sbuf", [128, 768], H16), "NL": ("sbuf", [128, 256], H16),
+    "CM": ("sbuf", [128, 768], H16),
     "TS": ("sbuf", [128, 512], H16), "FH": ("sbuf", [128, 512], H16), "NS": ("sbuf", [128, 512], H16), "PM": ("sbuf", [128, 512], H16),
     "YG": ("sbuf", [128, 8192], B16), "SN": ("sbuf", [128, 1024], H16), "SC": ("sbuf", [128, 1024], H16), "SF": ("sbuf", [128, 64], H16),
     "R0": ("sbuf", [128, 1024], H16), "IA": ("sbuf", [128, 704], B16), "TIE": ("sbuf", [2, 576], F),
-    "NFK": ("sbuf", [128, 256], F), "KI": ("sbuf", [128, 48], I32), "PD": ("sbuf", [128, 24], F),
-    "RR": ("sbuf", [128, 2048], F), "AB": ("sbuf", [128, 2048], F), "VA": ("sbuf", [128, 32], H16), "FL": ("sbuf", [128, 32], F),
+    "NFK": ("sbuf", [128, 256], F), "KI": ("sbuf", [128, 48], I32), "PD": ("sbuf", [128, 24], B16), "PS": ("sbuf", [128, 8], F),
+    "RR": ("sbuf", [128, 2048], F), "AB": ("sbuf", [128, 4096], F), "VA": ("sbuf", [128, 32], H16), "FL": ("sbuf", [128, 16], B16), "FL32": ("sbuf", [128, 16], F),
     "BB": ("sbuf", [128, 256], B16), "BW": ("sbuf", [128, 2048], B16), "SL": ("sbuf", [128, 768], B16),
     "VT": ("sbuf", [128, 128], H16), "WK": ("sbuf", [128, 1024], H16), "KB": ("sbuf", [128, 512], H16),
     "LM": ("sbuf", [128, 48], U16), "EE": ("sbuf", [128, 2176], B16), "E2": ("sbuf", [128, 2176], B16),
@@ -41,36 +48,54 @@ SCRATCH = {
     "RC": ("sbuf", [128, 48], F), "RH": ("sbuf", [128, 48], H16), "RO": ("sbuf", [8, 768], F),
     "T2": ("sbuf", [128, 768], H16), "MK": ("sbuf", [128, 256], H16),
     "CO": ("sbuf", [128, 512], F),
-    "PI": ("sbuf", [128, 16], I32), "PC": ("sbuf", [128, 16], F),
-    "IOX": ("sbuf", [128, 256], F), "IOA": ("sbuf", [128, 512], F), "IOB": ("sbuf", [128, 256], F),
-    "RK": ("sbuf", [128, 512], H16), "ID": ("sbuf", [128, 256], H16),
-    "IB": ("sbuf", [128, 256], B16),
-    "U1": ("sbuf", [128, 144], H16), "US": ("sbuf", [128, 144], H16), "UW": ("sbuf", [128, 144], B16),
-    "BK": ("sbuf", [128, 256], H16), "SJ": ("sbuf", [128, 2048], H16), "DG": ("sbuf", [128, 16], F),
+    "PI": ("sbuf", [128, 16], I32), "PC": ("sbuf", [128, 16], B16),
+    "IOX": ("sbuf", [128, 256], B16), "IOA": ("sbuf", [128, 512], B16), "IOB": ("sbuf", [128, 256], B16),
+    "RK": ("sbuf", [128, 512], H16), "ID": ("sbuf", [128, 384], H16), "RAMP": ("sbuf", [128, 32], B16),
+    "U1": ("sbuf", [128, 144], H16), "UW": ("sbuf", [128, 144], B16),
+    "BK": ("sbuf", [128, 384], H16), "SJ": ("sbuf", [128, 2048], H16), "DG": ("sbuf", [128, 16], B16),
     "WR": ("sbuf", [128, 32], F), "WC": ("sbuf", [128, 4], F), "SG": ("sbuf", [128, 512], F),
-    "THR": ("sbuf", [128, 256], F), "DUM": ("sbuf", [128, 32], F),
+    "THR": ("sbuf", [128, 256], F), "DUM": ("sbuf", [128, 64], F),
 }
 for _b in range(8):
     SCRATCH["P%d" % _b] = ("psum", [128, 512], F)
 
-MSGS = ["c0", "x0", "n0", "u1"] + [m + str(t) for m in ("v", "m", "o") for t in range(R)] + \
-       ["x1", "x2", "x3", "tb0", "tb1", "b3", "b4"] + [m + str(t) for m in ("a", "at", "ao", "b", "bo", "ta", "tn") for t in range(R - 1)]
-HAND = [0, 512, 1024]
+MSGS = ["c0", "h0", "h1", "n0", "u1", "l1"] + [m + str(t) for m in ("v", "m", "o") for t in range(R)] + \
+       ["x1", "x2", "x3", "tb0", "tb1", "y2", "y3", "yw2"] + \
+       [m + str(t) for m in ("a", "at", "ao", "bo", "k", "w", "ta", "tn") for t in range(R - 1)]
 NDMA = 16
 SEMAPHORES = ["sv", "sa", "sp", "sg"] + ["d%d" % i for i in range(NDMA)] + \
              ["arr_" + m for m in MSGS] + ["snt_" + m for m in MSGS]
 ENG_SEM = {"v": "sv", "a": "sa", "p": "sp", "g": "sg"}
 LAND = [0, 512, 1024, 1536]
-CYCLE, TENSOR_CYCLE, GATHER, SCATTER, WAKE = 0.9, 0.45, 1.56, 3.8, 150.0
-ISSUE = {"g": 400.0, "s": 60.0, "a": 60.0, "x": 0.0}
-PASSES, SLACK = 2, 3000.0
-HOP, LOAD, BYTE = 2600.0, 2000.0, 1.0
+PACES = [{"cycle": 0.85, "gather": 1.56, "scatter": 3.8, "wake": 170.0, "wait": 15.0, "issue": 350.0, "start": 1700.0, "row": 40.0, "byte": 0.055, "port": 0.013, "first": 3200.0, "load": 1500.0},
+         {"cycle": 1.18, "gather": 1.9, "scatter": 5.0, "wake": 130.0, "wait": 25.0, "issue": 320.0, "start": 1600.0, "row": 30.0, "byte": 0.05, "port": 0.015, "first": 3000.0, "load": 1500.0},
+         {"cycle": 0.98, "gather": 1.3, "scatter": 3.0, "wake": 220.0, "wait": 20.0, "issue": 500.0, "start": 2900.0, "row": 65.0, "byte": 0.08, "port": 0.022, "first": 4500.0, "load": 2000.0},
+         {"cycle": 0.9, "gather": 1.2, "scatter": 4.5, "wake": 260.0, "wait": 5.0, "issue": 250.0, "start": 2000.0, "row": 50.0, "byte": 0.05, "port": 0.028, "first": 4000.0, "load": 1600.0}]
+DRAIN = [0.0, 120.0, 60.0, 0.0, 0.0]
+MARGIN = 900.0
+MIXES = [(mix, slack, room) for room, slack in ((0.0, 0.0), (200.0, 1000.0)) for mix in ((0.3, 0.3, 0.2, 0.2), (0.3, 0.4, 0.15, 0.15))]
+TURNS = [0, 1, 2] * 3
+TRIES, LOOSE = 20000, 0.0
+EARLY = 9000.0
+ORDER = {}
 
 
 def reg(name, a=None, b=None, step=1, p0=0, p1=128, off=None):
     if a is None:
         a, b = 0, SCRATCH[name][1][1]
     return {"n": name, "a": a, "b": b, "s": step, "p0": p0, "p1": p1, "off": off}
+
+
+def entries(x, t, off):
+    return reg(x, P, P + W0 + P * t, off=off)
+
+
+def places(x, t, off):
+    return reg(x, 0, P + W0 + P * t, off=off)
+
+
+def built(x, t):
+    return reg(x, P + W0 + P * t, 2 * P + W0 + P * t)
 
 
 def ap(T, r):
@@ -96,18 +121,22 @@ def row_bytes(r):
     return width(r) * (4 if SCRATCH[r["n"]][2] in (F, I32) else 2)
 
 
-def duration(eng, out, ins, per):
+def duration(eng, out, ins, per, m):
     full = [r for r in [out] + list(ins) if isinstance(r, dict)]
     n = max(width(r) for r in full[:2])
     if eng == "p":
-        return TENSOR_CYCLE * max(64, width(out))
+        return 0.5 * m["cycle"] * max(min(64, width(ins[0])), width(out))
     if eng == "g":
-        return 130 + 2 * CYCLE * n
+        return 130 + 2 * m["cycle"] * n
     if any(r["off"] is not None for r in full):
-        return 60 + CYCLE * n * (SCATTER if out["off"] is not None else GATHER)
+        return 60 + m["cycle"] * n * m["scatter" if out["off"] is not None else "gather"]
     if per is None:
-        per = 0.5 if all(SCRATCH[r["n"]][2] in (H16, B16, U16) for r in full if width(r) == n) else 1.0
-    return CYCLE * max(64, per * n) + (70 if eng == "a" else 0)
+        per = 0.5 if all(SCRATCH[r["n"]][2] in (H16, B16, U16) for r in full) else 1.0
+    return m["cycle"] * max(64, per * n) + (60 if eng == "a" else 0)
+
+
+def parts_of(nh, nf):
+    return [p for p in ([(nh, 2, -1), (nf, -2, 3)] if nf <= nh else [(nf, 2, 1), (nh, -2, 1)]) if p[0]]
 
 
 def routes(T, topo, src, dst, mode):
@@ -117,7 +146,7 @@ def routes(T, topo, src, dst, mode):
     far = [c for c in ports if topo.die(c) != topo.die(src)]
     if topo.may_write(src, dst):
         near = [None, None]
-    return {"near": near[:2], "near1": near[:1], "near2": near[1:2], "far1": far[:1], "far": far[:2], "all": near[:2] + far[:2]}[mode]
+    return {"near": near[:2], "near1": near[:1], "near2": near[1:2], "far1": far[:1], "far2": far[1:2], "far": far[:2], "all": near[:2] + far[:2]}[mode]
 
 
 def messages(T, topo):
@@ -127,40 +156,54 @@ def messages(T, topo):
         w = (W0 + P * max(t - 1, 0)) // 4
         xf = "XF%d" % (t % 2)
         return ("x%d" % t, -1 - t % 2, "all",
-                [(reg("X", j * w, (j + 1) * w), reg("X", t * PIECE, t * PIECE + w), reg(xf, j * w, (j + 1) * w)) for j in range(4)])
+                [(reg("X", P + j * w, P + (j + 1) * w), reg("X", t * PIECE, t * PIECE + w), reg(xf, P + j * w, P + (j + 1) * w)) for j in range(4)])
 
-    def tab(name, step, cols, stage, mode="far", w=256):
-        tf = "TF%d" % (-step - 1)
-        return (name, step, mode, [(reg("TB", c, c + w), reg(stage[0], stage[1], stage[1] + w), reg(tf, c, c + w)) for c in cols])
+    def tab(name, step, mode, lists, names):
+        pieces = []
+        for own, far, stage, cols in (("TB", "TF", "FW", lists), ("TN", "NF", "YG", names)):
+            for c, w in cols:
+                pieces.append((reg(own, c, c + w), reg(stage, staged[stage], staged[stage] + w), reg(far + str(-step - 1), c, c + w)))
+                staged[stage] += w
+        return (name, step, mode, pieces)
 
     def plain(name, step, mode, pairs):
         return (name, step, mode, [(a, b, b) for a, b in pairs])
 
-    ms += [tab("c0", -1, [0, 256], ("TB", 0)), xship(0), tab("n0", -1, [512, 640, 768, 896], ("TB", 256), "all", 128),
-           tab("u1", -2, [256, 768], ("TB", 512)), xship(1)]
+    staged, quarters = {"FW": 0, "YG": 0}, [(128 * q, 128) for q in range(4)]
+    ms.append(plain("c0", -1, "all", [(reg("LO", c, c + w), reg("LC", c, c + w)) for c, w in quarters]))
+    for h in range(2):
+        cols = [2 * P + 4 * P * h + P * j for j in range(-1, 3)]
+        ms.append(("h%d" % h, -1, "all", [(reg("X", c, c + P), reg("X", P * h, P * h + P), reg("XF0", c, c + P)) for c in cols]))
+    ms += [tab("n0", -1, "all", [], quarters), tab("u1", -2, "far1", [], [(256, 256)]),
+           plain("l1", -2, "far2", [(reg("LO", 256, 512), reg("LC", 512, 768))]), xship(1)]
     for t in range(R):
         s, wx = t % 2, W0 + P * t
-        w, n = (128, 16) if t < 2 else (256, 32)
-        s0, l0, h0 = 512 * s, LAND[t], HAND[t % 3]
-        ms.append(plain("m%d" % t, 1 + s, "near1", [(reg("LM", 16, 16 + n), reg("LG", 32 * t, 32 * t + n))]))
-        ms.append(plain("v%d" % t, 1 + s, "near", [(reg("VY", s0 + j * w, s0 + (j + 1 + s) * w), reg("LV", l0 + j * w, l0 + (j + 1 + s) * w)) for j in range(2 - s)]))
+        n = 16 if t < 2 else 32
+        v, y, l0 = reg("VY", 512 * s, 512 * s + 256), reg("VY", 512 * s + 256, 512 * s + 512), LAND[t]
+        chosen = [plain("m%d" % t, 1 + s, "near1", [(reg("LM", 16, 16 + n), reg("LG", 32 * t, 32 * t + n))])]
         if t < R - 1:
-            ms.append(plain("at%d" % t, s - 2, "near1", [(reg("TM"), reg("LH", h0, h0 + 256))]))
-            ms.append(plain("a%d" % t, s - 2, "far", [(reg("VY", s0, s0 + 256), reg("LN", 256 * t, 256 * t + 256)), (reg("NB"), reg("LN", 768, 1024))][:1 + t // 2]))
-        ms.append(plain("o%d" % t, 1 + s, "near" if s else "far1", [(reg("OH", 0, 16), reg("LF", 16 * t, 16 * t + 16))]))
+            chosen.append(plain("k%d" % t, 2 * s - 1, "near2", [(reg("LM", 16, 16 + n), reg("LK", 32 * t, 32 * t + n))]))
+        if t >= 2:
+            ms.append(plain("y%d" % t, 1 + s, "near1" if s else "far1", [(y, reg("LV", l0 + 256, l0 + 512))]))
+        if t == 2:
+            ms.append(plain("yw2", 2 * s - 1, "far2", [(y, reg("LW", 768, 1024))]))
+        ms += chosen
+        if t < R - 1:
+            ms.append(plain("at%d" % t, s - 2, "near1", [(y, reg("LH", 256 * t, 256 * t + 256))]))
+        ms.append(plain("v%d" % t, 1 + s, "near1", [(v, reg("LV", l0, l0 + 256))]))
+        if t < R - 1:
+            ms.append(plain("w%d" % t, 2 * s - 1, "near2", [(v, reg("LW", 256 * t, 256 * t + 256))]))
+            ms.append(plain("a%d" % t, s - 2, "far1" if s else "near1", [(reg("TM"), reg("LN", 256 * t, 256 * t + 256))]))
+        ms.append(plain("o%d" % t, 1 + s, "near1" if s else "far1", [(reg("OH", 0, 16), reg("LF", 16 * t, 16 * t + 16))]))
         if t == R - 1:
             break
-        ms.append(plain("bo%d" % t, 2 * s - 1, "near1", [(reg("OH", 0, 16), reg("LB", 64 * t, 64 * t + 16))]))
-        ms.append(plain("ao%d" % t, s - 2, "near2", [(reg("OH", 16, 2 * n), reg("LB", 64 * t + 16, 64 * t + 2 * n))]))
-        stage = [("TB", 768), ("TF0", 0), ("TF0", 256)][t]
-        ms.append(tab("ta%d" % t, s - 2, [256 * s, 256 * s + 128], stage, "near", 128))
-        ms.append(tab("tn%d" % t, s - 2, [512 + 256 * s, 640 + 256 * s], stage, "far", 128))
-        for q in [0] if t < 2 else [1, 2, 0]:
-            c, l = 256 * q, h0 + 256 * (q + 1)
-            ms.append(plain("b%d" % (t + q), s - 2, "near", [(reg("TV", c + 128 * j, c + 128 * j + 256 - 128 * s), reg("LH", l + 128 * j, l + 128 * j + 256 - 128 * s)) for j in range(1 + s)]))
+        ms.append(plain("ao%d" % t, s - 2, "near2", [(reg("OH", 16, 16 + n), reg("LB", 64 * t, 64 * t + n))]))
+        ms.append(plain("bo%d" % t, 2 * s - 1, "far2" if s else "near1", [(reg("OH", 0, n), reg("LB", 64 * t + 32, 64 * t + 32 + n))]))
+        ms.append(tab("ta%d" % t, s - 2, "near", quarters[2:] if s else [(0, 256)], []))
+        ms.append(tab("tn%d" % t, s - 2, "far1" if s else "near1", [], [(256 * s, 256)]))
         if t < 2:
             ms.append(xship(t + 2))
-            ms.append(tab("tb%d" % t, -1 - s, [256 * s, 512 + 256 * s], ("TF0", 512 + 256 * t)))
+            ms.append(tab("tb%d" % t, -1 - s, "far", quarters[2 * s:2 * s + 2], [(256 * s, 256)]))
     return ms
 
 
@@ -193,7 +236,7 @@ def plan_message(T, topo, src, msg):
 
 
 def call_of(name):
-    return {"bo": "o", "tn": "ta", "a": "at"}.get(name[:-1], "o" if name == "ao1" else name[:-1]) + name[-1]
+    return {"l": "u", "k": "m", "w": "v", "yw": "y", "ao": "o" if name == "ao1" else "bo"}.get(name[:-1], name[:-1]) + name[-1]
 
 
 def deal(pool, items):
@@ -246,18 +289,19 @@ def rank_program(g, core, T, topo):
         carrier_program(g, core, T, topo)
         return
     ops = []
-    ndma, queued = [0], [0.0]
+    ndma = [0]
+    line = [""]
     ahead = [0.0]
     msgs = {m[0]: m for m in messages(T, topo)}
     queue = {"v": g.vector, "a": g.scalar, "p": g.tensor, "g": g, "s": g.sync}
 
-    def add(eng, fn, outs, ins, sem=None, per=1.0, lands=0.0, msg=None):
+    def add(eng, fn, outs, ins, sem=None, per=1.0, msg=None, legs=None):
         rd, wr = spans(ins), spans(outs)
         for r in list(ins) + list(outs):
             if isinstance(r, dict) and r["off"] is not None:
                 rd += spans([r["off"]])
-        ops.append({"e": eng, "f": fn, "r": rd, "w": wr, "sem": sem, "msg": msg, "lands": lands, "ahead": ahead[0],
-                    "busy": ISSUE[eng] if sem else duration(eng, outs[0], ins, per)})
+        busy = [{"g": m["issue"], "x": 0.0}.get(eng, 60.0) if sem else duration(eng, outs[0], ins, per, m) for m in PACES]
+        ops.append({"e": eng, "f": fn, "r": rd, "w": wr, "sem": sem, "msg": msg, "ahead": ahead[0], "busy": busy, "legs": legs, "line": eng in line[0]})
 
     A = lambda r: ap(T, r)
 
@@ -289,9 +333,16 @@ def rank_program(g, core, T, topo):
     def mm(out, lhs, rhs, start, stop):
         add("p", lambda: g.tensor.matmul(A(out), A(lhs), A(rhs), start, stop), [out], [lhs, rhs])
 
+    def join(k):
+        part = [ops.pop() for _ in range(k)][::-1]
+        ops.append(dict(part[0], f=lambda: [op["f"]() for op in part][-1], r=sorted({x for op in part for x in op["r"]}),
+                        w=sorted({x for op in part for x in op["w"]}), busy=[sum(b) for b in zip(*[op["busy"] for op in part])]))
+
     def total(out, terms):
         for q, (lhs, rhs) in enumerate(terms):
             mm(out, lhs, rhs, q == 0, q == len(terms) - 1)
+            if len(terms) == 16 and q % 8 == 7:
+                join(8)
 
     def iota(out, pattern, base, cm):
         if SCRATCH[out["n"]][2] == I32:
@@ -306,36 +357,37 @@ def rank_program(g, core, T, topo):
         def fn():
             for out, in_ in pairs:
                 queue[eng].dma_start(A(out), A(in_)).then_inc(T.sem[name], 16)
-        queued[0] = (queued[0] if ahead[0] else 0.0) + sum(250 + 0.35 * row_bytes(r) for p in pairs for r in p if isinstance(r, dict))
-        add(eng, fn, [p[0] for p in pairs], [p[1] for p in pairs], sem=(name, 16 * len(pairs)), lands=LOAD + queued[0])
+        add(eng, fn, [p[0] for p in pairs], [p[1] for p in pairs], sem=(name, 16 * len(pairs)),
+            legs=[(None, topo.engines(core, core), r["p1"] - r["p0"], row_bytes(r), None, [], None) for p in pairs for r in p if isinstance(r, dict)])
 
     def send(name, after=()):
-        trs = []
+        trs, legs = [], []
         for msg in [m for m in msgs.values() if call_of(m[0]) == name]:
             dst, way, engs, _ = plan_message(T, topo, core, msg)
             trs += [(msg[0], dst, engs[j], p[0], p[2]) if way[j] is None else (msg[0], way[j], engs[j], p[0], p[1]) for j, p in enumerate(msg[3])]
+            for j, c in enumerate(way):
+                second = deal(topo.engines(c, dst), [q for q in range(len(way)) if way[q] == c])[j] if c else []
+                legs.append((msg[0], engs[j], 128, row_bytes(msg[3][j][0]), c, second, topo.die(c or core)))
         add("g", lambda: write(g, T, topo, core, name, trs), [], [tr[3] for tr in trs] + list(after),
-            sem=("snt_" + name, sum(len(tr[2]) for tr in trs)), msg=name, lands=HOP + BYTE * sum(row_bytes(tr[3]) for tr in trs))
+            sem=("snt_" + name, sum(len(tr[2]) for tr in trs)), msg=name, legs=legs)
 
     def arrive(name):
         msg = msgs[name]
         src = T.cores[(rank - msg[1]) % NR]
         dst, way, engs, count = plan_message(T, topo, src, msg)
-        hops = 2 if set(way) - {None} else 1
-        add("x", None, [p[2] for p in msg[3]], [], sem=("arr_" + name, count), msg=(call_of(name), msg[1]),
-            lands=hops * (HOP + 2 * BYTE * sum(row_bytes(p[0]) for p in msg[3]) / len(set(way))))
+        add("x", None, [p[2] for p in msg[3]], [], sem=("arr_" + name, count), msg=(call_of(name), msg[1]))
 
     def bank(b, a=0, e=512, step=1, p1=128):
         return reg("P%d" % b, a, e, step, 0, p1)
 
     col = lambda n, c: reg(n, c, c + 1)
     P16, PG, PP, PG16, PPAIR, PODD, P24, P3, P4 = [col("PC", c) for c in range(9)]
-    BO, BOM = [reg("BK", 128 * j, 128 * j + 128) for j in range(2)]
+    BO, BOM, BO3 = [reg("BK", 128 * j, 128 * j + 128) for j in range(3)]
     BIG, NBIG = [reg("BB", 128 * j, 128 * j + 128) for j in range(2)]
-    ROW, CROW, NCROW, KROW, BIAS, PP2, NFC = [col("PD", c) for c in (0, 4, 5, 6, 7, 8, 9)]
-    ID, NID, IDB, NIDB = reg("ID", 0, 128), reg("ID", 128, 256), reg("IB", 0, 128), reg("IB", 128, 256)
+    ROW, CROW, NCROW, KROW, BIAS, PP2, NFC, SIDE = [col("PD", c) for c in (0, 4, 5, 6, 7, 8, 9, 12)]
+    ID, NID, ID3 = [reg("ID", 128 * j, 128 * j + 128) for j in range(3)]
     START, MINUS8 = reg("R0", 0, 256), reg("R0", 128, 136)
-    sign = lambda n: {0: 1.0, 128: -1.0}.get(n, col("PD", 12 + n // 32))
+    sign = lambda n: {0: 1.0, 128: -1.0}.get(n, col("PS", n // 32))
     times = lambda c: reg("R0", *{-1: (128, 256), 2: (256, 384), -2: (384, 512), 1: (512, 640), 3: (640, 768)}[c])
 
     def to_list(out, sel, src, a, n):
@@ -346,51 +398,51 @@ def rank_program(g, core, T, topo):
         copy(reg("RV", 48 * (t % 2), 48 * (t % 2) + 16), reg("BI", 0, 16))
         ts(reg("BI", 32, 48), reg("BI", 16, 32), 1, OP.logical_shift_right, 511, OP.bitwise_and)
         if t < R - 1:
-            ts(reg("BH"), reg("BI", 0, 16), 16.0, OP.mult)
+            ts(reg("BH"), reg("BI", 0, 16), 256.0, OP.subtract)
         copy(reg("BO16"), reg("BI", 32, 48))
 
     ahead[0] = 20000.0
-    dma("s", [(reg("FR"), T.fr0[:])])
     dma("a", [(reg("PL"), T.pl[:])])
+    dma("s", [(reg("FR"), T.fr0[:])])
+    dma("s", [(reg("ZB", 0, 256), T.z0[:])])
+    dma("s", [(reg("X", P, P + 1024), T.x0[:, 0:1024])])
+    dma("s", [(reg("X", P + 1024, P + 2048), T.x0[:, 1024:2048])])
     dma("s", [(reg("BI", 0, 16), T.b0[:])])
-    dma("a", [(reg("ZB", 0, 256), T.z0[:])])
-    dma("s", [(reg("X", 0, 1024), T.x0[:, 0:1024])])
-    dma("a", [(reg("X", 1024, 2048), T.x0[:, 1024:2048])])
     iota(col("PI", 0), [[0, 1]], 0, 1)
     iota(reg("IOA", 0, 128), [[1, 8], [0, 16]], 0, 0)
     iota(reg("IOX"), [[1, 256]], 0, 0)
     iota(reg("IA", 576, 704), [[0, 16], [1, 8]], 0, 0)
     iota(reg("IA", 0, 512, 1, 0, 64), [[1, 2], [4, 16], [0, 16]], 0, 0)
     iota(reg("IA", 0, 512, 1, 64, 128), [[1, 2], [0, 16], [4, 16]], 64, 0)
-    fill(reg("X", W0, XW), 0.0)
+    fill(reg("X", 0, P), 0.0)
+    fill(reg("XF1", 0, P), 0.0)
     for c, (shift, bits) in enumerate([(0, 15), (4, 7), (0, 127), (0, 112), (5, 3), (4, 1), (0, 24), (0, 3), (2, 1)]):
         ts(col("PI", 1 + c), col("PI", 0), shift, OP.logical_shift_right, bits, OP.bitwise_and)
     copy(reg("PC", 0, 9), reg("PI", 1, 10))
     ts(BO, reg("IOA", 0, 128), PG, OP.is_equal)
     ts(reg("DG"), reg("IOX", 0, 16), P16, OP.is_equal)
     for j in range(16):
-        if j % 2:
-            act(reg("SJ", 128 * j, 128 * j + 128), BO, AF.Copy, scale=col("DG", j))
-        else:
-            ts(reg("SJ", 128 * j, 128 * j + 128), BO, col("DG", j), OP.mult)
-    copy(reg("FR16"), reg("FR"))
+        ts(reg("SJ", 128 * j, 128 * j + 128), BO, col("DG", j), OP.mult)
     ts(reg("U1"), reg("IOX", 0, 144), 15.0, OP.subtract, PG16, OP.is_equal)
     ts(ID, reg("IOX", 0, 128), PP, OP.is_equal)
-    copy(reg("TB", 0, 256), reg("PL", 0, 512, 2))
-    copy(reg("TB", 256, 512), reg("PL", 1, 512, 2))
+    line[0] = "v"
+    copy(reg("LO", 0, 256), reg("PL", 0, 512, 2))
+    copy(reg("LO", 256, 512), reg("PL", 1, 512, 2))
+    copy(reg("FR16"), reg("FR"))
+    line[0] = ""
     send("c0")
-    send("x0")
+    send("h0")
+    send("h1")
     ahead[0] = 10000.0
     iota(reg("TIE", 0, 512, p1=2), [[0, 2], [32, 16], [1, 16]], 0, 0)
     iota(reg("TIE", 512, 576, p1=2), [[0, 4], [32, 16]], 16, 0)
     iota(reg("IA", 512, 576), [[1, 4], [4, 16]], 0, 0)
     iota(reg("IOB"), [[0, 16], [1, 16]], 0, 0)
     iota(reg("IOA", 128, 512), [[1, 24], [0, 16]], 8, 0)
-    for k in range(ZACT):
+    for k in range(ZACT[0]):
         act(reg("ZR", k, 4096, 16), reg("ZB", 0, 256), AF.Copy)
     for j in range(16):
         mm(bank(j // 4, 128 * (j % 4), 128 * (j % 4) + 128), reg("SJ", 128 * j, 128 * j + 128), reg("FR16"), True, True)
-    copy(reg("LO"), reg("TB", 0, 512))
     act(reg("FW", 0, 512), bank(0), AF.Copy)
     copy(reg("FW", 512, 1024), bank(1))
     act(reg("FW", 1024, 1536), bank(2), AF.Copy)
@@ -398,51 +450,45 @@ def rank_program(g, core, T, topo):
     for e in range(16):
         iota(col("WR", e), [[0, 1]], WT[e], 0)
 
-    pieces = {"a": [(0, 128), (128, 192), (192, 256)], "v": [(256, 384), (384, 448), (448, 512)]}
-    for q in range(3):
-        for eng, buf in (("a", "NG"), ("v", "MH")):
-            a, b = pieces[eng][q]
-            out, w = reg(buf, 16 * (a % 256), 16 * (a % 256) + 16 * (b - a)), reg("FW", off=reg("LO", a, b))
-            if eng == "a":
-                act(out, w, AF.Copy)
-            else:
-                copy(out, w)
-            total(bank(4 + a // 128, a % 128, a % 128 + b - a), [(reg("U1", 15 - k, 143 - k), reg(buf, out["a"] + k, out["b"], 16)) for k in range(16)])
-    for c in (0, 2, 1, 3):
-        act(reg("TB", 512 + 128 * c, 640 + 128 * c), bank(4 + c, 0, 128), AF.Copy)
+    for eng, a, b in NAMES:
+        buf = ["NG", "MH"][a // 256]
+        out, w = reg(buf, 16 * (a % 256), 16 * (a % 256) + 16 * (b - a)), reg("FW", off=reg("LO", a, b))
+        if eng == "a":
+            act(out, w, AF.Copy)
+        else:
+            copy(out, w)
+        total(bank(4 + a // 128, a % 128, a % 128 + b - a), [(reg("U1", 15 - k, 143 - k), reg(buf, out["a"] + k, out["b"], 16)) for k in range(16)])
+    for c in (0, 3, 1, 2):
+        act(reg("TN", 128 * c, 128 * c + 128), bank(4 + c, 0, 128), bias=-256.0, scale=1.0 / 16)
     send("n0")
     ahead[0] = 0.0
-    for k in range(ZACT, 16):
+    for k in range(ZACT[0], 16):
         copy(reg("ZR", k, 4096, 16), reg("ZB", 0, 256))
-    for m in ("c0", "x0", "n0"):
+    copy(reg("TB"), reg("LO"))
+    for m in ("c0", "h0", "h1", "n0"):
         arrive(m)
-    send("u1", after=[reg("TF0", 512, 1024)])
+    send("u1", after=[reg("XF0", P, P + W0)])
     send("x1")
     payee(0)
-
-    def home_names(c):
-        act(reg("NL"), reg("TB", c, c + 256), AF.Copy, scale=-1.0)
 
     def sum_constants():
         parts = sorted({n for sh in SHARE for n in sh} - {0, 128})
         ts(times(-1), reg("IA", 576, 704), PG, OP.is_equal, -1.0, OP.mult)
         for n in parts:
-            ts(col("PD", 16 + n // 32), PP, float(n), OP.is_ge, 2.0, OP.mult)
+            ts(col("PS", 4 + n // 32), PP, float(n), OP.is_ge, 2.0, OP.mult)
         for n in parts:
-            ts(sign(n), col("PD", 16 + n // 32), 1.0, OP.subtract)
-        act(IDB, ID, AF.Copy)
-        act(NIDB, ID, AF.Copy, scale=-1.0)
-        act(reg("R0", 0, 8), MINUS8, AF.Copy, scale=0.0)
-        act(reg("R0", 8, 128), reg("R0", 136, 256), AF.Copy, scale=-1.0)
-        for c in (2, -2, 1, 3):
-            act(times(c), times(-1), AF.Copy, scale=-float(c))
-        act(reg("R0", 768, 1024), reg("R0", 0, 256), AF.Copy, scale=0.0)
-        act(reg("R0", 896, 904), MINUS8, AF.Copy)
+            ts(sign(n), col("PS", 4 + n // 32), 1.0, OP.subtract)
+        ts(NID, ID, -1.0, OP.mult)
+        fill(reg("R0", 0, 8), 0.0)
+        ts(reg("R0", 8, 128), reg("IA", 584, 704), PG, OP.is_equal)
+        for c in sorted({c for sh in SHARE for h in range(2) for n, y0, z0 in parts_of(sh[h], sh[2 + h]) for c in (y0, z0)} - {-1}):
+            ts(times(c), reg("IA", 576, 704), PG, OP.is_equal, float(c), OP.mult)
 
     def pair_constants():
         ts(ROW, P16, 4.0, OP.mult, PPAIR, OP.add)
-        ts(col("PD", 3), PODD, 8.0, OP.mult)
-        ts(col("PD", 2), PODD, -8.0, OP.mult, 8.0, OP.add)
+        ts(col("PD", 3), PODD, 128.0, OP.mult)
+        ts(col("PD", 2), PODD, -128.0, OP.mult, 128.0, OP.add)
+        ts(col("PD", 13), PP, 64.0, OP.is_ge, 65536.0, OP.mult)
         ts(CROW, PP, 4.0, OP.is_ge, 512.0, OP.mult)
         ts(NCROW, PP, 4.0, OP.is_ge, -512.0, OP.mult)
         ts(KROW, P3, 2.0, OP.mult, P24, OP.add)
@@ -453,10 +499,12 @@ def rank_program(g, core, T, topo):
         ts(col("PD", 1), ROW, 64.0, OP.add)
         ts(KROW, KROW, P4, OP.add)
         ts(BIAS, PP, 0.0, OP.is_equal, col("PD", 10), OP.add)
+        ts(SIDE, col("PD", 13), 32768.0, OP.subtract)
+        ts(col("PS", 0), PP, 0.0, OP.is_equal)
         for j, c in enumerate((PP, PP2)):
-            ts(reg("SN", 512 * j, 512 * j + 512), reg("IA", 0, 512), c, OP.is_equal, 32768.0, OP.mult)
+            ts(reg("SN", 512 * j, 512 * j + 512), reg("IA", 0, 512), c, OP.is_equal, SIDE, OP.mult)
             ts(reg("SC", 512 * j, 512 * j + 512), reg("IA", 0, 512), c, OP.is_equal, CROW, OP.mult)
-            act(reg("SC", 512 * j, 512 * j + 512, p1=2), reg("TIE", 0, 512, p1=2), AF.Copy, scale=reg("DG", 0, 1, p1=2))
+            act(reg("SC", 512 * j, 512 * j + 512, p1=2), reg("TIE", 0, 512, p1=2), AF.Copy, scale=reg("PS", 0, 1, p1=2))
         ts(BIAS, BIAS, col("PD", 11), OP.add)
         for side in range(2):
             for odd in range(2):
@@ -465,23 +513,29 @@ def rank_program(g, core, T, topo):
         ts(reg("SG", 0, 256), reg("IOB"), 0.0, OP.is_equal, 2.0 ** 23, OP.mult)
         ts(reg("SF", p1=2), reg("TIE", 512, 576, p1=2), reg("DG", 0, 1, p1=2), OP.mult, reg("PD", 9, 10, p1=2), OP.add)
 
+    ts(reg("CM", 0, 256), reg("LO", 0, 256), MID, OP.subtract, 2.0, OP.mult)
+    act(reg("N0"), reg("TN", 0, 256), AF.Copy)
+    act(reg("PL16"), reg("TB"), AF.Copy)
+
     def later_constants():
-        act(reg("CM", 0, 256), reg("TB", 0, 256), bias=-MID)
-        act(reg("N0"), reg("TB", 512, 768), AF.Copy)
         act(reg("SG", 256, 512), reg("SG", 0, 256), bias=0.5, scale=2.0 ** -24)
-        act(BOM, BO, AF.Copy, scale=-2048.0)
-        act(reg("SL", 0, 256), reg("SG", 0, 256), bias=1.0, scale=-2.0 ** -23)
-        act(NID, ID, AF.Copy, scale=-1.0)
+        ts(BOM, BO, -4096.0, OP.mult)
+        ts(BO3, BO, 3072.0, OP.mult)
+        ts(ID3, ID, 3072.0, OP.mult)
+        ts(reg("SL", 0, 256), reg("IOB"), 0.0, OP.not_equal)
+        fill(reg("D0"), -1024.0)
+        fill(reg("RAMP", 0, 16), 0.0)
+        ts(reg("RAMP", 16, 32), reg("IOX", 0, 16), 20.0, OP.mult, -150.0, OP.add)
 
     def last_constants():
         ts(col("WC", 2), PP, 0.0, OP.mult, 2.0 ** 61, OP.add)
         ts(reg("RK"), reg("IOA"), KROW, OP.is_equal)
         tt(reg("WR", 16, 32), reg("WR", 0, 16), reg("DG"), OP.mult)
         ts(col("WC", 3), col("WC", 2), 2.0 ** 60, OP.mult)
-        for a in (0, 16):
-            ts(reg("DUM", a, a + 16), reg("IOX", 0, 256, 16), P16, OP.add, 3072.0, OP.add)
+        for a in (0, 16, 32, 48):
+            ts(reg("DUM", a, a + 16), reg("IOX", 0, 256, 16), P16, OP.add, -256.0 * (a // 32), OP.add)
         red(col("WC", 0), reg("WR", 16, 32), OP.add)
-        scan(reg("THR"), reg("SG", 256, 512), reg("X", 3072, XW), col("WC", 3), OP.mult, OP.add)
+        scan(reg("THR"), reg("SG", 256, 512), reg("X", 0, P), col("WC", 3), OP.mult, OP.add)
         ts(BIG, BO, col("WC", 3), OP.mult, 2.0, OP.mult)
         ts(reg("NFK"), reg("IOB"), P16, OP.is_equal)
         act(reg("UW"), reg("U1"), AF.Copy, scale=col("WC", 0))
@@ -489,41 +543,75 @@ def rank_program(g, core, T, topo):
         tt(reg("THR"), reg("THR"), reg("NFK"), OP.mult)
         scan(reg("NFK"), reg("SL", 0, 256), reg("THR"), 0.0, OP.mult, OP.max)
         act(reg("FL", 0, 16), reg("NFK", 15, 256, 16), AF.Copy, scale=0.5)
+        act(reg("FL32"), reg("NFK", 15, 256, 16), AF.Copy, scale=0.5)
         for h in range(16):
-            act(reg("BW", 128 * h, 128 * h + 128), BO, AF.Copy, scale=col("FL", h))
+            if h < BWACT:
+                act(reg("BW", 128 * h, 128 * h + 128), BO, AF.Copy, scale=col("FL32", h))
+            else:
+                ts(reg("BW", 128 * h, 128 * h + 128), BO, col("FL", h), OP.mult)
+
+    def settle(x, t, chosen, fv, gifts, buf, taken, ps):
+        before, left, after = [reg(buf, 256 * q, 256 * q + 256) for q in range(3)]
+        if x != "X" and t < 2:
+            act(left, fv, AF.Copy, scale=-1.0)
+            tt(taken, entries(x, t, chosen), fv, OP.max)
+            return
+        act(before, entries(x, t, chosen), AF.Copy)
+        if t == R - 1:
+            act(after, before, AF.Relu, bias=-63.0)
+        total(ps, [(ID, before), (NID, fv)] + [(NID, after)] * (t == R - 1))
+        act(left if gifts else taken, ps, AF.Relu)
+        if gifts:
+            total(ps, [(ID, left), (NID, before)])
+            act(taken, ps, AF.Copy)
+            for q, (off, w) in enumerate(gifts):
+                held = reg(buf, 768 + 256 * q, 1024 + 256 * q)
+                change(t, places(x, t, off), places(x, t, off), held, w)
+
+    def change(t, read, put, held, w):
+        if t < R - 1:
+            act(held, read, AF.Copy)
+            tt(put, held, w, OP.add)
+        else:
+            tt(held, read, w, OP.add)
+            copy(put, held)
+
+    def far_takes(x, t, chosen, off, buf, taken):
+        if t >= 2:
+            change(t, entries(x, t, chosen), places(x, t, off), reg(buf, 512, 768), taken)
+        elif x == "X":
+            copy(places(x, t, off), taken)
+        else:
+            tt(places(x, t, off), taken, reg(buf, 256, 512), OP.add)
 
     def follow_home(t):
-        xf, h0 = "XF%d" % (1 - t % 2), HAND[t]
-        for m in ("x%d" % (t + 1), "ao%d" % t, "at%d" % t):
+        xf = "XF%d" % (1 - t % 2)
+        for m in ["x%d" % (t + 1), "a%d" % t, "ao%d" % t, "at%d" % t, "k%d" % t, "w%d" % t] + ["yw2"] * (t == 2):
             arrive(m)
-        copy(reg(xf, off=reg("LB", 64 * t + 16, 64 * t + 32)), reg("LH", h0, h0 + 256))
+        y, less = reg("LH", 256 * t, 256 * t + 256), reg("LN", 256 * t, 256 * t + 256)
+        act(built(xf, t), less, AF.Copy, scale=-1.0)
+        tt(places(xf, t, reg("LB", 64 * t, 64 * t + 16)), y, less, OP.add)
+        gifts = [(reg("LB", 144, 160), y), (reg("LK", 80, 96), reg("LW", 768, 1024))] if t == 2 else []
+        settle(xf, t, reg("LK", 32 * t, 32 * t + 16), reg("LW", 256 * t, 256 * t + 256), gifts, "NW", reg("TV", 256, 512), bank(0, 256, 512))
 
     def follow_far(t):
-        xf, h0, wx = "XF%d" % (1 - t % 2), HAND[t], W0 + P * t
-        arrive("a%d" % t)
-        copy(reg(xf, wx, wx + 256), reg("LN", 256 * t, 256 * t + 256))
-        if t >= 2:
-            copy(reg(xf, wx - 512, wx - 256), reg("LN", 256 * t + 256, 256 * t + 512))
         arrive("bo%d" % t)
-        for q in range(1 if t < 2 else 3):
-            arrive("b%d" % (t + q))
         if t < 2:
-            send("x%d" % (t + 2), after=[reg("LH", h0 + 256, h0 + 512)])
+            send("x%d" % (t + 2), after=[reg("LB", 64 * t + 32, 64 * t + 48)])
             send("tb%d" % t)
-        for q, o in [(0, 0)] if t < 2 else [(1, 32), (2, 48), (0, 0)]:
-            copy(reg(xf, off=reg("LB", 64 * t + o, 64 * t + o + 16)), reg("LH", h0 + 256 * (q + 1), h0 + 256 * (q + 2)))
+        far_takes("XF%d" % (1 - t % 2), t, reg("LK", 32 * t, 32 * t + 16), reg("LB", 64 * t + 32, 64 * t + 48), "NW", reg("TV", 256, 512))
 
     for t in range(R):
         s = t % 2
         wx = W0 + P * t
-        XF, TF = "XF%d" % s, "TF%d" % s
+        XF, TF, NF = "XF%d" % s, "TF%d" % s, "NF%d" % s
         z = reg("ZB", 256 * s, 256 * s + 256)
         zn = reg("ZB", 256 * (1 - s), 256 * (1 - s) + 256)
-        C, Nn = reg("TB", 256 * s, 256 * s + 256), reg("TB", 512 + 256 * s, 768 + 256 * s)
-        zb = [1, 2, 3, 0, 6, 7, 4, 1]
+        C, Nn = reg("TB", 256 * s, 256 * s + 256), reg("TN", 256 * s, 256 * s + 256)
+        zb = [1, 2, 3, 0, 6, 7, 1, 2]
         HOME, FAR = 0, 1
         share = lambda side, h: SHARE[t][2 * side + h]
-        window = lambda side, h, a, b: reg(["X", XF][side], 0, wx, off=reg(["LO", "MO"][side], [256 * s, 0][side] + 128 * h + a, [256 * s, 0][side] + 128 * h + b))
+        window = lambda side, h, a, b: entries(["X", XF][side], t, reg(["LO", "MO"][side], [256 * s, 0][side] + 128 * h + a, [256 * s, 0][side] + 128 * h + b))
         mins = ["MY", "MH"]
         ready, staged, free = [], [], [6, 7, 1, 2, 3]
 
@@ -543,7 +631,7 @@ def rank_program(g, core, T, topo):
         def stage():
             while ready and free:
                 (side, c), b = ready.pop(0), free.pop(0)
-                total(bank(b), [(IDB, reg("ZR", c, c + 512)), (NIDB, reg("YG", 4096 * side + c, 4096 * side + c + 512))])
+                total(bank(b), [(ID, reg("ZR", c, c + 512)), (NID, reg("YG", 4096 * side + c, 4096 * side + c + 512))])
                 staged.append((side, c, b))
 
         def short(n=1):
@@ -557,18 +645,20 @@ def rank_program(g, core, T, topo):
         def home_sums(h, first):
             c, nh, nf = 2048 * h, share(HOME, h), share(FAR, h)
             mm(bank(4 + h, 0, 256), reg("MY", c, c + 2048, 16), START, first, False)
-            for n, y0, z0 in ([(nh, 2, -1), (nf, -2, 3)] if nf <= nh else [(nf, 2, 1), (nh, -2, 1)]):
+            for n, y0, z0 in parts_of(nh, nf):
                 if n:
                     mm(bank(4 + h, 128, 256, p1=n), reg("MY", c, c + 16 * n, 16), times(y0), False, False)
                     mm(bank(4 + h, 128, 256, p1=n), reg("ZB", 256 * s + 128 * h, 256 * s + 128 * h + n), times(z0), False, False)
             for k in range(1, 16):
-                mm(bank(4 + h, 8 * k, 8 * k + 8), reg("MY", c + k, c + 2048, 16), MINUS8, False, k == 15 and not first)
+                mm(bank(4 + h, 8 * k, 8 * k + 8), reg("MY", c + k, c + 2048, 16), MINUS8, False, False)
+                if k % 8 == 7:
+                    join(7 + k // 8)
 
-        def far_sums(h, first):
-            if first:
-                mm(bank(4 + h, 0, 256), reg("MH", 2048 * h, 2048 * h + 2048, 16), reg("R0", 768, 1024), True, False)
-            for l in range(1 if first else 0, 16):
-                mm(bank(4 + h, 128 + 8 * l, 136 + 8 * l), reg("MH", 2048 * h + l, 2048 * h + 2048, 16), MINUS8, False, l == 15 and not first)
+        def far_sums(h):
+            for l in range(16):
+                mm(bank(4 + h, 128 + 8 * l, 136 + 8 * l), reg("MH", 2048 * h + l, 2048 * h + 2048, 16), MINUS8, False, l == 15)
+                if l % 8 == 7:
+                    join(8)
 
         def turn(h):
             nh, nf = share(HOME, h), share(FAR, h)
@@ -583,7 +673,10 @@ def rank_program(g, core, T, topo):
         def least(h):
             for odd in range(2):
                 a = 128 * h + 64 * odd
-                mm(bank(5, a, a + 64), reg("FH", 256 * h + 128 * odd, 256 * h + 128 * odd + 128), reg("SF"), True, True)
+                mm(bank(4, a, a + 64), reg("FH", 256 * h + 128 * odd, 256 * h + 128 * odd + 128), reg("SF"), True, True)
+            was, line[0] = line[0], ""
+            scan(reg("NFK", 128 * h, 128 * h + 128), reg("SG", 0, 128), bank(4, 128 * h, 128 * h + 128), 0.0, OP.add, OP.min)
+            line[0] = was
 
         def names(*qs):
             for q in qs:
@@ -597,11 +690,11 @@ def rank_program(g, core, T, topo):
 
         def best(*qs):
             for q in qs:
-                if q >= 8 - HELPED:
-                    act(reg("AB", 512 * (7 - q), 512 * (8 - q)), bank(zb[q]), AF.Abs)
+                if q in HELPED[t]:
+                    act(reg("AB", 512 * q, 512 * q + 512), bank(zb[q]), AF.Abs)
                 for g2 in range(2):
-                    a, b = 128 * (2 * q + g2), 512 * (7 - q) + 256 * g2
-                    if q >= 8 - HELPED:
+                    a, b = 128 * (2 * q + g2), 512 * q + 256 * g2
+                    if q in HELPED[t]:
                         scan(reg("RR", a, a + 128), reg("AB", b, b + 128), reg("AB", b + 128, b + 256), 2.0 ** 23, OP.min, OP.min)
                     else:
                         red(col("RR", a + 127), bank(zb[q], 256 * g2, 256 * g2 + 256), OP.min, True)
@@ -610,38 +703,50 @@ def rank_program(g, core, T, topo):
             copy(reg("MO"), reg(TF, 0, 512, off=reg("BO16")))
 
         def far_names():
-            act(reg("CM", 512, 768), reg(TF, 512, 1024, off=reg("BO16")), AF.Copy)
+            act(reg("CM", 512, 768), reg(NF, off=reg("BO16")), AF.Copy)
 
         def far_entries():
-            act(reg("CM", 256, 512), reg(TF, 0, 512, off=reg("BO16")), bias=-MID)
+            ts(reg("CM", 256, 512), reg("MO"), MID, OP.subtract, 2.0, OP.mult)
 
         def stack_names():
             for odd in range(2):
-                total(bank(0, 256 * odd, 256 * odd + 256), [(reg("PM", 128 * odd, 128 * odd + 128), reg("NL")), (reg("PM", 256 + 128 * odd, 384 + 128 * odd), reg("CM", 512, 768))])
+                total(bank(0, 256 * odd, 256 * odd + 256), [(reg("PM", 128 * odd, 128 * odd + 128), Nn), (reg("PM", 256 + 128 * odd, 384 + 128 * odd), reg("CM", 512, 768))])
             act(reg("NS"), bank(0), AF.Copy)
             names(0, 1, 2, 3)
 
-        def slots(side):
-            for h in range(2):
-                gather(side, h)
-                fetch(side, h, 0, 64)
-                fetch(side, h, 64, 128)
-            stage()
+        def bring(side, h):
+            for a in (0, 64):
+                fetch(side, h, a, a + 64)
+                stage()
+
+        def rows(h):
+            far_sums(h)
+            turn(h)
+            stack(h)
 
         if t == 0:
             sum_constants()
             pair_constants()
-            home_names(512)
+            ahead[0] = EARLY
             later_constants()
             last_constants()
+            ahead[0] = 0.0
         else:
             arrive("ta%d" % (t - 1))
             arrive("tn%d" % (t - 1))
             arrive("u1" if t == 1 else "tb%d" % (t - 2))
-        slots(HOME)
-        for h in range(2):
-            short(share(HOME, h) // 32)
+        if t == 1:
+            arrive("l1")
+            copy(reg("TF1", 256, 512), reg("LC", 512, 768))
+        line[0] = "va"
+        for h in [0] if t in HALVES else [0, 1]:
+            gather(HOME, h)
+            bring(HOME, h)
+            short(4)
             home_sums(h, True)
+        if t == 0:
+            copy(reg("TF0"), reg("LC", 0, 512))
+        line[0] = ""
         if t == 2:
             follow_home(t - 1)
         far_offsets()
@@ -650,30 +755,34 @@ def rank_program(g, core, T, topo):
         free[:] = [6, 7]
         far_names()
         stack_names()
-        slots(FAR)
-        short(share(FAR, 0) // 32)
-        far_sums(0, False)
-        turn(0)
-        stack(0)
+        line[0] = "va"
+        gather(FAR, 0)
+        bring(FAR, 0)
+        short(4)
+        if t in HALVES:
+            gather(HOME, 1)
+            bring(HOME, 1)
+            gather(FAR, 1)
+            rows(0)
+            short(4)
+            home_sums(1, True)
+            bring(FAR, 1)
+        else:
+            gather(FAR, 1)
+            bring(FAR, 1)
+            rows(0)
         short(4)
         costs(0, 1, 2, 3)
-        far_sums(1, False)
-        turn(1)
-        names(4, 5, 6)
-        stack(1)
-        far_entries()
-        best(0, 1, 2, 3)
-        costs(4, 5)
         least(0)
+        best(0, 1, 2, 3)
+        names(6, 7, 4, 5)
+        rows(1)
+        costs(6, 7, 4, 5)
+        best(6, 4, 7, 5)
+        line[0] = ""
         least(1)
-        costs(6)
-        names(7)
-        costs(7)
-        best(4)
-        scan(reg("NFK"), reg("SG", 0, 256), bank(5, 0, 256), 0.0, OP.add, OP.min)
-        best(5, 6)
+        far_entries()
         mm(bank(5), ID, reg("CM", 0, 512), True, True)
-        best(7)
 
         tt(reg("KI", 32, 48), reg("RR", 127, 2048, 128), reg("NFK", 15, 256, 16), OP.min)
         ts(reg("KI", 0, 16), reg("KI", 32, 48), 5, OP.logical_shift_right, 15, OP.bitwise_and)
@@ -685,11 +794,13 @@ def rank_program(g, core, T, topo):
             mm(bank(2, 128 * q, 128 * q + 128), reg("RK", 128 * q, 128 * q + 128, p1=32), reg("VT", p1=32), True, True)
         dn = bank(0, 0, 256)
         if t < R - 1:
-            mm(dn, ID, reg("NL"), True, False)
+            mm(dn, NID, Nn, True, False)
             for j in range(16):
                 mm(bank(0, j, 256, 16), reg("SJ", 128 * j, 128 * j + 128), reg("BH"), False, j == 15)
+                if j % 8 == 7:
+                    join(8)
         if t == 2:
-            total(bank(6, 256, 512), [(NID, reg("NL")), (NID, reg("N0"))])
+            total(bank(6, 256, 512), [(ID, Nn), (NID, reg("N0"))])
             act(reg("T2", 512, 768), bank(6, 256, 512), AF.Copy)
         ts(reg("WK", 0, 512), bank(2), P16, OP.is_equal)
         tt(reg("WK", 512, 1024), reg("WK", 0, 512), bank(5), OP.mult)
@@ -701,152 +812,142 @@ def rank_program(g, core, T, topo):
         act(reg("KB", 0, 256), bank(4, 0, 256), AF.Copy)
         if t >= 2:
             total(bank(7, 0, 256), [(BO, reg("WK", 512, 768)), (BOM, reg("WK", 256, 512))])
-        ts(reg("LM", 0, 32), bank(3, 16, 48), MID, OP.add)
         rv, dm = 48 * s, 32 * t
-        ts(reg("RV", rv + 16, rv + 48), bank(3, 16, 48), MID, OP.add)
-        keep, old = bank(7, 256, 512), reg("X", wx - 512, wx - 256)
+        tt(reg("HL", 0, 32), bank(3, 16, 48), reg("RAMP"), OP.subtract)
+        ts(reg("K1"), bank(3, 16, 48), 1.0, OP.add)
+        ts(reg("LM", 0, 32), bank(3, 16, 48), 0.5, OP.mult, MID, OP.add)
+        tt(reg("HL", 32, 48), reg("K1", 0, 16), reg("HL", 0, 16), OP.subtract)
+        ts(reg("RV", rv + 16, rv + 48), bank(3, 16, 48), 0.5, OP.mult, MID, OP.add)
+        tt(reg("HL", 64, 80), reg("HL", 32, 48), bank(3, 0, 16), OP.subtract)
+        tt(reg("D0", 0, 256, 16), reg("K1", 16, 32), reg("HL", 16, 32), OP.subtract)
+        keep, old = bank(7, 256, 512), built("X", t - 2)
         if t >= 2:
-            ts(reg("G2", 64, 80), bank(3, 0, 16), -4096.0, OP.mult)
-            tt(reg("G2", 64, 80), reg("G2", 64, 80), reg("RV", rv + 16, rv + 32), OP.add)
-            ts(reg("G2", 80, 96), reg("G2", 64, 80), 2048.0, OP.is_ge)
+            ts(reg("G2", 64, 80), reg("K1", 0, 16), 2 * (W0 - MID), OP.is_ge)
+            tt(reg("G2", 80, 96), reg("G2", 64, 80), bank(3, 0, 16), OP.is_gt)
             tt(reg("G2", 48, 64), reg("G2", 80, 96), reg("DM", dm - 48, dm - 32), OP.mult)
             tt(reg("G2", 32, 48), reg("G2", 80, 96), reg("DM", dm - 64, dm - 48), OP.mult)
-            tt(reg("G2", 32, 64), reg("G2", 32, 64), reg("DUM"), OP.add)
+            tt(reg("G2", 32, 64), reg("G2", 32, 64), reg("DUM", 0, 32), OP.add)
             copy(reg("LM", 32, 48), reg("G2", 48, 64))
             copy(reg("OH", 32, 48), reg("G2", 32, 48))
-        send("m%d" % t)
+        else:
+            send("m%d" % t)
         offL, offM = reg("LM", 0, 16), reg("LM", 16, 32)
         v = reg("VY", 512 * s, 512 * s + 256)
         yk = reg("VY", 512 * s + 256, 512 * s + 512)
         if t < R - 1:
-            act(yk, reg("X", 0, wx, off=offL), AF.Copy)
+            act(yk, entries("X", t, offL), AF.Copy)
         else:
-            act(reg("TM"), reg("X", 0, wx, off=offL), AF.Relu, bias=63.0, scale=-1.0)
+            act(reg("TM"), entries("X", t, offL), AF.Relu, bias=63.0, scale=-1.0)
             act(yk, reg("TM"), bias=63.0, scale=-1.0)
-        act(reg("KB", 256, 512), bank(5, 0, 256), AF.Copy)
-        nrow = bank(1, 256, 512)
-        act(nrow, reg("IOX"), bias=float(wx))
-
-        def first_of(ebuf, key, kcol, flag, cnt):
-            o = 0
-            for h in range(16):
-                e = reg(ebuf, o, o + 256 - 16 * h)
-                ts(e, reg("KB", key + 16 * h, key + 256), bank(3, kcol + h, kcol + h + 1), OP.is_equal, flag(h), OP.mult)
-                mm(bank(cnt, 16 * h, 256), reg("BW", 128 * h, 128 * h + 128), e, False, h == 15)
-                o += 256 - 16 * h
-
-        def firsts(out, cnt, a):
-            tt(reg(out), bank(cnt, 0, 256), reg("THR"), OP.is_lt)
-            scan(a, reg("SL", 0, 256), reg(out), 0.0, OP.mult, OP.max)
-
-        first_of("EE", 0, 16, lambda h: bank(3, h, h + 1), 6)
-        mm(bank(2, 0, 256), BIG, reg("WK", 0, 256), True, False)
-        over, more, xm = [reg("TP", 256 * q, 256 * q + 256) for q in range(3)]
-        act(xm, reg(XF, 0, wx, off=offM), AF.Copy)
-        total(bank(4, 256, 512), [(IDB, yk), (NIDB, z)])
-        act(over, bank(4, 256, 512), AF.Relu)
-        total(bank(5, 256, 512), [(IDB, yk), (NIDB, xm), (NIDB, over)])
-        act(more, bank(5, 256, 512), AF.Relu)
-        total(bank(5, 0, 256), [(IDB, yk), (NIDB, over), (NIDB, more)])
-        act(v, bank(5, 0, 256), AF.Copy)
-        send("v%d" % t)
-        if t < R - 1:
-            act(zn, bank(4, 256, 512), AF.Abs)
-        total(bank(4, 256, 512), [(IDB, over), (IDB, more)])
-        act(reg("TM"), bank(4, 256, 512), AF.Copy)
-        if t < R - 1:
-            to_list(bank(4, 0, 16), "UW", "ZB", 256 * (1 - s), 256)
-        firsts("ST", 6, reg("NFK"))
-        mm(bank(2, 0, 256), NBIG, reg("ST"), False, False)
         if t >= 2:
-            ts(keep, bank(7, 0, 256), 512.0, OP.is_lt)
-            tt(reg("NB") if t < R - 1 else old, old, keep, OP.mult)
-        if t == 2:
-            copy(old, reg("NB"))
+            send("y%d" % t)
+            send("m%d" % t)
         if t < R - 1:
             send("at%d" % t)
+        act(reg("KB", 256, 512), bank(5, 0, 256), AF.Copy)
+        nrow = bank(1, 256, 512)
+        act(reg("NR"), reg("IOX"), bias=float(P * t))
+        for q, (lhs, rhs) in enumerate([(ID, reg("NR")), (ID3, reg("WK", 0, 256)), (BOM, reg("WK", 0, 256))]):
+            mm(nrow, lhs, rhs, q == 0, False)
+
+        def first_of(ebuf, key, kcol, rest, cnt):
+            e = [reg(ebuf, 264 * h - 8 * h * h, 264 * h - 8 * h * h + 256 - 16 * h) for h in range(16)]
+            for a, b in zip(BLOCKS, BLOCKS[1:]):
+                for h in range(a, b):
+                    ts(e[h], reg("KB", key + 16 * h, key + 256), col("HL", kcol + h), OP.subtract, rest(h), OP.is_equal)
+                for h in range(a, b):
+                    mm(bank(cnt, 16 * h, 256), reg("BW", 128 * h, 128 * h + 128), e[h], False, h == 15)
+                join(b - a)
+
+        tt(reg("TP"), entries("X", t, offL), z, OP.min)
+        first_of("EE", 0, 0, lambda h: col("HL", 64 + h), 6)
+        tt(v, entries(XF, t, offM), reg("TP"), OP.min)
+        send("v%d" % t)
+        mm(bank(2, 0, 256), BIG, reg("WK", 0, 256), True, False)
+        act(reg("TM"), v, AF.Copy, scale=-1.0)
+        if t < R - 1:
+            total(bank(4, 256, 512), [(ID, yk), (NID, z)])
+            act(zn, bank(4, 256, 512), AF.Abs)
+            to_list(bank(4, 0, 16), "UW", "ZB", 256 * (1 - s), 256)
+        tt(reg("ST"), bank(6, 0, 256), reg("THR"), OP.is_lt)
+        scan(reg("SL", 512, 768), reg("D0"), reg("ST"), -1024.0, OP.max, OP.subtract)
+        mm(bank(2, 0, 256), NBIG, reg("ST"), False, False)
+        if t >= 2:
+            act(reg("SK"), bank(7, 0, 256), AF.Sign, bias=1023.5, scale=-1.0)
+            total(bank(5, 256, 512), [(ID, old), (ID3, reg("SK"))])
+            act(old, bank(5, 256, 512), AF.Relu, bias=-3072.0)
+            if t == 2:
+                act(keep, reg("SK"), bias=0.5, scale=0.5)
+        if t < R - 1:
+            send("a%d" % t)
             for k in range(16):
-                act(reg("ZR", k, 4096, 16), zn, AF.Copy)
-        first_of("E2", 256, 32, lambda h: col("NFK", 16 * h + 15), 2)
-        tt(reg("DM", dm, dm + 32), reg("RV", rv + 16, rv + 48), reg("DUM"), OP.subtract)
-        firsts("BD", 2, reg("SL", 256, 512))
+                if k < ZACT[t + 1]:
+                    act(reg("ZR", k, 4096, 16), zn, AF.Copy)
+                else:
+                    copy(reg("ZR", k, 4096, 16), zn)
+        first_of("E2", 256, 16, lambda h: col("SL", 512 + 16 * h + 15), 2)
+        tt(reg("DM", dm, dm + 32), reg("RV", rv + 16, rv + 48), reg("DUM", 32, 64), OP.subtract)
+        tt(reg("BD"), bank(2, 0, 256), reg("THR"), OP.is_lt)
+        scan(reg("SL", 256, 512), reg("SL", 0, 256), reg("BD"), 0.0, OP.mult, OP.max)
         build, builds = bank(2, 256, 512), reg("SL", 256 + 15, 512, 16)
-        mm(build, BO, reg("BD"), True, True)
+        mm(nrow, BO3, reg("BD"), False, True)
+        total(bank(5, 256, 512), [(ID, v), (BO3, reg("BD"))])
+        act(built("X", t), bank(5, 256, 512), AF.Relu, bias=-3072.0)
+        if t < R - 1:
+            mm(build, BO, reg("BD"), True, True)
         tt(reg("G2", 0, 16), builds, reg("DM", dm + 16, dm + 32), OP.mult)
         tt(reg("G2", 16, 32), builds, reg("DM", dm, dm + 16), OP.mult)
-        tt(reg("G2", 0, 32), reg("G2", 0, 32), reg("DUM"), OP.add)
+        tt(reg("G2", 0, 32), reg("G2", 0, 32), reg("DUM", 0, 32), OP.add)
         copy(reg("OH", 0, 32), reg("G2", 0, 32))
         send("o%d" % t)
         arrive("m%d" % t)
         chosen, given = reg("LG", 32 * t, 32 * t + 16), reg("LG", 32 * t + 16, 32 * t + 32)
-        if t == 2:
-            copy(reg("OH", 48, 64), given)
-        if s == 0:
-            send("ao%d" % t)
-        tt(reg("MK"), reg("WK", 0, 256), build, OP.mult)
         if t < R - 1:
+            send("bo%d" % t)
             copy(reg("BI", 48, 64), bank(4, 0, 16))
             ts(reg("BI", 0, 16), reg("BI", 48, 64), 511, OP.bitwise_and)
             payee(t + 1)
 
         if t >= 2:
-            tt(C, C, keep, OP.mult)
-            tt(C, C, reg("PL", s, 512, 2), OP.max)
+            total(bank(4, 256, 512), [(ID, reg("PL16", 256 * s, 256 * s + 256)), (ID3, reg("SK")), (BO3, reg("WK", 0, 256))])
+            tt(C, C, bank(4, 256, 512), OP.min)
+        tt(C, C, nrow, OP.max)
         if t == 2:
             tt(reg("T2", 256, 512), reg("T2", 512, 768), keep, OP.mult)
         if t < R - 1:
+            tt(reg("MK"), reg("WK", 0, 256), build, OP.mult)
             tt(reg("T2", 0, 256), reg("MK"), dn, OP.mult)
-            base = [(NID, reg("NL"))] if t < 2 else [(ID, reg("N0")), (ID, reg("T2", 256, 512))]
+            base = [(ID, Nn)] if t < 2 else [(ID, reg("N0")), (ID, reg("T2", 256, 512))]
             total(bank(0, 256, 512), base + [(ID, reg("T2", 0, 256))])
             act(Nn, bank(0, 256, 512), AF.Copy)
-        tt(nrow, reg("MK"), nrow, OP.mult)
-        tt(C, C, nrow, OP.max)
         if t >= 2:
             act(reg("CO", s, 512, 2), C, AF.Copy)
         if t < R - 1:
             send("ta%d" % t)
+            send("tn%d" % t)
         else:
             dma("s", [(T.co[:], reg("CO"))])
 
         arrive("v%d" % t)
         fv, fw = reg("LV", LAND[t], LAND[t] + 256), reg("LV", LAND[t] + 256, LAND[t] + 512)
-        before, left, after = [reg("NV", 256 * q, 256 * q + 256) for q in range(3)]
         taken = reg("TV", 0, 256)
-        tt(reg("X", wx, wx + 256), v, build, OP.mult)
-        copy(reg("X", off=reg("OH", 16, 32)), reg("TM"))
-        act(before, reg("X", 0, wx, off=chosen), AF.Copy)
-        if t == R - 1:
-            act(after, before, AF.Relu, bias=-63.0)
-        total(bank(5, 0, 256), [(IDB, before), (NIDB, fv)] + [(NIDB, after)] * (t == R - 1))
-        act(left if t >= 2 else taken, bank(5, 0, 256), AF.Relu)
+        tt(places("X", t, reg("OH", 16, 32)), yk, reg("TM"), OP.add)
         if t >= 2:
-            for q, off, w in ((1, reg("OH", 32, 48), yk), (2, given, fw)):
-                held = reg("NV", 512 + 256 * q, 768 + 256 * q)
-                act(held, reg("X", off=off), AF.Copy)
-                tt(reg("X", off=off), held, w, OP.add)
-                if t < R - 1:
-                    total(bank(4, 256, 512), [(IDB, held), (IDB, w)])
-                    act(reg("TV", 256 * q, 256 * q + 256), bank(4, 256, 512), AF.Copy)
-                    send("b%d" % (t + q))
-            act(after, reg("X", 0, wx, off=chosen), AF.Copy)
-            total(bank(5, 0, 256), [(IDB, left), (NIDB, before), (IDB, after)])
-            if t == R - 1:
-                ts(reg("X", 0, wx - 512), reg("X", 0, wx - 512), 63.0, OP.min)
-            ts(taken, bank(5, 0, 256), 63.0, OP.min)
-        if t < R - 1:
-            send("b%d" % t)
+            arrive("y%d" % t)
+        settle("X", t, chosen, fv, [(reg("OH", 32, 48), yk), (given, fw)] if t >= 2 else [], "NV", taken, bank(5, 0, 256))
 
         for q in range(3):
             tt(reg("RC", 16 * q, 16 * q + 16), builds, reg("RV", rv + 16 * q, rv + 16 * q + 16), OP.mult)
         if t < R - 1:
             c2 = 256 * (1 - s)
-            home_names(512 + c2)
-            act(reg("CM", 0, 256), reg("TB", c2, c2 + 256), bias=-MID)
+            act(reg("CM", 0, 256), reg("TB", c2, c2 + 256), bias=-2 * MID, scale=2.0)
         ts(reg("RH"), reg("RC"), MID, OP.subtract)
         for j in range(16):
             mm(bank(6, j, 512, 16, p1=8), reg("ID", j, 128, 16), reg("RH", 0, 32), True, True)
+        join(16)
         for j in range(16):
             mm(bank(3, 256 + j, 512, 16, p1=8), reg("ID", j, 128, 16), reg("RH", 32, 48), True, True)
+        join(16)
         act(reg("RO", 0, 512, p1=8), bank(6, 0, 512, p1=8), bias=MID)
         act(reg("RO", 512, 768, p1=8), bank(3, 256, 512, p1=8), bias=MID)
         dma("s", [(T.rec[8 * q:8 * q + 8, P * t:P * t + P], reg("RO", 256 * q, 256 * q + 256, p1=8)) for q in range(3)])
@@ -855,10 +956,12 @@ def rank_program(g, core, T, topo):
             copy(reg("LO", 256 * s, 256 * s + 256), C)
         if s == 0:
             follow_home(t)
-        copy(reg("X", off=reg("LF", 16 * t, 16 * t + 16)), taken)
+        far_takes("X", t, chosen, reg("LF", 16 * t, 16 * t + 16), "NV", taken)
         if t == R - 1:
-            dma("s", [(T.xo[:, 0:1536], reg("X", 0, 1536))])
-            dma("a", [(T.xo[:, 1536:3072], reg("X", 1536, 3072))])
+            for q, (a, b) in enumerate(((2304, 3072), (0, 1152), (1152, 2304))):
+                if q:
+                    ts(reg("X", P + a, P + b), reg("X", P + a, P + b), 63.0, OP.min)
+                dma("sa"[q % 2], [(T.xo[:, a:b], reg("X", P + a, P + b))])
 
     emit(g, T, ops, queue)
 
@@ -884,7 +987,7 @@ def depend(ops):
             if "c" in last and (op["w"][0][4] or ops[last["c"]]["w"][0][4]):
                 need.add(last["c"])
             last["c"] = i
-        if e in "gs":
+        if e in "gs" or op["line"]:
             after |= {last[e]} if e in last else set()
             last[e] = i
         if e == "x":
@@ -911,49 +1014,295 @@ def depend(ops):
 
 
 def schedule(ops):
-    n = len(ops)
-    busy = [op["busy"] for op in ops]
-    pred, succ = [[] for _ in range(n)], [[] for _ in range(n)]
+    n, paces = len(ops), range(len(PACES))
+    eng = ["vapgsx".index(op["e"]) for op in ops]
+    busy = [[op["busy"][k] for op in ops] for k in paces]
+    legs = [op["legs"] for op in ops]
+    source = [6 + i if op["sem"] else eng[i] for i, op in enumerate(ops)]
+    waits, done = [], []
     for i, op in enumerate(ops):
-        edges = [(j, max(busy[j], ops[j]["lands"] if ops[j]["e"] != "x" else 0.0) + WAKE) for j in op["need"]]
-        edges += [(j, op["lands"] if op["e"] == "x" else busy[j]) for j in op["after"] - op["need"]]
-        for j, d in edges:
-            pred[i].append((j, d))
-            succ[j].append((i, d + busy[i] - busy[j]))
+        implied = 0
+        for j in op["need"] | op["after"]:
+            implied |= done[j]
+        done.append(implied | sum(1 << j for j in op["need"] | op["after"] if j in op["need"] or not ops[j]["sem"]))
+        waits.append([(j, int(j not in op["need"])) for j in sorted(op["need"] | op["after"]) if not implied >> j & 1])
+    later, succ, tip = [[] for _ in range(n)], [set() for _ in range(n)], {}
+    for i in range(n):
+        for j, follow in waits[i]:
+            later[j].append((i, follow))
+            succ[j].add(i)
 
-    def place(order, before, first):
-        start, taken = [0.0] * n, {e: [] for e in "vapgsx"}
-        for i in order:
-            t = max([first[i]] + [start[j] + d for j, d in before[i]])
-            slots = taken[ops[i]["e"]]
-            q = len(slots)
-            while q and slots[q - 1][1] > t:
-                q -= 1
-            while q < len(slots) and t + busy[i] > slots[q][0]:
-                t = max(t, slots[q][1])
-                q += 1
-            slots.insert(q, (t, t + busy[i]))
-            start[i] = t
-        return start
-
-    tail = [max(0.0, op["lands"] - op["busy"]) if op["e"] != "x" else 0.0 for op in ops]
-    start = place(range(n), pred, [0.0] * n)
-    for last in [False] * (PASSES - 1) + [True]:
-        back = place(sorted(range(n), key=lambda i: (-start[i] - busy[i], -i)), succ, tail)
-        end = max(back[i] + busy[i] for i in range(n))
-        room = [max(0.0, end - back[i] - busy[i] - start[i]) for i in range(n)]
-        late = [start[i] + (min(SLACK, room[i]) if ops[i]["e"] == "x" else min(400.0, room[i] / 2)) if last and ops[i]["e"] in "xpva" else 0.0 for i in range(n)]
-        due = [-back[i] - busy[i] - ops[i]["ahead"] for i in range(n)]
-        for i in reversed(range(n)):
+    def build(mix, slack, room_share):
+        blend = lambda f: sum(w * f(k) for k, w in enumerate(mix))
+        hold = [blend(lambda k: starts[k][2][i]) for i in range(n)]
+        pred = [[(j, blend(lambda k: gap(j, i, follow, k))) for j, follow in waits[i]] for i in range(n)]
+        post = [[] for _ in range(n)]
+        for i in range(n):
             for j, d in pred[i]:
-                due[j] = min(due[j], due[i] - d)
-        start = place(sorted(range(n), key=lambda i: (due[i], i)), pred, late)
-    return sorted(range(n), key=lambda i: (start[i], i))
+                post[j].append((i, d + hold[i] - hold[j]))
+
+        def place(seq, before, first):
+            start, taken = [0.0] * n, [[] for _ in range(6)]
+            for i in seq:
+                t = max([first[i]] + [start[j] + d for j, d in before[i]])
+                slots = taken[eng[i]]
+                q = len(slots)
+                while q and slots[q - 1][1] > t:
+                    q -= 1
+                while q < len(slots) and t + hold[i] > slots[q][0]:
+                    t = max(t, slots[q][1])
+                    q += 1
+                slots.insert(q, (t, t + hold[i]))
+                start[i] = t
+            return start
+
+        tail = [blend(lambda k: starts[k][1][i] - starts[k][0][i]) - hold[i] for i in range(n)]
+        start = place(order, pred, [0.0] * n)
+        for last in (False, True):
+            back = place(sorted(range(n), key=lambda i: (-start[i] - hold[i], -i)), post, tail)
+            end = max(back[i] + hold[i] for i in range(n))
+            room = [max(0.0, end - back[i] - hold[i] - start[i]) for i in range(n)]
+            late = [start[i] + (min(slack, room[i]) if eng[i] == 5 else min(room_share, room[i] / 2)) if last and eng[i] not in (3, 4) else 0.0 for i in range(n)]
+            due = [-back[i] - hold[i] - ops[i]["ahead"] for i in range(n)]
+            for i in reversed(range(n)):
+                for j, d in pred[i]:
+                    due[j] = min(due[j], due[i] - d)
+            start = place(sorted(range(n), key=lambda i: (due[i], i)), pred, late)
+        return sorted(range(n), key=lambda i: (start[i], i))
+
+    def again(e, mix):
+        blend = lambda f: sum(w * f(k) for k, w in enumerate(mix))
+        hold = [blend(lambda k: starts[k][2][i]) for i in range(n)]
+        post, count, last = [[] for _ in range(n)], [0] * n, {}
+        for i in order:
+            arcs = [(j, blend(lambda k: gap(j, i, follow, k))) for j, follow in waits[i]]
+            if eng[i] not in (e, 5):
+                arcs += [(last[eng[i]], hold[last[eng[i]]])] if eng[i] in last else []
+                last[eng[i]] = i
+            count[i] = len(arcs)
+            for j, d in arcs:
+                post[j].append((i, d))
+        tail = [0.0] * n
+        for j in reversed(order):
+            tail[j] = max([blend(lambda k: starts[k][1][j] - starts[k][0][j])] + [d + tail[i] for i, d in post[j]])
+        start, seq, ready, can, t = [0.0] * n, [], [i for i in range(n) if not count[i]], [], 0.0
+        while ready or can:
+            if not ready:
+                now = max(t, min(start[i] for i in can))
+                i = max((q for q in can if start[q] <= now), key=lambda q: tail[q])
+                soon = [q for q in can if now < start[q] < now + hold[i] and
+                        max(start[q] + tail[q], start[q] + hold[q] + tail[i]) < max(now + tail[i], now + hold[i] + tail[q])]
+                if soon:
+                    urgent = max(soon, key=lambda q: tail[q])
+                    fits = [q for q in can if max(now, start[q]) + hold[q] <= start[urgent]]
+                    i = max(fits, key=lambda q: tail[q]) if fits else urgent
+                can.remove(i)
+                start[i] = max(start[i], t)
+                t = start[i] + hold[i]
+            else:
+                i = ready.pop()
+                if eng[i] == e:
+                    can.append(i)
+                    continue
+            seq.append(i)
+            for q, d in post[i]:
+                start[q] = max(start[q], start[i] + d)
+                count[q] -= 1
+                if not count[q]:
+                    ready.append(q)
+        rank = {q: a for a, q in enumerate(seq)}
+        return sorted(range(n), key=lambda q: (start[q], rank[q]))
+
+    def fly(i, t, m, at):
+        def leg(core, engs, rows, size, die, t0):
+            free, a, b = at.setdefault(("engines", core), [0.0] * 16), engs[0], engs[-1] + 1
+            end = max(t0, max(free[a:b])) + max(1, rows // (b - a)) * (m["row"] + m["byte"] * size)
+            free[a:b] = [end] * (b - a)
+            if die is not None:
+                at["port", die] = max(t0, at.get(("port", die), 0.0)) + rows * size * m["port"]
+                end = max(end, at["port", die])
+            return end
+
+        def begin(core, t0):
+            t0 += m["start"] + (0.0 if core in at else m["first"])
+            at.setdefault(core, 0.0)
+            return t0
+        t0, left, on = begin(None, t) if eng[i] == 3 else t + m["load"], t, {}
+        for name, engs, rows, size, c, second, die in legs[i]:
+            end = leg(None, engs, rows, size, None if c else die, t0)
+            left = max(left, end)
+            if c:
+                on.setdefault((name, c), []).append((end, second, size, die))
+            else:
+                at[name] = max(at.get(name, 0.0), end)
+        for (name, c), parts in on.items():
+            t1 = max([at.get(c, 0.0)] + [p[0] + m["wake"] for p in parts])
+            t2 = begin(c, t1)
+            at[c] = t1 + m["issue"]
+            at[name] = max([at.get(name, 0.0)] + [leg(c, p[1], 128, p[2], p[3], t2) for p in parts])
+        return left
+
+    def run(seq, k):
+        start, end, hold = [0.0] * n, [0.0] * n, list(busy[k])
+        free, m, air, cover = [0.0] * 6, PACES[k], {}, [[-1.0] * (n + 6) for _ in range(5)]
+        wake, cost = m["wake"], m["wait"]
+        for i in seq:
+            e = eng[i]
+            if e == 5:
+                start[i] = end[i] = air[ops[i]["sem"][0][4:]]
+                continue
+            t, seen = free[e], cover[e]
+            for j, follow in waits[i]:
+                if follow:
+                    d = start[j] + hold[j]
+                else:
+                    d = end[j]
+                    if d > seen[source[j]]:
+                        seen[source[j]] = max(d, t - MARGIN)
+                        hold[i] += cost
+                    d += wake
+                if d > t:
+                    t = d
+            start[i] = t
+            free[e] = end[i] = t + hold[i]
+            end[i] = fly(i, end[i] - busy[k][i], m, air) if legs[i] else end[i] + DRAIN[e]
+        return start, end, hold
+
+    def worth(starts):
+        return sum((max(starts[k][1]) + 0.01 * sum(starts[k][0]) / n) / scale[k] for k in paces)
+
+    def held(seq, times, k):
+        (start, end, hold), before, last = times, {}, {}
+        for i in seq:
+            before[i] = last.get(eng[i])
+            last[eng[i]] = i
+        i, out = max(range(n), key=lambda q: end[q]), []
+        while start[i] > 0.0:
+            j = before[i]
+            if j is not None and eng[i] != 5 and start[j] + hold[j] >= start[i] - 1e-6:
+                out.append((i, j))
+                i = j
+            else:
+                i = max(waits[i], key=lambda q: start[q[0]] + hold[q[0]] if q[1] else end[q[0]] + PACES[k]["wake"])[0]
+        return out, before
+
+    def moved(seq, place, i, j):
+        a, b = place[j], place[i]
+        up = {i}
+        for q in reversed(seq[a:b]):
+            if succ[q] & up:
+                if q == j:
+                    return None
+                up.add(q)
+        part = seq[a:b + 1]
+        return [q for q in part if q in up] + [q for q in part if q not in up]
+
+    def delayed(seq, place, i, j):
+        a, b = place[j], place[i]
+        down, hit = {j}, set(succ[j])
+        for q in seq[a + 1:b + 1]:
+            if q in hit:
+                if q == i:
+                    return None
+                down.add(q)
+                hit |= succ[q]
+        part = seq[a:b + 1]
+        return [q for q in part if q not in down] + [q for q in part if q in down]
+
+    def gap(j, i, follow, k):
+        start, end, hold = starts[k]
+        return start[i] - start[j] if eng[i] == 5 else hold[j] if follow else end[j] - start[j] + PACES[k]["wake"]
+
+    def rest(k):
+        start, end, hold = starts[k]
+        out = [0.0] * n
+        for j in reversed(order):
+            t = end[j] - start[j]
+            if eng[j] != 5 and j in behind:
+                t = max(t, hold[j] + out[behind[j]])
+            for i, follow in later[j]:
+                t = max(t, gap(j, i, follow, k) + out[i])
+            out[j] = t
+        return out
+
+    def through(part, a, b, k):
+        start, head, free, longest = starts[k][0], {}, {}, 0.0
+        for i in order[a:b + 1]:
+            if eng[i] not in free:
+                j = before[i]
+                free[eng[i]] = start[j] + starts[k][2][j] if j is not None else 0.0
+            tip[eng[i]] = behind.get(i)
+        for i in part:
+            t = free[eng[i]] if eng[i] != 5 else 0.0
+            for j, follow in waits[i]:
+                t = max(t, head.get(j, start[j]) + gap(j, i, follow, k))
+            head[i] = t
+            free[eng[i]] = t + starts[k][2][i]
+            for q, follow in later[i]:
+                if place[q] > b:
+                    longest = max(longest, t + gap(i, q, follow, k) + tails[k][q])
+            longest = max(longest, t + starts[k][1][i] - start[i])
+        for e in free:
+            if e != 5 and tip[e] is not None:
+                longest = max(longest, free[e] + tails[k][tip[e]])
+        return longest + 0.002 * sum(head.values()) - 0.002 * sum(start[i] for i in part)
+
+    order = list(range(n))
+    starts = [run(order, k) for k in paces]
+    order = build(MIXES[0][0], 0.0, 0.0)
+    starts = [run(order, k) for k in paces]
+    scale = [max(s[1]) for s in starts]
+    best, seed, fresh = worth(starts), 1, True
+    for mix in MIXES:
+        seq = build(*mix)
+        new = [run(seq, k) for k in paces]
+        if worth(new) < best:
+            order, starts, best = seq, new, worth(new)
+    kept = (order, starts)
+    for e in TURNS:
+        order = again(e, MIXES[0][0])
+        starts = [run(order, k) for k in paces]
+        if worth(starts) < best:
+            kept, best = (order, starts), worth(starts)
+    order, starts = kept
+    now = best
+    for turn in range(TRIES):
+        allow = LOOSE * max(0.0, 1.0 - 1.3 * turn / TRIES)
+        if fresh:
+            place = {q: a for a, q in enumerate(order)}
+            chains = [held(order, starts[k], k) for k in paces]
+            before, pairs, fresh = chains[0][1], [p for c in chains for p in c[0]], False
+            behind = {j: i for i, j in before.items()}
+            tails = [rest(k) for k in paces]
+        seed = (seed * 1103515245 + 12345) % 2 ** 31
+        i, j = pairs[(seed >> 8) % len(pairs)]
+        steps = (seed >> 4) % (4, 16, 64)[seed % 3]
+        if seed >> 20 & 1:
+            for _ in range(steps):
+                j = before[j] if before[j] is not None else j
+            seq = moved(order, place, i, j)
+        else:
+            for _ in range(steps):
+                i = behind.get(i, i)
+            seq = delayed(order, place, i, j)
+        a, b = place[j], place[i]
+        if seq is not None and sum((through(seq, a, b, k) - through(order[a:b + 1], a, b, k)) / scale[k] for k in paces) < allow - 1e-7:
+            seq = order[:a] + seq + order[b + 1:]
+            new = [run(seq, k) for k in paces]
+            w = worth(new)
+            if w < now + allow:
+                order, starts, now, fresh = seq, new, w, True
+                if w < best:
+                    kept, best = (order, starts), w
+    order, starts = kept
+    return order, starts
 
 
 def emit(g, T, program, queue):
     depend(program)
-    order = schedule(program)
+    if "calls" not in ORDER:
+        ORDER["calls"] = schedule(program)
+    order, times = ORDER["calls"]
     place = {j: i for i, j in enumerate(order)}
     ops = [program[j] for j in order]
     n = len(ops)
@@ -962,13 +1311,15 @@ def emit(g, T, program, queue):
     known = {e: {} for e in queue}
     marked = [False] * n
     key = lambda j: ops[j]["sem"][0] if ops[j]["sem"] else ops[j]["e"]
+    wanted = {(e, f): sorted({place[j] for op in ops if op["e"] == e for j in op["need"] if key(place[j]) == f}) for e in queue for f in ENG_SEM}
     for i, op in enumerate(ops):
         e = op["e"]
         if e != "x":
             for j in sorted((place[j] for j in op["need"]), reverse=True):
                 if known[e].get(key(j), -1) >= j:
                     continue
-                waits[i].append(j)
+                j = max([j] + [q for q in wanted.get((e, key(j)), []) if j < q < i and all(end[order[q]] + MARGIN <= start[order[i]] for start, end, hold in times)])
+                waits[i].insert(0, j)
                 marked[j] = True
                 for k, val in clock[j].items():
                     if known[e].get(k, -1) < val:

@@ -4,69 +4,75 @@ from concourse.mybir import AluOpType, AxisListType, ActivationFunctionType
 OP = AluOpType
 AF = ActivationFunctionType
 NR, W0, P, R = 4, 2048, 256, 4
+BLK = 128 // NR
 WT = [1, 64, 5, 83, 17, 131, 29, 211, 43, 157, 61, 239, 71, 113, 97, 199]
 XW = 3328
-PIECE = 704
 MID = 1536.0
-SHARE = [(64, 64, 32, 0)] * 4
-HELPED = [(3, 5, 7)] * 4
-HALVES = (1, 3)
+GATE, FLOOR = 8192.0, -3200.0
+MIDP = 1664.0
+XQW, BQW = (W0 + 3 * P) // 4, 248
+SHARE = [(0, 0, 96, 64)] * 4
+HELPED = [(5, 7)] * 4
 BWACT = 10
 BLOCKS = (0, 2, 4, 6, 8, 11, 14, 16)
-NAMES = [("a", 0, 128), ("v", 384, 512), ("a", 128, 256), ("v", 304, 384), ("a", 256, 304)]
-ZACT = (2, 16, 16, 16)
+ZBY = ("vvavvavvavvavvav", "a" * 16, "a" * 16, "a" * 16)
+ENDS = ((0, 1152), (1152, 2304))
 
 F, H16, B16, I32, U16 = "float32", "float16", "bfloat16", "int32", "uint16"
 SCRATCH = {
-    "X": ("sbuf", [128, XW], B16), "XF0": ("sbuf", [128, XW], B16), "XF1": ("sbuf", [128, XW], B16),
-    "LH": ("sbuf", [128, 768], B16), "LN": ("sbuf", [128, 1024], B16), "LB": ("sbuf", [128, 192], U16), "TV": ("sbuf", [128, 512], B16),
-    "LW": ("sbuf", [128, 1024], B16), "LK": ("sbuf", [128, 96], U16), "NW": ("sbuf", [128, 1280], B16),
-    "NV": ("sbuf", [128, 1280], B16), "TP": ("sbuf", [128, 256], B16), "HL": ("sbuf", [128, 96], B16), "K1": ("sbuf", [128, 32], F),
-    "TB": ("sbuf", [128, 512], F), "TF0": ("sbuf", [128, 512], F), "TF1": ("sbuf", [128, 512], F),
-    "TN": ("sbuf", [128, 512], B16), "NF0": ("sbuf", [128, 512], B16), "NF1": ("sbuf", [128, 512], B16),
-    "PL16": ("sbuf", [128, 512], H16), "NR": ("sbuf", [128, 256], H16), "SK": ("sbuf", [128, 256], B16), "D0": ("sbuf", [128, 256], B16),
-    "PL": ("sbuf", [128, 512], I32), "FR": ("sbuf", [128, 128], I32), "FR16": ("sbuf", [128, 128], H16),
+    "X": ("sbuf", [128, XW], B16), "XO": ("sbuf", [128, XW], B16),
+    "XP": ("sbuf", [128, 2048], B16), "XL": ("sbuf", [128, 1536], B16), "PK": ("sbuf", [128, 432], H16), "PA": ("sbuf", [128, 432], H16),
+    "ZS": ("sbuf", [128, 256], B16), "ZL": ("sbuf", [128, 192], B16), "NN": ("sbuf", [128, 512], B16), "NK": ("sbuf", [128, 512], B16), "NL": ("sbuf", [128, 384], B16),
+    "XQ": ("sbuf", [128, 3 * XQW], B16), "XK": ("sbuf", [128, 3 * XQW], B16),
+    "BG": ("sbuf", [128, 4 * BQW], H16), "BQ": ("sbuf", [128, 3 * BQW], H16), "BL": ("sbuf", [128, 3 * BQW], H16), "BN": ("sbuf", [128, 4 * BQW], H16),
+    "RS": ("sbuf", [128, 128], H16), "RL": ("sbuf", [128, 240], H16), "VL": ("sbuf", [128, 768], B16),
+    "UK": ("sbuf", [128, 144], H16), "FS": ("sbuf", [128, 16], B16), "FA": ("sbuf", [128, 48], B16),
+    "PL": ("sbuf", [128, 528], I32), "PN": ("sbuf", [128, 528], H16), "LN": ("sbuf", [128, 512], U16),
+    "TP": ("sbuf", [128, 256], B16), "HL": ("sbuf", [128, 96], B16), "K1": ("sbuf", [128, 32], F),
+    "TB": ("sbuf", [128, 512], F), "TN": ("sbuf", [128, 512], B16),
+    "PL16": ("sbuf", [128, 256], H16), "NR": ("sbuf", [128, 256], H16), "SK": ("sbuf", [128, 512], B16), "D0": ("sbuf", [128, 256], B16),
+    "FR": ("sbuf", [128, 128], I32), "FR16": ("sbuf", [128, 128], H16),
     "FW": ("sbuf", [128, 2048], F), "NG": ("sbuf", [128, 4096], H16), "N0": ("sbuf", [128, 256], H16),
-    "MY": ("sbuf", [128, 4096], H16), "MH": ("sbuf", [128, 4096], H16), "ZR": ("sbuf", [128, 4096], B16),
+    "MY": ("sbuf", [128, 4096], H16), "MH": ("sbuf", [128, 4096], H16), "ZR": ("sbuf", [128, 4096], B16), "ZF": ("sbuf", [128, 4096], B16),
     "ZB": ("sbuf", [128, 512], B16),
-    "LO": ("sbuf", [128, 512], U16), "LC": ("sbuf", [128, 768], U16), "MO": ("sbuf", [128, 256], U16), "BO16": ("sbuf", [128, 16], U16),
+    "LO": ("sbuf", [128, 512], U16), "MO": ("sbuf", [128, 256], U16), "BO16": ("sbuf", [128, 16], U16),
     "BI": ("sbuf", [128, 64], I32), "BH": ("sbuf", [128, 16], H16),
     "CM": ("sbuf", [128, 768], H16),
-    "TS": ("sbuf", [128, 512], H16), "FH": ("sbuf", [128, 512], H16), "NS": ("sbuf", [128, 512], H16), "PM": ("sbuf", [128, 512], H16),
+    "TS": ("sbuf", [128, 512], H16), "FH": ("sbuf", [128, 512], H16), "NS": ("sbuf", [128, 512], H16), "PM": ("sbuf", [128, 768], H16),
     "YG": ("sbuf", [128, 8192], B16), "SN": ("sbuf", [128, 1024], H16), "SC": ("sbuf", [128, 1024], H16), "SF": ("sbuf", [128, 64], H16),
     "R0": ("sbuf", [128, 1024], H16), "IA": ("sbuf", [128, 704], B16), "TIE": ("sbuf", [2, 576], F),
-    "NFK": ("sbuf", [128, 256], F), "KI": ("sbuf", [128, 48], I32), "PD": ("sbuf", [128, 24], B16), "PS": ("sbuf", [128, 8], F),
-    "RR": ("sbuf", [128, 2048], F), "AB": ("sbuf", [128, 4096], F), "VA": ("sbuf", [128, 32], H16), "FL": ("sbuf", [128, 16], B16), "FL32": ("sbuf", [128, 16], F),
+    "NFK": ("sbuf", [128, 256], F), "KI": ("sbuf", [128, 64], I32), "PD": ("sbuf", [128, 24], B16), "PS": ("sbuf", [128, 16], F),
+    "RR": ("sbuf", [128, 2048], F), "AB": ("sbuf", [128, 4096], F), "VA": ("sbuf", [128, 112], H16), "FL": ("sbuf", [128, 16], B16), "FL32": ("sbuf", [128, 16], F),
     "BB": ("sbuf", [128, 256], B16), "BW": ("sbuf", [128, 2048], B16), "SL": ("sbuf", [128, 768], B16),
     "VT": ("sbuf", [128, 128], H16), "WK": ("sbuf", [128, 1024], H16), "KB": ("sbuf", [128, 512], H16),
-    "LM": ("sbuf", [128, 48], U16), "EE": ("sbuf", [128, 2176], B16), "E2": ("sbuf", [128, 2176], B16),
+    "LM": ("sbuf", [128, 64], U16), "EE": ("sbuf", [128, 2176], B16), "E2": ("sbuf", [128, 2176], B16),
     "ST": ("sbuf", [128, 256], B16), "BD": ("sbuf", [128, 256], B16),
-    "VY": ("sbuf", [128, 1024], B16), "TM": ("sbuf", [128, 256], B16),
-    "RV": ("sbuf", [128, 96], F), "DM": ("sbuf", [128, 128], F), "G2": ("sbuf", [128, 96], F),
-    "OH": ("sbuf", [128, 64], U16),
-    "LV": ("sbuf", [128, 2048], B16), "LF": ("sbuf", [128, 64], U16), "LG": ("sbuf", [128, 128], U16),
-    "RC": ("sbuf", [128, 48], F), "RH": ("sbuf", [128, 48], H16), "RO": ("sbuf", [8, 768], F),
-    "T2": ("sbuf", [128, 768], H16), "MK": ("sbuf", [128, 256], H16),
+    "VY": ("sbuf", [128, 1024], B16), "NV": ("sbuf", [128, 2560], B16),
+    "RV": ("sbuf", [128, 160], F), "DM": ("sbuf", [128, 64], F), "G2": ("sbuf", [128, 64], F), "GH": ("sbuf", [128, 16], H16),
+    "OH": ("sbuf", [128, 160], U16), "FB": ("sbuf", [128, 16], B16),
+    "RC": ("sbuf", [128, 48], F), "RO": ("sbuf", [24, 1024], F),
+    "T2": ("sbuf", [128, 512], H16), "MK": ("sbuf", [128, 256], H16),
     "CO": ("sbuf", [128, 512], F),
     "PI": ("sbuf", [128, 16], I32), "PC": ("sbuf", [128, 16], B16),
-    "IOX": ("sbuf", [128, 256], B16), "IOA": ("sbuf", [128, 512], B16), "IOB": ("sbuf", [128, 256], B16),
-    "RK": ("sbuf", [128, 512], H16), "ID": ("sbuf", [128, 384], H16), "RAMP": ("sbuf", [128, 32], B16),
-    "U1": ("sbuf", [128, 144], H16), "UW": ("sbuf", [128, 144], B16),
+    "IOX": ("sbuf", [128, 256], B16), "IOA": ("sbuf", [128, 384], B16), "IOB": ("sbuf", [128, 256], B16), "IOK": ("sbuf", [128, 128], B16),
+    "RK": ("sbuf", [128, 1024], B16), "DIAG": ("sbuf", [128, 256], B16), "ID": ("sbuf", [128, 640], H16), "RAMP": ("sbuf", [128, 32], F),
+    "SE": ("sbuf", [128, 1024], H16), "IZ": ("sbuf", [128, 640], B16), "ONE": ("sbuf", [128, 256], B16),
+    "U1": ("sbuf", [128, 240], H16), "UW": ("sbuf", [128, 240], B16),
     "BK": ("sbuf", [128, 384], H16), "SJ": ("sbuf", [128, 2048], H16), "DG": ("sbuf", [128, 16], B16),
     "WR": ("sbuf", [128, 32], F), "WC": ("sbuf", [128, 4], F), "SG": ("sbuf", [128, 512], F),
-    "THR": ("sbuf", [128, 256], F), "DUM": ("sbuf", [128, 64], F),
+    "THR": ("sbuf", [128, 256], F), "DUM": ("sbuf", [128, 80], F),
 }
 for _b in range(8):
     SCRATCH["P%d" % _b] = ("psum", [128, 512], F)
 
-MSGS = ["c0", "h0", "h1", "n0", "u1", "l1"] + [m + str(t) for m in ("v", "m", "o") for t in range(R)] + \
-       ["x1", "x2", "x3", "tb0", "tb1", "y2", "y3", "yw2"] + \
-       [m + str(t) for m in ("a", "at", "ao", "bo", "k", "w", "ta", "tn") for t in range(R - 1)]
-NDMA = 16
-SEMAPHORES = ["sv", "sa", "sp", "sg"] + ["d%d" % i for i in range(NDMA)] + \
-             ["arr_" + m for m in MSGS] + ["snt_" + m for m in MSGS]
+MSGS = [("z", "ZS", 0, "ZL", 0, 64, True, ("near", 0, "far", 0)), ("p", "PK", 0, "PA", 0, 144, True, ("near", 0, "far", 0)),
+        ("x", "XP", 0, "XL", 0, 512, True, ("near", 0, "far", 0)), ("n", "NK", 0, "NL", 0, 128, True, ("near", 0, "far", 0)),
+        ("xo", "XQ", 0, "XK", 0, XQW, True, ("near", 0, "far", 0)), ("b", "BQ", 0, "BL", 0, BQW, True, ("near", 0, "far", 0)),
+        ("r", "RS", 0, "RL", 0, 80, False, ("near", 0, "far", 0)),
+        ("v", "VY", 0, "VL", 0, 256, False, ("near", 0, "far", 0)), ("f", "FS", 0, "FA", 0, 16, False, ("near", 0, "far", 0))]
+NDMA = 32
+SEMAPHORES = ["sv", "sa", "sp", "sg"] + ["d%d" % i for i in range(NDMA)] + [k + m[0] for m in MSGS for k in ("arr_", "ard_", "snt_", "snd_")]
 ENG_SEM = {"v": "sv", "a": "sa", "p": "sp", "g": "sg"}
-LAND = [0, 512, 1024, 1536]
 PACES = [{"cycle": 0.85, "gather": 1.56, "scatter": 3.8, "wake": 170.0, "wait": 15.0, "issue": 350.0, "start": 1700.0, "row": 40.0, "byte": 0.055, "port": 0.013, "first": 3200.0, "load": 1500.0},
          {"cycle": 1.18, "gather": 1.9, "scatter": 5.0, "wake": 130.0, "wait": 25.0, "issue": 320.0, "start": 1600.0, "row": 30.0, "byte": 0.05, "port": 0.015, "first": 3000.0, "load": 1500.0},
          {"cycle": 0.98, "gather": 1.3, "scatter": 3.0, "wake": 220.0, "wait": 20.0, "issue": 500.0, "start": 2900.0, "row": 65.0, "byte": 0.08, "port": 0.022, "first": 4500.0, "load": 2000.0},
@@ -75,8 +81,14 @@ DRAIN = [0.0, 120.0, 60.0, 0.0, 0.0]
 MARGIN = 900.0
 MIXES = [(mix, slack, room) for room, slack in ((0.0, 0.0), (200.0, 1000.0)) for mix in ((0.3, 0.3, 0.2, 0.2), (0.3, 0.4, 0.15, 0.15))]
 TURNS = [0, 1, 2] * 3
-TRIES, LOOSE = 20000, 0.0
+TRIES, LOOSE = 30000, 0.0
+TAIL = ((0, 1), (2,), (3,), "a", "a")
+PICK = "vp"
+LANDING = 3000.0
+LATER = 0.0
+NAMING = 4000.0
 EARLY = 9000.0
+LINE = "va"
 ORDER = {}
 
 
@@ -139,72 +151,19 @@ def parts_of(nh, nf):
     return [p for p in ([(nh, 2, -1), (nf, -2, 3)] if nf <= nh else [(nf, 2, 1), (nh, -2, 1)]) if p[0]]
 
 
-def routes(T, topo, src, dst, mode):
-    other = T.cores[(T.rank_of(src) + 1) % NR]
-    ports = [c for c in topo.cores_of(src) if T.rank_of(c) is None and topo.may_write(c, dst) and topo.may_write(c, other)]
-    near = [c for c in ports if topo.die(c) == topo.die(src)]
-    far = [c for c in ports if topo.die(c) != topo.die(src)]
-    if topo.may_write(src, dst):
-        near = [None, None]
-    return {"near": near[:2], "near1": near[:1], "near2": near[1:2], "far1": far[:1], "far2": far[1:2], "far": far[:2], "all": near[:2] + far[:2]}[mode]
-
-
-def messages(T, topo):
-    ms = []
-
-    def xship(t):
-        w = (W0 + P * max(t - 1, 0)) // 4
-        xf = "XF%d" % (t % 2)
-        return ("x%d" % t, -1 - t % 2, "all",
-                [(reg("X", P + j * w, P + (j + 1) * w), reg("X", t * PIECE, t * PIECE + w), reg(xf, P + j * w, P + (j + 1) * w)) for j in range(4)])
-
-    def tab(name, step, mode, lists, names):
-        pieces = []
-        for own, far, stage, cols in (("TB", "TF", "FW", lists), ("TN", "NF", "YG", names)):
-            for c, w in cols:
-                pieces.append((reg(own, c, c + w), reg(stage, staged[stage], staged[stage] + w), reg(far + str(-step - 1), c, c + w)))
-                staged[stage] += w
-        return (name, step, mode, pieces)
-
-    def plain(name, step, mode, pairs):
-        return (name, step, mode, [(a, b, b) for a, b in pairs])
-
-    staged, quarters = {"FW": 0, "YG": 0}, [(128 * q, 128) for q in range(4)]
-    ms.append(plain("c0", -1, "all", [(reg("LO", c, c + w), reg("LC", c, c + w)) for c, w in quarters]))
-    for h in range(2):
-        cols = [2 * P + 4 * P * h + P * j for j in range(-1, 3)]
-        ms.append(("h%d" % h, -1, "all", [(reg("X", c, c + P), reg("X", P * h, P * h + P), reg("XF0", c, c + P)) for c in cols]))
-    ms += [tab("n0", -1, "all", [], quarters), tab("u1", -2, "far1", [], [(256, 256)]),
-           plain("l1", -2, "far2", [(reg("LO", 256, 512), reg("LC", 512, 768))]), xship(1)]
-    for t in range(R):
-        s, wx = t % 2, W0 + P * t
-        n = 16 if t < 2 else 32
-        v, y, l0 = reg("VY", 512 * s, 512 * s + 256), reg("VY", 512 * s + 256, 512 * s + 512), LAND[t]
-        chosen = [plain("m%d" % t, 1 + s, "near1", [(reg("LM", 16, 16 + n), reg("LG", 32 * t, 32 * t + n))])]
-        if t < R - 1:
-            chosen.append(plain("k%d" % t, 2 * s - 1, "near2", [(reg("LM", 16, 16 + n), reg("LK", 32 * t, 32 * t + n))]))
-        if t >= 2:
-            ms.append(plain("y%d" % t, 1 + s, "near1" if s else "far1", [(y, reg("LV", l0 + 256, l0 + 512))]))
-        if t == 2:
-            ms.append(plain("yw2", 2 * s - 1, "far2", [(y, reg("LW", 768, 1024))]))
-        ms += chosen
-        if t < R - 1:
-            ms.append(plain("at%d" % t, s - 2, "near1", [(y, reg("LH", 256 * t, 256 * t + 256))]))
-        ms.append(plain("v%d" % t, 1 + s, "near1", [(v, reg("LV", l0, l0 + 256))]))
-        if t < R - 1:
-            ms.append(plain("w%d" % t, 2 * s - 1, "near2", [(v, reg("LW", 256 * t, 256 * t + 256))]))
-            ms.append(plain("a%d" % t, s - 2, "far1" if s else "near1", [(reg("TM"), reg("LN", 256 * t, 256 * t + 256))]))
-        ms.append(plain("o%d" % t, 1 + s, "near1" if s else "far1", [(reg("OH", 0, 16), reg("LF", 16 * t, 16 * t + 16))]))
-        if t == R - 1:
-            break
-        ms.append(plain("ao%d" % t, s - 2, "near2", [(reg("OH", 16, 16 + n), reg("LB", 64 * t, 64 * t + n))]))
-        ms.append(plain("bo%d" % t, 2 * s - 1, "far2" if s else "near1", [(reg("OH", 0, n), reg("LB", 64 * t + 32, 64 * t + 32 + n))]))
-        ms.append(tab("ta%d" % t, s - 2, "near", quarters[2:] if s else [(0, 256)], []))
-        ms.append(tab("tn%d" % t, s - 2, "far1" if s else "near1", [], [(256 * s, 256)]))
-        if t < 2:
-            ms.append(xship(t + 2))
-            ms.append(tab("tb%d" % t, -1 - s, "far", quarters[2 * s:2 * s + 2], [(256 * s, 256)]))
-    return ms
+def ways(T, topo, src, msg):
+    name, buf, a, land, b, w, packed, by = msg
+    dsts = [T.cores[(T.rank_of(src) + step) % NR] for step in range(1, NR)]
+    ports = [c for c in topo.cores_of(src) if T.rank_of(c) is None and all(topo.may_write(c, d) for d in dsts)]
+    side = {"near": [c for c in ports if topo.die(c) == topo.die(src)], "far": [c for c in ports if topo.die(c) != topo.die(src)]}
+    handed = [q for q, d in enumerate(dsts) if not topo.may_write(src, d)]
+    carrier = {q: side[by[2 * j]][by[2 * j + 1]] for j, q in enumerate(handed)}
+    share = deal(topo.engines(src, ports[0]), handed)
+    out = []
+    for q, d in enumerate(dsts):
+        piece = reg(buf, a + w * q * packed, a + w * q * packed + w)
+        out.append((d, carrier.get(q), share[q] if q in share else topo.engines(src, d), piece, reg(land, b + w * q, b + w * q + w)))
+    return out
 
 
 def mask_of(engs):
@@ -214,71 +173,34 @@ def mask_of(engs):
     return m
 
 
-def plan_message(T, topo, src, msg):
-    dsts, ways, direct, handed, used = {}, {}, [], [], []
-    for name, step, mode, pieces in [m for m in messages(T, topo) if call_of(m[0]) == call_of(msg[0])]:
-        dsts[name] = T.cores[(T.rank_of(src) + step) % NR]
-        rt = routes(T, topo, src, dsts[name], mode)
-        ways[name] = [rt[j % len(rt)] for j in range(len(pieces))]
-        direct += [(name, j) for j in range(len(pieces)) if ways[name][j] is None]
-        handed += [(name, j) for j in range(len(pieces)) if ways[name][j] is not None]
-        if topo.may_write(src, dsts[name]):
-            used = topo.engines(src, dsts[name])
-    share = deal(used, direct)
-    if handed:
-        share.update(deal([e for e in topo.engines(src, ways[handed[0][0]][handed[0][1]]) if e not in used], handed))
-    dst, way = dsts[msg[0]], ways[msg[0]]
-    engs = {j: share[(msg[0], j)] for j in range(len(way))}
-    total = sum(len(engs[j]) for j in engs if way[j] is None)
-    for c in set(way) - {None}:
-        total += sum(len(e) for e in deal(topo.engines(c, dst), [j for j in engs if way[j] == c]).values())
-    return dst, way, engs, total
-
-
-def call_of(name):
-    return {"l": "u", "k": "m", "w": "v", "yw": "y", "ao": "o" if name == "ao1" else "bo"}.get(name[:-1], name[:-1]) + name[-1]
-
-
 def deal(pool, items):
-    if not items:
-        return {}
     n = 1
     while 2 * n * len(items) <= len(pool):
         n *= 2
-    more = (len(pool) - n * len(items)) // n
-    out, at = {}, 0
-    for q, j in enumerate(items):
-        w = 2 * n if q < more else n
-        out[j] = pool[at:at + w]
-        at += w
-    return out
+    return {j: pool[n * q:n * q + n] for q, j in enumerate(items)}
 
 
-def write(g, T, topo, core, name, trs):
-    snt = T.sem["snt_" + name]
+def write(g, T, topo, core, snt, arr, trs):
     if len(trs) == 1:
-        m, to, engs, a, b = trs[0]
+        to, engs, a, b = trs[0]
         rid, pid = topo.addr(to, core)
-        g.remote_dma(ap(T, b), ap(T, a), T.sem["arr_" + m], snt, pid, rid, mask_of(engs))
+        g.remote_dma(ap(T, b), ap(T, a), T.sem[arr], T.sem[snt], pid, rid, mask_of(engs))
     else:
         g.remote_dma_fused([RemoteDMATransfer(dst_ids=[DstId(rid=topo.addr(to, core)[0], pnc=topo.addr(to, core)[1])], dma_engine_mask=mask_of(engs),
-                                              remote_sem=T.sem["arr_" + m], src=ap(T, a), dst=ap(T, b)) for m, to, engs, a, b in trs], local_sem=snt)
+                                              remote_sem=T.sem[arr], src=ap(T, a), dst=ap(T, b)) for to, engs, a, b in trs], local_sem=T.sem[snt])
 
 
 def carrier_program(g, core, T, topo):
     owners = [c for c in topo.cores_of(core) if T.rank_of(c) is not None]
     if not owners:
         return
-    src = owners[0]
     sent = []
-    for msg in messages(T, topo):
-        dst, way, engs, total = plan_message(T, topo, src, msg)
-        mine = [j for j in range(len(way)) if way[j] == core]
-        if mine:
-            second = deal(topo.engines(core, dst), mine)
-            g.wait_ge(T.sem["arr_" + msg[0]], sum(len(engs[j]) for j in mine))
-            write(g, T, topo, core, msg[0], [(msg[0], dst, second[j], msg[3][j][1], msg[3][j][2]) for j in mine])
-            sent.append((msg[0], sum(len(e) for e in second.values())))
+    for msg in MSGS:
+        for dst, by, engs, piece, land in ways(T, topo, owners[0], msg):
+            if by == core:
+                g.wait_ge(T.sem["arr_" + msg[0]], len(engs))
+                write(g, T, topo, core, "snt_" + msg[0], "arr_" + msg[0], [(dst, topo.engines(core, dst), land, land)])
+                sent.append((msg[0], len(topo.engines(core, dst))))
     for name, n in sent:
         g.wait_ge(T.sem["snt_" + name], n)
 
@@ -292,7 +214,7 @@ def rank_program(g, core, T, topo):
     ndma = [0]
     line = [""]
     ahead = [0.0]
-    msgs = {m[0]: m for m in messages(T, topo)}
+    msgs = {m[0]: m for m in MSGS}
     queue = {"v": g.vector, "a": g.scalar, "p": g.tensor, "g": g, "s": g.sync}
 
     def add(eng, fn, outs, ins, sem=None, per=1.0, msg=None, legs=None):
@@ -300,7 +222,7 @@ def rank_program(g, core, T, topo):
         for r in list(ins) + list(outs):
             if isinstance(r, dict) and r["off"] is not None:
                 rd += spans([r["off"]])
-        busy = [{"g": m["issue"], "x": 0.0}.get(eng, 60.0) if sem else duration(eng, outs[0], ins, per, m) for m in PACES]
+        busy = [{"g": m["issue"], "x": 0.0}.get(eng, 60.0 * len(outs)) if sem else duration(eng, outs[0], ins, per, m) for m in PACES]
         ops.append({"e": eng, "f": fn, "r": rd, "w": wr, "sem": sem, "msg": msg, "ahead": ahead[0], "busy": busy, "legs": legs, "line": eng in line[0]})
 
     A = lambda r: ap(T, r)
@@ -338,9 +260,9 @@ def rank_program(g, core, T, topo):
         ops.append(dict(part[0], f=lambda: [op["f"]() for op in part][-1], r=sorted({x for op in part for x in op["r"]}),
                         w=sorted({x for op in part for x in op["w"]}), busy=[sum(b) for b in zip(*[op["busy"] for op in part])]))
 
-    def total(out, terms):
+    def total(out, terms, first=True, last=True):
         for q, (lhs, rhs) in enumerate(terms):
-            mm(out, lhs, rhs, q == 0, q == len(terms) - 1)
+            mm(out, lhs, rhs, first and q == 0, last and q == len(terms) - 1)
             if len(terms) == 16 and q % 8 == 7:
                 join(8)
 
@@ -350,6 +272,14 @@ def rank_program(g, core, T, topo):
         else:
             add("g", lambda: g.iota(A(out), pattern, base, cm, allow_small_or_imprecise_dtypes=True), [out], [])
 
+    def same(eng, out, in_):
+        if eng == "v":
+            copy(out, in_)
+        elif eng == "a":
+            act(out, in_, AF.Copy)
+        else:
+            add("g", lambda: g.affine_select(A(out), A(in_), [[0, width(in_)]], OP.is_ge, 0.0, 0, 0), [out], [in_])
+
     def dma(eng, pairs):
         name = "d%d" % ndma[0]
         ndma[0] += 1
@@ -357,127 +287,166 @@ def rank_program(g, core, T, topo):
         def fn():
             for out, in_ in pairs:
                 queue[eng].dma_start(A(out), A(in_)).then_inc(T.sem[name], 16)
+        short = [min((r for r in p if isinstance(r, dict)), key=row_bytes) for p in pairs]
         add(eng, fn, [p[0] for p in pairs], [p[1] for p in pairs], sem=(name, 16 * len(pairs)),
-            legs=[(None, topo.engines(core, core), r["p1"] - r["p0"], row_bytes(r), None, [], None) for p in pairs for r in p if isinstance(r, dict)])
+            legs=[(None, topo.engines(core, core), r["p1"] - r["p0"], row_bytes(r), None, [], None) for r in short])
 
-    def send(name, after=()):
-        trs, legs = [], []
-        for msg in [m for m in msgs.values() if call_of(m[0]) == name]:
-            dst, way, engs, _ = plan_message(T, topo, core, msg)
-            trs += [(msg[0], dst, engs[j], p[0], p[2]) if way[j] is None else (msg[0], way[j], engs[j], p[0], p[1]) for j, p in enumerate(msg[3])]
-            for j, c in enumerate(way):
-                second = deal(topo.engines(c, dst), [q for q in range(len(way)) if way[q] == c])[j] if c else []
-                legs.append((msg[0], engs[j], 128, row_bytes(msg[3][j][0]), c, second, topo.die(c or core)))
-        add("g", lambda: write(g, T, topo, core, name, trs), [], [tr[3] for tr in trs] + list(after),
-            sem=("snt_" + name, sum(len(tr[2]) for tr in trs)), msg=name, legs=legs)
+    def send(name):
+        way = ways(T, topo, core, msgs[name])
+        for snt, arr, part in (("snt_", "arr_", [w for w in way if w[1] is not None]), ("snd_", "ard_", [w for w in way if w[1] is None])):
+            trs = [(by or dst, engs, piece, land) for dst, by, engs, piece, land in part]
+            legs = [(arr + name, engs, 128, row_bytes(piece), by, topo.engines(by, dst) if by else [], topo.die(by or core)) for dst, by, engs, piece, land in part]
+            add("g", lambda snt=snt, arr=arr, trs=trs: write(g, T, topo, core, snt + name, arr + name, trs), [], [tr[2] for tr in trs],
+                sem=(snt + name, sum(len(tr[1]) for tr in trs)), msg=snt + name, legs=legs)
 
-    def arrive(name):
-        msg = msgs[name]
-        src = T.cores[(rank - msg[1]) % NR]
-        dst, way, engs, count = plan_message(T, topo, src, msg)
-        add("x", None, [p[2] for p in msg[3]], [], sem=("arr_" + name, count), msg=(call_of(name), msg[1]))
+    def coming(name):
+        out = []
+        for step in range(1, NR):
+            src = T.cores[(rank - step) % NR]
+            dst, by, engs, piece, land = ways(T, topo, src, msgs[name])[step - 1]
+            out.append((by is not None, (rank - step) % NR, len(topo.engines(by or src, dst)), land))
+        return sorted(out, key=lambda w: w[0])
+
+    def arrive(name, *kinds):
+        for handed in kinds or (False, True):
+            part = [w for w in coming(name) if w[0] == handed]
+            add("x", None, [w[3] for w in part], [], sem=(["ard_", "arr_"][handed] + name, sum(w[2] for w in part)), msg=["snd_", "snt_"][handed] + name)
+
+    def landed(name, a=0, b=None):
+        buf, c, land, d, w, packed = msgs[name][1:7]
+        b, c = w if b is None else b, c + w * (NR - 1) * packed
+        return [(rank, reg(buf, c + a, c + b))] + [(r, reg(land, piece["a"] + a, piece["a"] + b)) for handed, r, n, piece in coming(name)]
+
+    def move(a, b):
+        c = 256 * a + BLK * ((a - b) % NR)
+        return reg("SE", c, c + 128)
+
+    def pick(name, far, a=0, b=None):
+        return [(move((rank - 2 * far) % NR, r), piece) for r, piece in landed(name, a, b)]
+
+    def unpack(outs, name, senders, a=0, b=None):
+        for q, out in enumerate(outs):
+            banks = [o["n"] == out["n"] for o in outs]
+            for j in senders:
+                r, piece = landed(name, a, b)[j]
+                mm(out, move(q, r), piece, j == 0 and True not in banks[:q], j == NR - 1 and True not in banks[q + 1:])
+
+    share_of = lambda n, r, a, b: reg(n, a, b, 1, BLK * r, BLK * r + BLK)
+    others = [(rank + q + 1) % NR for q in range(NR - 1)]
 
     def bank(b, a=0, e=512, step=1, p1=128):
         return reg("P%d" % b, a, e, step, 0, p1)
 
     col = lambda n, c: reg(n, c, c + 1)
-    P16, PG, PP, PG16, PPAIR, PODD, P24, P3, P4 = [col("PC", c) for c in range(9)]
+    P16, PG, PP, PG16, PPAIR, PODD, P24, P3, P4, PF0, PF1 = [col("PC", c) for c in range(11)]
     BO, BOM, BO3 = [reg("BK", 128 * j, 128 * j + 128) for j in range(3)]
     BIG, NBIG = [reg("BB", 128 * j, 128 * j + 128) for j in range(2)]
     ROW, CROW, NCROW, KROW, BIAS, PP2, NFC, SIDE = [col("PD", c) for c in (0, 4, 5, 6, 7, 8, 9, 12)]
-    ID, NID, ID3 = [reg("ID", 128 * j, 128 * j + 128) for j in range(3)]
-    START, MINUS8 = reg("R0", 0, 256), reg("R0", 128, 136)
-    sign = lambda n: {0: 1.0, 128: -1.0}.get(n, col("PS", n // 32))
+    ID, NID, ID3, NID3 = [reg("ID", 128 * j, 128 * j + 128) for j in (0, 2, 3, 4)]
+    START, MINUS8 = reg("R0", 0, 128), reg("R0", 128, 136)
+    sign = lambda n: {0: 1.0, 128: -1.0}.get(n, col("PS", n // 16))
     times = lambda c: reg("R0", *{-1: (128, 256), 2: (256, 384), -2: (384, 512), 1: (512, 640), 3: (640, 768)}[c])
+    nv = lambda q: reg("NV", 256 * q, 256 * q + 256)
 
-    def to_list(out, sel, src, a, n):
-        total(out, [(reg(sel, 15 - j, 143 - j), reg(src, a + j, a + n, 16)) for j in range(16)])
+    def to_list(out, sel, src, a, n, d=0):
+        c = 15 + (128 - d) % 128
+        total(out, [(reg(sel, c - j, c + 128 - j), reg(src, a + j, a + n, 16)) for j in range(16)])
 
-    def payee(t):
-        ts(reg("BI", 16, 32), reg("BI", 0, 16), 513.0, OP.mult)
-        copy(reg("RV", 48 * (t % 2), 48 * (t % 2) + 16), reg("BI", 0, 16))
-        ts(reg("BI", 32, 48), reg("BI", 16, 32), 1, OP.logical_shift_right, 511, OP.bitwise_and)
-        if t < R - 1:
-            ts(reg("BH"), reg("BI", 0, 16), 256.0, OP.subtract)
-        copy(reg("BO16"), reg("BI", 32, 48))
+    def spread(out, src, first, last):
+        for j in range(16):
+            mm(reg(out["n"], out["a"] + j, out["b"], 16), reg("SJ", 128 * j, 128 * j + 128), src, first and j == 0, last and j == 15)
+            if j % 8 == 7:
+                join(8)
 
     ahead[0] = 20000.0
-    dma("a", [(reg("PL"), T.pl[:])])
+    rows = lambda r: slice(BLK * r, BLK * r + BLK)
+    quarters = lambda n, src, w, js: [(share_of(n, q, w * j, w * j + w), src[rows((others + [rank])[j]), w * q:w * q + w]) for j in js for q in range(NR)]
+    dma("s", quarters("ZS", T.z0, 64, range(3))[:6])
+    dma("a", quarters("ZS", T.z0, 64, range(3))[6:])
     dma("s", [(reg("FR"), T.fr0[:])])
-    dma("s", [(reg("ZB", 0, 256), T.z0[:])])
-    dma("s", [(reg("X", P, P + 1024), T.x0[:, 0:1024])])
-    dma("s", [(reg("X", P + 1024, P + 2048), T.x0[:, 1024:2048])])
-    dma("s", [(reg("BI", 0, 16), T.b0[:])])
+    dma("a", [(reg("PL", 0, 512), T.pl[:]), (reg("PL", 512, 528), T.b0[:])])
+    dma("s", quarters("XP", T.x0, 512, range(3)))
+    dma("a", quarters("XP", T.x0, 512, [3]) + quarters("ZS", T.z0, 64, [3]))
     iota(col("PI", 0), [[0, 1]], 0, 1)
     iota(reg("IOA", 0, 128), [[1, 8], [0, 16]], 0, 0)
     iota(reg("IOX"), [[1, 256]], 0, 0)
+    send("z")
     iota(reg("IA", 576, 704), [[0, 16], [1, 8]], 0, 0)
     iota(reg("IA", 0, 512, 1, 0, 64), [[1, 2], [4, 16], [0, 16]], 0, 0)
     iota(reg("IA", 0, 512, 1, 64, 128), [[1, 2], [0, 16], [4, 16]], 64, 0)
-    fill(reg("X", 0, P), 0.0)
-    fill(reg("XF1", 0, P), 0.0)
-    for c, (shift, bits) in enumerate([(0, 15), (4, 7), (0, 127), (0, 112), (5, 3), (4, 1), (0, 24), (0, 3), (2, 1)]):
+    for c, (shift, bits) in enumerate([(0, 15), (4, 7), (0, 127), (0, 112), (5, 3), (4, 1), (0, 56), (0, 3), (2, 1)]):
         ts(col("PI", 1 + c), col("PI", 0), shift, OP.logical_shift_right, bits, OP.bitwise_and)
     copy(reg("PC", 0, 9), reg("PI", 1, 10))
     ts(BO, reg("IOA", 0, 128), PG, OP.is_equal)
     ts(reg("DG"), reg("IOX", 0, 16), P16, OP.is_equal)
     for j in range(16):
         ts(reg("SJ", 128 * j, 128 * j + 128), BO, col("DG", j), OP.mult)
-    ts(reg("U1"), reg("IOX", 0, 144), 15.0, OP.subtract, PG16, OP.is_equal)
+    ts(reg("U1", 0, 144), reg("IOX", 0, 144), 15.0, OP.subtract, PG16, OP.is_equal)
     ts(ID, reg("IOX", 0, 128), PP, OP.is_equal)
-    line[0] = "v"
-    copy(reg("LO", 0, 256), reg("PL", 0, 512, 2))
-    copy(reg("LO", 256, 512), reg("PL", 1, 512, 2))
+    copy(reg("ID", 128, 256), ID)
+    for r in range(NR):
+        ts(col("PD", 13 + r), PPAIR, float(r), OP.is_equal)
+    for r in range(NR):
+        ts(reg("SE", 256 * r, 256 * r + 256), reg("ID", 0, 256), col("PD", 13 + r), OP.mult)
+    line[0] = "vap"
     copy(reg("FR16"), reg("FR"))
-    line[0] = ""
-    send("c0")
-    send("h0")
-    send("h1")
-    ahead[0] = 10000.0
+    for j in range(16):
+        mm(bank(j // 4, 128 * (j % 4), 128 * (j % 4) + 128), reg("SJ", 128 * j, 128 * j + 128), reg("FR16"), True, True)
+    for q in range(4):
+        same("av"[q % 2], reg("FW", 512 * q, 512 * q + 512), bank(q))
+    copy(reg("PN"), reg("PL"))
+    copy(reg("LN"), reg("PN", 0, 512))
+    for j, r in enumerate(others):
+        total(bank(4, 144 * j, 144 * j + 128), [(move(r, q), reg("PN", 128 * q, 128 * q + 128)) for q in range(NR)])
+        mm(bank(4, 144 * j + 128, 144 * j + 144), move(r, 0), reg("PN", 512, 528), True, True)
+        join(NR + 1)
+    act(reg("PK"), bank(4, 0, 432), AF.Copy)
+    send("p")
+    send("x")
+    ahead[0] = NAMING
     iota(reg("TIE", 0, 512, p1=2), [[0, 2], [32, 16], [1, 16]], 0, 0)
     iota(reg("TIE", 512, 576, p1=2), [[0, 4], [32, 16]], 16, 0)
     iota(reg("IA", 512, 576), [[1, 4], [4, 16]], 0, 0)
     iota(reg("IOB"), [[0, 16], [1, 16]], 0, 0)
-    iota(reg("IOA", 128, 512), [[1, 24], [0, 16]], 8, 0)
-    for k in range(ZACT[0]):
-        act(reg("ZR", k, 4096, 16), reg("ZB", 0, 256), AF.Copy)
-    for j in range(16):
-        mm(bank(j // 4, 128 * (j % 4), 128 * (j % 4) + 128), reg("SJ", 128 * j, 128 * j + 128), reg("FR16"), True, True)
-    act(reg("FW", 0, 512), bank(0), AF.Copy)
-    copy(reg("FW", 512, 1024), bank(1))
-    act(reg("FW", 1024, 1536), bank(2), AF.Copy)
-    copy(reg("FW", 1536, 2048), bank(3))
+    iota(reg("IOA", 128, 384), [[1, 16], [0, 16]], 32, 0)
+    iota(reg("IOK"), [[0, 8], [1, 16]], 0, 0)
     for e in range(16):
         iota(col("WR", e), [[0, 1]], WT[e], 0)
+    OWN, DIRECT, HANDED = [0], [1], [2, 3]
+    xq, pq = [bank(q) for q in range(NR)], [bank(7, 128 * q, 128 * q + 128) for q in range(NR)]
+    mm(bank(7), move(rank, rank), reg("PN", 0, 512), True, False)
+    unpack(xq, "x", OWN)
 
-    for eng, a, b in NAMES:
-        buf = ["NG", "MH"][a // 256]
-        out, w = reg(buf, 16 * (a % 256), 16 * (a % 256) + 16 * (b - a)), reg("FW", off=reg("LO", a, b))
-        if eng == "a":
-            act(out, w, AF.Copy)
-        else:
-            copy(out, w)
-        total(bank(4 + a // 128, a % 128, a % 128 + b - a), [(reg("U1", 15 - k, 143 - k), reg(buf, out["a"] + k, out["b"], 16)) for k in range(16)])
-    for c in (0, 3, 1, 2):
-        act(reg("TN", 128 * c, 128 * c + 128), bank(4 + c, 0, 128), bias=-256.0, scale=1.0 / 16)
-    send("n0")
-    ahead[0] = 0.0
-    for k in range(ZACT[0], 16):
-        copy(reg("ZR", k, 4096, 16), reg("ZB", 0, 256))
-    copy(reg("TB"), reg("LO"))
-    for m in ("c0", "h0", "h1", "n0"):
-        arrive(m)
-    send("u1", after=[reg("XF0", P, P + W0)])
-    send("x1")
-    payee(0)
+    for half in range(2):
+        for q in (2 * half, 2 * half + 1):
+            out = reg(["NG", "MH"][half], 2048 * (q % 2), 2048 * (q % 2) + 2048)
+            same("av"[q % 2], out, reg("FW", off=reg("LN", 128 * q, 128 * q + 128)))
+            for k in range(16):
+                mm(bank(4 + q % 2, k, 128, 16), reg(out["n"], out["a"] + k, out["b"], 16), reg("BK", 0, 128, 16), True, True)
+            join(16)
+        if half == 0:
+            line[0] = "p"
+            arrive("p", False)
+            unpack(pq, "p", DIRECT, 0, 128)
+        for q in (2 * half, 2 * half + 1):
+            act(reg("NN", 128 * q, 128 * q + 128), bank(4 + q % 2, 0, 128), bias=-256.0, scale=1.0 / 16)
+            for j, r in enumerate(others + [rank]):
+                mm(reg("P6", 128 * j, 128 * j + 128, 1, BLK * q, BLK * q + BLK), reg("NN", 128 * q + BLK * r, 128 * q + BLK * r + BLK), ID, True, True)
+            join(NR)
+    act(reg("NK"), bank(6), AF.Copy)
+    line[0] = ""
+    send("n")
+    ahead[0] = EARLY
+    fill(reg("X", 0, P), 0.0)
+    ts(reg("U1", 143, 240), reg("IOX", 15, 112), 15.0, OP.subtract, PG16, OP.is_equal)
 
     def sum_constants():
         parts = sorted({n for sh in SHARE for n in sh} - {0, 128})
         ts(times(-1), reg("IA", 576, 704), PG, OP.is_equal, -1.0, OP.mult)
         for n in parts:
-            ts(col("PS", 4 + n // 32), PP, float(n), OP.is_ge, 2.0, OP.mult)
+            ts(col("PS", 8 + n // 16), PP, float(n), OP.is_ge, 2.0, OP.mult)
         for n in parts:
-            ts(sign(n), col("PS", 4 + n // 32), 1.0, OP.subtract)
+            ts(sign(n), col("PS", 8 + n // 16), 1.0, OP.subtract)
         ts(NID, ID, -1.0, OP.mult)
         fill(reg("R0", 0, 8), 0.0)
         ts(reg("R0", 8, 128), reg("IA", 584, 704), PG, OP.is_equal)
@@ -486,6 +455,10 @@ def rank_program(g, core, T, topo):
 
     def pair_constants():
         ts(ROW, P16, 4.0, OP.mult, PPAIR, OP.add)
+        for s in range(2):
+            ts(col("PI", 12 + s), col("PI", 5), float(NR - 1 - s), OP.add)
+            ts(col("PI", 10 + s), col("PI", 12 + s), NR - 1, OP.bitwise_and)
+        copy(reg("PC", 9, 11), reg("PI", 10, 12))
         ts(col("PD", 3), PODD, 128.0, OP.mult)
         ts(col("PD", 2), PODD, -128.0, OP.mult, 128.0, OP.add)
         ts(col("PD", 13), PP, 64.0, OP.is_ge, 65536.0, OP.mult)
@@ -496,7 +469,8 @@ def rank_program(g, core, T, topo):
         ts(col("PD", 10), PP, 64.0, OP.is_ge, 2016.0, OP.mult)
         ts(col("PD", 11), PP, 1.0, OP.is_equal, 1024.0, OP.mult)
         ts(NFC, PP, 1.0, OP.is_equal, 1528.0, OP.mult)
-        ts(col("PD", 1), ROW, 64.0, OP.add)
+        ts(col("PD", 17), P16, 4.0, OP.mult, PF0, OP.add)
+        ts(col("PD", 18), P16, 4.0, OP.mult, PF1, OP.add)
         ts(KROW, KROW, P4, OP.add)
         ts(BIAS, PP, 0.0, OP.is_equal, col("PD", 10), OP.add)
         ts(SIDE, col("PD", 13), 32768.0, OP.subtract)
@@ -506,40 +480,57 @@ def rank_program(g, core, T, topo):
             ts(reg("SC", 512 * j, 512 * j + 512), reg("IA", 0, 512), c, OP.is_equal, CROW, OP.mult)
             act(reg("SC", 512 * j, 512 * j + 512, p1=2), reg("TIE", 0, 512, p1=2), AF.Copy, scale=reg("PS", 0, 1, p1=2))
         ts(BIAS, BIAS, col("PD", 11), OP.add)
-        for side in range(2):
+        ts(reg("PD", 19, 21), reg("PD", 17, 19), 64.0, OP.add)
+        for side, c in enumerate((0, 19, 20)):
             for odd in range(2):
-                ts(reg("PM", 256 * side + 128 * odd, 256 * side + 128 * odd + 128), reg("IOX", 0, 128), col("PD", side), OP.is_equal, col("PD", 2 + odd), OP.mult)
+                ts(reg("PM", 256 * side + 128 * odd, 256 * side + 128 * odd + 128), reg("IOX", 0, 128), col("PD", c), OP.is_equal, col("PD", 2 + odd), OP.mult)
         ts(reg("SF"), reg("IA", 512, 576), PP, OP.is_equal, NCROW, OP.mult)
         ts(reg("SG", 0, 256), reg("IOB"), 0.0, OP.is_equal, 2.0 ** 23, OP.mult)
         ts(reg("SF", p1=2), reg("TIE", 512, 576, p1=2), reg("DG", 0, 1, p1=2), OP.mult, reg("PD", 9, 10, p1=2), OP.add)
-
-    ts(reg("CM", 0, 256), reg("LO", 0, 256), MID, OP.subtract, 2.0, OP.mult)
-    act(reg("N0"), reg("TN", 0, 256), AF.Copy)
-    act(reg("PL16"), reg("TB"), AF.Copy)
 
     def later_constants():
         act(reg("SG", 256, 512), reg("SG", 0, 256), bias=0.5, scale=2.0 ** -24)
         ts(BOM, BO, -4096.0, OP.mult)
         ts(BO3, BO, 3072.0, OP.mult)
         ts(ID3, ID, 3072.0, OP.mult)
+        ts(NID3, ID, -3072.0, OP.mult)
         ts(reg("SL", 0, 256), reg("IOB"), 0.0, OP.not_equal)
         fill(reg("D0"), -1024.0)
-        fill(reg("RAMP", 0, 16), 0.0)
-        ts(reg("RAMP", 16, 32), reg("IOX", 0, 16), 20.0, OP.mult, -150.0, OP.add)
+        fill(reg("RAMP", 0, 16), 15 * FLOOR)
+        ts(reg("RAMP", 16, 32), reg("IOX", 0, 16), 20.0, OP.mult, 15 * FLOOR - 150.0, OP.add)
+        fill(reg("XO", 0, P), 0.0)
+        fill(reg("BG", 512, 704), 0.0)
+        fill(reg("IZ"), 0.0)
+        copy(reg("IZ", 256, 384), ID)
+        fill(reg("ONE"), 1.0)
 
     def last_constants():
         ts(col("WC", 2), PP, 0.0, OP.mult, 2.0 ** 61, OP.add)
-        ts(reg("RK"), reg("IOA"), KROW, OP.is_equal)
+        ts(col("PD", 21), PP, 32.0, OP.is_lt, 2 * GATE, OP.mult)
+        ts(col("PD", 22), PP, 64.0, OP.is_ge, -GATE, OP.mult)
+        ts(reg("IOK"), reg("IOK"), col("PD", 21), OP.mult, col("PD", 22), OP.add)
+        for q in range(4):
+            for p0 in (0, 64):
+                out, in_ = reg("RK", 128 * q, 128 * q + 128, 1, p0, p0 + 64), reg("IOK", 0, 128, 1, p0, p0 + 64)
+                add("g", lambda q=q, out=out, in_=in_: g.affine_select(A(out), A(in_), [[1, 4], [4, 2], [0, 16]], OP.is_equal, 0.0, 8 * q, -1), [out], [in_])
+        fill(reg("VA", 0, 64), 0.0)
+        fill(reg("VT", p0=32, p1=64), 0.0)
+        ts(col("WC", 1), P16, P16, OP.mult, -GATE, OP.mult)
         tt(reg("WR", 16, 32), reg("WR", 0, 16), reg("DG"), OP.mult)
         ts(col("WC", 3), col("WC", 2), 2.0 ** 60, OP.mult)
-        for a in (0, 16, 32, 48):
-            ts(reg("DUM", a, a + 16), reg("IOX", 0, 256, 16), P16, OP.add, -256.0 * (a // 32), OP.add)
+        for a, c in ((0, 0.0), (16, 0.0), (32, -256.0), (48, -256.0), (64, -MIDP)):
+            ts(reg("DUM", a, a + 16), reg("IOX", 0, 256, 16), P16, OP.add, c, OP.add)
         red(col("WC", 0), reg("WR", 16, 32), OP.add)
         scan(reg("THR"), reg("SG", 256, 512), reg("X", 0, P), col("WC", 3), OP.mult, OP.add)
         ts(BIG, BO, col("WC", 3), OP.mult, 2.0, OP.mult)
         ts(reg("NFK"), reg("IOB"), P16, OP.is_equal)
+        ts(reg("DIAG"), reg("IOB"), P16, OP.is_equal)
+        copy(col("PD", 23), col("WC", 3))
+        ts(reg("RK", 512, 768), reg("IOA", 128, 384), KROW, OP.is_equal, col("PD", 23), OP.mult)
+        ts(reg("RK", 768, 1024), reg("IOA", 128, 384), KROW, OP.is_equal, 4096.0, OP.mult)
         act(reg("UW"), reg("U1"), AF.Copy, scale=col("WC", 0))
         act(NBIG, BIG, AF.Copy, scale=-1.0)
+        ts(reg("UK"), reg("U1", 0, 144), P16, OP.mult)
         tt(reg("THR"), reg("THR"), reg("NFK"), OP.mult)
         scan(reg("NFK"), reg("SL", 0, 256), reg("THR"), 0.0, OP.mult, OP.max)
         act(reg("FL", 0, 16), reg("NFK", 15, 256, 16), AF.Copy, scale=0.5)
@@ -550,125 +541,154 @@ def rank_program(g, core, T, topo):
             else:
                 ts(reg("BW", 128 * h, 128 * h + 128), BO, col("FL", h), OP.mult)
 
-    def settle(x, t, chosen, fv, gifts, buf, taken, ps):
-        before, left, after = [reg(buf, 256 * q, 256 * q + 256) for q in range(3)]
-        if x != "X" and t < 2:
-            act(left, fv, AF.Copy, scale=-1.0)
-            tt(taken, entries(x, t, chosen), fv, OP.max)
-            return
-        act(before, entries(x, t, chosen), AF.Copy)
-        if t == R - 1:
-            act(after, before, AF.Relu, bias=-63.0)
-        total(ps, [(ID, before), (NID, fv)] + [(NID, after)] * (t == R - 1))
-        act(left if gifts else taken, ps, AF.Relu)
-        if gifts:
-            total(ps, [(ID, left), (NID, before)])
-            act(taken, ps, AF.Copy)
-            for q, (off, w) in enumerate(gifts):
-                held = reg(buf, 768 + 256 * q, 1024 + 256 * q)
-                change(t, places(x, t, off), places(x, t, off), held, w)
+    sum_constants()
+    pair_constants()
+    ahead[0] = LATER
+    later_constants()
+    last_constants()
+    ahead[0] = LANDING
 
-    def change(t, read, put, held, w):
-        if t < R - 1:
-            act(held, read, AF.Copy)
-            tt(put, held, w, OP.add)
-        else:
-            tt(held, read, w, OP.add)
-            copy(put, held)
+    line[0] = "p"
+    arrive("z")
+    unpack([bank(4, 64 * q, 64 * q + 64) for q in range(NR)], "z", range(NR))
+    copy(reg("ZB", 0, 256), bank(4, 0, 256))
+    arrive("x", False)
+    unpack(xq, "x", DIRECT)
+    arrive("p", True)
+    unpack(pq, "p", HANDED, 0, 128)
+    for shift in range(2):
+        total(bank(5, 16 * shift, 16 * shift + 16), [(move(rank, (rank + shift) % NR), reg("PN", 512, 528))] +
+              [(move(0, (r + shift) % NR), piece) for r, piece in landed("p", 128, 144)[1:]])
+    arrive("x", True)
+    unpack(xq, "x", HANDED)
+    line[0] = ""
+    for q in range(NR):
+        same("av"[q % 2], reg("X", P + 512 * q, P + 512 * q + 512), bank(q))
+    act(reg("TB"), bank(7), AF.Copy)
+    copy(reg("LO", 0, 256), reg("TB", 0, 512, 2))
+    copy(reg("BO16"), bank(5, 16, 32))
+    copy(reg("RV", 0, 16), bank(5, 0, 16))
+    ts(reg("BH"), bank(5, 0, 16), 256.0, OP.subtract)
+    copy(reg("LO", 256, 512), reg("TB", 1, 512, 2))
+    ahead[0] = 0.0
+    arrive("n")
+    unpack([bank(0, 128 * q, 128 * q + 128) for q in range(NR)], "n", range(NR))
+    act(reg("TN"), bank(0), AF.Copy)
+    act(reg("CM", 0, 256), reg("TB", 0, 512, 2), bias=-2 * MID, scale=2.0)
+    act(reg("N0"), reg("TN", 0, 512, 2), AF.Copy)
+    act(reg("PL16"), reg("TB", 0, 512, 2), AF.Copy)
 
-    def far_takes(x, t, chosen, off, buf, taken):
-        if t >= 2:
-            change(t, entries(x, t, chosen), places(x, t, off), reg(buf, 512, 768), taken)
-        elif x == "X":
-            copy(places(x, t, off), taken)
-        else:
-            tt(places(x, t, off), taken, reg(buf, 256, 512), OP.add)
+    def repeat(t):
+        d = BLK * (1 + t % 2)
+        for k in range(16):
+            same(ZBY[t][k], reg("ZR", k, 4096, 16), reg("ZB", 256 * (t % 2), 256 * (t % 2) + 256))
+        for h in range(2):
+            a, b = 2048 * h + 16 * SHARE[t][2 + h], 2048 * h + 2048
+            if a < b:
+                dma("s", [(reg("ZF", a, b, 1, d, 128), reg("ZR", a, b, 1, 0, 128 - d)), (reg("ZF", a, b, 1, 0, d), reg("ZR", a, b, 1, 128 - d, 128))])
 
-    def follow_home(t):
-        xf = "XF%d" % (1 - t % 2)
-        for m in ["x%d" % (t + 1), "a%d" % t, "ao%d" % t, "at%d" % t, "k%d" % t, "w%d" % t] + ["yw2"] * (t == 2):
-            arrive(m)
-        y, less = reg("LH", 256 * t, 256 * t + 256), reg("LN", 256 * t, 256 * t + 256)
-        act(built(xf, t), less, AF.Copy, scale=-1.0)
-        tt(places(xf, t, reg("LB", 64 * t, 64 * t + 16)), y, less, OP.add)
-        gifts = [(reg("LB", 144, 160), y), (reg("LK", 80, 96), reg("LW", 768, 1024))] if t == 2 else []
-        settle(xf, t, reg("LK", 32 * t, 32 * t + 16), reg("LW", 256 * t, 256 * t + 256), gifts, "NW", reg("TV", 256, 512), bank(0, 256, 512))
+    def gifts(x, t, offs, w, at_home, at_far, less):
+        act(nv(7), places(x, t - 2, offs[0]), AF.Copy)
+        tt(places(x, t - 2, offs[0]), nv(7), w[0], OP.add)
+        tt(nv(8), places(x, t - 2, offs[1]), w[1], OP.add)
+        copy(places(x, t - 2, offs[1]), nv(8))
+        tt(nv(6), entries(x, t, at_far), less, OP.add)
+        act(nv(5), entries(x, t, at_home), AF.Copy)
 
-    def follow_far(t):
-        arrive("bo%d" % t)
-        if t < 2:
-            send("x%d" % (t + 2), after=[reg("LB", 64 * t + 32, 64 * t + 48)])
-            send("tb%d" % t)
-        far_takes("XF%d" % (1 - t % 2), t, reg("LK", 32 * t, 32 * t + 16), reg("LB", 64 * t + 32, 64 * t + 48), "NW", reg("TV", 256, 512))
+    def takes(x, t, offs, held, at_far, floor, between=lambda: None):
+        tt(places(x, t, offs[0]), held, nv(0), OP.add)
+        between()
+        tt(nv(9), entries(x, t, at_far), floor, OP.max)
+        tt(places(x, t, offs[1]), nv(9), nv(1), OP.add)
+
+    def records(pair, b):
+        for q in range(3):
+            c = 512 + 96 * pair + 32 * q
+            for j in range(16):
+                mm(bank(b, j, 512, 16, p1=24), reg("IZ", 256 - 128 * q + j, 640 - 128 * q, 16), reg("BN", c, c + 32), q + j == 0, q + j == 17)
+            join(16)
+        act(reg("RO", 512 * pair, 512 * pair + 512, p1=24), bank(b, p1=24), bias=MID)
+        dma("s", [(T.rec[:, 512 * pair:512 * pair + 512], reg("RO", 512 * pair, 512 * pair + 512, p1=24))])
+
+    repeat(0)
 
     for t in range(R):
         s = t % 2
-        wx = W0 + P * t
-        XF, TF, NF = "XF%d" % s, "TF%d" % s, "NF%d" % s
+        d = BLK * (1 + s)
+        FWD, BACK = reg("ID", 128 - d, 256 - d), reg("ID", d, d + 128)
         z = reg("ZB", 256 * s, 256 * s + 256)
         zn = reg("ZB", 256 * (1 - s), 256 * (1 - s) + 256)
-        C, Nn = reg("TB", 256 * s, 256 * s + 256), reg("TN", 256 * s, 256 * s + 256)
+        C, Nn = reg("TB", s, 512, 2), reg("TN", s, 512, 2)
         zb = [1, 2, 3, 0, 6, 7, 1, 2]
         HOME, FAR = 0, 1
         share = lambda side, h: SHARE[t][2 * side + h]
-        window = lambda side, h, a, b: entries(["X", XF][side], t, reg(["LO", "MO"][side], [256 * s, 0][side] + 128 * h + a, [256 * s, 0][side] + 128 * h + b))
+        window = lambda side, h, a, b: entries("X", t, reg(["LO", "MO"][side], [256 * s, 0][side] + 128 * h + a, [256 * s, 0][side] + 128 * h + b))
         mins = ["MY", "MH"]
-        ready, staged, free = [], [], [6, 7, 1, 2, 3]
+        ready, staged, free = [], [], [6, 7, 3]
 
         def gather(side, h):
             n = share(side, h)
             if n < 128:
                 a, b = 2048 * h + 16 * n, 2048 * h + 2048
-                tt(reg(mins[side], a, b), window(side, h, n, 128), reg("ZR", a, b), OP.min)
+                tt(reg(mins[side], a, b), window(side, h, n, 128), reg(["ZR", "ZF"][side], a, b), OP.min)
 
         def fetch(side, h, a, b):
             b = min(b, share(side, h))
             if a < b:
                 c = 4096 * side + 2048 * h
                 act(reg("YG", c + 16 * a, c + 16 * b), window(side, h, a, b), AF.Copy)
-                ready.extend((side, 2048 * h + 16 * q) for q in range(a, b, 32))
+                ready.extend((side, 2048 * h + 16 * q, 16 * min(32, b - q)) for q in range(a, b, 32))
+                stage()
 
         def stage():
             while ready and free:
-                (side, c), b = ready.pop(0), free.pop(0)
-                total(bank(b), [(ID, reg("ZR", c, c + 512)), (NID, reg("YG", 4096 * side + c, 4096 * side + c + 512))])
-                staged.append((side, c, b))
+                (side, c, w), b = ready.pop(0), free.pop(0)
+                total(bank(b, 0, w), [([ID, FWD][side], reg("ZR", c, c + w)), (NID, reg("YG", 4096 * side + c, 4096 * side + c + w))])
+                staged.append((side, c, w, b))
 
         def short(n=1):
             for _ in range(n):
                 if staged:
-                    side, c, b = staged.pop(0)
-                    act(reg(mins[side], c, c + 512), bank(b), AF.Relu)
+                    side, c, w, b = staged.pop(0)
+                    act(reg(mins[side], c, c + w), bank(b, 0, w), AF.Relu)
                     free.append(b)
                     stage()
 
-        def home_sums(h, first):
-            c, nh, nf = 2048 * h, share(HOME, h), share(FAR, h)
-            mm(bank(4 + h, 0, 256), reg("MY", c, c + 2048, 16), START, first, False)
-            for n, y0, z0 in parts_of(nh, nf):
-                if n:
-                    mm(bank(4 + h, 128, 256, p1=n), reg("MY", c, c + 16 * n, 16), times(y0), False, False)
-                    mm(bank(4 + h, 128, 256, p1=n), reg("ZB", 256 * s + 128 * h, 256 * s + 128 * h + n), times(z0), False, False)
+        def home_sums(h):
+            c = 2048 * h
+            mm(bank(4 + h, 0, 128), reg("MY", c, c + 2048, 16), START, True, False)
             for k in range(1, 16):
-                mm(bank(4 + h, 8 * k, 8 * k + 8), reg("MY", c + k, c + 2048, 16), MINUS8, False, False)
+                mm(bank(4 + h, 8 * k, 8 * k + 8), reg("MY", c + k, c + 2048, 16), MINUS8, False, k == 15)
                 if k % 8 == 7:
-                    join(7 + k // 8)
+                    join(8)
 
         def far_sums(h):
+            c = 2048 * h
+            mm(bank(4 + h, 128, 256), reg("MY", c, c + 2048, 16), times(-1), True, False)
+            for n, y0, z0 in parts_of(share(HOME, h), share(FAR, h)):
+                mm(bank(4 + h, 128, 256, p1=n), reg("MY", c, c + 16 * n, 16), times(y0), False, False)
+                mm(bank(4 + h, 128, 256, p1=n), reg("ZB", 256 * s + 128 * h, 256 * s + 128 * h + n), times(z0), False, False)
             for l in range(16):
-                mm(bank(4 + h, 128 + 8 * l, 136 + 8 * l), reg("MH", 2048 * h + l, 2048 * h + 2048, 16), MINUS8, False, l == 15)
+                mm(bank(4 + h, 128 + 8 * l, 136 + 8 * l), reg("MH", 2048 * h + l, 2048 * h + 2048, 16), reg("R0", 128 + d // 16, 136 + d // 16), False, l == 15)
                 if l % 8 == 7:
                     join(8)
 
+        def signed(side, h, eng):
+            a = 128 * side
+            if eng == "a":
+                act(reg("TS", 256 * h + a, 256 * h + a + 128), bank(4 + h, a, a + 128), AF.Copy, scale=sign(share(side, h)))
+            else:
+                ts(reg("TS", 256 * h + a, 256 * h + a + 128), bank(4 + h, a, a + 128), sign(share(side, h)), OP.mult)
+
         def turn(h):
-            nh, nf = share(HOME, h), share(FAR, h)
-            for a, b, n in ([(0, 256, nh)] if nh == nf else [(0, 128, nh), (128, 256, nf)]):
-                act(reg("TS", 256 * h + a, 256 * h + b), bank(4 + h, a, b), AF.Copy, scale=sign(n))
             for odd in range(2):
                 mm(bank(4 + h, 256 + 128 * odd, 384 + 128 * odd), reg("TS", 256 * h + odd, 256 * h + 256, 2), ID, True, True)
 
-        def stack(h):
-            act(reg("FH", 256 * h, 256 * h + 256), bank(4 + h, 256, 512), bias=BIAS)
+        def stack(h, eng):
+            if eng == "a":
+                act(reg("FH", 256 * h, 256 * h + 256), bank(4 + h, 256, 512), bias=BIAS)
+            else:
+                ts(reg("FH", 256 * h, 256 * h + 256), bank(4 + h, 256, 512), BIAS, OP.add)
 
         def least(h):
             for odd in range(2):
@@ -699,156 +719,125 @@ def rank_program(g, core, T, topo):
                     else:
                         red(col("RR", a + 127), bank(zb[q], 256 * g2, 256 * g2 + 256), OP.min, True)
 
-        def far_offsets():
-            copy(reg("MO"), reg(TF, 0, 512, off=reg("BO16")))
-
-        def far_names():
-            act(reg("CM", 512, 768), reg(NF, off=reg("BO16")), AF.Copy)
-
-        def far_entries():
-            ts(reg("CM", 256, 512), reg("MO"), MID, OP.subtract, 2.0, OP.mult)
-
-        def stack_names():
-            for odd in range(2):
-                total(bank(0, 256 * odd, 256 * odd + 256), [(reg("PM", 128 * odd, 128 * odd + 128), Nn), (reg("PM", 256 + 128 * odd, 384 + 128 * odd), reg("CM", 512, 768))])
-            act(reg("NS"), bank(0), AF.Copy)
-            names(0, 1, 2, 3)
-
-        def bring(side, h):
-            for a in (0, 64):
-                fetch(side, h, a, a + 64)
-                stage()
-
-        def rows(h):
-            far_sums(h)
-            turn(h)
-            stack(h)
-
-        if t == 0:
-            sum_constants()
-            pair_constants()
-            ahead[0] = EARLY
-            later_constants()
-            last_constants()
-            ahead[0] = 0.0
-        else:
-            arrive("ta%d" % (t - 1))
-            arrive("tn%d" % (t - 1))
-            arrive("u1" if t == 1 else "tb%d" % (t - 2))
-        if t == 1:
-            arrive("l1")
-            copy(reg("TF1", 256, 512), reg("LC", 512, 768))
-        line[0] = "va"
-        for h in [0] if t in HALVES else [0, 1]:
-            gather(HOME, h)
-            bring(HOME, h)
-            short(4)
-            home_sums(h, True)
-        if t == 0:
-            copy(reg("TF0"), reg("LC", 0, 512))
-        line[0] = ""
-        if t == 2:
-            follow_home(t - 1)
-        far_offsets()
-        if t > 0:
-            follow_far(t - 1)
-        free[:] = [6, 7]
-        far_names()
-        stack_names()
-        line[0] = "va"
+        copy(reg("MO"), reg("TB", 0, 512, off=reg("BO16")))
+        act(reg("CM", 512, 768), reg("TN", off=reg("BO16")), AF.Copy)
+        for odd in range(2):
+            c = 256 * (1 + s) + 128 * odd
+            total(bank(0, 256 * odd, 256 * odd + 256), [(reg("PM", 128 * odd, 128 * odd + 128), Nn), (reg("PM", c, c + 128), reg("CM", 512, 768))])
+        act(reg("NS"), bank(0), AF.Copy)
+        names(0, 1, 3)
+        line[0] = LINE
+        gather(HOME, 0)
+        fetch(FAR, 0, 0, 64)
+        fetch(FAR, 0, 64, 128)
         gather(FAR, 0)
-        bring(FAR, 0)
+        home_sums(0)
         short(4)
-        if t in HALVES:
-            gather(HOME, 1)
-            bring(HOME, 1)
-            gather(FAR, 1)
-            rows(0)
-            short(4)
-            home_sums(1, True)
-            bring(FAR, 1)
-        else:
-            gather(FAR, 1)
-            bring(FAR, 1)
-            rows(0)
-        short(4)
+        free.remove(3)
+        names(2)
+        gather(HOME, 1)
+        signed(HOME, 0, "a")
+        far_sums(0)
+        fetch(FAR, 1, 0, 32)
+        signed(FAR, 0, "a")
+        turn(0)
+        fetch(FAR, 1, 32, 64)
+        gather(FAR, 1)
+        stack(0, "a")
+        home_sums(1)
+        short(1)
+        fetch(FAR, 1, 64, 128)
         costs(0, 1, 2, 3)
         least(0)
-        best(0, 1, 2, 3)
+        short(1)
+        signed(HOME, 1, "a")
+        short(2)
+        best(*TAIL[0])
+        far_sums(1)
+        signed(FAR, 1, TAIL[3])
+        turn(1)
+        best(*TAIL[1])
         names(6, 7, 4, 5)
-        rows(1)
+        stack(1, TAIL[4])
+        best(*TAIL[2])
         costs(6, 7, 4, 5)
-        best(6, 4, 7, 5)
+        best(6, 7, 4, 5)
         line[0] = ""
         least(1)
-        far_entries()
-        mm(bank(5), ID, reg("CM", 0, 512), True, True)
+        ts(reg("CM", 256, 512), reg("MO"), MID, OP.subtract, 2.0, OP.mult)
+        mm(bank(5, 0, 256), ID, reg("CM", 0, 256), True, False)
+        mm(bank(5, 256, 512), BACK, reg("CM", 256, 512), False, False)
 
-        tt(reg("KI", 32, 48), reg("RR", 127, 2048, 128), reg("NFK", 15, 256, 16), OP.min)
-        ts(reg("KI", 0, 16), reg("KI", 32, 48), 5, OP.logical_shift_right, 15, OP.bitwise_and)
-        ts(reg("KI", 16, 32), reg("KI", 32, 48), 31, OP.bitwise_and)
-        copy(reg("VA"), reg("KI", 0, 32))
-        mm(bank(1, 0, 128, p1=32), reg("VA"), ID, True, True)
-        copy(reg("VT", p1=32), bank(1, 0, 128, p1=32))
+        tt(reg("KI", 48, 64), reg("RR", 127, 2048, 128), reg("NFK", 15, 256, 16), OP.min)
+        ts(reg("KI", 0, 16), reg("KI", 48, 64), 5, OP.logical_shift_right, 15, OP.bitwise_and)
+        ts(reg("KI", 16, 32), reg("KI", 48, 64), 31, OP.bitwise_and)
+        ts(reg("KI", 32, 48), reg("KI", 48, 64), 4, OP.logical_shift_right, 1, OP.bitwise_and)
+        copy(reg("VA", 64, 112), reg("KI", 0, 48))
+        mm(bank(2, 0, 128, p1=96), reg("VA", 0, 96), ID, True, True)
+        mm(bank(1, 0, 128, p1=48), reg("VA", 64, 112), ID, True, True)
+        slot = reg("VT", p1=48)
+        act(reg("VT", p0=64, p1=96), reg("P2", 0, 128, 1, 64, 96), AF.Square)
+        copy(slot, bank(1, 0, 128, p1=48))
         for q in range(4):
-            mm(bank(2, 128 * q, 128 * q + 128), reg("RK", 128 * q, 128 * q + 128, p1=32), reg("VT", p1=32), True, True)
+            mm(bank(5, 128 * q, 128 * q + 128), reg("RK", 128 * q, 128 * q + 128, p1=96), reg("VT", p1=96), False, q == 3)
+        join(4)
+
+        def missed(b, c, first, last):
+            for h in range(2):
+                mm(bank(b, 128 * h, 128 * h + 128), reg("RK", c + 128 * h, c + 128 * h + 128, p1=48), slot, first and not h, last and h == 1)
+
         dn = bank(0, 0, 256)
         if t < R - 1:
             mm(dn, NID, Nn, True, False)
-            for j in range(16):
-                mm(bank(0, j, 256, 16), reg("SJ", 128 * j, 128 * j + 128), reg("BH"), False, j == 15)
-                if j % 8 == 7:
-                    join(8)
-        if t == 2:
-            total(bank(6, 256, 512), [(ID, Nn), (NID, reg("N0"))])
-            act(reg("T2", 512, 768), bank(6, 256, 512), AF.Copy)
-        ts(reg("WK", 0, 512), bank(2), P16, OP.is_equal)
-        tt(reg("WK", 512, 1024), reg("WK", 0, 512), bank(5), OP.mult)
-        mm(bank(6, 0, 256), BIG, reg("WK", 0, 256), True, False)
-        mm(bank(6, 0, 256), NBIG, reg("WK", 256, 512), False, False)
+            spread(dn, reg("BH"), False, False)
+        missed(6, 512, True, False)
+        line[0] = PICK
+        ts(reg("WK", 512, 1024), bank(5), col("WC", 1), OP.add, FLOOR, OP.max)
         mm(bank(4, 0, 256), BO, reg("WK", 512, 768), True, True)
-        to_list(bank(3, 0, 48), "U1", "WK", 256, 768)
+        to_list(bank(3, 16, 48), "U1", "WK", 512, 512)
+        ts(reg("WK", 0, 256), reg("WK", 512, 768), FLOOR, OP.is_gt)
+        act(reg("KB", 0, 256), bank(4, 0, 256), bias=-15 * FLOOR)
+        to_list(bank(7, 256, 272), "U1", "WK", 768, 256, d)
         mm(bank(5, 0, 256), BO, reg("WK", 768, 1024), True, True)
-        act(reg("KB", 0, 256), bank(4, 0, 256), AF.Copy)
-        if t >= 2:
-            total(bank(7, 0, 256), [(BO, reg("WK", 512, 768)), (BOM, reg("WK", 256, 512))])
-        rv, dm = 48 * s, 32 * t
-        tt(reg("HL", 0, 32), bank(3, 16, 48), reg("RAMP"), OP.subtract)
-        ts(reg("K1"), bank(3, 16, 48), 1.0, OP.add)
-        ts(reg("LM", 0, 32), bank(3, 16, 48), 0.5, OP.mult, MID, OP.add)
-        tt(reg("HL", 32, 48), reg("K1", 0, 16), reg("HL", 0, 16), OP.subtract)
-        ts(reg("RV", rv + 16, rv + 48), bank(3, 16, 48), 0.5, OP.mult, MID, OP.add)
-        tt(reg("HL", 64, 80), reg("HL", 32, 48), bank(3, 0, 16), OP.subtract)
-        tt(reg("D0", 0, 256, 16), reg("K1", 16, 32), reg("HL", 16, 32), OP.subtract)
-        keep, old = bank(7, 256, 512), built("X", t - 2)
-        if t >= 2:
-            ts(reg("G2", 64, 80), reg("K1", 0, 16), 2 * (W0 - MID), OP.is_ge)
-            tt(reg("G2", 80, 96), reg("G2", 64, 80), bank(3, 0, 16), OP.is_gt)
-            tt(reg("G2", 48, 64), reg("G2", 80, 96), reg("DM", dm - 48, dm - 32), OP.mult)
-            tt(reg("G2", 32, 48), reg("G2", 80, 96), reg("DM", dm - 64, dm - 48), OP.mult)
-            tt(reg("G2", 32, 64), reg("G2", 32, 64), reg("DUM", 0, 32), OP.add)
-            copy(reg("LM", 32, 48), reg("G2", 48, 64))
-            copy(reg("OH", 32, 48), reg("G2", 32, 48))
-        else:
-            send("m%d" % t)
+        if t == 2:
+            mm(bank(7, 0, 256), BO, reg("WK", 512, 768), True, False)
+            missed(7, 768, False, True)
+        rv = 48 * s
         offL, offM = reg("LM", 0, 16), reg("LM", 16, 32)
-        v = reg("VY", 512 * s, 512 * s + 256)
-        yk = reg("VY", 512 * s + 256, 512 * s + 512)
+        tt(reg("HL", 0, 32), bank(3, 16, 48), reg("RAMP"), OP.subtract)
+        ts(reg("K1"), bank(3, 16, 48), -15 * FLOOR, OP.add)
+        ts(reg("HL", 48, 64), bank(3, 32, 48), 16 * FLOOR, OP.is_equal, GATE, OP.mult)
+        ts(offL, bank(3, 16, 32), 0.5, OP.mult, MID - 7.5 * FLOOR, OP.add)
+        tt(reg("HL", 32, 48), reg("K1", 0, 16), reg("HL", 0, 16), OP.subtract)
+        tt(reg("HL", 64, 80), reg("HL", 0, 16), reg("HL", 48, 64), OP.add)
+        line[0] = ""
+        if t < R - 1:
+            ts(reg("RV", rv + 16, rv + 48), bank(3, 16, 48), 0.5, OP.mult, MID - 7.5 * FLOOR, OP.add)
+        else:
+            to_list(bank(1, 128, 144), "UK", "WK", 0, 256)
+            ts(reg("RS", 16, 48), bank(3, 16, 48), 0.5, OP.mult, -7.5 * FLOOR, OP.add)
+            ts(reg("G2", 0, 16), bank(3, 16, 32), 2 * (W0 - MID) + 15 * FLOOR, OP.is_ge, -3072.0 / GATE, OP.mult)
+            copy(reg("RS", 48, 64), bank(1, 128, 144))
+            tt(reg("RS", 64, 80), reg("G2", 0, 16), reg("HL", 48, 64), OP.mult)
+            send("r")
+        ts(reg("K1", 0, 16), reg("K1", 16, 32), 1.0, OP.add)
+        tt(reg("D0", 0, 256, 16), reg("K1", 0, 16), reg("HL", 16, 32), OP.subtract)
+        ts(offM, bank(7, 256, 272), 0.5, OP.mult, MID - 7.5 * FLOOR, OP.add)
+        v, yk, xm, wq = [reg("VY", 256 * q, 256 * q + 256) for q in range(4)]
+        SK, keep, old = reg("SK", 0, 256), reg("SK", 256, 512), built("X", t - 2)
         if t < R - 1:
             act(yk, entries("X", t, offL), AF.Copy)
-        else:
-            act(reg("TM"), entries("X", t, offL), AF.Relu, bias=63.0, scale=-1.0)
-            act(yk, reg("TM"), bias=63.0, scale=-1.0)
-        if t >= 2:
-            send("y%d" % t)
-            send("m%d" % t)
-        if t < R - 1:
-            send("at%d" % t)
-        act(reg("KB", 256, 512), bank(5, 0, 256), AF.Copy)
+        if t == 2:
+            act(SK, bank(7, 0, 256), AF.Sign, bias=1023.5 + 4096.0 + 15 * FLOOR, scale=-1.0)
+            total(bank(7, 256, 512), [(ID, old), (NID3, SK)])
+            act(wq, bank(7, 256, 512), AF.Relu, bias=-3072.0)
+        act(reg("KB", 256, 512), bank(5, 0, 256), bias=-15 * FLOOR)
+        act(xm, entries("X", t, offM), AF.Copy)
+        mm(bank(3, 256, 512), BACK, xm, True, True)
         nrow = bank(1, 256, 512)
-        act(reg("NR"), reg("IOX"), bias=float(P * t))
-        for q, (lhs, rhs) in enumerate([(ID, reg("NR")), (ID3, reg("WK", 0, 256)), (BOM, reg("WK", 0, 256))]):
-            mm(nrow, lhs, rhs, q == 0, False)
+        if t < R - 1:
+            act(reg("NR"), reg("IOX"), bias=float(P * t))
+            total(nrow, [(ID, reg("NR")), (ID3, reg("WK", 0, 256)), (BOM, reg("WK", 0, 256))], last=False)
 
         def first_of(ebuf, key, kcol, rest, cnt):
             e = [reg(ebuf, 264 * h - 8 * h * h, 264 * h - 8 * h * h + 256 - 16 * h) for h in range(16)]
@@ -860,115 +849,185 @@ def rank_program(g, core, T, topo):
                 join(b - a)
 
         tt(reg("TP"), entries("X", t, offL), z, OP.min)
-        first_of("EE", 0, 0, lambda h: col("HL", 64 + h), 6)
-        tt(v, entries(XF, t, offM), reg("TP"), OP.min)
-        send("v%d" % t)
-        mm(bank(2, 0, 256), BIG, reg("WK", 0, 256), True, False)
-        act(reg("TM"), v, AF.Copy, scale=-1.0)
+        first_of("EE", 0, 64, lambda h: col("HL", 32 + h), 6)
+        tt(v, bank(3, 256, 512), reg("TP"), OP.min)
+        mm(bank(2, 0, 256), BIG, reg("DIAG"), True, False)
         if t < R - 1:
             total(bank(4, 256, 512), [(ID, yk), (NID, z)])
             act(zn, bank(4, 256, 512), AF.Abs)
             to_list(bank(4, 0, 16), "UW", "ZB", 256 * (1 - s), 256)
+            to_list(bank(4, 16, 32), "UW", "ZB", 256 * (1 - s), 256, BLK * (2 - s))
+            act(nv(0), v, AF.Copy, scale=-1.0)
+            mm(bank(5, 0, 256), FWD, v, True, True)
+            act(nv(1), bank(5, 0, 256), AF.Copy, scale=-1.0)
+            if t < 2:
+                act(nv(6), bank(5, 0, 256), AF.Copy)
+        else:
+            send("v")
+        if t == 2:
+            mm(bank(7, 0, 256), FWD, wq, True, True)
+            act(nv(3), bank(7, 0, 256), AF.Copy)
+            total(bank(5, 256, 512), [(FWD, v), (NID, xm)])
+            act(nv(4), bank(5, 256, 512), AF.Copy)
+            act(keep, SK, bias=0.5, scale=0.5)
+            total(bank(7, 256, 512), [(ID, Nn), (NID, reg("N0"))])
         tt(reg("ST"), bank(6, 0, 256), reg("THR"), OP.is_lt)
         scan(reg("SL", 512, 768), reg("D0"), reg("ST"), -1024.0, OP.max, OP.subtract)
         mm(bank(2, 0, 256), NBIG, reg("ST"), False, False)
-        if t >= 2:
-            act(reg("SK"), bank(7, 0, 256), AF.Sign, bias=1023.5, scale=-1.0)
-            total(bank(5, 256, 512), [(ID, old), (ID3, reg("SK"))])
-            act(old, bank(5, 256, 512), AF.Relu, bias=-3072.0)
-            if t == 2:
-                act(keep, reg("SK"), bias=0.5, scale=0.5)
+        if t == 2:
+            gifts("X", t, [reg("OH", 0, 16), reg("OH", 16, 32)], [wq, nv(3)], offL, offM, nv(4))
+            total(bank(5, 0, 256), [(ID, old), (NID, wq)])
+            act(old, bank(5, 0, 256), AF.Copy)
         if t < R - 1:
-            send("a%d" % t)
-            for k in range(16):
-                if k < ZACT[t + 1]:
-                    act(reg("ZR", k, 4096, 16), zn, AF.Copy)
-                else:
-                    copy(reg("ZR", k, 4096, 16), zn)
+            repeat(t + 1)
         first_of("E2", 256, 16, lambda h: col("SL", 512 + 16 * h + 15), 2)
-        tt(reg("DM", dm, dm + 32), reg("RV", rv + 16, rv + 48), reg("DUM", 32, 64), OP.subtract)
+        if t < R - 1:
+            tt(reg("DM", 0, 32), reg("RV", rv + 16, rv + 48), reg("DUM", 32, 64), OP.subtract)
         tt(reg("BD"), bank(2, 0, 256), reg("THR"), OP.is_lt)
         scan(reg("SL", 256, 512), reg("SL", 0, 256), reg("BD"), 0.0, OP.mult, OP.max)
         build, builds = bank(2, 256, 512), reg("SL", 256 + 15, 512, 16)
+        if t == R - 1:
+            copy(reg("FS"), builds)
+            send("f")
+            break
         mm(nrow, BO3, reg("BD"), False, True)
         total(bank(5, 256, 512), [(ID, v), (BO3, reg("BD"))])
         act(built("X", t), bank(5, 256, 512), AF.Relu, bias=-3072.0)
-        if t < R - 1:
-            mm(build, BO, reg("BD"), True, True)
-        tt(reg("G2", 0, 16), builds, reg("DM", dm + 16, dm + 32), OP.mult)
-        tt(reg("G2", 16, 32), builds, reg("DM", dm, dm + 16), OP.mult)
-        tt(reg("G2", 0, 32), reg("G2", 0, 32), reg("DUM", 0, 32), OP.add)
-        copy(reg("OH", 0, 32), reg("G2", 0, 32))
-        send("o%d" % t)
-        arrive("m%d" % t)
-        chosen, given = reg("LG", 32 * t, 32 * t + 16), reg("LG", 32 * t + 16, 32 * t + 32)
-        if t < R - 1:
-            send("bo%d" % t)
-            copy(reg("BI", 48, 64), bank(4, 0, 16))
-            ts(reg("BI", 0, 16), reg("BI", 48, 64), 511, OP.bitwise_and)
-            payee(t + 1)
-
-        if t >= 2:
-            total(bank(4, 256, 512), [(ID, reg("PL16", 256 * s, 256 * s + 256)), (ID3, reg("SK")), (BO3, reg("WK", 0, 256))])
-            tt(C, C, bank(4, 256, 512), OP.min)
-        tt(C, C, nrow, OP.max)
-        if t == 2:
-            tt(reg("T2", 256, 512), reg("T2", 512, 768), keep, OP.mult)
-        if t < R - 1:
-            tt(reg("MK"), reg("WK", 0, 256), build, OP.mult)
-            tt(reg("T2", 0, 256), reg("MK"), dn, OP.mult)
-            base = [(ID, Nn)] if t < 2 else [(ID, reg("N0")), (ID, reg("T2", 256, 512))]
-            total(bank(0, 256, 512), base + [(ID, reg("T2", 0, 256))])
-            act(Nn, bank(0, 256, 512), AF.Copy)
-        if t >= 2:
-            act(reg("CO", s, 512, 2), C, AF.Copy)
-        if t < R - 1:
-            send("ta%d" % t)
-            send("tn%d" % t)
+        total(dn, [(ID3, reg("WK", 0, 256)), (BO3, reg("BD"))], first=False)
+        total(build, [(ID, reg("WK", 0, 256)), (BO, reg("BD"))])
+        home, far = reg("OH", 32 * t, 32 * t + 16), reg("OH", 32 * t + 16, 32 * t + 32)
+        tt(reg("G2", 0, 16), builds, reg("DM", 0, 16), OP.mult)
+        tt(reg("G2", 16, 32), builds, reg("DM", 16, 32), OP.mult)
+        tt(reg("G2", 32, 48), reg("G2", 0, 16), reg("DUM", 0, 16), OP.add)
+        tt(reg("GH"), reg("G2", 16, 32), reg("DUM", 64, 80), OP.add)
+        copy(home, reg("G2", 32, 48))
+        mm(bank(3, 64, 80), FWD, reg("GH"), True, True)
+        ts(far, bank(3, 64, 80), MIDP, OP.add)
+        if t == 1:
+            ts(reg("BG", 704, 720), reg("G2", 32, 48), MIDP, OP.subtract)
+            copy(reg("BG", 720, 736), bank(3, 64, 80))
+        copy(reg("BI", 32, 64), bank(4, 0, 32))
+        ts(reg("BI", 0, 32), reg("BI", 32, 64), 511, OP.bitwise_and)
+        copy(reg("BO16"), reg("BI", 16, 32))
+        if t < 2:
+            copy(reg("RV", 48 * (1 - s), 48 * (1 - s) + 16), reg("BI", 0, 16))
+            ts(reg("BH"), reg("BI", 0, 16), 256.0, OP.subtract)
         else:
-            dma("s", [(T.co[:], reg("CO"))])
+            ts(reg("RS", 0, 16), reg("BI", 0, 16), MID, OP.subtract)
 
-        arrive("v%d" % t)
-        fv, fw = reg("LV", LAND[t], LAND[t] + 256), reg("LV", LAND[t] + 256, LAND[t] + 512)
-        taken = reg("TV", 0, 256)
-        tt(places("X", t, reg("OH", 16, 32)), yk, reg("TM"), OP.add)
-        if t >= 2:
-            arrive("y%d" % t)
-        settle("X", t, chosen, fv, [(reg("OH", 32, 48), yk), (given, fw)] if t >= 2 else [], "NV", taken, bank(5, 0, 256))
-
+        if t == 2:
+            total(bank(4, 256, 512), [(ID, reg("PL16")), (ID3, SK), (BO3, reg("WK", 0, 256))])
+            tt(C, C, bank(4, 256, 512), OP.min)
+            tt(reg("T2", 256, 512), bank(7, 256, 512), keep, OP.mult)
+        tt(C, C, nrow, OP.max)
+        act(reg("T2", 0, 256), dn, AF.Relu, bias=512.0 - 6144.0)
+        act(reg("MK"), build, AF.Relu, bias=-512.0, scale=512.0)
+        base = [(ID, Nn)] if t < 2 else [(ID, reg("N0")), (ID, reg("T2", 256, 512))]
+        total(bank(0, 256, 512), base + [(ID, reg("T2", 0, 256)), (NID, reg("MK"))])
+        act(Nn, bank(0, 256, 512), AF.Copy)
+        takes("X", t, [home, far], yk if t < 2 else nv(5), offM, nv(6))
         for q in range(3):
             tt(reg("RC", 16 * q, 16 * q + 16), builds, reg("RV", rv + 16 * q, rv + 16 * q + 16), OP.mult)
-        if t < R - 1:
-            c2 = 256 * (1 - s)
-            act(reg("CM", 0, 256), reg("TB", c2, c2 + 256), bias=-2 * MID, scale=2.0)
-        ts(reg("RH"), reg("RC"), MID, OP.subtract)
-        for j in range(16):
-            mm(bank(6, j, 512, 16, p1=8), reg("ID", j, 128, 16), reg("RH", 0, 32), True, True)
-        join(16)
-        for j in range(16):
-            mm(bank(3, 256 + j, 512, 16, p1=8), reg("ID", j, 128, 16), reg("RH", 32, 48), True, True)
-        join(16)
-        act(reg("RO", 0, 512, p1=8), bank(6, 0, 512, p1=8), bias=MID)
-        act(reg("RO", 512, 768, p1=8), bank(3, 256, 512, p1=8), bias=MID)
-        dma("s", [(T.rec[8 * q:8 * q + 8, P * t:P * t + P], reg("RO", 256 * q, 256 * q + 256, p1=8)) for q in range(3)])
-        arrive("o%d" % t)
+        for q in range(3):
+            c = 512 + 96 * (t // 2) + 32 * q + 16 * s
+            act(reg("BG", c, c + 16), reg("RC", 16 * q, 16 * q + 16), bias=-MID)
+        act(reg("CM", 0, 256), reg("TB", 1 - s, 512, 2), bias=-2 * MID, scale=2.0)
         if t < 2:
             copy(reg("LO", 256 * s, 256 * s + 256), C)
-        if s == 0:
-            follow_home(t)
-        far_takes("X", t, chosen, reg("LF", 16 * t, 16 * t + 16), "NV", taken)
-        if t == R - 1:
-            for q, (a, b) in enumerate(((2304, 3072), (0, 1152), (1152, 2304))):
-                if q:
-                    ts(reg("X", P + a, P + b), reg("X", P + a, P + b), 63.0, OP.min)
-                dma("sa"[q % 2], [(T.xo[:, a:b], reg("X", P + a, P + b))])
+        else:
+            dma("s", [(reg("XQ", XQW * q, XQW * q + XQW), share_of("X", r, P, P + 4 * XQW)) for q, r in enumerate(others)])
+            send("xo")
+            act(reg("BG", 0, 512), reg("TB"), bias=-MID)
+            mm(bank(3, 256, 512), reg("ID", 2 * BLK, 2 * BLK + 128), built("X", 1), True, True)
+            act(reg("BG", 736, 992), bank(3, 256, 512), AF.Copy)
+            dma("s", [(reg("BQ", BQW * q, BQW * q + BQW), share_of("BG", r, 0, 4 * BQW)) for q, r in enumerate(others)] +
+                [(share_of("BN", rank, 0, 4 * BQW), share_of("BG", rank, 0, 4 * BQW))])
+            send("b")
+            dma("s", [(share_of("XO", rank, P, P + 4 * XQW), share_of("X", rank, P, P + 4 * XQW))])
+
+    t = R - 1
+    arrive("xo")
+    dma("s", [(share_of("XO", r, P, P + 4 * XQW), piece) for r, piece in landed("xo")[1:2]])
+    dma("s", [(share_of("XO", r, P, P + 4 * XQW), piece) for r, piece in landed("xo")[2:]])
+    arrive("b")
+    dma("s", [(share_of("BN", r, 0, 4 * BQW), piece) for r, piece in landed("b")[1:]])
+    for a in range(P, P + W0, 512):
+        ts(reg("XO", a, a + 512), reg("XO", a, a + 512), 63.0, OP.min)
+    back = [reg("OH", 96, 112), reg("OH", 112, 128)]
+    ts(reg("OH", 96, 128), reg("BN", 704, 736), MIDP, OP.add)
+    act(reg("CO"), reg("BN", 0, 512), bias=MID)
+    arrive("r")
+    total(bank(1, 0, 48), pick("r", 0, 0, 48))
+    total(bank(1, 48, 64), pick("r", 1, 32, 48))
+    total(bank(1, 64, 96), pick("r", 0, 48, 80))
+    total(bank(1, 96, 112), pick("r", 1, 64, 80))
+    copy(reg("RS", 80, 128), bank(1, 64, 112))
+    atL, atM = reg("LM", 32, 48), reg("LM", 48, 64)
+    ts(atL, bank(1, 16, 32), MID, OP.add)
+    ts(atM, bank(1, 48, 64), MID, OP.add)
+    ts(reg("RV", 96, 160), bank(1, 0, 64), MID, OP.add)
+    tt(reg("DM", 32, 48), reg("RV", 112, 128), reg("DUM", 32, 48), OP.subtract)
+    tt(reg("DM", 48, 64), reg("RV", 144, 160), reg("DUM", 32, 48), OP.subtract)
+    act(nv(9), entries("XO", t, atM), AF.Copy)
+    old = built("XO", t - 2)
+    for q, (b, held) in enumerate(((1, old), (3, reg("BN", 736, 992)))):
+        mm(bank(b, 256, 512), NID, held, True, False)
+        spread(bank(b, 256, 512), reg("RS", 96 + 16 * q, 112 + 16 * q), False, True)
+        act(nv(2 + q), bank(b, 256, 512), AF.Relu, bias=-3072.0, scale=-1.0)
+    arrive("v")
+    total(bank(4, 0, 256), pick("v", 1))
+    act(nv(1), bank(4, 0, 256), AF.Copy, scale=-1.0)
+    total(bank(5, 0, 256), [(NID, nv(1)), (NID, nv(9))])
+    act(nv(4), bank(5, 0, 256), AF.Copy)
+    total(bank(0, 256, 512), pick("v", 0))
+    act(nv(0), bank(0, 256, 512), AF.Copy, scale=-1.0)
+    ahead[0] = 8000.0
+    records(0, 6)
+    ahead[0] = 0.0
+    C = reg("CO", 1, 512, 2)
+    spread(bank(7, 0, 256), reg("RS", 80, 96), True, True)
+    ts(reg("MK"), bank(7, 0, 256), P16, OP.is_equal)
+    total(bank(2, 256, 512), [(ID, reg("PN", 1, 512, 2)), (ID3, reg("ONE"))], last=False)
+    spread(bank(2, 256, 512), reg("RS", 96, 112), False, True)
+    tt(C, C, bank(2, 256, 512), OP.min)
+    line[0] = "v"
+    gifts("XO", t, back, [nv(2), nv(3)], atL, atM, nv(4))
+    tt(old, old, nv(2), OP.subtract)
+    act(reg("NR"), reg("IOX"), bias=-256.0)
+    total(bank(7, 0, 256), [(ID, reg("NR")), (NID3, reg("ONE")), (ID3, reg("MK"))], last=False)
+    mm(bank(0, 0, 256), NID, nv(0), True, False)
+    arrive("f")
+    total(bank(2, 0, 16), pick("f", 0))
+    total(bank(2, 16, 32), pick("f", 1))
+    tt(reg("G2", 0, 32), bank(2, 0, 32), reg("DM", 32, 64), OP.mult)
+    ts(reg("FB"), bank(2, 0, 16), 3072.0, OP.mult)
+    tt(reg("G2", 32, 64), reg("G2", 0, 32), reg("DUM", 0, 32), OP.add)
+    copy(reg("OH", 128, 160), reg("G2", 32, 64))
+    line[0] = ""
+    for q in range(3):
+        tt(reg("RC", 16 * q, 16 * q + 16), bank(2, 0, 16), reg("RV", 96 + 16 * q, 112 + 16 * q), OP.mult)
+    spread(bank(7, 0, 256), reg("FB"), False, True)
+    spread(bank(0, 0, 256), reg("FB"), False, True)
+    ahead[0] = 3000.0
+    act(built("XO", t), bank(0, 0, 256), AF.Relu, bias=-3072.0)
+    dma("a", [(T.xo[:, W0 + P * t:W0 + P * R], built("XO", t))])
+    for q in range(3):
+        act(reg("BN", 624 + 32 * q, 640 + 32 * q), reg("RC", 16 * q, 16 * q + 16), bias=-MID)
+    records(1, 3)
+    ahead[0] = 0.0
+    line[0] = "v"
+    takes("XO", t, [reg("OH", 128, 144), reg("OH", 144, 160)], nv(5), atM, nv(6), lambda: tt(C, C, bank(7, 0, 256), OP.max))
+    dma("s", [(T.co[:], reg("CO"))])
+    dma("a", [(T.xo[:, ENDS[-1][1]:W0 + P * t], reg("XO", P + ENDS[-1][1], P + W0 + P * t))])
+    for q, (a, b) in enumerate(ENDS):
+        ts(reg("XO", P + a, P + b), reg("XO", P + a, P + b), 63.0, OP.min)
+        dma("sa"[q % 2], [(T.xo[:, a:b], reg("XO", P + a, P + b))])
 
     emit(g, T, ops, queue)
 
 
 def depend(ops):
     hist, sent, last = {}, {}, {}
-    reach = []
     for i, op in enumerate(ops):
         e = op["e"]
         need, after = set(), set()
@@ -991,22 +1050,10 @@ def depend(ops):
             after |= {last[e]} if e in last else set()
             last[e] = i
         if e == "x":
-            call, step = op["msg"]
-            gate = reach[sent[call]][-step % NR]
-            for j in need:
-                assert j < gate or ops[j]["e"] == "x"
-                if j < gate:
-                    ops[gate]["need"].add(j)
-            known = [-1] * NR
-            for o in range(NR):
-                known[(o + step) % NR] = reach[sent[call]][o]
-            known[step % NR] = sent[call]
-            need, after = set(), {sent[call]}
-        else:
-            known = [max([-1] + [reach[j][o] for j in need | (after if e == "g" else set())]) for o in range(NR)]
-            if op["msg"]:
-                sent[op["msg"]] = i
-        reach.append(known)
+            assert not need
+            after = {sent[op["msg"]]}
+        elif op["msg"]:
+            sent[op["msg"]] = i
         op["need"], op["after"] = need, after
         for kind, lst in (("r", op["r"]), ("w", op["w"])):
             for name, a, b, st, p0, p1 in lst:
@@ -1119,8 +1166,13 @@ def schedule(ops):
             end = max(t0, max(free[a:b])) + max(1, rows // (b - a)) * (m["row"] + m["byte"] * size)
             free[a:b] = [end] * (b - a)
             if die is not None:
-                at["port", die] = max(t0, at.get(("port", die), 0.0)) + rows * size * m["port"]
-                end = max(end, at["port", die])
+                need, t1, slots = rows * size * m["port"], t0, at.setdefault(("port", die), [])
+                for u, w in slots:
+                    if t1 + need > u:
+                        t1 = max(t1, w)
+                slots.append((t1, t1 + need))
+                slots.sort()
+                end = max(end, t1 + need)
             return end
 
         def begin(core, t0):
@@ -1149,7 +1201,7 @@ def schedule(ops):
         for i in seq:
             e = eng[i]
             if e == 5:
-                start[i] = end[i] = air[ops[i]["sem"][0][4:]]
+                start[i] = end[i] = air[ops[i]["sem"][0]]
                 continue
             t, seen = free[e], cover[e]
             for j, follow in waits[i]:

@@ -9,28 +9,28 @@ WT = [1, 64, 5, 83, 17, 131, 29, 211, 43, 157, 61, 239, 71, 113, 97, 199]
 XW = 3328
 MID = 1536.0
 GATE, FLOOR = 8192.0, -3200.0
+DEEP = 2.0 ** 22
 MIDP = 1664.0
-XQW, BQW = (W0 + 3 * P) // 4, 248
-SHARE = [(0, 0, 96, 64)] * 4
-HELPED = [(5, 7)] * 4
-BWACT = 10
+XQW, AQW, BQW = (W0 + 3 * P) // 4, 96, 152
+SHARE = [(0, 0, 80, 64)] + [(0, 0, 96, 64)] * 3
+HELPED = [(1, 3, 5, 7)] * 4
 BLOCKS = (0, 2, 4, 6, 8, 11, 14, 16)
-ZBY = ("vvavvavvavvavvav", "a" * 16, "a" * 16, "a" * 16)
+ZBY = [("vvva" * 4, "ggv" * 5 + "g"), ("a" * 16, "g" * 16), ("a" * 16, "g" * 16), ("aaag" * 4, "gggv" * 4)]
 ENDS = ((0, 1152), (1152, 2304))
 
 F, H16, B16, I32, U16 = "float32", "float16", "bfloat16", "int32", "uint16"
 SCRATCH = {
     "X": ("sbuf", [128, XW], B16), "XO": ("sbuf", [128, XW], B16),
-    "XP": ("sbuf", [128, 2048], B16), "XL": ("sbuf", [128, 1536], B16), "PK": ("sbuf", [128, 432], H16), "PA": ("sbuf", [128, 432], H16),
-    "ZS": ("sbuf", [128, 256], B16), "ZL": ("sbuf", [128, 192], B16), "NN": ("sbuf", [128, 512], B16), "NK": ("sbuf", [128, 512], B16), "NL": ("sbuf", [128, 384], B16),
-    "XQ": ("sbuf", [128, 3 * XQW], B16), "XK": ("sbuf", [128, 3 * XQW], B16),
-    "BG": ("sbuf", [128, 4 * BQW], H16), "BQ": ("sbuf", [128, 3 * BQW], H16), "BL": ("sbuf", [128, 3 * BQW], H16), "BN": ("sbuf", [128, 4 * BQW], H16),
-    "RS": ("sbuf", [128, 128], H16), "RL": ("sbuf", [128, 240], H16), "VL": ("sbuf", [128, 768], B16),
+    "XP": ("dram", [3, 128, 512], B16), "XS": ("sbuf", [128, 576], B16), "W4": ("sbuf", [128, 1120], B16), "XL": ("sbuf", [128, 1536], B16), "PK": ("sbuf", [128, 432], H16), "PA": ("sbuf", [128, 432], H16),
+    "ZS": ("dram", [3, 128, 64], B16), "ZL": ("sbuf", [128, 192], B16), "NN": ("sbuf", [128, 512], B16), "NK": ("sbuf", [128, 512], B16), "NL": ("sbuf", [128, 384], B16),
+    "XQ": ("dram", [3, 128, XQW], B16), "XK": ("dram", [3, 128, XQW], B16), "BG": ("sbuf", [128, 992], H16), "BN": ("sbuf", [128, 992], H16),
+    "AQ": ("dram", [3, 128, AQW], H16), "AL": ("dram", [3, 128, AQW], H16), "BQ": ("dram", [3, 128, BQW], H16), "BL": ("dram", [3, 128, BQW], H16),
+    "RS": ("sbuf", [128, 128], H16), "RL": ("sbuf", [128, 192], H16), "VL": ("sbuf", [128, 816], B16),
     "UK": ("sbuf", [128, 144], H16), "FS": ("sbuf", [128, 16], B16), "FA": ("sbuf", [128, 48], B16),
     "PL": ("sbuf", [128, 528], I32), "PN": ("sbuf", [128, 528], H16), "LN": ("sbuf", [128, 512], U16),
     "TP": ("sbuf", [128, 256], B16), "HL": ("sbuf", [128, 96], B16), "K1": ("sbuf", [128, 32], F),
     "TB": ("sbuf", [128, 512], F), "TN": ("sbuf", [128, 512], B16),
-    "PL16": ("sbuf", [128, 256], H16), "NR": ("sbuf", [128, 256], H16), "SK": ("sbuf", [128, 512], B16), "D0": ("sbuf", [128, 256], B16),
+    "PL16": ("sbuf", [128, 256], H16), "NR": ("sbuf", [128, 256], H16), "SK": ("sbuf", [128, 256], B16), "D0": ("sbuf", [128, 768], F),
     "FR": ("sbuf", [128, 128], I32), "FR16": ("sbuf", [128, 128], H16),
     "FW": ("sbuf", [128, 2048], F), "NG": ("sbuf", [128, 4096], H16), "N0": ("sbuf", [128, 256], H16),
     "MY": ("sbuf", [128, 4096], H16), "MH": ("sbuf", [128, 4096], H16), "ZR": ("sbuf", [128, 4096], B16), "ZF": ("sbuf", [128, 4096], B16),
@@ -42,53 +42,58 @@ SCRATCH = {
     "YG": ("sbuf", [128, 8192], B16), "SN": ("sbuf", [128, 1024], H16), "SC": ("sbuf", [128, 1024], H16), "SF": ("sbuf", [128, 64], H16),
     "R0": ("sbuf", [128, 1024], H16), "IA": ("sbuf", [128, 704], B16), "TIE": ("sbuf", [2, 576], F),
     "NFK": ("sbuf", [128, 256], F), "KI": ("sbuf", [128, 64], I32), "PD": ("sbuf", [128, 24], B16), "PS": ("sbuf", [128, 16], F),
-    "RR": ("sbuf", [128, 2048], F), "AB": ("sbuf", [128, 4096], F), "VA": ("sbuf", [128, 112], H16), "FL": ("sbuf", [128, 16], B16), "FL32": ("sbuf", [128, 16], F),
-    "BB": ("sbuf", [128, 256], B16), "BW": ("sbuf", [128, 2048], B16), "SL": ("sbuf", [128, 768], B16),
+    "RR": ("sbuf", [128, 2048], F), "AB": ("sbuf", [128, 4096], F), "VA": ("sbuf", [128, 112], H16), "FL": ("sbuf", [128, 16], B16),
+    "BB": ("sbuf", [128, 256], B16), "SL": ("sbuf", [128, 256], B16),
     "VT": ("sbuf", [128, 128], H16), "WK": ("sbuf", [128, 1024], H16), "KB": ("sbuf", [128, 512], H16),
-    "LM": ("sbuf", [128, 64], U16), "EE": ("sbuf", [128, 2176], B16), "E2": ("sbuf", [128, 2176], B16),
+    "LM": ("sbuf", [128, 64], U16), "EE": ("sbuf", [128, 16, 256], B16), "E2": ("sbuf", [128, 16, 256], B16),
     "ST": ("sbuf", [128, 256], B16), "BD": ("sbuf", [128, 256], B16),
     "VY": ("sbuf", [128, 1024], B16), "NV": ("sbuf", [128, 2560], B16),
-    "RV": ("sbuf", [128, 160], F), "DM": ("sbuf", [128, 64], F), "G2": ("sbuf", [128, 64], F), "GH": ("sbuf", [128, 16], H16),
+    "RV": ("sbuf", [128, 160], F), "DM": ("sbuf", [128, 64], F), "G2": ("sbuf", [128, 64], F), "GH": ("sbuf", [128, 48], H16),
     "OH": ("sbuf", [128, 160], U16), "FB": ("sbuf", [128, 16], B16),
     "RC": ("sbuf", [128, 48], F), "RO": ("sbuf", [24, 1024], F),
     "T2": ("sbuf", [128, 512], H16), "MK": ("sbuf", [128, 256], H16),
     "CO": ("sbuf", [128, 512], F),
     "PI": ("sbuf", [128, 16], I32), "PC": ("sbuf", [128, 16], B16),
     "IOX": ("sbuf", [128, 256], B16), "IOA": ("sbuf", [128, 384], B16), "IOB": ("sbuf", [128, 256], B16), "IOK": ("sbuf", [128, 128], B16),
-    "RK": ("sbuf", [128, 1024], B16), "DIAG": ("sbuf", [128, 256], B16), "ID": ("sbuf", [128, 640], H16), "RAMP": ("sbuf", [128, 32], F),
+    "RK": ("sbuf", [128, 768], B16), "DIAG": ("sbuf", [128, 256], B16), "ID": ("sbuf", [128, 640], H16),
     "SE": ("sbuf", [128, 1024], H16), "IZ": ("sbuf", [128, 640], B16), "ONE": ("sbuf", [128, 256], B16),
     "U1": ("sbuf", [128, 240], H16), "UW": ("sbuf", [128, 240], B16),
     "BK": ("sbuf", [128, 384], H16), "SJ": ("sbuf", [128, 2048], H16), "DG": ("sbuf", [128, 16], B16),
-    "WR": ("sbuf", [128, 32], F), "WC": ("sbuf", [128, 4], F), "SG": ("sbuf", [128, 512], F),
-    "THR": ("sbuf", [128, 256], F), "DUM": ("sbuf", [128, 80], F),
+    "WR": ("sbuf", [128, 32], F), "WC": ("sbuf", [128, 4], F), "SG": ("sbuf", [128, 256], F),
+    "S2": ("sbuf", [128, 256], F), "DUM": ("sbuf", [128, 48], F),
 }
 for _b in range(8):
     SCRATCH["P%d" % _b] = ("psum", [128, 512], F)
 
 MSGS = [("z", "ZS", 0, "ZL", 0, 64, True, ("near", 0, "far", 0)), ("p", "PK", 0, "PA", 0, 144, True, ("near", 0, "far", 0)),
         ("x", "XP", 0, "XL", 0, 512, True, ("near", 0, "far", 0)), ("n", "NK", 0, "NL", 0, 128, True, ("near", 0, "far", 0)),
+        ("a", "AQ", 0, "AL", 0, AQW, True, ("near", 0, "far", 0)),
         ("xo", "XQ", 0, "XK", 0, XQW, True, ("near", 0, "far", 0)), ("b", "BQ", 0, "BL", 0, BQW, True, ("near", 0, "far", 0)),
-        ("r", "RS", 0, "RL", 0, 80, False, ("near", 0, "far", 0)),
-        ("v", "VY", 0, "VL", 0, 256, False, ("near", 0, "far", 0)), ("f", "FS", 0, "FA", 0, 16, False, ("near", 0, "far", 0))]
+        ("r", "RS", 0, "RL", 0, 64, False, ("near", 0, "far", 0)),
+        ("v", "VY", 0, "VL", 0, 272, False, ("near", 0, "far", 0)), ("f", "FS", 0, "FA", 0, 16, False, ("near", 0, "far", 0))]
 NDMA = 32
 SEMAPHORES = ["sv", "sa", "sp", "sg"] + ["d%d" % i for i in range(NDMA)] + [k + m[0] for m in MSGS for k in ("arr_", "ard_", "snt_", "snd_")]
 ENG_SEM = {"v": "sv", "a": "sa", "p": "sp", "g": "sg"}
 PACES = [{"cycle": 0.85, "gather": 1.56, "scatter": 3.8, "wake": 170.0, "wait": 15.0, "issue": 350.0, "start": 1700.0, "row": 40.0, "byte": 0.055, "port": 0.013, "first": 3200.0, "load": 1500.0},
          {"cycle": 1.18, "gather": 1.9, "scatter": 5.0, "wake": 130.0, "wait": 25.0, "issue": 320.0, "start": 1600.0, "row": 30.0, "byte": 0.05, "port": 0.015, "first": 3000.0, "load": 1500.0},
          {"cycle": 0.98, "gather": 1.3, "scatter": 3.0, "wake": 220.0, "wait": 20.0, "issue": 500.0, "start": 2900.0, "row": 65.0, "byte": 0.08, "port": 0.022, "first": 4500.0, "load": 2000.0},
-         {"cycle": 0.9, "gather": 1.2, "scatter": 4.5, "wake": 260.0, "wait": 5.0, "issue": 250.0, "start": 2000.0, "row": 50.0, "byte": 0.05, "port": 0.028, "first": 4000.0, "load": 1600.0}]
+         {"cycle": 0.85, "gather": 1.15, "scatter": 2.5, "wake": 150.0, "wait": 10.0, "issue": 300.0, "start": 2200.0, "row": 60.0, "byte": 0.065, "port": 0.02, "first": 3200.0, "load": 2000.0},
+         {"cycle": 0.95, "gather": 1.8, "scatter": 4.0, "wake": 60.0, "wait": 10.0, "issue": 300.0, "start": 1500.0, "row": 35.0, "byte": 0.05, "port": 0.012, "first": 3000.0, "load": 1400.0},
+         {"cycle": 1.05, "gather": 1.05, "scatter": 2.0, "wake": 90.0, "wait": 15.0, "issue": 350.0, "start": 1800.0, "row": 45.0, "byte": 0.055, "port": 0.014, "first": 3200.0, "load": 1800.0}]
 DRAIN = [0.0, 120.0, 60.0, 0.0, 0.0]
 MARGIN = 900.0
-MIXES = [(mix, slack, room) for room, slack in ((0.0, 0.0), (200.0, 1000.0)) for mix in ((0.3, 0.3, 0.2, 0.2), (0.3, 0.4, 0.15, 0.15))]
+MIXES = [(mix, slack, room) for room, slack in ((0.0, 0.0), (200.0, 1000.0)) for mix in ((0.25, 0.2, 0.1, 0.1, 0.15, 0.2), (0.3, 0.2, 0.1, 0.1, 0.1, 0.2))]
 TURNS = [0, 1, 2] * 3
-TRIES, LOOSE = 30000, 0.0
-TAIL = ((0, 1), (2,), (3,), "a", "a")
-PICK = "vp"
+TRIES, LOOSE = 70000, 0.0
+REGROW, WINDOW, SHAKE = 2, 30, 400.0
+TAIL = ((7, 6, 5, 4), (6, 7, 4, 5), "v")
+PICK, DEDUP = "vp", "v"
+BOUND = 1024
 LANDING = 3000.0
 LATER = 0.0
 NAMING = 4000.0
-EARLY = 9000.0
-LINE = "va"
+EARLY = 0.0
+LINE = ""
 ORDER = {}
 
 
@@ -116,6 +121,11 @@ def ap(T, r):
     t = T[r["n"]]
     if r["off"] is not None:
         return t[:, r["a"]:r["b"]].indirect(ap(T, r["off"]))
+    if SCRATCH[r["n"]][0] == "dram":
+        return t[r["a"] // SCRATCH[r["n"]][1][2]]
+    if len(SCRATCH[r["n"]][1]) == 3:
+        w = SCRATCH[r["n"]][1][2]
+        return t[:, :, 0:16] if r.get("heads") else t[:, r["a"] // w, r["a"] % w:r["a"] % w + r["b"] - r["a"]]
     if r["s"] == 1:
         return t[r["p0"]:r["p1"], r["a"]:r["b"]]
     return t[r["p0"]:r["p1"], r["a"]:r["b"]:r["s"]]
@@ -139,7 +149,7 @@ def duration(eng, out, ins, per, m):
     if eng == "p":
         return 0.5 * m["cycle"] * max(min(64, width(ins[0])), width(out))
     if eng == "g":
-        return 130 + 2 * m["cycle"] * n
+        return m["cycle"] * ((200 if ins else 155) + 2 * n)
     if any(r["off"] is not None for r in full):
         return 60 + m["cycle"] * n * m["scatter" if out["off"] is not None else "gather"]
     if per is None:
@@ -164,6 +174,16 @@ def ways(T, topo, src, msg):
         piece = reg(buf, a + w * q * packed, a + w * q * packed + w)
         out.append((d, carrier.get(q), share[q] if q in share else topo.engines(src, d), piece, reg(land, b + w * q, b + w * q + w)))
     return out
+
+
+def staging(piece, land):
+    return piece if SCRATCH[piece["n"]][0] == "dram" else land
+
+
+def runs(a, b, engs):
+    if SCRATCH[a["n"]][0] == SCRATCH[b["n"]][0] == "dram":
+        return len(engs), 128 * row_bytes(a) // len(engs)
+    return 128, row_bytes(a)
 
 
 def mask_of(engs):
@@ -199,7 +219,7 @@ def carrier_program(g, core, T, topo):
         for dst, by, engs, piece, land in ways(T, topo, owners[0], msg):
             if by == core:
                 g.wait_ge(T.sem["arr_" + msg[0]], len(engs))
-                write(g, T, topo, core, "snt_" + msg[0], "arr_" + msg[0], [(dst, topo.engines(core, dst), land, land)])
+                write(g, T, topo, core, "snt_" + msg[0], "arr_" + msg[0], [(dst, topo.engines(core, dst), staging(piece, land), land)])
                 sent.append((msg[0], len(topo.engines(core, dst))))
     for name, n in sent:
         g.wait_ge(T.sem["snt_" + name], n)
@@ -280,22 +300,29 @@ def rank_program(g, core, T, topo):
         else:
             add("g", lambda: g.affine_select(A(out), A(in_), [[0, width(in_)]], OP.is_ge, 0.0, 0, 0), [out], [in_])
 
-    def dma(eng, pairs):
+    def dma(eng, pairs, after=()):
         name = "d%d" % ndma[0]
         ndma[0] += 1
 
         def fn():
             for out, in_ in pairs:
                 queue[eng].dma_start(A(out), A(in_)).then_inc(T.sem[name], 16)
-        short = [min((r for r in p if isinstance(r, dict)), key=row_bytes) for p in pairs]
-        add(eng, fn, [p[0] for p in pairs], [p[1] for p in pairs], sem=(name, 16 * len(pairs)),
-            legs=[(None, topo.engines(core, core), r["p1"] - r["p0"], row_bytes(r), None, [], None) for r in short])
+        every = topo.engines(core, core)
+        sides = [[r for r in p if isinstance(r, dict) and SCRATCH[r["n"]][0] != "dram"] for p in pairs]
+        moved = [min((r["p1"] - r["p0"], row_bytes(r)) for r in rs) if len(rs) < 2 else max((r["p1"] - r["p0"], row_bytes(r)) for r in rs)
+                 for rs in sides if rs] + [runs(p[0], p[0], every) for p, rs in zip(pairs, sides) if not rs]
+        add(eng, fn, [p[0] for p in pairs], [p[1] for p in pairs] + list(after), sem=(name, 16 * len(pairs)),
+            legs=[(None, every, rows, size, None, [], None, None) for rows, size in moved])
 
-    def send(name):
+    def send(name, *kinds):
         way = ways(T, topo, core, msgs[name])
         for snt, arr, part in (("snt_", "arr_", [w for w in way if w[1] is not None]), ("snd_", "ard_", [w for w in way if w[1] is None])):
-            trs = [(by or dst, engs, piece, land) for dst, by, engs, piece, land in part]
-            legs = [(arr + name, engs, 128, row_bytes(piece), by, topo.engines(by, dst) if by else [], topo.die(by or core)) for dst, by, engs, piece, land in part]
+            if kinds and (snt == "snt_") not in kinds:
+                continue
+            trs = [(by or dst, engs, piece, staging(piece, land) if by else land) for dst, by, engs, piece, land in part]
+            legs = [(arr + name, engs) + runs(piece, tr[3], engs) + (by, topo.engines(by, dst) if by else [], topo.die(by or core),
+                                                                     runs(tr[3], land, topo.engines(by, dst)) if by else None)
+                    for tr, (dst, by, engs, piece, land) in zip(trs, part)]
             add("g", lambda snt=snt, arr=arr, trs=trs: write(g, T, topo, core, snt + name, arr + name, trs), [], [tr[2] for tr in trs],
                 sem=(snt + name, sum(len(tr[1]) for tr in trs)), msg=snt + name, legs=legs)
 
@@ -315,6 +342,7 @@ def rank_program(g, core, T, topo):
     def landed(name, a=0, b=None):
         buf, c, land, d, w, packed = msgs[name][1:7]
         b, c = w if b is None else b, c + w * (NR - 1) * packed
+        buf, c = {"x": ("XS", 0), "z": ("XS", 512)}.get(name, (buf, c))
         return [(rank, reg(buf, c + a, c + b))] + [(r, reg(land, piece["a"] + a, piece["a"] + b)) for handed, r, n, piece in coming(name)]
 
     def move(a, b):
@@ -329,7 +357,8 @@ def rank_program(g, core, T, topo):
             banks = [o["n"] == out["n"] for o in outs]
             for j in senders:
                 r, piece = landed(name, a, b)[j]
-                mm(out, move(q, r), piece, j == 0 and True not in banks[:q], j == NR - 1 and True not in banks[q + 1:])
+                lhs = reg("W4", 224 * q + 96 - BLK * r, 224 * q + 224 - BLK * r) if name in "xz" else move(q, r)
+                mm(out, lhs, piece, j == 0 and True not in banks[:q], j == NR - 1 and True not in banks[q + 1:])
 
     share_of = lambda n, r, a, b: reg(n, a, b, 1, BLK * r, BLK * r + BLK)
     others = [(rank + q + 1) % NR for q in range(NR - 1)]
@@ -340,7 +369,7 @@ def rank_program(g, core, T, topo):
     col = lambda n, c: reg(n, c, c + 1)
     P16, PG, PP, PG16, PPAIR, PODD, P24, P3, P4, PF0, PF1 = [col("PC", c) for c in range(11)]
     BO, BOM, BO3 = [reg("BK", 128 * j, 128 * j + 128) for j in range(3)]
-    BIG, NBIG = [reg("BB", 128 * j, 128 * j + 128) for j in range(2)]
+    ALL, EARLIER = [reg("BB", 128 * j, 128 * j + 128) for j in range(2)]
     ROW, CROW, NCROW, KROW, BIAS, PP2, NFC, SIDE = [col("PD", c) for c in (0, 4, 5, 6, 7, 8, 9, 12)]
     ID, NID, ID3, NID3 = [reg("ID", 128 * j, 128 * j + 128) for j in (0, 2, 3, 4)]
     START, MINUS8 = reg("R0", 0, 128), reg("R0", 128, 136)
@@ -360,17 +389,16 @@ def rank_program(g, core, T, topo):
 
     ahead[0] = 20000.0
     rows = lambda r: slice(BLK * r, BLK * r + BLK)
-    quarters = lambda n, src, w, js: [(share_of(n, q, w * j, w * j + w), src[rows((others + [rank])[j]), w * q:w * q + w]) for j in js for q in range(NR)]
-    dma("s", quarters("ZS", T.z0, 64, range(3))[:6])
-    dma("a", quarters("ZS", T.z0, 64, range(3))[6:])
-    dma("s", [(reg("FR"), T.fr0[:])])
+    shares = lambda n, src, w: [(reg(n, w * j, w * j + w), src[rows(r), :]) for j, r in enumerate(others)]
+    line[0] = "va"
+    dma("s", shares("ZS", T.z0, 64))
+    dma("a", [(reg("FR"), T.fr0[:])])
     dma("a", [(reg("PL", 0, 512), T.pl[:]), (reg("PL", 512, 528), T.b0[:])])
-    dma("s", quarters("XP", T.x0, 512, range(3)))
-    dma("a", quarters("XP", T.x0, 512, [3]) + quarters("ZS", T.z0, 64, [3]))
+    dma("s", shares("XP", T.x0, 512))
     iota(col("PI", 0), [[0, 1]], 0, 1)
     iota(reg("IOA", 0, 128), [[1, 8], [0, 16]], 0, 0)
     iota(reg("IOX"), [[1, 256]], 0, 0)
-    send("z")
+    send("z", True)
     iota(reg("IA", 576, 704), [[0, 16], [1, 8]], 0, 0)
     iota(reg("IA", 0, 512, 1, 0, 64), [[1, 2], [4, 16], [0, 16]], 0, 0)
     iota(reg("IA", 0, 512, 1, 64, 128), [[1, 2], [0, 16], [4, 16]], 64, 0)
@@ -381,28 +409,36 @@ def rank_program(g, core, T, topo):
     ts(reg("DG"), reg("IOX", 0, 16), P16, OP.is_equal)
     for j in range(16):
         ts(reg("SJ", 128 * j, 128 * j + 128), BO, col("DG", j), OP.mult)
-    ts(reg("U1", 0, 144), reg("IOX", 0, 144), 15.0, OP.subtract, PG16, OP.is_equal)
+    line[0] = ""
+    ts(col("PI", 14), col("PI", 0), 2, OP.logical_shift_right)
+    for q, c in enumerate((1, 2, 3, 7)):
+        ts(col("PS", c), P3, float(q), OP.is_equal)
+    copy(col("PC", 11), col("PI", 14))
+    ts(reg("W4", 896, 1120), reg("IOX", 0, 224), 96.0, OP.subtract, col("PC", 11), OP.is_equal)
+    for q, c in enumerate((1, 2, 3, 7)):
+        act(reg("W4", 224 * q, 224 * q + 224), reg("W4", 896, 1120), AF.Copy, scale=col("PS", c))
+    line[0] = "vap"
     ts(ID, reg("IOX", 0, 128), PP, OP.is_equal)
-    copy(reg("ID", 128, 256), ID)
     for r in range(NR):
         ts(col("PD", 13 + r), PPAIR, float(r), OP.is_equal)
+    copy(reg("FR16"), reg("FR"))
+    copy(reg("ID", 128, 256), ID)
     for r in range(NR):
         ts(reg("SE", 256 * r, 256 * r + 256), reg("ID", 0, 256), col("PD", 13 + r), OP.mult)
-    line[0] = "vap"
-    copy(reg("FR16"), reg("FR"))
     for j in range(16):
         mm(bank(j // 4, 128 * (j % 4), 128 * (j % 4) + 128), reg("SJ", 128 * j, 128 * j + 128), reg("FR16"), True, True)
     for q in range(4):
-        same("av"[q % 2], reg("FW", 512 * q, 512 * q + 512), bank(q))
+        same("avaa"[q], reg("FW", 512 * q, 512 * q + 512), bank(q))
     copy(reg("PN"), reg("PL"))
     copy(reg("LN"), reg("PN", 0, 512))
     for j, r in enumerate(others):
         total(bank(4, 144 * j, 144 * j + 128), [(move(r, q), reg("PN", 128 * q, 128 * q + 128)) for q in range(NR)])
         mm(bank(4, 144 * j + 128, 144 * j + 144), move(r, 0), reg("PN", 512, 528), True, True)
         join(NR + 1)
-    act(reg("PK"), bank(4, 0, 432), AF.Copy)
-    send("p")
-    send("x")
+    copy(reg("PK"), bank(4, 0, 432))
+    for handed, name in ((True, "p"), (True, "x"), (False, "x"), (False, "z"), (False, "p")):
+        send(name, handed)
+    dma("s", [(reg("XS", 0, 512), T.x0[rows(rank), :]), (reg("XS", 512, 576), T.z0[rows(rank), :])], [reg("PK")])
     ahead[0] = NAMING
     iota(reg("TIE", 0, 512, p1=2), [[0, 2], [32, 16], [1, 16]], 0, 0)
     iota(reg("TIE", 512, 576, p1=2), [[0, 4], [32, 16]], 16, 0)
@@ -415,29 +451,37 @@ def rank_program(g, core, T, topo):
     OWN, DIRECT, HANDED = [0], [1], [2, 3]
     xq, pq = [bank(q) for q in range(NR)], [bank(7, 128 * q, 128 * q + 128) for q in range(NR)]
     mm(bank(7), move(rank, rank), reg("PN", 0, 512), True, False)
-    unpack(xq, "x", OWN)
 
-    for half in range(2):
-        for q in (2 * half, 2 * half + 1):
-            out = reg(["NG", "MH"][half], 2048 * (q % 2), 2048 * (q % 2) + 2048)
-            same("av"[q % 2], out, reg("FW", off=reg("LN", 128 * q, 128 * q + 128)))
-            for k in range(16):
-                mm(bank(4 + q % 2, k, 128, 16), reg(out["n"], out["a"] + k, out["b"], 16), reg("BK", 0, 128, 16), True, True)
-            join(16)
-        if half == 0:
-            line[0] = "p"
-            arrive("p", False)
-            unpack(pq, "p", DIRECT, 0, 128)
-        for q in (2 * half, 2 * half + 1):
-            act(reg("NN", 128 * q, 128 * q + 128), bank(4 + q % 2, 0, 128), bias=-256.0, scale=1.0 / 16)
-            for j, r in enumerate(others + [rank]):
-                mm(reg("P6", 128 * j, 128 * j + 128, 1, BLK * q, BLK * q + BLK), reg("NN", 128 * q + BLK * r, 128 * q + BLK * r + BLK), ID, True, True)
-            join(NR)
+    def named(q):
+        act(reg("NN", 128 * q, 128 * q + 128), bank(4 + q % 2, 0, 128), bias=-256.0, scale=1.0 / 16)
+
+    def turned(q):
+        for j, r in enumerate(others + [rank]):
+            mm(reg("P6", 128 * j, 128 * j + 128, 1, BLK * q, BLK * q + BLK), reg("NN", 128 * q + BLK * r, 128 * q + BLK * r + BLK), ID, True, True)
+        join(NR)
+
+    looked = [reg(["NG", "MH"][q // 2], 2048 * (q % 2), 2048 * (q % 2) + 2048) for q in range(NR)]
+    for q in range(NR):
+        same("av"[q % 2], looked[q], reg("FW", off=reg("LN", 128 * q, 128 * q + 128)))
+    for q in range(NR):
+        if q >= 2:
+            named(q - 2)
+        for k in range(16):
+            mm(bank(4 + q % 2, k, 128, 16), reg(looked[q]["n"], looked[q]["a"] + k, looked[q]["b"], 16), reg("BK", 0, 128, 16), True, True)
+        join(16)
+        if q == 1:
+            unpack(xq, "x", OWN)
+        if q >= 2:
+            turned(q - 2)
+    for q in (2, 3):
+        named(q)
+        turned(q)
     act(reg("NK"), bank(6), AF.Copy)
     line[0] = ""
     send("n")
     ahead[0] = EARLY
     fill(reg("X", 0, P), 0.0)
+    ts(reg("U1", 0, 143), reg("IOX", 0, 143), 15.0, OP.subtract, PG16, OP.is_equal)
     ts(reg("U1", 143, 240), reg("IOX", 15, 112), 15.0, OP.subtract, PG16, OP.is_equal)
 
     def sum_constants():
@@ -447,11 +491,11 @@ def rank_program(g, core, T, topo):
             ts(col("PS", 8 + n // 16), PP, float(n), OP.is_ge, 2.0, OP.mult)
         for n in parts:
             ts(sign(n), col("PS", 8 + n // 16), 1.0, OP.subtract)
-        ts(NID, ID, -1.0, OP.mult)
+        act(NID, ID, AF.Copy, scale=-1.0)
         fill(reg("R0", 0, 8), 0.0)
         ts(reg("R0", 8, 128), reg("IA", 584, 704), PG, OP.is_equal)
         for c in sorted({c for sh in SHARE for h in range(2) for n, y0, z0 in parts_of(sh[h], sh[2 + h]) for c in (y0, z0)} - {-1}):
-            ts(times(c), reg("IA", 576, 704), PG, OP.is_equal, float(c), OP.mult)
+            act(times(c), times(-1), AF.Copy, scale=-float(c))
 
     def pair_constants():
         ts(ROW, P16, 4.0, OP.mult, PPAIR, OP.add)
@@ -489,71 +533,41 @@ def rank_program(g, core, T, topo):
         ts(reg("SF", p1=2), reg("TIE", 512, 576, p1=2), reg("DG", 0, 1, p1=2), OP.mult, reg("PD", 9, 10, p1=2), OP.add)
 
     def later_constants():
-        act(reg("SG", 256, 512), reg("SG", 0, 256), bias=0.5, scale=2.0 ** -24)
-        ts(BOM, BO, -4096.0, OP.mult)
-        ts(BO3, BO, 3072.0, OP.mult)
-        ts(ID3, ID, 3072.0, OP.mult)
-        ts(NID3, ID, -3072.0, OP.mult)
-        ts(reg("SL", 0, 256), reg("IOB"), 0.0, OP.not_equal)
-        fill(reg("D0"), -1024.0)
-        fill(reg("RAMP", 0, 16), 15 * FLOOR)
-        ts(reg("RAMP", 16, 32), reg("IOX", 0, 16), 20.0, OP.mult, 15 * FLOOR - 150.0, OP.add)
-        fill(reg("XO", 0, P), 0.0)
-        fill(reg("BG", 512, 704), 0.0)
-        fill(reg("IZ"), 0.0)
-        copy(reg("IZ", 256, 384), ID)
-        fill(reg("ONE"), 1.0)
-
-    def last_constants():
-        ts(col("WC", 2), PP, 0.0, OP.mult, 2.0 ** 61, OP.add)
+        for out, in_, c in ((BOM, BO, -4096.0), (BO3, BO, 3072.0), (ID3, ID, 3072.0), (NID3, ID, -3072.0), (ALL, BO, GATE)):
+            act(out, in_, AF.Copy, scale=c)
         ts(col("PD", 21), PP, 32.0, OP.is_lt, 2 * GATE, OP.mult)
         ts(col("PD", 22), PP, 64.0, OP.is_ge, -GATE, OP.mult)
         ts(reg("IOK"), reg("IOK"), col("PD", 21), OP.mult, col("PD", 22), OP.add)
-        for q in range(4):
-            for p0 in (0, 64):
-                out, in_ = reg("RK", 128 * q, 128 * q + 128, 1, p0, p0 + 64), reg("IOK", 0, 128, 1, p0, p0 + 64)
-                add("g", lambda q=q, out=out, in_=in_: g.affine_select(A(out), A(in_), [[1, 4], [4, 2], [0, 16]], OP.is_equal, 0.0, 8 * q, -1), [out], [in_])
         fill(reg("VA", 0, 64), 0.0)
         fill(reg("VT", p0=32, p1=64), 0.0)
         ts(col("WC", 1), P16, P16, OP.mult, -GATE, OP.mult)
+        copy(col("WC", 2), P16)
         tt(reg("WR", 16, 32), reg("WR", 0, 16), reg("DG"), OP.mult)
-        ts(col("WC", 3), col("WC", 2), 2.0 ** 60, OP.mult)
-        for a, c in ((0, 0.0), (16, 0.0), (32, -256.0), (48, -256.0), (64, -MIDP)):
-            ts(reg("DUM", a, a + 16), reg("IOX", 0, 256, 16), P16, OP.add, c, OP.add)
+        ts(reg("DUM", 0, 16), reg("IOX", 0, 256, 16), P16, OP.add, -1.0, OP.mult)
+        for a in (16, 32):
+            act(reg("DUM", a, a + 16), reg("DUM", 0, 16), bias=MIDP)
         red(col("WC", 0), reg("WR", 16, 32), OP.add)
-        scan(reg("THR"), reg("SG", 256, 512), reg("X", 0, P), col("WC", 3), OP.mult, OP.add)
-        ts(BIG, BO, col("WC", 3), OP.mult, 2.0, OP.mult)
-        ts(reg("NFK"), reg("IOB"), P16, OP.is_equal)
-        ts(reg("DIAG"), reg("IOB"), P16, OP.is_equal)
-        copy(col("PD", 23), col("WC", 3))
-        ts(reg("RK", 512, 768), reg("IOA", 128, 384), KROW, OP.is_equal, col("PD", 23), OP.mult)
-        ts(reg("RK", 768, 1024), reg("IOA", 128, 384), KROW, OP.is_equal, 4096.0, OP.mult)
         act(reg("UW"), reg("U1"), AF.Copy, scale=col("WC", 0))
-        act(NBIG, BIG, AF.Copy, scale=-1.0)
-        ts(reg("UK"), reg("U1", 0, 144), P16, OP.mult)
-        tt(reg("THR"), reg("THR"), reg("NFK"), OP.mult)
-        scan(reg("NFK"), reg("SL", 0, 256), reg("THR"), 0.0, OP.mult, OP.max)
-        act(reg("FL", 0, 16), reg("NFK", 15, 256, 16), AF.Copy, scale=0.5)
-        act(reg("FL32"), reg("NFK", 15, 256, 16), AF.Copy, scale=0.5)
-        for h in range(16):
-            if h < BWACT:
-                act(reg("BW", 128 * h, 128 * h + 128), BO, AF.Copy, scale=col("FL32", h))
-            else:
-                ts(reg("BW", 128 * h, 128 * h + 128), BO, col("FL", h), OP.mult)
+        ts(reg("RK", 512, 768), reg("IOA", 128, 384), KROW, OP.is_equal, GATE, OP.mult)
+        ts(EARLIER, reg("IOB", 0, 128), P16, OP.is_gt, GATE, OP.mult)
+        tt(EARLIER, EARLIER, BO, OP.mult)
+        ts(reg("DIAG"), reg("IOB"), P16, OP.is_equal, -3 * DEEP, OP.mult)
+        act(reg("DIAG"), reg("DIAG"), bias=2 * DEEP)
 
     sum_constants()
     pair_constants()
     ahead[0] = LATER
     later_constants()
-    last_constants()
     ahead[0] = LANDING
 
     line[0] = "p"
+    arrive("x", False)
+    unpack(xq, "x", DIRECT)
     arrive("z")
     unpack([bank(4, 64 * q, 64 * q + 64) for q in range(NR)], "z", range(NR))
     copy(reg("ZB", 0, 256), bank(4, 0, 256))
-    arrive("x", False)
-    unpack(xq, "x", DIRECT)
+    arrive("p", False)
+    unpack(pq, "p", DIRECT, 0, 128)
     arrive("p", True)
     unpack(pq, "p", HANDED, 0, 128)
     for shift in range(2):
@@ -563,7 +577,7 @@ def rank_program(g, core, T, topo):
     unpack(xq, "x", HANDED)
     line[0] = ""
     for q in range(NR):
-        same("av"[q % 2], reg("X", P + 512 * q, P + 512 * q + 512), bank(q))
+        same("aaav"[q], reg("X", P + 512 * q, P + 512 * q + 512), bank(q))
     act(reg("TB"), bank(7), AF.Copy)
     copy(reg("LO", 0, 256), reg("TB", 0, 512, 2))
     copy(reg("BO16"), bank(5, 16, 32))
@@ -579,38 +593,60 @@ def rank_program(g, core, T, topo):
     act(reg("PL16"), reg("TB", 0, 512, 2), AF.Copy)
 
     def repeat(t):
-        d = BLK * (1 + t % 2)
-        for k in range(16):
-            same(ZBY[t][k], reg("ZR", k, 4096, 16), reg("ZB", 256 * (t % 2), 256 * (t % 2) + 256))
         for h in range(2):
-            a, b = 2048 * h + 16 * SHARE[t][2 + h], 2048 * h + 2048
-            if a < b:
-                dma("s", [(reg("ZF", a, b, 1, d, 128), reg("ZR", a, b, 1, 0, 128 - d)), (reg("ZF", a, b, 1, 0, d), reg("ZR", a, b, 1, 128 - d, 128))])
+            for k in range(16):
+                same(ZBY[t][h][k], reg("ZR", 2048 * h + k, 2048 * h + 2048, 16), reg("ZB", 256 * (t % 2) + 128 * h, 256 * (t % 2) + 128 * h + 128))
+        shifted(t, 0)
+
+    def shifted(t, h):
+        d, a, b = BLK * (1 + t % 2), 2048 * h + 16 * SHARE[t][2 + h], 2048 * h + 2048
+        dma("s", [(reg("ZF", a, b, 1, d, 128), reg("ZR", a, b, 1, 0, 128 - d)), (reg("ZF", a, b, 1, 0, d), reg("ZR", a, b, 1, 128 - d, 128))])
 
     def gifts(x, t, offs, w, at_home, at_far, less):
         act(nv(7), places(x, t - 2, offs[0]), AF.Copy)
         tt(places(x, t - 2, offs[0]), nv(7), w[0], OP.add)
-        tt(nv(8), places(x, t - 2, offs[1]), w[1], OP.add)
-        copy(places(x, t - 2, offs[1]), nv(8))
-        tt(nv(6), entries(x, t, at_far), less, OP.add)
-        act(nv(5), entries(x, t, at_home), AF.Copy)
+        if less["n"] == "NV":
+            tt(nv(8), places(x, t - 2, offs[1]), w[1], OP.add)
+            copy(places(x, t - 2, offs[1]), nv(8))
+            tt(nv(6), entries(x, t, at_far), less, OP.add)
+            act(nv(5), entries(x, t, at_home), AF.Copy)
+        else:
+            act(nv(8), places(x, t - 2, offs[1]), AF.Copy)
+            tt(places(x, t - 2, offs[1]), nv(8), w[1], OP.add)
+            act(nv(4), entries(x, t, at_far), AF.Copy)
+            act(nv(5), entries(x, t, at_home), AF.Copy)
+            mm(less, ID, nv(4), False, True)
+            act(nv(6), less, AF.Copy)
 
-    def takes(x, t, offs, held, at_far, floor, between=lambda: None):
+    def takes(x, t, offs, held, at_far, floor):
         tt(places(x, t, offs[0]), held, nv(0), OP.add)
-        between()
         tt(nv(9), entries(x, t, at_far), floor, OP.max)
         tt(places(x, t, offs[1]), nv(9), nv(1), OP.add)
 
     def records(pair, b):
         for q in range(3):
-            c = 512 + 96 * pair + 32 * q
+            c = 256 + 384 * pair + 32 * q
             for j in range(16):
                 mm(bank(b, j, 512, 16, p1=24), reg("IZ", 256 - 128 * q + j, 640 - 128 * q, 16), reg("BN", c, c + 32), q + j == 0, q + j == 17)
             join(16)
         act(reg("RO", 512 * pair, 512 * pair + 512, p1=24), bank(b, p1=24), bias=MID)
         dma("s", [(T.rec[:, 512 * pair:512 * pair + 512], reg("RO", 512 * pair, 512 * pair + 512, p1=24))])
 
+    def homeward(name, packed, a, w):
+        dma("s", [(reg(packed, w * q, w * q + w), share_of("BG", r, a, a + 4 * w)) for q, r in enumerate(others)] +
+            [(share_of("BN", rank, a, a + 4 * w), share_of("BG", rank, a, a + 4 * w))])
+        send(name)
+
     repeat(0)
+    shifted(0, 1)
+    iota(reg("D0"), [[0, 768]], 0, 0)
+    iota(reg("D0", 512 + 15, 768, 16), [[0, 16]], int(DEEP), 0)
+    for q in range(4):
+        for p0 in (0, 64):
+            out, in_ = reg("RK", 128 * q, 128 * q + 128, 1, p0, p0 + 64), reg("IOK", 0, 128, 1, p0, p0 + 64)
+            add("g", lambda q=q, out=out, in_=in_: g.affine_select(A(out), A(in_), [[1, 4], [4, 2], [0, 16]], OP.is_equal, 0.0, 8 * q, -1), [out], [in_])
+    for out, c in ((reg("XO", 0, P), 0), (reg("ONE"), 1), (reg("IZ", 0, 256), 0), (reg("IZ", 384, 640), 0)):
+        iota(out, [[0, 256]], c, 0)
 
     for t in range(R):
         s = t % 2
@@ -630,13 +666,17 @@ def rank_program(g, core, T, topo):
             n = share(side, h)
             if n < 128:
                 a, b = 2048 * h + 16 * n, 2048 * h + 2048
+                line[0] = LINE + "v"
                 tt(reg(mins[side], a, b), window(side, h, n, 128), reg(["ZR", "ZF"][side], a, b), OP.min)
+                line[0] = LINE
 
         def fetch(side, h, a, b):
             b = min(b, share(side, h))
             if a < b:
                 c = 4096 * side + 2048 * h
                 act(reg("YG", c + 16 * a, c + 16 * b), window(side, h, a, b), AF.Copy)
+                if t == R - 1 and h == 0:
+                    ops[-1]["r"] += spans([reg("BG", *[(384, 736), (736, 992), (736, 992)][a // 32])])
                 ready.extend((side, 2048 * h + 16 * q, 16 * min(32, b - q)) for q in range(a, b, 32))
                 stage()
 
@@ -644,6 +684,8 @@ def rank_program(g, core, T, topo):
             while ready and free:
                 (side, c, w), b = ready.pop(0), free.pop(0)
                 total(bank(b, 0, w), [([ID, FWD][side], reg("ZR", c, c + w)), (NID, reg("YG", 4096 * side + c, 4096 * side + c + w))])
+                if t == 0:
+                    ops[-2]["r"] += spans([reg("X", P, P + 512)])
                 staged.append((side, c, w, b))
 
         def short(n=1):
@@ -662,23 +704,23 @@ def rank_program(g, core, T, topo):
                 if k % 8 == 7:
                     join(8)
 
-        def far_sums(h):
+        def far_start(h):
             c = 2048 * h
             mm(bank(4 + h, 128, 256), reg("MY", c, c + 2048, 16), times(-1), True, False)
             for n, y0, z0 in parts_of(share(HOME, h), share(FAR, h)):
                 mm(bank(4 + h, 128, 256, p1=n), reg("MY", c, c + 16 * n, 16), times(y0), False, False)
                 mm(bank(4 + h, 128, 256, p1=n), reg("ZB", 256 * s + 128 * h, 256 * s + 128 * h + n), times(z0), False, False)
+            join(1 + 2 * len(parts_of(share(HOME, h), share(FAR, h))))
+
+        def far_sums(h):
             for l in range(16):
                 mm(bank(4 + h, 128 + 8 * l, 136 + 8 * l), reg("MH", 2048 * h + l, 2048 * h + 2048, 16), reg("R0", 128 + d // 16, 136 + d // 16), False, l == 15)
                 if l % 8 == 7:
                     join(8)
 
-        def signed(side, h, eng):
+        def signed(side, h):
             a = 128 * side
-            if eng == "a":
-                act(reg("TS", 256 * h + a, 256 * h + a + 128), bank(4 + h, a, a + 128), AF.Copy, scale=sign(share(side, h)))
-            else:
-                ts(reg("TS", 256 * h + a, 256 * h + a + 128), bank(4 + h, a, a + 128), sign(share(side, h)), OP.mult)
+            act(reg("TS", 256 * h + a, 256 * h + a + 128), bank(4 + h, a, a + 128), AF.Copy, scale=sign(share(side, h)))
 
         def turn(h):
             for odd in range(2):
@@ -690,13 +732,14 @@ def rank_program(g, core, T, topo):
             else:
                 ts(reg("FH", 256 * h, 256 * h + 256), bank(4 + h, 256, 512), BIAS, OP.add)
 
-        def least(h):
+        def slots(h):
             for odd in range(2):
                 a = 128 * h + 64 * odd
                 mm(bank(4, a, a + 64), reg("FH", 256 * h + 128 * odd, 256 * h + 128 * odd + 128), reg("SF"), True, True)
-            was, line[0] = line[0], ""
+            join(2)
+
+        def least(h):
             scan(reg("NFK", 128 * h, 128 * h + 128), reg("SG", 0, 128), bank(4, 128 * h, 128 * h + 128), 0.0, OP.add, OP.min)
-            line[0] = was
 
         def names(*qs):
             for q in qs:
@@ -724,44 +767,49 @@ def rank_program(g, core, T, topo):
         for odd in range(2):
             c = 256 * (1 + s) + 128 * odd
             total(bank(0, 256 * odd, 256 * odd + 256), [(reg("PM", 128 * odd, 128 * odd + 128), Nn), (reg("PM", c, c + 128), reg("CM", 512, 768))])
-        act(reg("NS"), bank(0), AF.Copy)
-        names(0, 1, 3)
         line[0] = LINE
         gather(HOME, 0)
-        fetch(FAR, 0, 0, 64)
-        fetch(FAR, 0, 64, 128)
+        for a in (0, 32, 64):
+            fetch(FAR, 0, a, a + 32)
         gather(FAR, 0)
         home_sums(0)
-        short(4)
+        short(3)
         free.remove(3)
-        names(2)
         gather(HOME, 1)
-        signed(HOME, 0, "a")
+        signed(HOME, 0)
+        far_start(0)
         far_sums(0)
-        fetch(FAR, 1, 0, 32)
-        signed(FAR, 0, "a")
+        act(reg("NS"), bank(0), AF.Copy)
+        signed(FAR, 0)
+        names(0)
         turn(0)
+        fetch(FAR, 1, 0, 32)
+        stack(0, "a")
+        names(1, 2, 3)
         fetch(FAR, 1, 32, 64)
         gather(FAR, 1)
-        stack(0, "a")
         home_sums(1)
+        costs(0, 1)
         short(1)
-        fetch(FAR, 1, 64, 128)
-        costs(0, 1, 2, 3)
-        least(0)
-        short(1)
-        signed(HOME, 1, "a")
+        fetch(FAR, 1, 64, 96)
+        signed(HOME, 1)
         short(2)
-        best(*TAIL[0])
+        far_start(1)
+        costs(2)
         far_sums(1)
-        signed(FAR, 1, TAIL[3])
+        costs(3)
+        slots(0)
+        best(0, 1)
+        signed(FAR, 1)
+        names(6, 7)
         turn(1)
+        best(2, 3)
+        names(4, 5)
+        stack(1, TAIL[2])
+        least(0)
+        costs(*TAIL[0])
+        slots(1)
         best(*TAIL[1])
-        names(6, 7, 4, 5)
-        stack(1, TAIL[4])
-        best(*TAIL[2])
-        costs(6, 7, 4, 5)
-        best(6, 7, 4, 5)
         line[0] = ""
         least(1)
         ts(reg("CM", 256, 512), reg("MO"), MID, OP.subtract, 2.0, OP.mult)
@@ -782,133 +830,167 @@ def rank_program(g, core, T, topo):
             mm(bank(5, 128 * q, 128 * q + 128), reg("RK", 128 * q, 128 * q + 128, p1=96), reg("VT", p1=96), False, q == 3)
         join(4)
 
-        def missed(b, c, first, last):
+        def missed(b, c, last):
             for h in range(2):
-                mm(bank(b, 128 * h, 128 * h + 128), reg("RK", c + 128 * h, c + 128 * h + 128, p1=48), slot, first and not h, last and h == 1)
+                mm(bank(b, c + 128 * h, c + 128 * h + 128), reg("RK", 512 + 128 * h, 640 + 128 * h, p1=48), slot, False, last and h == 1)
 
         dn = bank(0, 0, 256)
         if t < R - 1:
             mm(dn, NID, Nn, True, False)
             spread(dn, reg("BH"), False, False)
-        missed(6, 512, True, False)
+        for b in (3, 6):
+            mm(bank(b, 0, 256), ID, reg("DIAG"), True, False)
+            missed(b, 0, b == 3)
+        rv = 48 * s
+        offL, offM = reg("LM", 0, 16), reg("LM", 16, 32)
+        keyL, keyM = bank(3, 16, 32), bank(1, 144, 160)
+        v, yk, xm, wq = [reg("VY", 256 * q, 256 * q + 256) for q in range(4)]
+        SK, old, nrow = reg("SK"), built("X", t - 2), bank(1, 256, 512)
+        total(bank(2, 0, 256), [(ID, reg("DIAG"))] * 2, last=False)
         line[0] = PICK
-        ts(reg("WK", 512, 1024), bank(5), col("WC", 1), OP.add, FLOOR, OP.max)
+        scan(reg("SL"), bank(3, 0, 256), reg("D0", 512, 768), 0.0, OP.min, OP.add)
+        lost = reg("SL", 15, 256, 16)
+        ts(reg("WK", 512, 768), bank(5, 0, 256), col("WC", 1), OP.add, FLOOR, OP.max)
         mm(bank(4, 0, 256), BO, reg("WK", 512, 768), True, True)
-        to_list(bank(3, 16, 48), "U1", "WK", 512, 512)
+        to_list(keyL, "U1", "WK", 512, 256)
+        ts(reg("WK", 768, 1024), bank(5, 256, 512), col("WC", 1), OP.add, FLOOR, OP.max)
         ts(reg("WK", 0, 256), reg("WK", 512, 768), FLOOR, OP.is_gt)
         act(reg("KB", 0, 256), bank(4, 0, 256), bias=-15 * FLOOR)
         to_list(bank(7, 256, 272), "U1", "WK", 768, 256, d)
-        mm(bank(5, 0, 256), BO, reg("WK", 768, 1024), True, True)
         if t == 2:
-            mm(bank(7, 0, 256), BO, reg("WK", 512, 768), True, False)
-            missed(7, 768, False, True)
-        rv = 48 * s
-        offL, offM = reg("LM", 0, 16), reg("LM", 16, 32)
-        tt(reg("HL", 0, 32), bank(3, 16, 48), reg("RAMP"), OP.subtract)
-        ts(reg("K1"), bank(3, 16, 48), -15 * FLOOR, OP.add)
-        ts(reg("HL", 48, 64), bank(3, 32, 48), 16 * FLOOR, OP.is_equal, GATE, OP.mult)
-        ts(offL, bank(3, 16, 32), 0.5, OP.mult, MID - 7.5 * FLOOR, OP.add)
+            mm(bank(4, 256, 512), BO, reg("WK", 512, 768), True, False)
+            missed(4, 256, True)
+        to_list(keyM, "U1", "WK", 768, 256)
+        mm(bank(5, 0, 256), BO, reg("WK", 768, 1024), True, True)
+        ts(reg("HL", 0, 16), keyL, -15 * FLOOR, OP.add)
+        ts(reg("K1", 0, 16), keyL, -15 * FLOOR, OP.add)
+        ts(offL, keyL, 0.5, OP.mult, MID - 7.5 * FLOOR, OP.add)
+        if t == R - 1:
+            ts(reg("G2", 0, 16), keyL, 2 * (W0 - MID) + 15 * FLOOR, OP.is_ge, -3072.0 / GATE, OP.mult)
         tt(reg("HL", 32, 48), reg("K1", 0, 16), reg("HL", 0, 16), OP.subtract)
-        tt(reg("HL", 64, 80), reg("HL", 0, 16), reg("HL", 48, 64), OP.add)
-        line[0] = ""
+        tt(reg("HL", 64, 80), reg("HL", 0, 16), lost, OP.add)
         if t < R - 1:
-            ts(reg("RV", rv + 16, rv + 48), bank(3, 16, 48), 0.5, OP.mult, MID - 7.5 * FLOOR, OP.add)
+            ts(reg("RV", rv + 16, rv + 32), keyL, 0.5, OP.mult, MID - 7.5 * FLOOR, OP.add)
+            ts(reg("D0", 256 + 15, 512, 16), keyL, -0.5, OP.mult, 2 * DEEP - P - MID + 7.5 * FLOOR, OP.add)
         else:
-            to_list(bank(1, 128, 144), "UK", "WK", 0, 256)
-            ts(reg("RS", 16, 48), bank(3, 16, 48), 0.5, OP.mult, -7.5 * FLOOR, OP.add)
-            ts(reg("G2", 0, 16), bank(3, 16, 32), 2 * (W0 - MID) + 15 * FLOOR, OP.is_ge, -3072.0 / GATE, OP.mult)
-            copy(reg("RS", 48, 64), bank(1, 128, 144))
-            tt(reg("RS", 64, 80), reg("G2", 0, 16), reg("HL", 48, 64), OP.mult)
-            send("r")
-        ts(reg("K1", 0, 16), reg("K1", 16, 32), 1.0, OP.add)
-        tt(reg("D0", 0, 256, 16), reg("K1", 0, 16), reg("HL", 16, 32), OP.subtract)
-        ts(offM, bank(7, 256, 272), 0.5, OP.mult, MID - 7.5 * FLOOR, OP.add)
-        v, yk, xm, wq = [reg("VY", 256 * q, 256 * q + 256) for q in range(4)]
-        SK, keep, old = reg("SK", 0, 256), reg("SK", 256, 512), built("X", t - 2)
+            ts(reg("RS", 16, 32), keyL, 0.5, OP.mult, -7.5 * FLOOR, OP.add)
+            tt(reg("RS", 48, 64), reg("G2", 0, 16), lost, OP.mult)
+        if t == 2:
+            act(SK, bank(4, 256, 512), AF.Sign, bias=1023.5 + GATE + 15 * FLOOR, scale=-1.0)
         if t < R - 1:
             act(yk, entries("X", t, offL), AF.Copy)
-        if t == 2:
-            act(SK, bank(7, 0, 256), AF.Sign, bias=1023.5 + 4096.0 + 15 * FLOOR, scale=-1.0)
-            total(bank(7, 256, 512), [(ID, old), (NID3, SK)])
-            act(wq, bank(7, 256, 512), AF.Relu, bias=-3072.0)
-        act(reg("KB", 256, 512), bank(5, 0, 256), bias=-15 * FLOOR)
-        act(xm, entries("X", t, offM), AF.Copy)
-        mm(bank(3, 256, 512), BACK, xm, True, True)
-        nrow = bank(1, 256, 512)
-        if t < R - 1:
-            act(reg("NR"), reg("IOX"), bias=float(P * t))
-            total(nrow, [(ID, reg("NR")), (ID3, reg("WK", 0, 256)), (BOM, reg("WK", 0, 256))], last=False)
 
-        def first_of(ebuf, key, kcol, rest, cnt):
-            e = [reg(ebuf, 264 * h - 8 * h * h, 264 * h - 8 * h * h + 256 - 16 * h) for h in range(16)]
+        def far_entry():
+            ts(offM, bank(7, 256, 272), 0.5, OP.mult, MID - 7.5 * FLOOR, OP.add)
+            if t == 2:
+                total(bank(7, 0, 256), [(ID, old), (NID3, SK)])
+            act(xm, entries("X", t, offM), AF.Copy)
+            if t == 2:
+                act(wq, bank(7, 0, 256), AF.Relu, bias=-3072.0)
+
+        def far_key():
+            ts(reg("HL", 16, 32), keyM, -15 * FLOOR, OP.add)
+            ts(reg("K1", 16, 32), keyM, DEEP - 15 * FLOOR, OP.add)
+            if t < R - 1:
+                ts(reg("RV", rv + 32, rv + 48), keyM, 0.5, OP.mult, MID - 7.5 * FLOOR, OP.add)
+                total(bank(4, 256, 512), [(ID, yk), (NID, z)])
+                act(zn, bank(4, 256, 512), AF.Abs)
+            else:
+                ts(reg("RS", 32, 48), keyM, 0.5, OP.mult, -7.5 * FLOOR, OP.add)
+                send("r")
+            act(reg("KB", 256, 512), bank(5, 0, 256), bias=-15 * FLOOR)
+
+        def far_rest():
+            tt(reg("D0", 15, 256, 16), reg("K1", 16, 32), reg("HL", 16, 32), OP.subtract)
+            if t < R - 1:
+                tt(reg("DM", 0, 16), reg("RV", rv + 16, rv + 32), reg("RV", rv + 32, rv + 48), OP.subtract)
+
+        def payees(step):
+            if t < R - 1:
+                [lambda: copy(reg("BI", 32, 64), bank(4, 0, 32)), lambda: ts(reg("BI", 0, 32), reg("BI", 32, 64), 511, OP.bitwise_and),
+                 lambda: copy(reg("BO16"), reg("BI", 16, 32))][step]()
+
+        def first_of(ebuf, key, kcol, rest, cnt, between):
+            e = [reg(ebuf, 256 * h, 256 * h + 256 - 16 * h) for h in range(16)]
             for a, b in zip(BLOCKS, BLOCKS[1:]):
                 for h in range(a, b):
                     ts(e[h], reg("KB", key + 16 * h, key + 256), col("HL", kcol + h), OP.subtract, rest(h), OP.is_equal)
-                for h in range(a, b):
-                    mm(bank(cnt, 16 * h, 256), reg("BW", 128 * h, 128 * h + 128), e[h], False, h == 15)
-                join(b - a)
+                for h in range(a, min(b, 15)):
+                    mm(bank(cnt, 16 * h + 16, 256), ALL, reg(ebuf, e[h]["a"] + 16, e[h]["b"]), False, False)
+                join(b - a - (b == 16))
+                between.get(b, lambda: None)()
+            mm(bank(cnt, 0, 256), EARLIER, dict(reg(ebuf, 0, 4096), heads=True), False, True)
 
+        line[0] = DEDUP
+        first_of("EE", 0, 64, lambda h: col("HL", 32 + h), 6, {2: far_entry, 4: far_key, 11: far_rest})
         tt(reg("TP"), entries("X", t, offL), z, OP.min)
-        first_of("EE", 0, 64, lambda h: col("HL", 32 + h), 6)
-        tt(v, bank(3, 256, 512), reg("TP"), OP.min)
-        mm(bank(2, 0, 256), BIG, reg("DIAG"), True, False)
-        if t < R - 1:
-            total(bank(4, 256, 512), [(ID, yk), (NID, z)])
-            act(zn, bank(4, 256, 512), AF.Abs)
-            to_list(bank(4, 0, 16), "UW", "ZB", 256 * (1 - s), 256)
+        mm(bank(3, 256, 512), BACK, xm, True, True)
+        if t == R - 1:
+            tt(v, bank(3, 256, 512), reg("TP"), OP.min)
+            to_list(bank(1, 128, 144), "UK", "WK", 0, 256)
+            act(reg("VY", 256, 272), bank(1, 128, 144), AF.Copy)
+            send("v")
+        else:
             to_list(bank(4, 16, 32), "UW", "ZB", 256 * (1 - s), 256, BLK * (2 - s))
+            to_list(bank(4, 0, 16), "UW", "ZB", 256 * (1 - s), 256)
+        scan(reg("SL"), bank(6, 0, 256), reg("D0", 0, 256), 0.0, OP.min, OP.add)
+        act(reg("ST"), bank(6, 0, 256), bias=DEEP)
+        second = lambda: first_of("E2", 256, 16, lambda h: col("SL", 16 * h + 15), 2,
+                                  {6: lambda: payees(0), 11: lambda: payees(1), 14: lambda: [mm(bank(2, 0, 256), ID, reg("ST"), False, False), payees(2)]})
+        if t != 2:
+            second()
+        if t < R - 1:
+            tt(v, bank(3, 256, 512), reg("TP"), OP.min)
+            ts(reg("DM", 16, 32), reg("DM", 0, 16), MIDP, OP.add)
+        line[0] = ""
+        if t == R - 1:
+            fill(reg("D0", 256 + 15, 512, 16), 2 * DEEP)
+        else:
+            act(reg("NR"), reg("IOX"), bias=float(P * t))
+            total(nrow, [(ID, reg("NR")), (ID3, reg("WK", 0, 256)), (BOM, reg("WK", 0, 256))], last=False)
             act(nv(0), v, AF.Copy, scale=-1.0)
             mm(bank(5, 0, 256), FWD, v, True, True)
             act(nv(1), bank(5, 0, 256), AF.Copy, scale=-1.0)
             if t < 2:
                 act(nv(6), bank(5, 0, 256), AF.Copy)
-        else:
-            send("v")
         if t == 2:
-            mm(bank(7, 0, 256), FWD, wq, True, True)
-            act(nv(3), bank(7, 0, 256), AF.Copy)
-            total(bank(5, 256, 512), [(FWD, v), (NID, xm)])
-            act(nv(4), bank(5, 256, 512), AF.Copy)
-            act(keep, SK, bias=0.5, scale=0.5)
-            total(bank(7, 256, 512), [(ID, Nn), (NID, reg("N0"))])
-        tt(reg("ST"), bank(6, 0, 256), reg("THR"), OP.is_lt)
-        scan(reg("SL", 512, 768), reg("D0"), reg("ST"), -1024.0, OP.max, OP.subtract)
-        mm(bank(2, 0, 256), NBIG, reg("ST"), False, False)
-        if t == 2:
-            gifts("X", t, [reg("OH", 0, 16), reg("OH", 16, 32)], [wq, nv(3)], offL, offM, nv(4))
+            mm(bank(7, 256, 512), FWD, wq, True, True)
+            act(nv(3), bank(7, 256, 512), AF.Copy)
+            total(bank(6, 256, 512), [(ID, Nn), (ID3, SK)])
+            act(reg("T2", 256, 512), bank(6, 256, 512), AF.Relu, bias=512.0 - 3072.0)
+            total(bank(6, 0, 256), [(ID, reg("N0")), (NID3, SK)])
+            act(reg("N0"), bank(6, 0, 256), AF.Relu, bias=512.0 - 3072.0)
+            total(bank(7, 0, 256), [(FWD, v), (NID, xm)], last=False)
+            gifts("X", t, [reg("OH", 0, 16), reg("OH", 16, 32)], [wq, nv(3)], offL, offM, bank(7, 0, 256))
             total(bank(5, 0, 256), [(ID, old), (NID, wq)])
             act(old, bank(5, 0, 256), AF.Copy)
         if t < R - 1:
             repeat(t + 1)
-        first_of("E2", 256, 16, lambda h: col("SL", 512 + 16 * h + 15), 2)
-        if t < R - 1:
-            tt(reg("DM", 0, 32), reg("RV", rv + 16, rv + 48), reg("DUM", 32, 64), OP.subtract)
-        tt(reg("BD"), bank(2, 0, 256), reg("THR"), OP.is_lt)
-        scan(reg("SL", 256, 512), reg("SL", 0, 256), reg("BD"), 0.0, OP.mult, OP.max)
-        build, builds = bank(2, 256, 512), reg("SL", 256 + 15, 512, 16)
+        if t == 2:
+            second()
+        scan(reg("S2"), bank(2, 0, 256), reg("D0", 256, 512), 0.0, OP.min, OP.add)
+        build, counted, builds = bank(2, 256, 512), reg("S2", 15, 256, 16), reg("FL")
         if t == R - 1:
-            copy(reg("FS"), builds)
+            copy(reg("FS"), counted)
             send("f")
             break
+        act(reg("BD"), bank(2, 0, 256), AF.Relu, bias=1.0 - 2 * DEEP, scale=-1.0)
         mm(nrow, BO3, reg("BD"), False, True)
         total(bank(5, 256, 512), [(ID, v), (BO3, reg("BD"))])
         act(built("X", t), bank(5, 256, 512), AF.Relu, bias=-3072.0)
         total(dn, [(ID3, reg("WK", 0, 256)), (BO3, reg("BD"))], first=False)
         total(build, [(ID, reg("WK", 0, 256)), (BO, reg("BD"))])
         home, far = reg("OH", 32 * t, 32 * t + 16), reg("OH", 32 * t + 16, 32 * t + 32)
-        tt(reg("G2", 0, 16), builds, reg("DM", 0, 16), OP.mult)
-        tt(reg("G2", 16, 32), builds, reg("DM", 16, 32), OP.mult)
-        tt(reg("G2", 32, 48), reg("G2", 0, 16), reg("DUM", 0, 16), OP.add)
-        tt(reg("GH"), reg("G2", 16, 32), reg("DUM", 64, 80), OP.add)
-        copy(home, reg("G2", 32, 48))
-        mm(bank(3, 64, 80), FWD, reg("GH"), True, True)
-        ts(far, bank(3, 64, 80), MIDP, OP.add)
+        tt(reg("G2", 0, 16), counted, reg("DUM", 0, 16), OP.min)
+        tt(reg("G2", 16, 32), counted, reg("DM", 16, 32), OP.add)
+        ts(builds, counted, 0.0, OP.is_lt)
+        ts(home, reg("G2", 0, 16), -1.0, OP.mult)
+        tt(reg("GH", 0, 16), reg("G2", 16, 32), reg("DUM", 16, 32), OP.min)
+        mm(bank(3, 64, 80), FWD, reg("GH", 0, 16), True, True)
+        ts(far, bank(3, 64, 80), -1.0, OP.mult, MIDP, OP.add)
         if t == 1:
-            ts(reg("BG", 704, 720), reg("G2", 32, 48), MIDP, OP.subtract)
-            copy(reg("BG", 720, 736), bank(3, 64, 80))
-        copy(reg("BI", 32, 64), bank(4, 0, 32))
-        ts(reg("BI", 0, 32), reg("BI", 32, 64), 511, OP.bitwise_and)
-        copy(reg("BO16"), reg("BI", 16, 32))
+            ts(reg("BG", 352, 368), reg("G2", 0, 16), MIDP, OP.add)
+            copy(reg("BG", 368, 384), bank(3, 64, 80))
         if t < 2:
             copy(reg("RV", 48 * (1 - s), 48 * (1 - s) + 16), reg("BI", 0, 16))
             ts(reg("BH"), reg("BI", 0, 16), 256.0, OP.subtract)
@@ -918,69 +1000,82 @@ def rank_program(g, core, T, topo):
         if t == 2:
             total(bank(4, 256, 512), [(ID, reg("PL16")), (ID3, SK), (BO3, reg("WK", 0, 256))])
             tt(C, C, bank(4, 256, 512), OP.min)
-            tt(reg("T2", 256, 512), bank(7, 256, 512), keep, OP.mult)
         tt(C, C, nrow, OP.max)
         act(reg("T2", 0, 256), dn, AF.Relu, bias=512.0 - 6144.0)
         act(reg("MK"), build, AF.Relu, bias=-512.0, scale=512.0)
         base = [(ID, Nn)] if t < 2 else [(ID, reg("N0")), (ID, reg("T2", 256, 512))]
         total(bank(0, 256, 512), base + [(ID, reg("T2", 0, 256)), (NID, reg("MK"))])
-        act(Nn, bank(0, 256, 512), AF.Copy)
+        act(Nn, bank(0, 256, 512), bias=-512.0 * (t == 2))
         takes("X", t, [home, far], yk if t < 2 else nv(5), offM, nv(6))
         for q in range(3):
             tt(reg("RC", 16 * q, 16 * q + 16), builds, reg("RV", rv + 16 * q, rv + 16 * q + 16), OP.mult)
         for q in range(3):
-            c = 512 + 96 * (t // 2) + 32 * q + 16 * s
+            c = 256 + 384 * (t // 2) + 32 * q + 16 * s
             act(reg("BG", c, c + 16), reg("RC", 16 * q, 16 * q + 16), bias=-MID)
         act(reg("CM", 0, 256), reg("TB", 1 - s, 512, 2), bias=-2 * MID, scale=2.0)
+        if t == 1:
+            act(reg("IZ", 256, 384), ID, AF.Copy)
+            act(reg("UK"), reg("U1", 0, 144), AF.Copy, scale=col("WC", 2))
+            for q in range(3):
+                act(reg("BG", 656 + 32 * q, 672 + 32 * q), reg("RC", 0, 16), AF.Copy)
+            act(reg("BG", 0, 256), C, bias=-MID)
+            homeward("a", "AQ", 0, AQW)
         if t < 2:
             copy(reg("LO", 256 * s, 256 * s + 256), C)
+            shifted(t + 1, 1)
         else:
             dma("s", [(reg("XQ", XQW * q, XQW * q + XQW), share_of("X", r, P, P + 4 * XQW)) for q, r in enumerate(others)])
+            shifted(t + 1, 1)
             send("xo")
-            act(reg("BG", 0, 512), reg("TB"), bias=-MID)
+            act(reg("BG", 384, 640), C, bias=-MID)
             mm(bank(3, 256, 512), reg("ID", 2 * BLK, 2 * BLK + 128), built("X", 1), True, True)
             act(reg("BG", 736, 992), bank(3, 256, 512), AF.Copy)
-            dma("s", [(reg("BQ", BQW * q, BQW * q + BQW), share_of("BG", r, 0, 4 * BQW)) for q, r in enumerate(others)] +
-                [(share_of("BN", rank, 0, 4 * BQW), share_of("BG", rank, 0, 4 * BQW))])
-            send("b")
-            dma("s", [(share_of("XO", rank, P, P + 4 * XQW), share_of("X", rank, P, P + 4 * XQW))])
+            homeward("b", "BQ", 384, BQW)
 
     t = R - 1
+    arrive("a")
+    dma("s", [(share_of("BN", r, 0, 384), piece) for r, piece in landed("a")[1:]])
     arrive("xo")
-    dma("s", [(share_of("XO", r, P, P + 4 * XQW), piece) for r, piece in landed("xo")[1:2]])
+    dma("s", [(share_of("XO", rank, P, P + 4 * XQW), share_of("X", rank, P, P + 4 * XQW))] +
+        [(share_of("XO", r, P, P + 4 * XQW), piece) for r, piece in landed("xo")[1:2]])
     dma("s", [(share_of("XO", r, P, P + 4 * XQW), piece) for r, piece in landed("xo")[2:]])
     arrive("b")
-    dma("s", [(share_of("BN", r, 0, 4 * BQW), piece) for r, piece in landed("b")[1:]])
-    for a in range(P, P + W0, 512):
-        ts(reg("XO", a, a + 512), reg("XO", a, a + 512), 63.0, OP.min)
+    dma("s", [(share_of("BN", r, 384, 992), piece) for r, piece in landed("b")[1:]])
+    for a in range(P, P + BOUND, 512):
+        act(reg("YG", a, a + 512), reg("XO", a, a + 512), AF.Relu, bias=63.0, scale=-1.0)
+        act(reg("XO", a, a + 512), reg("YG", a, a + 512), bias=63.0, scale=-1.0)
+    ts(reg("XO", P + BOUND, P + W0), reg("XO", P + BOUND, P + W0), 63.0, OP.min)
+    ops[-1]["r"] += spans([reg("FS")])
     back = [reg("OH", 96, 112), reg("OH", 112, 128)]
-    ts(reg("OH", 96, 128), reg("BN", 704, 736), MIDP, OP.add)
-    act(reg("CO"), reg("BN", 0, 512), bias=MID)
+    ts(reg("OH", 96, 128), reg("BN", 352, 384), -1.0, OP.mult, MIDP, OP.add)
+    for s in range(2):
+        act(reg("CO", s, 512, 2), reg("BN", 384 - 384 * s, 640 - 384 * s), bias=MID)
     arrive("r")
+    total(bank(3, 0, 16), pick("r", 0, 48, 64))
+    total(bank(3, 16, 32), pick("r", 1, 48, 64))
+    copy(reg("RS", 96, 128), bank(3, 0, 32))
     total(bank(1, 0, 48), pick("r", 0, 0, 48))
     total(bank(1, 48, 64), pick("r", 1, 32, 48))
-    total(bank(1, 64, 96), pick("r", 0, 48, 80))
-    total(bank(1, 96, 112), pick("r", 1, 64, 80))
-    copy(reg("RS", 80, 128), bank(1, 64, 112))
     atL, atM = reg("LM", 32, 48), reg("LM", 48, 64)
     ts(atL, bank(1, 16, 32), MID, OP.add)
     ts(atM, bank(1, 48, 64), MID, OP.add)
     ts(reg("RV", 96, 160), bank(1, 0, 64), MID, OP.add)
-    tt(reg("DM", 32, 48), reg("RV", 112, 128), reg("DUM", 32, 48), OP.subtract)
-    tt(reg("DM", 48, 64), reg("RV", 144, 160), reg("DUM", 32, 48), OP.subtract)
+    ts(reg("GH", 16, 32), bank(1, 16, 32), MID + P - MIDP, OP.add)
+    ts(reg("GH", 32, 48), bank(1, 48, 64), MID + P - MIDP, OP.add)
     act(nv(9), entries("XO", t, atM), AF.Copy)
     old = built("XO", t - 2)
-    for q, (b, held) in enumerate(((1, old), (3, reg("BN", 736, 992)))):
+    for q, (b, held) in enumerate(((5, old), (3, reg("BN", 736, 992)))):
         mm(bank(b, 256, 512), NID, held, True, False)
         spread(bank(b, 256, 512), reg("RS", 96 + 16 * q, 112 + 16 * q), False, True)
         act(nv(2 + q), bank(b, 256, 512), AF.Relu, bias=-3072.0, scale=-1.0)
     arrive("v")
-    total(bank(4, 0, 256), pick("v", 1))
-    act(nv(1), bank(4, 0, 256), AF.Copy, scale=-1.0)
-    total(bank(5, 0, 256), [(NID, nv(1)), (NID, nv(9))])
+    total(bank(5, 0, 256), [(NID, nv(9))] + pick("v", 1, 0, 256))
     act(nv(4), bank(5, 0, 256), AF.Copy)
-    total(bank(0, 256, 512), pick("v", 0))
-    act(nv(0), bank(0, 256, 512), AF.Copy, scale=-1.0)
+    total(bank(4, 256, 512), pick("v", 1, 0, 256))
+    act(nv(1), bank(4, 256, 512), AF.Copy, scale=-1.0)
+    total(bank(0, 240, 512), pick("v", 0))
+    act(nv(0), bank(0, 240, 496), AF.Copy, scale=-1.0)
+    act(reg("RS", 80, 96), bank(0, 496, 512), AF.Copy)
     ahead[0] = 8000.0
     records(0, 6)
     ahead[0] = 0.0
@@ -990,34 +1085,34 @@ def rank_program(g, core, T, topo):
     total(bank(2, 256, 512), [(ID, reg("PN", 1, 512, 2)), (ID3, reg("ONE"))], last=False)
     spread(bank(2, 256, 512), reg("RS", 96, 112), False, True)
     tt(C, C, bank(2, 256, 512), OP.min)
-    line[0] = "v"
-    gifts("XO", t, back, [nv(2), nv(3)], atL, atM, nv(4))
-    tt(old, old, nv(2), OP.subtract)
+    mm(bank(1, 0, 256), ID3, reg("ONE"), True, False)
+    spread(bank(1, 0, 256), reg("RS", 96, 112), False, True)
     act(reg("NR"), reg("IOX"), bias=-256.0)
-    total(bank(7, 0, 256), [(ID, reg("NR")), (NID3, reg("ONE")), (ID3, reg("MK"))], last=False)
-    mm(bank(0, 0, 256), NID, nv(0), True, False)
+    total(bank(7, 0, 256), [(ID, reg("NR")), (ID3, reg("MK"))], last=False)
+    mm(bank(6, 0, 256), NID, nv(0), True, False)
+    mm(bank(2, 0, 32), NID, reg("GH", 16, 48), True, False)
+    gifts("XO", t, back, [nv(2), nv(3)], atL, atM, nv(4))
+    tt(old, old, bank(1, 0, 256), OP.min)
     arrive("f")
-    total(bank(2, 0, 16), pick("f", 0))
-    total(bank(2, 16, 32), pick("f", 1))
-    tt(reg("G2", 0, 32), bank(2, 0, 32), reg("DM", 32, 64), OP.mult)
-    ts(reg("FB"), bank(2, 0, 16), 3072.0, OP.mult)
-    tt(reg("G2", 32, 64), reg("G2", 0, 32), reg("DUM", 0, 32), OP.add)
-    copy(reg("OH", 128, 160), reg("G2", 32, 64))
-    line[0] = ""
-    for q in range(3):
-        tt(reg("RC", 16 * q, 16 * q + 16), bank(2, 0, 16), reg("RV", 96 + 16 * q, 112 + 16 * q), OP.mult)
+    total(bank(4, 0, 16), pick("f", 0))
+    total(bank(2, 0, 16), pick("f", 0), False, False)
+    total(bank(2, 16, 32), pick("f", 1), False, True)
+    act(reg("FB"), bank(4, 0, 16), AF.Copy, scale=-1.0)
     spread(bank(7, 0, 256), reg("FB"), False, True)
-    spread(bank(0, 0, 256), reg("FB"), False, True)
-    ahead[0] = 3000.0
-    act(built("XO", t), bank(0, 0, 256), AF.Relu, bias=-3072.0)
-    dma("a", [(T.xo[:, W0 + P * t:W0 + P * R], built("XO", t))])
-    for q in range(3):
-        act(reg("BN", 624 + 32 * q, 640 + 32 * q), reg("RC", 16 * q, 16 * q + 16), bias=-MID)
-    records(1, 3)
-    ahead[0] = 0.0
+    spread(bank(6, 0, 256), reg("FB"), False, True)
+    act(built("XO", t), bank(6, 0, 256), AF.Relu)
+    act(reg("FL"), bank(4, 0, 16), AF.Relu, bias=1.0, scale=-1.0)
     line[0] = "v"
-    takes("XO", t, [reg("OH", 128, 144), reg("OH", 144, 160)], nv(5), atM, nv(6), lambda: tt(C, C, bank(7, 0, 256), OP.max))
+    tt(reg("G2", 0, 32), bank(2, 0, 32), reg("DUM", 16, 48), OP.min)
+    ts(reg("OH", 128, 160), reg("G2", 0, 32), -1.0, OP.mult, MIDP, OP.add)
+    for q in range(3):
+        tt(reg("RC", 16 * q, 16 * q + 16), reg("FL"), reg("RV", 96 + 16 * q, 112 + 16 * q), OP.mult)
+        act(reg("BN", 656 + 32 * q, 672 + 32 * q), reg("RC", 16 * q, 16 * q + 16), bias=-MID)
+    tt(C, C, bank(7, 0, 256), OP.max)
     dma("s", [(T.co[:], reg("CO"))])
+    dma("s", [(T.xo[:, W0 + P * t:W0 + P * R], built("XO", t))])
+    records(1, 3)
+    takes("XO", t, [reg("OH", 128, 144), reg("OH", 144, 160)], nv(5), atM, nv(6))
     dma("a", [(T.xo[:, ENDS[-1][1]:W0 + P * t], reg("XO", P + ENDS[-1][1], P + W0 + P * t))])
     for q, (a, b) in enumerate(ENDS):
         ts(reg("XO", P + a, P + b), reg("XO", P + a, P + b), 63.0, OP.min)
@@ -1065,6 +1160,7 @@ def schedule(ops):
     eng = ["vapgsx".index(op["e"]) for op in ops]
     busy = [[op["busy"][k] for op in ops] for k in paces]
     legs = [op["legs"] for op in ops]
+    half = max(len(way[1]) for ways_ in legs if ways_ for way in ways_) // 2
     source = [6 + i if op["sem"] else eng[i] for i, op in enumerate(ops)]
     waits, done = [], []
     for i, op in enumerate(ops):
@@ -1161,37 +1257,47 @@ def schedule(ops):
         return sorted(range(n), key=lambda q: (start[q], rank[q]))
 
     def fly(i, t, m, at):
+        def serve(key, t0, need):
+            slots, mine = at.setdefault(key, []), []
+            for u, w in slots:
+                if w > t0:
+                    if u > t0:
+                        part = min(need, u - t0)
+                        mine.append((t0, t0 + part))
+                        need -= part
+                        if need <= 0.0:
+                            t0 += part
+                            break
+                    t0 = w
+            if need > 0.0:
+                mine.append((t0, t0 + need))
+                t0 += need
+            slots.extend(mine)
+            slots.sort()
+            return t0
+
         def leg(core, engs, rows, size, die, t0):
-            free, a, b = at.setdefault(("engines", core), [0.0] * 16), engs[0], engs[-1] + 1
-            end = max(t0, max(free[a:b])) + max(1, rows // (b - a)) * (m["row"] + m["byte"] * size)
-            free[a:b] = [end] * (b - a)
-            if die is not None:
-                need, t1, slots = rows * size * m["port"], t0, at.setdefault(("port", die), [])
-                for u, w in slots:
-                    if t1 + need > u:
-                        t1 = max(t1, w)
-                slots.append((t1, t1 + need))
-                slots.sort()
-                end = max(end, t1 + need)
-            return end
+            need = max(1, rows // len(engs)) * (m["row"] + m["byte"] * size)
+            end = max(serve((core, part), t0, need) for part in {e // half for e in engs})
+            return end if die is None else max(end, serve(("port", die), t0, rows * size * m["port"]))
 
         def begin(core, t0):
             t0 += m["start"] + (0.0 if core in at else m["first"])
             at.setdefault(core, 0.0)
             return t0
         t0, left, on = begin(None, t) if eng[i] == 3 else t + m["load"], t, {}
-        for name, engs, rows, size, c, second, die in legs[i]:
+        for name, engs, rows, size, c, second, die, onward in legs[i]:
             end = leg(None, engs, rows, size, None if c else die, t0)
             left = max(left, end)
             if c:
-                on.setdefault((name, c), []).append((end, second, size, die))
-            else:
+                on.setdefault((name, c), []).append((end, second, onward, die))
+            elif name:
                 at[name] = max(at.get(name, 0.0), end)
         for (name, c), parts in on.items():
             t1 = max([at.get(c, 0.0)] + [p[0] + m["wake"] for p in parts])
             t2 = begin(c, t1)
             at[c] = t1 + m["issue"]
-            at[name] = max([at.get(name, 0.0)] + [leg(c, p[1], 128, p[2], p[3], t2) for p in parts])
+            at[name] = max([at.get(name, 0.0)] + [leg(c, p[1], p[2][0], p[2][1], p[3], t2) for p in parts])
         return left
 
     def run(seq, k):
@@ -1261,6 +1367,38 @@ def schedule(ops):
         part = seq[a:b + 1]
         return [q for q in part if q not in down] + [q for q in part if q in down]
 
+    def draw():
+        state[0] = (state[0] * 1103515245 + 12345) % 2 ** 31
+        return (state[0] >> 8) / 2.0 ** 23
+
+    def regrown(a, b, k, shake):
+        (start, end, hold), part = starts[k], order[a:b + 1]
+        count, ready, free, can, seq = {}, {}, {}, [], []
+        for i in part:
+            if eng[i] not in free:
+                j = before[i]
+                free[eng[i]] = start[j] + hold[j] if j is not None and eng[i] != 5 else 0.0
+            count[i] = sum(place[j] >= a for j, follow in waits[i])
+            ready[i] = max([0.0] + [start[j] + gap(j, i, follow, k) for j, follow in waits[i] if place[j] < a])
+            if not count[i]:
+                can.append(i)
+        rank = {i: shake * draw() + max([end[i] - start[i]] + [gap(i, q, follow, k) + tails[k][q] for q, follow in later[i]]) for i in part}
+        while can:
+            first, e = min((max(free[eng[q]], ready[q]) + hold[q], eng[q]) for q in can)
+            i = max((q for q in can if eng[q] == e and ready[q] <= first), key=lambda q: rank[q])
+            can.remove(i)
+            t = max(free[e], ready[i])
+            if e != 5:
+                free[e] = t + hold[i]
+            seq.append(i)
+            for q, follow in later[i]:
+                if q in count:
+                    ready[q] = max(ready[q], t + gap(i, q, follow, k))
+                    count[q] -= 1
+                    if not count[q]:
+                        can.append(q)
+        return seq
+
     def gap(j, i, follow, k):
         start, end, hold = starts[k]
         return start[i] - start[j] if eng[i] == 5 else hold[j] if follow else end[j] - start[j] + PACES[k]["wake"]
@@ -1299,7 +1437,7 @@ def schedule(ops):
                 longest = max(longest, free[e] + tails[k][tip[e]])
         return longest + 0.002 * sum(head.values()) - 0.002 * sum(start[i] for i in part)
 
-    order = list(range(n))
+    order, state = list(range(n)), [1]
     starts = [run(order, k) for k in paces]
     order = build(MIXES[0][0], 0.0, 0.0)
     starts = [run(order, k) for k in paces]
@@ -1329,15 +1467,18 @@ def schedule(ops):
         seed = (seed * 1103515245 + 12345) % 2 ** 31
         i, j = pairs[(seed >> 8) % len(pairs)]
         steps = (seed >> 4) % (4, 16, 64)[seed % 3]
-        if seed >> 20 & 1:
+        if turn % REGROW == 0:
+            a = max(0, place[j] - int(draw() * WINDOW))
+            b = min(n - 1, place[i] + int(draw() * WINDOW))
+            seq = regrown(a, b, int(draw() * len(PACES)), draw() * SHAKE)
+        elif seed >> 20 & 1:
             for _ in range(steps):
                 j = before[j] if before[j] is not None else j
-            seq = moved(order, place, i, j)
+            seq, a, b = moved(order, place, i, j), place[j], place[i]
         else:
             for _ in range(steps):
                 i = behind.get(i, i)
-            seq = delayed(order, place, i, j)
-        a, b = place[j], place[i]
+            seq, a, b = delayed(order, place, i, j), place[j], place[i]
         if seq is not None and sum((through(seq, a, b, k) - through(order[a:b + 1], a, b, k)) / scale[k] for k in paces) < allow - 1e-7:
             seq = order[:a] + seq + order[b + 1:]
             new = [run(seq, k) for k in paces]

from concourse.bass import DstId, RemoteDMATransfer
from concourse.mybir import AluOpType, AxisListType, ActivationFunctionType

OP = AluOpType
AF = ActivationFunctionType
NR, W0, P, R = 4, 2048, 256, 4
BLK = 128 // NR
WT = [1, 64, 5, 83, 17, 131, 29, 211, 43, 157, 61, 239, 71, 113, 97, 199]
XW = 3328
MID = 1536.0
GATE, FLOOR = 8192.0, -3200.0
DEEP = 2.0 ** 22
MIDP = 1664.0
XQW, AQW, BQW = (W0 + 3 * P) // 4, 96, 152
SHARE = [(0, 0, 80, 64)] + [(0, 0, 96, 64)] * 3
HELPED = [(1, 3, 5, 7)] * 4
BLOCKS = (0, 2, 4, 6, 8, 11, 14, 16)
ZBY = [("vvva" * 4, "ggv" * 5 + "g"), ("a" * 16, "g" * 16), ("a" * 16, "g" * 16), ("aaag" * 4, "gggv" * 4)]
ENDS = ((0, 1152), (1152, 2304))

F, H16, B16, I32, U16 = "float32", "float16", "bfloat16", "int32", "uint16"
SCRATCH = {
    "X": ("sbuf", [128, XW], B16), "XO": ("sbuf", [128, XW], B16),
    "XP": ("dram", [3, 128, 512], B16), "XS": ("sbuf", [128, 576], B16), "W4": ("sbuf", [128, 1120], B16), "XL": ("sbuf", [128, 1536], B16), "PK": ("sbuf", [128, 432], H16), "PA": ("sbuf", [128, 432], H16),
    "ZS": ("dram", [3, 128, 64], B16), "ZL": ("sbuf", [128, 192], B16), "NN": ("sbuf", [128, 512], B16), "NK": ("sbuf", [128, 512], B16), "NL": ("sbuf", [128, 384], B16),
    "XQ": ("dram", [3, 128, XQW], B16), "XK": ("dram", [3, 128, XQW], B16), "BG": ("sbuf", [128, 992], H16), "BN": ("sbuf", [128, 992], H16),
    "AQ": ("dram", [3, 128, AQW], H16), "AL": ("dram", [3, 128, AQW], H16), "BQ": ("dram", [3, 128, BQW], H16), "BL": ("dram", [3, 128, BQW], H16),
    "RS": ("sbuf", [128, 128], H16), "RL": ("sbuf", [128, 192], H16), "VL": ("sbuf", [128, 816], B16),
    "UK": ("sbuf", [128, 144], H16), "FS": ("sbuf", [128, 16], B16), "FA": ("sbuf", [128, 48], B16),
    "PL": ("sbuf", [128, 528], I32), "PN": ("sbuf", [128, 528], H16), "LN": ("sbuf", [128, 512], U16),
    "TP": ("sbuf", [128, 256], B16), "HL": ("sbuf", [128, 96], B16), "K1": ("sbuf", [128, 32], F),
    "TB": ("sbuf", [128, 512], F), "TN": ("sbuf", [128, 512], B16),
    "PL16": ("sbuf", [128, 256], H16), "NR": ("sbuf", [128, 256], H16), "SK": ("sbuf", [128, 256], B16), "D0": ("sbuf", [128, 768], F),
    "FR": ("sbuf", [128, 128], I32), "FR16": ("sbuf", [128, 128], H16),
    "FW": ("sbuf", [128, 2048], F), "NG": ("sbuf", [128, 4096], H16), "N0": ("sbuf", [128, 256], H16),
    "MY": ("sbuf", [128, 4096], H16), "MH": ("sbuf", [128, 4096], H16), "ZR": ("sbuf", [128, 4096], B16), "ZF": ("sbuf", [128, 4096], B16),
    "ZB": ("sbuf", [128, 512], B16),
    "LO": ("sbuf", [128, 512], U16), "MO": ("sbuf", [128, 256], U16), "BO16": ("sbuf", [128, 16], U16),
    "BI": ("sbuf", [128, 64], I32), "BH": ("sbuf", [128, 16], H16),
    "CM": ("sbuf", [128, 768], H16),
    "TS": ("sbuf", [128, 512], H16), "FH": ("sbuf", [128, 512], H16), "NS": ("sbuf", [128, 512], H16), "PM": ("sbuf", [128, 768], H16),
    "YG": ("sbuf", [128, 8192], B16), "SN": ("sbuf", [128, 1024], H16), "SC": ("sbuf", [128, 1024], H16), "SF": ("sbuf", [128, 64], H16),
    "R0": ("sbuf", [128, 1024], H16), "IA": ("sbuf", [128, 704], B16), "TIE": ("sbuf", [2, 576], F),
    "NFK": ("sbuf", [128, 256], F), "KI": ("sbuf", [128, 64], I32), "PD": ("sbuf", [128, 24], B16), "PS": ("sbuf", [128, 16], F),
    "RR": ("sbuf", [128, 2048], F), "AB": ("sbuf", [128, 4096], F), "VA": ("sbuf", [128, 112], H16), "FL": ("sbuf", [128, 16], B16),
    "BB": ("sbuf", [128, 256], B16), "SL": ("sbuf", [128, 256], B16),
    "VT": ("sbuf", [128, 128], H16), "WK": ("sbuf", [128, 1024], H16), "KB": ("sbuf", [128, 512], H16),
    "LM": ("sbuf", [128, 64], U16), "EE": ("sbuf", [128, 16, 256], B16), "E2": ("sbuf", [128, 16, 256], B16),
    "ST": ("sbuf", [128, 256], B16), "BD": ("sbuf", [128, 256], B16),
    "VY": ("sbuf", [128, 1024], B16), "NV": ("sbuf", [128, 2560], B16),
    "RV": ("sbuf", [128, 160], F), "DM": ("sbuf", [128, 64], F), "G2": ("sbuf", [128, 64], F), "GH": ("sbuf", [128, 48], H16),
    "OH": ("sbuf", [128, 160], U16), "FB": ("sbuf", [128, 16], B16),
    "RC": ("sbuf", [128, 48], F), "RO": ("sbuf", [24, 1024], F),
    "T2": ("sbuf", [128, 512], H16), "MK": ("sbuf", [128, 256], H16),
    "CO": ("sbuf", [128, 512], F),
    "PI": ("sbuf", [128, 16], I32), "PC": ("sbuf", [128, 16], B16),
    "IOX": ("sbuf", [128, 256], B16), "IOA": ("sbuf", [128, 384], B16), "IOB": ("sbuf", [128, 256], B16), "IOK": ("sbuf", [128, 128], B16),
    "RK": ("sbuf", [128, 768], B16), "DIAG": ("sbuf", [128, 256], B16), "ID": ("sbuf", [128, 640], H16),
    "SE": ("sbuf", [128, 1024], H16), "IZ": ("sbuf", [128, 640], B16), "ONE": ("sbuf", [128, 256], B16),
    "U1": ("sbuf", [128, 240], H16), "UW": ("sbuf", [128, 240], B16),
    "BK": ("sbuf", [128, 384], H16), "SJ": ("sbuf", [128, 2048], H16), "DG": ("sbuf", [128, 16], B16),
    "WR": ("sbuf", [128, 32], F), "WC": ("sbuf", [128, 4], F), "SG": ("sbuf", [128, 256], F),
    "S2": ("sbuf", [128, 256], F), "DUM": ("sbuf", [128, 48], F),
}
for _b in range(8):
    SCRATCH["P%d" % _b] = ("psum", [128, 512], F)

MSGS = [("z", "ZS", 0, "ZL", 0, 64, True, ("near", 0, "far", 0)), ("p", "PK", 0, "PA", 0, 144, True, ("near", 0, "far", 0)),
        ("x", "XP", 0, "XL", 0, 512, True, ("near", 0, "far", 0)), ("n", "NK", 0, "NL", 0, 128, True, ("near", 0, "far", 0)),
        ("a", "AQ", 0, "AL", 0, AQW, True, ("near", 0, "far", 0)),
        ("xo", "XQ", 0, "XK", 0, XQW, True, ("near", 0, "far", 0)), ("b", "BQ", 0, "BL", 0, BQW, True, ("near", 0, "far", 0)),
        ("r", "RS", 0, "RL", 0, 64, False, ("near", 0, "far", 0)),
        ("v", "VY", 0, "VL", 0, 272, False, ("near", 0, "far", 0)), ("f", "FS", 0, "FA", 0, 16, False, ("near", 0, "far", 0))]
NDMA = 32
SEMAPHORES = ["sv", "sa", "sp", "sg"] + ["d%d" % i for i in range(NDMA)] + [k + m[0] for m in MSGS for k in ("arr_", "ard_", "snt_", "snd_")]
ENG_SEM = {"v": "sv", "a": "sa", "p": "sp", "g": "sg"}
PACES = [{"cycle": 0.85, "gather": 1.56, "scatter": 3.8, "wake": 170.0, "wait": 15.0, "issue": 350.0, "start": 1700.0, "row": 40.0, "byte": 0.055, "port": 0.013, "first": 3200.0, "load": 1500.0},
         {"cycle": 1.18, "gather": 1.9, "scatter": 5.0, "wake": 130.0, "wait": 25.0, "issue": 320.0, "start": 1600.0, "row": 30.0, "byte": 0.05, "port": 0.015, "first": 3000.0, "load": 1500.0},
         {"cycle": 0.98, "gather": 1.3, "scatter": 3.0, "wake": 220.0, "wait": 20.0, "issue": 500.0, "start": 2900.0, "row": 65.0, "byte": 0.08, "port": 0.022, "first": 4500.0, "load": 2000.0},
         {"cycle": 0.85, "gather": 1.15, "scatter": 2.5, "wake": 150.0, "wait": 10.0, "issue": 300.0, "start": 2200.0, "row": 60.0, "byte": 0.065, "port": 0.02, "first": 3200.0, "load": 2000.0},
         {"cycle": 0.95, "gather": 1.8, "scatter": 4.0, "wake": 60.0, "wait": 10.0, "issue": 300.0, "start": 1500.0, "row": 35.0, "byte": 0.05, "port": 0.012, "first": 3000.0, "load": 1400.0},
         {"cycle": 1.05, "gather": 1.05, "scatter": 2.0, "wake": 90.0, "wait": 15.0, "issue": 350.0, "start": 1800.0, "row": 45.0, "byte": 0.055, "port": 0.014, "first": 3200.0, "load": 1800.0}]
DRAIN = [0.0, 120.0, 60.0, 0.0, 0.0]
MARGIN = 900.0
MIXES = [(mix, slack, room) for room, slack in ((0.0, 0.0), (200.0, 1000.0)) for mix in ((0.25, 0.2, 0.1, 0.1, 0.15, 0.2), (0.3, 0.2, 0.1, 0.1, 0.1, 0.2))]
TURNS = [0, 1, 2] * 3
TRIES, LOOSE = 70000, 0.0
REGROW, WINDOW, SHAKE = 2, 30, 400.0
TAIL = ((7, 6, 5, 4), (6, 7, 4, 5), "v")
PICK, DEDUP = "vp", "v"
BOUND = 1024
LANDING = 3000.0
LATER = 0.0
NAMING = 4000.0
EARLY = 0.0
LINE = ""
ORDER = {}


def reg(name, a=None, b=None, step=1, p0=0, p1=128, off=None):
    if a is None:
        a, b = 0, SCRATCH[name][1][1]
    return {"n": name, "a": a, "b": b, "s": step, "p0": p0, "p1": p1, "off": off}


def entries(x, t, off):
    return reg(x, P, P + W0 + P * t, off=off)


def places(x, t, off):
    return reg(x, 0, P + W0 + P * t, off=off)


def built(x, t):
    return reg(x, P + W0 + P * t, 2 * P + W0 + P * t)


def ap(T, r):
    if not isinstance(r, dict):
        return r
    t = T[r["n"]]
    if r["off"] is not None:
        return t[:, r["a"]:r["b"]].indirect(ap(T, r["off"]))
    if SCRATCH[r["n"]][0] == "dram":
        return t[r["a"] // SCRATCH[r["n"]][1][2]]
    if len(SCRATCH[r["n"]][1]) == 3:
        w = SCRATCH[r["n"]][1][2]
        return t[:, :, 0:16] if r.get("heads") else t[:, r["a"] // w, r["a"] % w:r["a"] % w + r["b"] - r["a"]]
    if r["s"] == 1:
        return t[r["p0"]:r["p1"], r["a"]:r["b"]]
    return t[r["p0"]:r["p1"], r["a"]:r["b"]:r["s"]]


def spans(rs):
    return [(r["n"], r["a"], r["b"], r["s"], r["p0"], r["p1"]) for r in rs if isinstance(r, dict)]


def width(r):
    return 16 * width(r["off"]) if r["off"] is not None else len(range(r["a"], r["b"], r["s"]))


def row_bytes(r):
    return width(r) * (4 if SCRATCH[r["n"]][2] in (F, I32) else 2)


def duration(eng, out, ins, per, m):
    full = [r for r in [out] + list(ins) if isinstance(r, dict)]
    n = max(width(r) for r in full[:2])
    if eng == "p":
        return 0.5 * m["cycle"] * max(min(64, width(ins[0])), width(out))
    if eng == "g":
        return m["cycle"] * ((200 if ins else 155) + 2 * n)
    if any(r["off"] is not None for r in full):
        return 60 + m["cycle"] * n * m["scatter" if out["off"] is not None else "gather"]
    if per is None:
        per = 0.5 if all(SCRATCH[r["n"]][2] in (H16, B16, U16) for r in full) else 1.0
    return m["cycle"] * max(64, per * n) + (60 if eng == "a" else 0)


def parts_of(nh, nf):
    return [p for p in ([(nh, 2, -1), (nf, -2, 3)] if nf <= nh else [(nf, 2, 1), (nh, -2, 1)]) if p[0]]


def ways(T, topo, src, msg):
    name, buf, a, land, b, w, packed, by = msg
    dsts = [T.cores[(T.rank_of(src) + step) % NR] for step in range(1, NR)]
    ports = [c for c in topo.cores_of(src) if T.rank_of(c) is None and all(topo.may_write(c, d) for d in dsts)]
    side = {"near": [c for c in ports if topo.die(c) == topo.die(src)], "far": [c for c in ports if topo.die(c) != topo.die(src)]}
    handed = [q for q, d in enumerate(dsts) if not topo.may_write(src, d)]
    carrier = {q: side[by[2 * j]][by[2 * j + 1]] for j, q in enumerate(handed)}
    share = deal(topo.engines(src, ports[0]), handed)
    out = []
    for q, d in enumerate(dsts):
        piece = reg(buf, a + w * q * packed, a + w * q * packed + w)
        out.append((d, carrier.get(q), share[q] if q in share else topo.engines(src, d), piece, reg(land, b + w * q, b + w * q + w)))
    return out


def staging(piece, land):
    return piece if SCRATCH[piece["n"]][0] == "dram" else land


def runs(a, b, engs):
    if SCRATCH[a["n"]][0] == SCRATCH[b["n"]][0] == "dram":
        return len(engs), 128 * row_bytes(a) // len(engs)
    return 128, row_bytes(a)


def mask_of(engs):
    m = 0
    for e in engs:
        m |= 1 << e
    return m


def deal(pool, items):
    n = 1
    while 2 * n * len(items) <= len(pool):
        n *= 2
    return {j: pool[n * q:n * q + n] for q, j in enumerate(items)}


def write(g, T, topo, core, snt, arr, trs):
    if len(trs) == 1:
        to, engs, a, b = trs[0]
        rid, pid = topo.addr(to, core)
        g.remote_dma(ap(T, b), ap(T, a), T.sem[arr], T.sem[snt], pid, rid, mask_of(engs))
    else:
        g.remote_dma_fused([RemoteDMATransfer(dst_ids=[DstId(rid=topo.addr(to, core)[0], pnc=topo.addr(to, core)[1])], dma_engine_mask=mask_of(engs),
                                              remote_sem=T.sem[arr], src=ap(T, a), dst=ap(T, b)) for to, engs, a, b in trs], local_sem=T.sem[snt])


def carrier_program(g, core, T, topo):
    owners = [c for c in topo.cores_of(core) if T.rank_of(c) is not None]
    if not owners:
        return
    sent = []
    for msg in MSGS:
        for dst, by, engs, piece, land in ways(T, topo, owners[0], msg):
            if by == core:
                g.wait_ge(T.sem["arr_" + msg[0]], len(engs))
                write(g, T, topo, core, "snt_" + msg[0], "arr_" + msg[0], [(dst, topo.engines(core, dst), staging(piece, land), land)])
                sent.append((msg[0], len(topo.engines(core, dst))))
    for name, n in sent:
        g.wait_ge(T.sem["snt_" + name], n)


def rank_program(g, core, T, topo):
    rank = T.rank_of(core)
    if rank is None:
        carrier_program(g, core, T, topo)
        return
    ops = []
    ndma = [0]
    line = [""]
    ahead = [0.0]
    msgs = {m[0]: m for m in MSGS}
    queue = {"v": g.vector, "a": g.scalar, "p": g.tensor, "g": g, "s": g.sync}

    def add(eng, fn, outs, ins, sem=None, per=1.0, msg=None, legs=None):
        rd, wr = spans(ins), spans(outs)
        for r in list(ins) + list(outs):
            if isinstance(r, dict) and r["off"] is not None:
                rd += spans([r["off"]])
        busy = [{"g": m["issue"], "x": 0.0}.get(eng, 60.0 * len(outs)) if sem else duration(eng, outs[0], ins, per, m) for m in PACES]
        ops.append({"e": eng, "f": fn, "r": rd, "w": wr, "sem": sem, "msg": msg, "ahead": ahead[0], "busy": busy, "legs": legs, "line": eng in line[0]})

    A = lambda r: ap(T, r)

    def copy(out, in_):
        add("v", lambda: g.vector.tensor_copy(A(out), A(in_)), [out], [in_], per=None)

    def tt(out, a, b, op):
        both = SCRATCH[a["n"]][0] == SCRATCH[b["n"]][0]
        add("v", lambda: g.vector.tensor_tensor(A(out), A(a), A(b), op), [out], [a, b], per=2.0 if both else 1.0)

    def ts(out, a, s1, op0, s2=None, op1=None):
        if op1 is None:
            add("v", lambda: g.vector.tensor_scalar(A(out), A(a), A(s1), None, op0), [out], [a, s1], per=None)
        else:
            add("v", lambda: g.vector.tensor_scalar(A(out), A(a), A(s1), A(s2), op0, op1), [out], [a, s1, s2], per=None)

    def fill(out, c):
        add("v", lambda: g.vector.memset(A(out), c), [out], [], per=None)

    def red(out, a, op, absolute=False):
        add("v", lambda: g.vector.tensor_reduce(A(out), A(a), AxisListType.X, op, apply_absolute_value=absolute), [out], [a])

    def scan(out, d0, d1, init, op0, op1):
        add("v", lambda: g.vector.tensor_tensor_scan(A(out), A(d0), A(d1), A(init), op0, op1), [out], [d0, d1, init], per=None)

    def act(out, a, func=AF.Identity, bias=0.0, scale=1.0):
        add("a", lambda: g.scalar.activation(A(out), A(a), func, bias=A(bias), scale=A(scale)), [out], [a, bias, scale])

    def mm(out, lhs, rhs, start, stop):
        add("p", lambda: g.tensor.matmul(A(out), A(lhs), A(rhs), start, stop), [out], [lhs, rhs])

    def join(k):
        part = [ops.pop() for _ in range(k)][::-1]
        ops.append(dict(part[0], f=lambda: [op["f"]() for op in part][-1], r=sorted({x for op in part for x in op["r"]}),
                        w=sorted({x for op in part for x in op["w"]}), busy=[sum(b) for b in zip(*[op["busy"] for op in part])]))

    def total(out, terms, first=True, last=True):
        for q, (lhs, rhs) in enumerate(terms):
            mm(out, lhs, rhs, first and q == 0, last and q == len(terms) - 1)
            if len(terms) == 16 and q % 8 == 7:
                join(8)

    def iota(out, pattern, base, cm):
        if SCRATCH[out["n"]][2] == I32:
            add("g", lambda: g.iota(A(out), pattern, base, cm), [out], [])
        else:
            add("g", lambda: g.iota(A(out), pattern, base, cm, allow_small_or_imprecise_dtypes=True), [out], [])

    def same(eng, out, in_):
        if eng == "v":
            copy(out, in_)
        elif eng == "a":
            act(out, in_, AF.Copy)
        else:
            add("g", lambda: g.affine_select(A(out), A(in_), [[0, width(in_)]], OP.is_ge, 0.0, 0, 0), [out], [in_])

    def dma(eng, pairs, after=()):
        name = "d%d" % ndma[0]
        ndma[0] += 1

        def fn():
            for out, in_ in pairs:
                queue[eng].dma_start(A(out), A(in_)).then_inc(T.sem[name], 16)
        every = topo.engines(core, core)
        sides = [[r for r in p if isinstance(r, dict) and SCRATCH[r["n"]][0] != "dram"] for p in pairs]
        moved = [min((r["p1"] - r["p0"], row_bytes(r)) for r in rs) if len(rs) < 2 else max((r["p1"] - r["p0"], row_bytes(r)) for r in rs)
                 for rs in sides if rs] + [runs(p[0], p[0], every) for p, rs in zip(pairs, sides) if not rs]
        add(eng, fn, [p[0] for p in pairs], [p[1] for p in pairs] + list(after), sem=(name, 16 * len(pairs)),
            legs=[(None, every, rows, size, None, [], None, None) for rows, size in moved])

    def send(name, *kinds):
        way = ways(T, topo, core, msgs[name])
        for snt, arr, part in (("snt_", "arr_", [w for w in way if w[1] is not None]), ("snd_", "ard_", [w for w in way if w[1] is None])):
            if kinds and (snt == "snt_") not in kinds:
                continue
            trs = [(by or dst, engs, piece, staging(piece, land) if by else land) for dst, by, engs, piece, land in part]
            legs = [(arr + name, engs) + runs(piece, tr[3], engs) + (by, topo.engines(by, dst) if by else [], topo.die(by or core),
                                                                     runs(tr[3], land, topo.engines(by, dst)) if by else None)
                    for tr, (dst, by, engs, piece, land) in zip(trs, part)]
            add("g", lambda snt=snt, arr=arr, trs=trs: write(g, T, topo, core, snt + name, arr + name, trs), [], [tr[2] for tr in trs],
                sem=(snt + name, sum(len(tr[1]) for tr in trs)), msg=snt + name, legs=legs)

    def coming(name):
        out = []
        for step in range(1, NR):
            src = T.cores[(rank - step) % NR]
            dst, by, engs, piece, land = ways(T, topo, src, msgs[name])[step - 1]
            out.append((by is not None, (rank - step) % NR, len(topo.engines(by or src, dst)), land))
        return sorted(out, key=lambda w: w[0])

    def arrive(name, *kinds):
        for handed in kinds or (False, True):
            part = [w for w in coming(name) if w[0] == handed]
            add("x", None, [w[3] for w in part], [], sem=(["ard_", "arr_"][handed] + name, sum(w[2] for w in part)), msg=["snd_", "snt_"][handed] + name)

    def landed(name, a=0, b=None):
        buf, c, land, d, w, packed = msgs[name][1:7]
        b, c = w if b is None else b, c + w * (NR - 1) * packed
        buf, c = {"x": ("XS", 0), "z": ("XS", 512)}.get(name, (buf, c))
        return [(rank, reg(buf, c + a, c + b))] + [(r, reg(land, piece["a"] + a, piece["a"] + b)) for handed, r, n, piece in coming(name)]

    def move(a, b):
        c = 256 * a + BLK * ((a - b) % NR)
        return reg("SE", c, c + 128)

    def pick(name, far, a=0, b=None):
        return [(move((rank - 2 * far) % NR, r), piece) for r, piece in landed(name, a, b)]

    def unpack(outs, name, senders, a=0, b=None):
        for q, out in enumerate(outs):
            banks = [o["n"] == out["n"] for o in outs]
            for j in senders:
                r, piece = landed(name, a, b)[j]
                lhs = reg("W4", 224 * q + 96 - BLK * r, 224 * q + 224 - BLK * r) if name in "xz" else move(q, r)
                mm(out, lhs, piece, j == 0 and True not in banks[:q], j == NR - 1 and True not in banks[q + 1:])

    share_of = lambda n, r, a, b: reg(n, a, b, 1, BLK * r, BLK * r + BLK)
    others = [(rank + q + 1) % NR for q in range(NR - 1)]

    def bank(b, a=0, e=512, step=1, p1=128):
        return reg("P%d" % b, a, e, step, 0, p1)

    col = lambda n, c: reg(n, c, c + 1)
    P16, PG, PP, PG16, PPAIR, PODD, P24, P3, P4, PF0, PF1 = [col("PC", c) for c in range(11)]
    BO, BOM, BO3 = [reg("BK", 128 * j, 128 * j + 128) for j in range(3)]
    ALL, EARLIER = [reg("BB", 128 * j, 128 * j + 128) for j in range(2)]
    ROW, CROW, NCROW, KROW, BIAS, PP2, NFC, SIDE = [col("PD", c) for c in (0, 4, 5, 6, 7, 8, 9, 12)]
    ID, NID, ID3, NID3 = [reg("ID", 128 * j, 128 * j + 128) for j in (0, 2, 3, 4)]
    START, MINUS8 = reg("R0", 0, 128), reg("R0", 128, 136)
    sign = lambda n: {0: 1.0, 128: -1.0}.get(n, col("PS", n // 16))
    times = lambda c: reg("R0", *{-1: (128, 256), 2: (256, 384), -2: (384, 512), 1: (512, 640), 3: (640, 768)}[c])
    nv = lambda q: reg("NV", 256 * q, 256 * q + 256)

    def to_list(out, sel, src, a, n, d=0):
        c = 15 + (128 - d) % 128
        total(out, [(reg(sel, c - j, c + 128 - j), reg(src, a + j, a + n, 16)) for j in range(16)])

    def spread(out, src, first, last):
        for j in range(16):
            mm(reg(out["n"], out["a"] + j, out["b"], 16), reg("SJ", 128 * j, 128 * j + 128), src, first and j == 0, last and j == 15)
            if j % 8 == 7:
                join(8)

    ahead[0] = 20000.0
    rows = lambda r: slice(BLK * r, BLK * r + BLK)
    shares = lambda n, src, w: [(reg(n, w * j, w * j + w), src[rows(r), :]) for j, r in enumerate(others)]
    line[0] = "va"
    dma("s", shares("ZS", T.z0, 64))
    dma("a", [(reg("FR"), T.fr0[:])])
    dma("a", [(reg("PL", 0, 512), T.pl[:]), (reg("PL", 512, 528), T.b0[:])])
    dma("s", shares("XP", T.x0, 512))
    iota(col("PI", 0), [[0, 1]], 0, 1)
    iota(reg("IOA", 0, 128), [[1, 8], [0, 16]], 0, 0)
    iota(reg("IOX"), [[1, 256]], 0, 0)
    send("z", True)
    iota(reg("IA", 576, 704), [[0, 16], [1, 8]], 0, 0)
    iota(reg("IA", 0, 512, 1, 0, 64), [[1, 2], [4, 16], [0, 16]], 0, 0)
    iota(reg("IA", 0, 512, 1, 64, 128), [[1, 2], [0, 16], [4, 16]], 64, 0)
    for c, (shift, bits) in enumerate([(0, 15), (4, 7), (0, 127), (0, 112), (5, 3), (4, 1), (0, 56), (0, 3), (2, 1)]):
        ts(col("PI", 1 + c), col("PI", 0), shift, OP.logical_shift_right, bits, OP.bitwise_and)
    copy(reg("PC", 0, 9), reg("PI", 1, 10))
    ts(BO, reg("IOA", 0, 128), PG, OP.is_equal)
    ts(reg("DG"), reg("IOX", 0, 16), P16, OP.is_equal)
    for j in range(16):
        ts(reg("SJ", 128 * j, 128 * j + 128), BO, col("DG", j), OP.mult)
    line[0] = ""
    ts(col("PI", 14), col("PI", 0), 2, OP.logical_shift_right)
    for q, c in enumerate((1, 2, 3, 7)):
        ts(col("PS", c), P3, float(q), OP.is_equal)
    copy(col("PC", 11), col("PI", 14))
    ts(reg("W4", 896, 1120), reg("IOX", 0, 224), 96.0, OP.subtract, col("PC", 11), OP.is_equal)
    for q, c in enumerate((1, 2, 3, 7)):
        act(reg("W4", 224 * q, 224 * q + 224), reg("W4", 896, 1120), AF.Copy, scale=col("PS", c))
    line[0] = "vap"
    ts(ID, reg("IOX", 0, 128), PP, OP.is_equal)
    for r in range(NR):
        ts(col("PD", 13 + r), PPAIR, float(r), OP.is_equal)
    copy(reg("FR16"), reg("FR"))
    copy(reg("ID", 128, 256), ID)
    for r in range(NR):
        ts(reg("SE", 256 * r, 256 * r + 256), reg("ID", 0, 256), col("PD", 13 + r), OP.mult)
    for j in range(16):
        mm(bank(j // 4, 128 * (j % 4), 128 * (j % 4) + 128), reg("SJ", 128 * j, 128 * j + 128), reg("FR16"), True, True)
    for q in range(4):
        same("avaa"[q], reg("FW", 512 * q, 512 * q + 512), bank(q))
    copy(reg("PN"), reg("PL"))
    copy(reg("LN"), reg("PN", 0, 512))
    for j, r in enumerate(others):
        total(bank(4, 144 * j, 144 * j + 128), [(move(r, q), reg("PN", 128 * q, 128 * q + 128)) for q in range(NR)])
        mm(bank(4, 144 * j + 128, 144 * j + 144), move(r, 0), reg("PN", 512, 528), True, True)
        join(NR + 1)
    copy(reg("PK"), bank(4, 0, 432))
    for handed, name in ((True, "p"), (True, "x"), (False, "x"), (False, "z"), (False, "p")):
        send(name, handed)
    dma("s", [(reg("XS", 0, 512), T.x0[rows(rank), :]), (reg("XS", 512, 576), T.z0[rows(rank), :])], [reg("PK")])
    ahead[0] = NAMING
    iota(reg("TIE", 0, 512, p1=2), [[0, 2], [32, 16], [1, 16]], 0, 0)
    iota(reg("TIE", 512, 576, p1=2), [[0, 4], [32, 16]], 16, 0)
    iota(reg("IA", 512, 576), [[1, 4], [4, 16]], 0, 0)
    iota(reg("IOB"), [[0, 16], [1, 16]], 0, 0)
    iota(reg("IOA", 128, 384), [[1, 16], [0, 16]], 32, 0)
    iota(reg("IOK"), [[0, 8], [1, 16]], 0, 0)
    for e in range(16):
        iota(col("WR", e), [[0, 1]], WT[e], 0)
    OWN, DIRECT, HANDED = [0], [1], [2, 3]
    xq, pq = [bank(q) for q in range(NR)], [bank(7, 128 * q, 128 * q + 128) for q in range(NR)]
    mm(bank(7), move(rank, rank), reg("PN", 0, 512), True, False)

    def named(q):
        act(reg("NN", 128 * q, 128 * q + 128), bank(4 + q % 2, 0, 128), bias=-256.0, scale=1.0 / 16)

    def turned(q):
        for j, r in enumerate(others + [rank]):
            mm(reg("P6", 128 * j, 128 * j + 128, 1, BLK * q, BLK * q + BLK), reg("NN", 128 * q + BLK * r, 128 * q + BLK * r + BLK), ID, True, True)
        join(NR)

    looked = [reg(["NG", "MH"][q // 2], 2048 * (q % 2), 2048 * (q % 2) + 2048) for q in range(NR)]
    for q in range(NR):
        same("av"[q % 2], looked[q], reg("FW", off=reg("LN", 128 * q, 128 * q + 128)))
    for q in range(NR):
        if q >= 2:
            named(q - 2)
        for k in range(16):
            mm(bank(4 + q % 2, k, 128, 16), reg(looked[q]["n"], looked[q]["a"] + k, looked[q]["b"], 16), reg("BK", 0, 128, 16), True, True)
        join(16)
        if q == 1:
            unpack(xq, "x", OWN)
        if q >= 2:
            turned(q - 2)
    for q in (2, 3):
        named(q)
        turned(q)
    act(reg("NK"), bank(6), AF.Copy)
    line[0] = ""
    send("n")
    ahead[0] = EARLY
    fill(reg("X", 0, P), 0.0)
    ts(reg("U1", 0, 143), reg("IOX", 0, 143), 15.0, OP.subtract, PG16, OP.is_equal)
    ts(reg("U1", 143, 240), reg("IOX", 15, 112), 15.0, OP.subtract, PG16, OP.is_equal)

    def sum_constants():
        parts = sorted({n for sh in SHARE for n in sh} - {0, 128})
        ts(times(-1), reg("IA", 576, 704), PG, OP.is_equal, -1.0, OP.mult)
        for n in parts:
            ts(col("PS", 8 + n // 16), PP, float(n), OP.is_ge, 2.0, OP.mult)
        for n in parts:
            ts(sign(n), col("PS", 8 + n // 16), 1.0, OP.subtract)
        act(NID, ID, AF.Copy, scale=-1.0)
        fill(reg("R0", 0, 8), 0.0)
        ts(reg("R0", 8, 128), reg("IA", 584, 704), PG, OP.is_equal)
        for c in sorted({c for sh in SHARE for h in range(2) for n, y0, z0 in parts_of(sh[h], sh[2 + h]) for c in (y0, z0)} - {-1}):
            act(times(c), times(-1), AF.Copy, scale=-float(c))

    def pair_constants():
        ts(ROW, P16, 4.0, OP.mult, PPAIR, OP.add)
        for s in range(2):
            ts(col("PI", 12 + s), col("PI", 5), float(NR - 1 - s), OP.add)
            ts(col("PI", 10 + s), col("PI", 12 + s), NR - 1, OP.bitwise_and)
        copy(reg("PC", 9, 11), reg("PI", 10, 12))
        ts(col("PD", 3), PODD, 128.0, OP.mult)
        ts(col("PD", 2), PODD, -128.0, OP.mult, 128.0, OP.add)
        ts(col("PD", 13), PP, 64.0, OP.is_ge, 65536.0, OP.mult)
        ts(CROW, PP, 4.0, OP.is_ge, 512.0, OP.mult)
        ts(NCROW, PP, 4.0, OP.is_ge, -512.0, OP.mult)
        ts(KROW, P3, 2.0, OP.mult, P24, OP.add)
        ts(PP2, PP, 2.0, OP.subtract)
        ts(col("PD", 10), PP, 64.0, OP.is_ge, 2016.0, OP.mult)
        ts(col("PD", 11), PP, 1.0, OP.is_equal, 1024.0, OP.mult)
        ts(NFC, PP, 1.0, OP.is_equal, 1528.0, OP.mult)
        ts(col("PD", 17), P16, 4.0, OP.mult, PF0, OP.add)
        ts(col("PD", 18), P16, 4.0, OP.mult, PF1, OP.add)
        ts(KROW, KROW, P4, OP.add)
        ts(BIAS, PP, 0.0, OP.is_equal, col("PD", 10), OP.add)
        ts(SIDE, col("PD", 13), 32768.0, OP.subtract)
        ts(col("PS", 0), PP, 0.0, OP.is_equal)
        for j, c in enumerate((PP, PP2)):
            ts(reg("SN", 512 * j, 512 * j + 512), reg("IA", 0, 512), c, OP.is_equal, SIDE, OP.mult)
            ts(reg("SC", 512 * j, 512 * j + 512), reg("IA", 0, 512), c, OP.is_equal, CROW, OP.mult)
            act(reg("SC", 512 * j, 512 * j + 512, p1=2), reg("TIE", 0, 512, p1=2), AF.Copy, scale=reg("PS", 0, 1, p1=2))
        ts(BIAS, BIAS, col("PD", 11), OP.add)
        ts(reg("PD", 19, 21), reg("PD", 17, 19), 64.0, OP.add)
        for side, c in enumerate((0, 19, 20)):
            for odd in range(2):
                ts(reg("PM", 256 * side + 128 * odd, 256 * side + 128 * odd + 128), reg("IOX", 0, 128), col("PD", c), OP.is_equal, col("PD", 2 + odd), OP.mult)
        ts(reg("SF"), reg("IA", 512, 576), PP, OP.is_equal, NCROW, OP.mult)
        ts(reg("SG", 0, 256), reg("IOB"), 0.0, OP.is_equal, 2.0 ** 23, OP.mult)
        ts(reg("SF", p1=2), reg("TIE", 512, 576, p1=2), reg("DG", 0, 1, p1=2), OP.mult, reg("PD", 9, 10, p1=2), OP.add)

    def later_constants():
        for out, in_, c in ((BOM, BO, -4096.0), (BO3, BO, 3072.0), (ID3, ID, 3072.0), (NID3, ID, -3072.0), (ALL, BO, GATE)):
            act(out, in_, AF.Copy, scale=c)
        ts(col("PD", 21), PP, 32.0, OP.is_lt, 2 * GATE, OP.mult)
        ts(col("PD", 22), PP, 64.0, OP.is_ge, -GATE, OP.mult)
        ts(reg("IOK"), reg("IOK"), col("PD", 21), OP.mult, col("PD", 22), OP.add)
        fill(reg("VA", 0, 64), 0.0)
        fill(reg("VT", p0=32, p1=64), 0.0)
        ts(col("WC", 1), P16, P16, OP.mult, -GATE, OP.mult)
        copy(col("WC", 2), P16)
        tt(reg("WR", 16, 32), reg("WR", 0, 16), reg("DG"), OP.mult)
        ts(reg("DUM", 0, 16), reg("IOX", 0, 256, 16), P16, OP.add, -1.0, OP.mult)
        for a in (16, 32):
            act(reg("DUM", a, a + 16), reg("DUM", 0, 16), bias=MIDP)
        red(col("WC", 0), reg("WR", 16, 32), OP.add)
        act(reg("UW"), reg("U1"), AF.Copy, scale=col("WC", 0))
        ts(reg("RK", 512, 768), reg("IOA", 128, 384), KROW, OP.is_equal, GATE, OP.mult)
        ts(EARLIER, reg("IOB", 0, 128), P16, OP.is_gt, GATE, OP.mult)
        tt(EARLIER, EARLIER, BO, OP.mult)
        ts(reg("DIAG"), reg("IOB"), P16, OP.is_equal, -3 * DEEP, OP.mult)
        act(reg("DIAG"), reg("DIAG"), bias=2 * DEEP)

    sum_constants()
    pair_constants()
    ahead[0] = LATER
    later_constants()
    ahead[0] = LANDING

    line[0] = "p"
    arrive("x", False)
    unpack(xq, "x", DIRECT)
    arrive("z")
    unpack([bank(4, 64 * q, 64 * q + 64) for q in range(NR)], "z", range(NR))
    copy(reg("ZB", 0, 256), bank(4, 0, 256))
    arrive("p", False)
    unpack(pq, "p", DIRECT, 0, 128)
    arrive("p", True)
    unpack(pq, "p", HANDED, 0, 128)
    for shift in range(2):
        total(bank(5, 16 * shift, 16 * shift + 16), [(move(rank, (rank + shift) % NR), reg("PN", 512, 528))] +
              [(move(0, (r + shift) % NR), piece) for r, piece in landed("p", 128, 144)[1:]])
    arrive("x", True)
    unpack(xq, "x", HANDED)
    line[0] = ""
    for q in range(NR):
        same("aaav"[q], reg("X", P + 512 * q, P + 512 * q + 512), bank(q))
    act(reg("TB"), bank(7), AF.Copy)
    copy(reg("LO", 0, 256), reg("TB", 0, 512, 2))
    copy(reg("BO16"), bank(5, 16, 32))
    copy(reg("RV", 0, 16), bank(5, 0, 16))
    ts(reg("BH"), bank(5, 0, 16), 256.0, OP.subtract)
    copy(reg("LO", 256, 512), reg("TB", 1, 512, 2))
    ahead[0] = 0.0
    arrive("n")
    unpack([bank(0, 128 * q, 128 * q + 128) for q in range(NR)], "n", range(NR))
    act(reg("TN"), bank(0), AF.Copy)
    act(reg("CM", 0, 256), reg("TB", 0, 512, 2), bias=-2 * MID, scale=2.0)
    act(reg("N0"), reg("TN", 0, 512, 2), AF.Copy)
    act(reg("PL16"), reg("TB", 0, 512, 2), AF.Copy)

    def repeat(t):
        for h in range(2):
            for k in range(16):
                same(ZBY[t][h][k], reg("ZR", 2048 * h + k, 2048 * h + 2048, 16), reg("ZB", 256 * (t % 2) + 128 * h, 256 * (t % 2) + 128 * h + 128))
        shifted(t, 0)

    def shifted(t, h):
        d, a, b = BLK * (1 + t % 2), 2048 * h + 16 * SHARE[t][2 + h], 2048 * h + 2048
        dma("s", [(reg("ZF", a, b, 1, d, 128), reg("ZR", a, b, 1, 0, 128 - d)), (reg("ZF", a, b, 1, 0, d), reg("ZR", a, b, 1, 128 - d, 128))])

    def gifts(x, t, offs, w, at_home, at_far, less):
        act(nv(7), places(x, t - 2, offs[0]), AF.Copy)
        tt(places(x, t - 2, offs[0]), nv(7), w[0], OP.add)
        if less["n"] == "NV":
            tt(nv(8), places(x, t - 2, offs[1]), w[1], OP.add)
            copy(places(x, t - 2, offs[1]), nv(8))
            tt(nv(6), entries(x, t, at_far), less, OP.add)
            act(nv(5), entries(x, t, at_home), AF.Copy)
        else:
            act(nv(8), places(x, t - 2, offs[1]), AF.Copy)
            tt(places(x, t - 2, offs[1]), nv(8), w[1], OP.add)
            act(nv(4), entries(x, t, at_far), AF.Copy)
            act(nv(5), entries(x, t, at_home), AF.Copy)
            mm(less, ID, nv(4), False, True)
            act(nv(6), less, AF.Copy)

    def takes(x, t, offs, held, at_far, floor):
        tt(places(x, t, offs[0]), held, nv(0), OP.add)
        tt(nv(9), entries(x, t, at_far), floor, OP.max)
        tt(places(x, t, offs[1]), nv(9), nv(1), OP.add)

    def records(pair, b):
        for q in range(3):
            c = 256 + 384 * pair + 32 * q
            for j in range(16):
                mm(bank(b, j, 512, 16, p1=24), reg("IZ", 256 - 128 * q + j, 640 - 128 * q, 16), reg("BN", c, c + 32), q + j == 0, q + j == 17)
            join(16)
        act(reg("RO", 512 * pair, 512 * pair + 512, p1=24), bank(b, p1=24), bias=MID)
        dma("s", [(T.rec[:, 512 * pair:512 * pair + 512], reg("RO", 512 * pair, 512 * pair + 512, p1=24))])

    def homeward(name, packed, a, w):
        dma("s", [(reg(packed, w * q, w * q + w), share_of("BG", r, a, a + 4 * w)) for q, r in enumerate(others)] +
            [(share_of("BN", rank, a, a + 4 * w), share_of("BG", rank, a, a + 4 * w))])
        send(name)

    repeat(0)
    shifted(0, 1)
    iota(reg("D0"), [[0, 768]], 0, 0)
    iota(reg("D0", 512 + 15, 768, 16), [[0, 16]], int(DEEP), 0)
    for q in range(4):
        for p0 in (0, 64):
            out, in_ = reg("RK", 128 * q, 128 * q + 128, 1, p0, p0 + 64), reg("IOK", 0, 128, 1, p0, p0 + 64)
            add("g", lambda q=q, out=out, in_=in_: g.affine_select(A(out), A(in_), [[1, 4], [4, 2], [0, 16]], OP.is_equal, 0.0, 8 * q, -1), [out], [in_])
    for out, c in ((reg("XO", 0, P), 0), (reg("ONE"), 1), (reg("IZ", 0, 256), 0), (reg("IZ", 384, 640), 0)):
        iota(out, [[0, 256]], c, 0)

    for t in range(R):
        s = t % 2
        d = BLK * (1 + s)
        FWD, BACK = reg("ID", 128 - d, 256 - d), reg("ID", d, d + 128)
        z = reg("ZB", 256 * s, 256 * s + 256)
        zn = reg("ZB", 256 * (1 - s), 256 * (1 - s) + 256)
        C, Nn = reg("TB", s, 512, 2), reg("TN", s, 512, 2)
        zb = [1, 2, 3, 0, 6, 7, 1, 2]
        HOME, FAR = 0, 1
        share = lambda side, h: SHARE[t][2 * side + h]
        window = lambda side, h, a, b: entries("X", t, reg(["LO", "MO"][side], [256 * s, 0][side] + 128 * h + a, [256 * s, 0][side] + 128 * h + b))
        mins = ["MY", "MH"]
        ready, staged, free = [], [], [6, 7, 3]

        def gather(side, h):
            n = share(side, h)
            if n < 128:
                a, b = 2048 * h + 16 * n, 2048 * h + 2048
                line[0] = LINE + "v"
                tt(reg(mins[side], a, b), window(side, h, n, 128), reg(["ZR", "ZF"][side], a, b), OP.min)
                line[0] = LINE

        def fetch(side, h, a, b):
            b = min(b, share(side, h))
            if a < b:
                c = 4096 * side + 2048 * h
                act(reg("YG", c + 16 * a, c + 16 * b), window(side, h, a, b), AF.Copy)
                if t == R - 1 and h == 0:
                    ops[-1]["r"] += spans([reg("BG", *[(384, 736), (736, 992), (736, 992)][a // 32])])
                ready.extend((side, 2048 * h + 16 * q, 16 * min(32, b - q)) for q in range(a, b, 32))
                stage()

        def stage():
            while ready and free:
                (side, c, w), b = ready.pop(0), free.pop(0)
                total(bank(b, 0, w), [([ID, FWD][side], reg("ZR", c, c + w)), (NID, reg("YG", 4096 * side + c, 4096 * side + c + w))])
                if t == 0:
                    ops[-2]["r"] += spans([reg("X", P, P + 512)])
                staged.append((side, c, w, b))

        def short(n=1):
            for _ in range(n):
                if staged:
                    side, c, w, b = staged.pop(0)
                    act(reg(mins[side], c, c + w), bank(b, 0, w), AF.Relu)
                    free.append(b)
                    stage()

        def home_sums(h):
            c = 2048 * h
            mm(bank(4 + h, 0, 128), reg("MY", c, c + 2048, 16), START, True, False)
            for k in range(1, 16):
                mm(bank(4 + h, 8 * k, 8 * k + 8), reg("MY", c + k, c + 2048, 16), MINUS8, False, k == 15)
                if k % 8 == 7:
                    join(8)

        def far_start(h):
            c = 2048 * h
            mm(bank(4 + h, 128, 256), reg("MY", c, c + 2048, 16), times(-1), True, False)
            for n, y0, z0 in parts_of(share(HOME, h), share(FAR, h)):
                mm(bank(4 + h, 128, 256, p1=n), reg("MY", c, c + 16 * n, 16), times(y0), False, False)
                mm(bank(4 + h, 128, 256, p1=n), reg("ZB", 256 * s + 128 * h, 256 * s + 128 * h + n), times(z0), False, False)
            join(1 + 2 * len(parts_of(share(HOME, h), share(FAR, h))))

        def far_sums(h):
            for l in range(16):
                mm(bank(4 + h, 128 + 8 * l, 136 + 8 * l), reg("MH", 2048 * h + l, 2048 * h + 2048, 16), reg("R0", 128 + d // 16, 136 + d // 16), False, l == 15)
                if l % 8 == 7:
                    join(8)

        def signed(side, h):
            a = 128 * side
            act(reg("TS", 256 * h + a, 256 * h + a + 128), bank(4 + h, a, a + 128), AF.Copy, scale=sign(share(side, h)))

        def turn(h):
            for odd in range(2):
                mm(bank(4 + h, 256 + 128 * odd, 384 + 128 * odd), reg("TS", 256 * h + odd, 256 * h + 256, 2), ID, True, True)

        def stack(h, eng):
            if eng == "a":
                act(reg("FH", 256 * h, 256 * h + 256), bank(4 + h, 256, 512), bias=BIAS)
            else:
                ts(reg("FH", 256 * h, 256 * h + 256), bank(4 + h, 256, 512), BIAS, OP.add)

        def slots(h):
            for odd in range(2):
                a = 128 * h + 64 * odd
                mm(bank(4, a, a + 64), reg("FH", 256 * h + 128 * odd, 256 * h + 128 * odd + 128), reg("SF"), True, True)
            join(2)

        def least(h):
            scan(reg("NFK", 128 * h, 128 * h + 128), reg("SG", 0, 128), bank(4, 128 * h, 128 * h + 128), 0.0, OP.add, OP.min)

        def names(*qs):
            for q in qs:
                a = 256 * (q % 4 // 2) + 128 * (q // 4)
                mm(bank(zb[q]), reg("NS", a, a + 128), reg("SN", 512 * (q % 2), 512 * (q % 2) + 512), True, False)

        def costs(*qs):
            for q in qs:
                a = 128 * (q // 2)
                mm(bank(zb[q]), reg("FH", a, a + 128), reg("SC", 512 * (q % 2), 512 * (q % 2) + 512), False, True)

        def best(*qs):
            for q in qs:
                if q in HELPED[t]:
                    act(reg("AB", 512 * q, 512 * q + 512), bank(zb[q]), AF.Abs)
                for g2 in range(2):
                    a, b = 128 * (2 * q + g2), 512 * q + 256 * g2
                    if q in HELPED[t]:
                        scan(reg("RR", a, a + 128), reg("AB", b, b + 128), reg("AB", b + 128, b + 256), 2.0 ** 23, OP.min, OP.min)
                    else:
                        red(col("RR", a + 127), bank(zb[q], 256 * g2, 256 * g2 + 256), OP.min, True)

        copy(reg("MO"), reg("TB", 0, 512, off=reg("BO16")))
        act(reg("CM", 512, 768), reg("TN", off=reg("BO16")), AF.Copy)
        for odd in range(2):
            c = 256 * (1 + s) + 128 * odd
            total(bank(0, 256 * odd, 256 * odd + 256), [(reg("PM", 128 * odd, 128 * odd + 128), Nn), (reg("PM", c, c + 128), reg("CM", 512, 768))])
        line[0] = LINE
        gather(HOME, 0)
        for a in (0, 32, 64):
            fetch(FAR, 0, a, a + 32)
        gather(FAR, 0)
        home_sums(0)
        short(3)
        free.remove(3)
        gather(HOME, 1)
        signed(HOME, 0)
        far_start(0)
        far_sums(0)
        act(reg("NS"), bank(0), AF.Copy)
        signed(FAR, 0)
        names(0)
        turn(0)
        fetch(FAR, 1, 0, 32)
        stack(0, "a")
        names(1, 2, 3)
        fetch(FAR, 1, 32, 64)
        gather(FAR, 1)
        home_sums(1)
        costs(0, 1)
        short(1)
        fetch(FAR, 1, 64, 96)
        signed(HOME, 1)
        short(2)
        far_start(1)
        costs(2)
        far_sums(1)
        costs(3)
        slots(0)
        best(0, 1)
        signed(FAR, 1)
        names(6, 7)
        turn(1)
        best(2, 3)
        names(4, 5)
        stack(1, TAIL[2])
        least(0)
        costs(*TAIL[0])
        slots(1)
        best(*TAIL[1])
        line[0] = ""
        least(1)
        ts(reg("CM", 256, 512), reg("MO"), MID, OP.subtract, 2.0, OP.mult)
        mm(bank(5, 0, 256), ID, reg("CM", 0, 256), True, False)
        mm(bank(5, 256, 512), BACK, reg("CM", 256, 512), False, False)

        tt(reg("KI", 48, 64), reg("RR", 127, 2048, 128), reg("NFK", 15, 256, 16), OP.min)
        ts(reg("KI", 0, 16), reg("KI", 48, 64), 5, OP.logical_shift_right, 15, OP.bitwise_and)
        ts(reg("KI", 16, 32), reg("KI", 48, 64), 31, OP.bitwise_and)
        ts(reg("KI", 32, 48), reg("KI", 48, 64), 4, OP.logical_shift_right, 1, OP.bitwise_and)
        copy(reg("VA", 64, 112), reg("KI", 0, 48))
        mm(bank(2, 0, 128, p1=96), reg("VA", 0, 96), ID, True, True)
        mm(bank(1, 0, 128, p1=48), reg("VA", 64, 112), ID, True, True)
        slot = reg("VT", p1=48)
        act(reg("VT", p0=64, p1=96), reg("P2", 0, 128, 1, 64, 96), AF.Square)
        copy(slot, bank(1, 0, 128, p1=48))
        for q in range(4):
            mm(bank(5, 128 * q, 128 * q + 128), reg("RK", 128 * q, 128 * q + 128, p1=96), reg("VT", p1=96), False, q == 3)
        join(4)

        def missed(b, c, last):
            for h in range(2):
                mm(bank(b, c + 128 * h, c + 128 * h + 128), reg("RK", 512 + 128 * h, 640 + 128 * h, p1=48), slot, False, last and h == 1)

        dn = bank(0, 0, 256)
        if t < R - 1:
            mm(dn, NID, Nn, True, False)
            spread(dn, reg("BH"), False, False)
        for b in (3, 6):
            mm(bank(b, 0, 256), ID, reg("DIAG"), True, False)
            missed(b, 0, b == 3)
        rv = 48 * s
        offL, offM = reg("LM", 0, 16), reg("LM", 16, 32)
        keyL, keyM = bank(3, 16, 32), bank(1, 144, 160)
        v, yk, xm, wq = [reg("VY", 256 * q, 256 * q + 256) for q in range(4)]
        SK, old, nrow = reg("SK"), built("X", t - 2), bank(1, 256, 512)
        total(bank(2, 0, 256), [(ID, reg("DIAG"))] * 2, last=False)
        line[0] = PICK
        scan(reg("SL"), bank(3, 0, 256), reg("D0", 512, 768), 0.0, OP.min, OP.add)
        lost = reg("SL", 15, 256, 16)
        ts(reg("WK", 512, 768), bank(5, 0, 256), col("WC", 1), OP.add, FLOOR, OP.max)
        mm(bank(4, 0, 256), BO, reg("WK", 512, 768), True, True)
        to_list(keyL, "U1", "WK", 512, 256)
        ts(reg("WK", 768, 1024), bank(5, 256, 512), col("WC", 1), OP.add, FLOOR, OP.max)
        ts(reg("WK", 0, 256), reg("WK", 512, 768), FLOOR, OP.is_gt)
        act(reg("KB", 0, 256), bank(4, 0, 256), bias=-15 * FLOOR)
        to_list(bank(7, 256, 272), "U1", "WK", 768, 256, d)
        if t == 2:
            mm(bank(4, 256, 512), BO, reg("WK", 512, 768), True, False)
            missed(4, 256, True)
        to_list(keyM, "U1", "WK", 768, 256)
        mm(bank(5, 0, 256), BO, reg("WK", 768, 1024), True, True)
        ts(reg("HL", 0, 16), keyL, -15 * FLOOR, OP.add)
        ts(reg("K1", 0, 16), keyL, -15 * FLOOR, OP.add)
        ts(offL, keyL, 0.5, OP.mult, MID - 7.5 * FLOOR, OP.add)
        if t == R - 1:
            ts(reg("G2", 0, 16), keyL, 2 * (W0 - MID) + 15 * FLOOR, OP.is_ge, -3072.0 / GATE, OP.mult)
        tt(reg("HL", 32, 48), reg("K1", 0, 16), reg("HL", 0, 16), OP.subtract)
        tt(reg("HL", 64, 80), reg("HL", 0, 16), lost, OP.add)
        if t < R - 1:
            ts(reg("RV", rv + 16, rv + 32), keyL, 0.5, OP.mult, MID - 7.5 * FLOOR, OP.add)
            ts(reg("D0", 256 + 15, 512, 16), keyL, -0.5, OP.mult, 2 * DEEP - P - MID + 7.5 * FLOOR, OP.add)
        else:
            ts(reg("RS", 16, 32), keyL, 0.5, OP.mult, -7.5 * FLOOR, OP.add)
            tt(reg("RS", 48, 64), reg("G2", 0, 16), lost, OP.mult)
        if t == 2:
            act(SK, bank(4, 256, 512), AF.Sign, bias=1023.5 + GATE + 15 * FLOOR, scale=-1.0)
        if t < R - 1:
            act(yk, entries("X", t, offL), AF.Copy)

        def far_entry():
            ts(offM, bank(7, 256, 272), 0.5, OP.mult, MID - 7.5 * FLOOR, OP.add)
            if t == 2:
                total(bank(7, 0, 256), [(ID, old), (NID3, SK)])
            act(xm, entries("X", t, offM), AF.Copy)
            if t == 2:
                act(wq, bank(7, 0, 256), AF.Relu, bias=-3072.0)

        def far_key():
            ts(reg("HL", 16, 32), keyM, -15 * FLOOR, OP.add)
            ts(reg("K1", 16, 32), keyM, DEEP - 15 * FLOOR, OP.add)
            if t < R - 1:
                ts(reg("RV", rv + 32, rv + 48), keyM, 0.5, OP.mult, MID - 7.5 * FLOOR, OP.add)
                total(bank(4, 256, 512), [(ID, yk), (NID, z)])
                act(zn, bank(4, 256, 512), AF.Abs)
            else:
                ts(reg("RS", 32, 48), keyM, 0.5, OP.mult, -7.5 * FLOOR, OP.add)
                send("r")
            act(reg("KB", 256, 512), bank(5, 0, 256), bias=-15 * FLOOR)

        def far_rest():
            tt(reg("D0", 15, 256, 16), reg("K1", 16, 32), reg("HL", 16, 32), OP.subtract)
            if t < R - 1:
                tt(reg("DM", 0, 16), reg("RV", rv + 16, rv + 32), reg("RV", rv + 32, rv + 48), OP.subtract)

        def payees(step):
            if t < R - 1:
                [lambda: copy(reg("BI", 32, 64), bank(4, 0, 32)), lambda: ts(reg("BI", 0, 32), reg("BI", 32, 64), 511, OP.bitwise_and),
                 lambda: copy(reg("BO16"), reg("BI", 16, 32))][step]()

        def first_of(ebuf, key, kcol, rest, cnt, between):
            e = [reg(ebuf, 256 * h, 256 * h + 256 - 16 * h) for h in range(16)]
            for a, b in zip(BLOCKS, BLOCKS[1:]):
                for h in range(a, b):
                    ts(e[h], reg("KB", key + 16 * h, key + 256), col("HL", kcol + h), OP.subtract, rest(h), OP.is_equal)
                for h in range(a, min(b, 15)):
                    mm(bank(cnt, 16 * h + 16, 256), ALL, reg(ebuf, e[h]["a"] + 16, e[h]["b"]), False, False)
                join(b - a - (b == 16))
                between.get(b, lambda: None)()
            mm(bank(cnt, 0, 256), EARLIER, dict(reg(ebuf, 0, 4096), heads=True), False, True)

        line[0] = DEDUP
        first_of("EE", 0, 64, lambda h: col("HL", 32 + h), 6, {2: far_entry, 4: far_key, 11: far_rest})
        tt(reg("TP"), entries("X", t, offL), z, OP.min)
        mm(bank(3, 256, 512), BACK, xm, True, True)
        if t == R - 1:
            tt(v, bank(3, 256, 512), reg("TP"), OP.min)
            to_list(bank(1, 128, 144), "UK", "WK", 0, 256)
            act(reg("VY", 256, 272), bank(1, 128, 144), AF.Copy)
            send("v")
        else:
            to_list(bank(4, 16, 32), "UW", "ZB", 256 * (1 - s), 256, BLK * (2 - s))
            to_list(bank(4, 0, 16), "UW", "ZB", 256 * (1 - s), 256)
        scan(reg("SL"), bank(6, 0, 256), reg("D0", 0, 256), 0.0, OP.min, OP.add)
        act(reg("ST"), bank(6, 0, 256), bias=DEEP)
        second = lambda: first_of("E2", 256, 16, lambda h: col("SL", 16 * h + 15), 2,
                                  {6: lambda: payees(0), 11: lambda: payees(1), 14: lambda: [mm(bank(2, 0, 256), ID, reg("ST"), False, False), payees(2)]})
        if t != 2:
            second()
        if t < R - 1:
            tt(v, bank(3, 256, 512), reg("TP"), OP.min)
            ts(reg("DM", 16, 32), reg("DM", 0, 16), MIDP, OP.add)
        line[0] = ""
        if t == R - 1:
            fill(reg("D0", 256 + 15, 512, 16), 2 * DEEP)
        else:
            act(reg("NR"), reg("IOX"), bias=float(P * t))
            total(nrow, [(ID, reg("NR")), (ID3, reg("WK", 0, 256)), (BOM, reg("WK", 0, 256))], last=False)
            act(nv(0), v, AF.Copy, scale=-1.0)
            mm(bank(5, 0, 256), FWD, v, True, True)
            act(nv(1), bank(5, 0, 256), AF.Copy, scale=-1.0)
            if t < 2:
                act(nv(6), bank(5, 0, 256), AF.Copy)
        if t == 2:
            mm(bank(7, 256, 512), FWD, wq, True, True)
            act(nv(3), bank(7, 256, 512), AF.Copy)
            total(bank(6, 256, 512), [(ID, Nn), (ID3, SK)])
            act(reg("T2", 256, 512), bank(6, 256, 512), AF.Relu, bias=512.0 - 3072.0)
            total(bank(6, 0, 256), [(ID, reg("N0")), (NID3, SK)])
            act(reg("N0"), bank(6, 0, 256), AF.Relu, bias=512.0 - 3072.0)
            total(bank(7, 0, 256), [(FWD, v), (NID, xm)], last=False)
            gifts("X", t, [reg("OH", 0, 16), reg("OH", 16, 32)], [wq, nv(3)], offL, offM, bank(7, 0, 256))
            total(bank(5, 0, 256), [(ID, old), (NID, wq)])
            act(old, bank(5, 0, 256), AF.Copy)
        if t < R - 1:
            repeat(t + 1)
        if t == 2:
            second()
        scan(reg("S2"), bank(2, 0, 256), reg("D0", 256, 512), 0.0, OP.min, OP.add)
        build, counted, builds = bank(2, 256, 512), reg("S2", 15, 256, 16), reg("FL")
        if t == R - 1:
            copy(reg("FS"), counted)
            send("f")
            break
        act(reg("BD"), bank(2, 0, 256), AF.Relu, bias=1.0 - 2 * DEEP, scale=-1.0)
        mm(nrow, BO3, reg("BD"), False, True)
        total(bank(5, 256, 512), [(ID, v), (BO3, reg("BD"))])
        act(built("X", t), bank(5, 256, 512), AF.Relu, bias=-3072.0)
        total(dn, [(ID3, reg("WK", 0, 256)), (BO3, reg("BD"))], first=False)
        total(build, [(ID, reg("WK", 0, 256)), (BO, reg("BD"))])
        home, far = reg("OH", 32 * t, 32 * t + 16), reg("OH", 32 * t + 16, 32 * t + 32)
        tt(reg("G2", 0, 16), counted, reg("DUM", 0, 16), OP.min)
        tt(reg("G2", 16, 32), counted, reg("DM", 16, 32), OP.add)
        ts(builds, counted, 0.0, OP.is_lt)
        ts(home, reg("G2", 0, 16), -1.0, OP.mult)
        tt(reg("GH", 0, 16), reg("G2", 16, 32), reg("DUM", 16, 32), OP.min)
        mm(bank(3, 64, 80), FWD, reg("GH", 0, 16), True, True)
        ts(far, bank(3, 64, 80), -1.0, OP.mult, MIDP, OP.add)
        if t == 1:
            ts(reg("BG", 352, 368), reg("G2", 0, 16), MIDP, OP.add)
            copy(reg("BG", 368, 384), bank(3, 64, 80))
        if t < 2:
            copy(reg("RV", 48 * (1 - s), 48 * (1 - s) + 16), reg("BI", 0, 16))
            ts(reg("BH"), reg("BI", 0, 16), 256.0, OP.subtract)
        else:
            ts(reg("RS", 0, 16), reg("BI", 0, 16), MID, OP.subtract)

        if t == 2:
            total(bank(4, 256, 512), [(ID, reg("PL16")), (ID3, SK), (BO3, reg("WK", 0, 256))])
            tt(C, C, bank(4, 256, 512), OP.min)
        tt(C, C, nrow, OP.max)
        act(reg("T2", 0, 256), dn, AF.Relu, bias=512.0 - 6144.0)
        act(reg("MK"), build, AF.Relu, bias=-512.0, scale=512.0)
        base = [(ID, Nn)] if t < 2 else [(ID, reg("N0")), (ID, reg("T2", 256, 512))]
        total(bank(0, 256, 512), base + [(ID, reg("T2", 0, 256)), (NID, reg("MK"))])
        act(Nn, bank(0, 256, 512), bias=-512.0 * (t == 2))
        takes("X", t, [home, far], yk if t < 2 else nv(5), offM, nv(6))
        for q in range(3):
            tt(reg("RC", 16 * q, 16 * q + 16), builds, reg("RV", rv + 16 * q, rv + 16 * q + 16), OP.mult)
        for q in range(3):
            c = 256 + 384 * (t // 2) + 32 * q + 16 * s
            act(reg("BG", c, c + 16), reg("RC", 16 * q, 16 * q + 16), bias=-MID)
        act(reg("CM", 0, 256), reg("TB", 1 - s, 512, 2), bias=-2 * MID, scale=2.0)
        if t == 1:
            act(reg("IZ", 256, 384), ID, AF.Copy)
            act(reg("UK"), reg("U1", 0, 144), AF.Copy, scale=col("WC", 2))
            for q in range(3):
                act(reg("BG", 656 + 32 * q, 672 + 32 * q), reg("RC", 0, 16), AF.Copy)
            act(reg("BG", 0, 256), C, bias=-MID)
            homeward("a", "AQ", 0, AQW)
        if t < 2:
            copy(reg("LO", 256 * s, 256 * s + 256), C)
            shifted(t + 1, 1)
        else:
            dma("s", [(reg("XQ", XQW * q, XQW * q + XQW), share_of("X", r, P, P + 4 * XQW)) for q, r in enumerate(others)])
            shifted(t + 1, 1)
            send("xo")
            act(reg("BG", 384, 640), C, bias=-MID)
            mm(bank(3, 256, 512), reg("ID", 2 * BLK, 2 * BLK + 128), built("X", 1), True, True)
            act(reg("BG", 736, 992), bank(3, 256, 512), AF.Copy)
            homeward("b", "BQ", 384, BQW)

    t = R - 1
    arrive("a")
    dma("s", [(share_of("BN", r, 0, 384), piece) for r, piece in landed("a")[1:]])
    arrive("xo")
    dma("s", [(share_of("XO", rank, P, P + 4 * XQW), share_of("X", rank, P, P + 4 * XQW))] +
        [(share_of("XO", r, P, P + 4 * XQW), piece) for r, piece in landed("xo")[1:2]])
    dma("s", [(share_of("XO", r, P, P + 4 * XQW), piece) for r, piece in landed("xo")[2:]])
    arrive("b")
    dma("s", [(share_of("BN", r, 384, 992), piece) for r, piece in landed("b")[1:]])
    for a in range(P, P + BOUND, 512):
        act(reg("YG", a, a + 512), reg("XO", a, a + 512), AF.Relu, bias=63.0, scale=-1.0)
        act(reg("XO", a, a + 512), reg("YG", a, a + 512), bias=63.0, scale=-1.0)
    ts(reg("XO", P + BOUND, P + W0), reg("XO", P + BOUND, P + W0), 63.0, OP.min)
    ops[-1]["r"] += spans([reg("FS")])
    back = [reg("OH", 96, 112), reg("OH", 112, 128)]
    ts(reg("OH", 96, 128), reg("BN", 352, 384), -1.0, OP.mult, MIDP, OP.add)
    for s in range(2):
        act(reg("CO", s, 512, 2), reg("BN", 384 - 384 * s, 640 - 384 * s), bias=MID)
    arrive("r")
    total(bank(3, 0, 16), pick("r", 0, 48, 64))
    total(bank(3, 16, 32), pick("r", 1, 48, 64))
    copy(reg("RS", 96, 128), bank(3, 0, 32))
    total(bank(1, 0, 48), pick("r", 0, 0, 48))
    total(bank(1, 48, 64), pick("r", 1, 32, 48))
    atL, atM = reg("LM", 32, 48), reg("LM", 48, 64)
    ts(atL, bank(1, 16, 32), MID, OP.add)
    ts(atM, bank(1, 48, 64), MID, OP.add)
    ts(reg("RV", 96, 160), bank(1, 0, 64), MID, OP.add)
    ts(reg("GH", 16, 32), bank(1, 16, 32), MID + P - MIDP, OP.add)
    ts(reg("GH", 32, 48), bank(1, 48, 64), MID + P - MIDP, OP.add)
    act(nv(9), entries("XO", t, atM), AF.Copy)
    old = built("XO", t - 2)
    for q, (b, held) in enumerate(((5, old), (3, reg("BN", 736, 992)))):
        mm(bank(b, 256, 512), NID, held, True, False)
        spread(bank(b, 256, 512), reg("RS", 96 + 16 * q, 112 + 16 * q), False, True)
        act(nv(2 + q), bank(b, 256, 512), AF.Relu, bias=-3072.0, scale=-1.0)
    arrive("v")
    total(bank(5, 0, 256), [(NID, nv(9))] + pick("v", 1, 0, 256))
    act(nv(4), bank(5, 0, 256), AF.Copy)
    total(bank(4, 256, 512), pick("v", 1, 0, 256))
    act(nv(1), bank(4, 256, 512), AF.Copy, scale=-1.0)
    total(bank(0, 240, 512), pick("v", 0))
    act(nv(0), bank(0, 240, 496), AF.Copy, scale=-1.0)
    act(reg("RS", 80, 96), bank(0, 496, 512), AF.Copy)
    ahead[0] = 8000.0
    records(0, 6)
    ahead[0] = 0.0
    C = reg("CO", 1, 512, 2)
    spread(bank(7, 0, 256), reg("RS", 80, 96), True, True)
    ts(reg("MK"), bank(7, 0, 256), P16, OP.is_equal)
    total(bank(2, 256, 512), [(ID, reg("PN", 1, 512, 2)), (ID3, reg("ONE"))], last=False)
    spread(bank(2, 256, 512), reg("RS", 96, 112), False, True)
    tt(C, C, bank(2, 256, 512), OP.min)
    mm(bank(1, 0, 256), ID3, reg("ONE"), True, False)
    spread(bank(1, 0, 256), reg("RS", 96, 112), False, True)
    act(reg("NR"), reg("IOX"), bias=-256.0)
    total(bank(7, 0, 256), [(ID, reg("NR")), (ID3, reg("MK"))], last=False)
    mm(bank(6, 0, 256), NID, nv(0), True, False)
    mm(bank(2, 0, 32), NID, reg("GH", 16, 48), True, False)
    gifts("XO", t, back, [nv(2), nv(3)], atL, atM, nv(4))
    tt(old, old, bank(1, 0, 256), OP.min)
    arrive("f")
    total(bank(4, 0, 16), pick("f", 0))
    total(bank(2, 0, 16), pick("f", 0), False, False)
    total(bank(2, 16, 32), pick("f", 1), False, True)
    act(reg("FB"), bank(4, 0, 16), AF.Copy, scale=-1.0)
    spread(bank(7, 0, 256), reg("FB"), False, True)
    spread(bank(6, 0, 256), reg("FB"), False, True)
    act(built("XO", t), bank(6, 0, 256), AF.Relu)
    act(reg("FL"), bank(4, 0, 16), AF.Relu, bias=1.0, scale=-1.0)
    line[0] = "v"
    tt(reg("G2", 0, 32), bank(2, 0, 32), reg("DUM", 16, 48), OP.min)
    ts(reg("OH", 128, 160), reg("G2", 0, 32), -1.0, OP.mult, MIDP, OP.add)
    for q in range(3):
        tt(reg("RC", 16 * q, 16 * q + 16), reg("FL"), reg("RV", 96 + 16 * q, 112 + 16 * q), OP.mult)
        act(reg("BN", 656 + 32 * q, 672 + 32 * q), reg("RC", 16 * q, 16 * q + 16), bias=-MID)
    tt(C, C, bank(7, 0, 256), OP.max)
    dma("s", [(T.co[:], reg("CO"))])
    dma("s", [(T.xo[:, W0 + P * t:W0 + P * R], built("XO", t))])
    records(1, 3)
    takes("XO", t, [reg("OH", 128, 144), reg("OH", 144, 160)], nv(5), atM, nv(6))
    dma("a", [(T.xo[:, ENDS[-1][1]:W0 + P * t], reg("XO", P + ENDS[-1][1], P + W0 + P * t))])
    for q, (a, b) in enumerate(ENDS):
        ts(reg("XO", P + a, P + b), reg("XO", P + a, P + b), 63.0, OP.min)
        dma("sa"[q % 2], [(T.xo[:, a:b], reg("XO", P + a, P + b))])

    emit(g, T, ops, queue)


def depend(ops):
    hist, sent, last = {}, {}, {}
    for i, op in enumerate(ops):
        e = op["e"]
        need, after = set(), set()
        for kind, lst in (("r", op["r"]), ("w", op["w"])):
            for name, a, b, st, p0, p1 in lst:
                psum = SCRATCH[name][0] == "psum"
                for j, k2, a2, b2, st2, q0, q1 in hist.get(name, []):
                    same = ops[j]["e"] == e and not ops[j]["sem"] and not op["sem"]
                    over = a < b2 and a2 < b and p0 < q1 and q0 < p1 and not (st == st2 and (a - a2) % st)
                    if same and e == "p":
                        if psum:
                            after.add(j)
                    elif (psum and not same) or (over and (kind == "w" or k2 == "w")):
                        need.add(j)
        if e == "g" and not op["sem"]:
            if "c" in last and (op["w"][0][4] or ops[last["c"]]["w"][0][4]):
                need.add(last["c"])
            last["c"] = i
        if e in "gs" or op["line"]:
            after |= {last[e]} if e in last else set()
            last[e] = i
        if e == "x":
            assert not need
            after = {sent[op["msg"]]}
        elif op["msg"]:
            sent[op["msg"]] = i
        op["need"], op["after"] = need, after
        for kind, lst in (("r", op["r"]), ("w", op["w"])):
            for name, a, b, st, p0, p1 in lst:
                hist.setdefault(name, []).append((i, kind, a, b, st, p0, p1))


def schedule(ops):
    n, paces = len(ops), range(len(PACES))
    eng = ["vapgsx".index(op["e"]) for op in ops]
    busy = [[op["busy"][k] for op in ops] for k in paces]
    legs = [op["legs"] for op in ops]
    half = max(len(way[1]) for ways_ in legs if ways_ for way in ways_) // 2
    source = [6 + i if op["sem"] else eng[i] for i, op in enumerate(ops)]
    waits, done = [], []
    for i, op in enumerate(ops):
        implied = 0
        for j in op["need"] | op["after"]:
            implied |= done[j]
        done.append(implied | sum(1 << j for j in op["need"] | op["after"] if j in op["need"] or not ops[j]["sem"]))
        waits.append([(j, int(j not in op["need"])) for j in sorted(op["need"] | op["after"]) if not implied >> j & 1])
    later, succ, tip = [[] for _ in range(n)], [set() for _ in range(n)], {}
    for i in range(n):
        for j, follow in waits[i]:
            later[j].append((i, follow))
            succ[j].add(i)

    def build(mix, slack, room_share):
        blend = lambda f: sum(w * f(k) for k, w in enumerate(mix))
        hold = [blend(lambda k: starts[k][2][i]) for i in range(n)]
        pred = [[(j, blend(lambda k: gap(j, i, follow, k))) for j, follow in waits[i]] for i in range(n)]
        post = [[] for _ in range(n)]
        for i in range(n):
            for j, d in pred[i]:
                post[j].append((i, d + hold[i] - hold[j]))

        def place(seq, before, first):
            start, taken = [0.0] * n, [[] for _ in range(6)]
            for i in seq:
                t = max([first[i]] + [start[j] + d for j, d in before[i]])
                slots = taken[eng[i]]
                q = len(slots)
                while q and slots[q - 1][1] > t:
                    q -= 1
                while q < len(slots) and t + hold[i] > slots[q][0]:
                    t = max(t, slots[q][1])
                    q += 1
                slots.insert(q, (t, t + hold[i]))
                start[i] = t
            return start

        tail = [blend(lambda k: starts[k][1][i] - starts[k][0][i]) - hold[i] for i in range(n)]
        start = place(order, pred, [0.0] * n)
        for last in (False, True):
            back = place(sorted(range(n), key=lambda i: (-start[i] - hold[i], -i)), post, tail)
            end = max(back[i] + hold[i] for i in range(n))
            room = [max(0.0, end - back[i] - hold[i] - start[i]) for i in range(n)]
            late = [start[i] + (min(slack, room[i]) if eng[i] == 5 else min(room_share, room[i] / 2)) if last and eng[i] not in (3, 4) else 0.0 for i in range(n)]
            due = [-back[i] - hold[i] - ops[i]["ahead"] for i in range(n)]
            for i in reversed(range(n)):
                for j, d in pred[i]:
                    due[j] = min(due[j], due[i] - d)
            start = place(sorted(range(n), key=lambda i: (due[i], i)), pred, late)
        return sorted(range(n), key=lambda i: (start[i], i))

    def again(e, mix):
        blend = lambda f: sum(w * f(k) for k, w in enumerate(mix))
        hold = [blend(lambda k: starts[k][2][i]) for i in range(n)]
        post, count, last = [[] for _ in range(n)], [0] * n, {}
        for i in order:
            arcs = [(j, blend(lambda k: gap(j, i, follow, k))) for j, follow in waits[i]]
            if eng[i] not in (e, 5):
                arcs += [(last[eng[i]], hold[last[eng[i]]])] if eng[i] in last else []
                last[eng[i]] = i
            count[i] = len(arcs)
            for j, d in arcs:
                post[j].append((i, d))
        tail = [0.0] * n
        for j in reversed(order):
            tail[j] = max([blend(lambda k: starts[k][1][j] - starts[k][0][j])] + [d + tail[i] for i, d in post[j]])
        start, seq, ready, can, t = [0.0] * n, [], [i for i in range(n) if not count[i]], [], 0.0
        while ready or can:
            if not ready:
                now = max(t, min(start[i] for i in can))
                i = max((q for q in can if start[q] <= now), key=lambda q: tail[q])
                soon = [q for q in can if now < start[q] < now + hold[i] and
                        max(start[q] + tail[q], start[q] + hold[q] + tail[i]) < max(now + tail[i], now + hold[i] + tail[q])]
                if soon:
                    urgent = max(soon, key=lambda q: tail[q])
                    fits = [q for q in can if max(now, start[q]) + hold[q] <= start[urgent]]
                    i = max(fits, key=lambda q: tail[q]) if fits else urgent
                can.remove(i)
                start[i] = max(start[i], t)
                t = start[i] + hold[i]
            else:
                i = ready.pop()
                if eng[i] == e:
                    can.append(i)
                    continue
            seq.append(i)
            for q, d in post[i]:
                start[q] = max(start[q], start[i] + d)
                count[q] -= 1
                if not count[q]:
                    ready.append(q)
        rank = {q: a for a, q in enumerate(seq)}
        return sorted(range(n), key=lambda q: (start[q], rank[q]))

    def fly(i, t, m, at):
        def serve(key, t0, need):
            slots, mine = at.setdefault(key, []), []
            for u, w in slots:
                if w > t0:
                    if u > t0:
                        part = min(need, u - t0)
                        mine.append((t0, t0 + part))
                        need -= part
                        if need <= 0.0:
                            t0 += part
                            break
                    t0 = w
            if need > 0.0:
                mine.append((t0, t0 + need))
                t0 += need
            slots.extend(mine)
            slots.sort()
            return t0

        def leg(core, engs, rows, size, die, t0):
            need = max(1, rows // len(engs)) * (m["row"] + m["byte"] * size)
            end = max(serve((core, part), t0, need) for part in {e // half for e in engs})
            return end if die is None else max(end, serve(("port", die), t0, rows * size * m["port"]))

        def begin(core, t0):
            t0 += m["start"] + (0.0 if core in at else m["first"])
            at.setdefault(core, 0.0)
            return t0
        t0, left, on = begin(None, t) if eng[i] == 3 else t + m["load"], t, {}
        for name, engs, rows, size, c, second, die, onward in legs[i]:
            end = leg(None, engs, rows, size, None if c else die, t0)
            left = max(left, end)
            if c:
                on.setdefault((name, c), []).append((end, second, onward, die))
            elif name:
                at[name] = max(at.get(name, 0.0), end)
        for (name, c), parts in on.items():
            t1 = max([at.get(c, 0.0)] + [p[0] + m["wake"] for p in parts])
            t2 = begin(c, t1)
            at[c] = t1 + m["issue"]
            at[name] = max([at.get(name, 0.0)] + [leg(c, p[1], p[2][0], p[2][1], p[3], t2) for p in parts])
        return left

    def run(seq, k):
        start, end, hold = [0.0] * n, [0.0] * n, list(busy[k])
        free, m, air, cover = [0.0] * 6, PACES[k], {}, [[-1.0] * (n + 6) for _ in range(5)]
        wake, cost = m["wake"], m["wait"]
        for i in seq:
            e = eng[i]
            if e == 5:
                start[i] = end[i] = air[ops[i]["sem"][0]]
                continue
            t, seen = free[e], cover[e]
            for j, follow in waits[i]:
                if follow:
                    d = start[j] + hold[j]
                else:
                    d = end[j]
                    if d > seen[source[j]]:
                        seen[source[j]] = max(d, t - MARGIN)
                        hold[i] += cost
                    d += wake
                if d > t:
                    t = d
            start[i] = t
            free[e] = end[i] = t + hold[i]
            end[i] = fly(i, end[i] - busy[k][i], m, air) if legs[i] else end[i] + DRAIN[e]
        return start, end, hold

    def worth(starts):
        return sum((max(starts[k][1]) + 0.01 * sum(starts[k][0]) / n) / scale[k] for k in paces)

    def held(seq, times, k):
        (start, end, hold), before, last = times, {}, {}
        for i in seq:
            before[i] = last.get(eng[i])
            last[eng[i]] = i
        i, out = max(range(n), key=lambda q: end[q]), []
        while start[i] > 0.0:
            j = before[i]
            if j is not None and eng[i] != 5 and start[j] + hold[j] >= start[i] - 1e-6:
                out.append((i, j))
                i = j
            else:
                i = max(waits[i], key=lambda q: start[q[0]] + hold[q[0]] if q[1] else end[q[0]] + PACES[k]["wake"])[0]
        return out, before

    def moved(seq, place, i, j):
        a, b = place[j], place[i]
        up = {i}
        for q in reversed(seq[a:b]):
            if succ[q] & up:
                if q == j:
                    return None
                up.add(q)
        part = seq[a:b + 1]
        return [q for q in part if q in up] + [q for q in part if q not in up]

    def delayed(seq, place, i, j):
        a, b = place[j], place[i]
        down, hit = {j}, set(succ[j])
        for q in seq[a + 1:b + 1]:
            if q in hit:
                if q == i:
                    return None
                down.add(q)
                hit |= succ[q]
        part = seq[a:b + 1]
        return [q for q in part if q not in down] + [q for q in part if q in down]

    def draw():
        state[0] = (state[0] * 1103515245 + 12345) % 2 ** 31
        return (state[0] >> 8) / 2.0 ** 23

    def regrown(a, b, k, shake):
        (start, end, hold), part = starts[k], order[a:b + 1]
        count, ready, free, can, seq = {}, {}, {}, [], []
        for i in part:
            if eng[i] not in free:
                j = before[i]
                free[eng[i]] = start[j] + hold[j] if j is not None and eng[i] != 5 else 0.0
            count[i] = sum(place[j] >= a for j, follow in waits[i])
            ready[i] = max([0.0] + [start[j] + gap(j, i, follow, k) for j, follow in waits[i] if place[j] < a])
            if not count[i]:
                can.append(i)
        rank = {i: shake * draw() + max([end[i] - start[i]] + [gap(i, q, follow, k) + tails[k][q] for q, follow in later[i]]) for i in part}
        while can:
            first, e = min((max(free[eng[q]], ready[q]) + hold[q], eng[q]) for q in can)
            i = max((q for q in can if eng[q] == e and ready[q] <= first), key=lambda q: rank[q])
            can.remove(i)
            t = max(free[e], ready[i])
            if e != 5:
                free[e] = t + hold[i]
            seq.append(i)
            for q, follow in later[i]:
                if q in count:
                    ready[q] = max(ready[q], t + gap(i, q, follow, k))
                    count[q] -= 1
                    if not count[q]:
                        can.append(q)
        return seq

    def gap(j, i, follow, k):
        start, end, hold = starts[k]
        return start[i] - start[j] if eng[i] == 5 else hold[j] if follow else end[j] - start[j] + PACES[k]["wake"]

    def rest(k):
        start, end, hold = starts[k]
        out = [0.0] * n
        for j in reversed(order):
            t = end[j] - start[j]
            if eng[j] != 5 and j in behind:
                t = max(t, hold[j] + out[behind[j]])
            for i, follow in later[j]:
                t = max(t, gap(j, i, follow, k) + out[i])
            out[j] = t
        return out

    def through(part, a, b, k):
        start, head, free, longest = starts[k][0], {}, {}, 0.0
        for i in order[a:b + 1]:
            if eng[i] not in free:
                j = before[i]
                free[eng[i]] = start[j] + starts[k][2][j] if j is not None else 0.0
            tip[eng[i]] = behind.get(i)
        for i in part:
            t = free[eng[i]] if eng[i] != 5 else 0.0
            for j, follow in waits[i]:
                t = max(t, head.get(j, start[j]) + gap(j, i, follow, k))
            head[i] = t
            free[eng[i]] = t + starts[k][2][i]
            for q, follow in later[i]:
                if place[q] > b:
                    longest = max(longest, t + gap(i, q, follow, k) + tails[k][q])
            longest = max(longest, t + starts[k][1][i] - start[i])
        for e in free:
            if e != 5 and tip[e] is not None:
                longest = max(longest, free[e] + tails[k][tip[e]])
        return longest + 0.002 * sum(head.values()) - 0.002 * sum(start[i] for i in part)

    order, state = list(range(n)), [1]
    starts = [run(order, k) for k in paces]
    order = build(MIXES[0][0], 0.0, 0.0)
    starts = [run(order, k) for k in paces]
    scale = [max(s[1]) for s in starts]
    best, seed, fresh = worth(starts), 1, True
    for mix in MIXES:
        seq = build(*mix)
        new = [run(seq, k) for k in paces]
        if worth(new) < best:
            order, starts, best = seq, new, worth(new)
    kept = (order, starts)
    for e in TURNS:
        order = again(e, MIXES[0][0])
        starts = [run(order, k) for k in paces]
        if worth(starts) < best:
            kept, best = (order, starts), worth(starts)
    order, starts = kept
    now = best
    for turn in range(TRIES):
        allow = LOOSE * max(0.0, 1.0 - 1.3 * turn / TRIES)
        if fresh:
            place = {q: a for a, q in enumerate(order)}
            chains = [held(order, starts[k], k) for k in paces]
            before, pairs, fresh = chains[0][1], [p for c in chains for p in c[0]], False
            behind = {j: i for i, j in before.items()}
            tails = [rest(k) for k in paces]
        seed = (seed * 1103515245 + 12345) % 2 ** 31
        i, j = pairs[(seed >> 8) % len(pairs)]
        steps = (seed >> 4) % (4, 16, 64)[seed % 3]
        if turn % REGROW == 0:
            a = max(0, place[j] - int(draw() * WINDOW))
            b = min(n - 1, place[i] + int(draw() * WINDOW))
            seq = regrown(a, b, int(draw() * len(PACES)), draw() * SHAKE)
        elif seed >> 20 & 1:
            for _ in range(steps):
                j = before[j] if before[j] is not None else j
            seq, a, b = moved(order, place, i, j), place[j], place[i]
        else:
            for _ in range(steps):
                i = behind.get(i, i)
            seq, a, b = delayed(order, place, i, j), place[j], place[i]
        if seq is not None and sum((through(seq, a, b, k) - through(order[a:b + 1], a, b, k)) / scale[k] for k in paces) < allow - 1e-7:
            seq = order[:a] + seq + order[b + 1:]
            new = [run(seq, k) for k in paces]
            w = worth(new)
            if w < now + allow:
                order, starts, now, fresh = seq, new, w, True
                if w < best:
                    kept, best = (order, starts), w
    order, starts = kept
    return order, starts


def emit(g, T, program, queue):
    depend(program)
    if "calls" not in ORDER:
        ORDER["calls"] = schedule(program)
    order, times = ORDER["calls"]
    place = {j: i for i, j in enumerate(order)}
    ops = [program[j] for j in order]
    n = len(ops)
    waits = [[] for _ in range(n)]
    clock = [None] * n
    known = {e: {} for e in queue}
    marked = [False] * n
    key = lambda j: ops[j]["sem"][0] if ops[j]["sem"] else ops[j]["e"]
    wanted = {(e, f): sorted({place[j] for op in ops if op["e"] == e for j in op["need"] if key(place[j]) == f}) for e in queue for f in ENG_SEM}
    for i, op in enumerate(ops):
        e = op["e"]
        if e != "x":
            for j in sorted((place[j] for j in op["need"]), reverse=True):
                if known[e].get(key(j), -1) >= j:
                    continue
                j = max([j] + [q for q in wanted.get((e, key(j)), []) if j < q < i and all(end[order[q]] + MARGIN <= start[order[i]] for start, end, hold in times)])
                waits[i].insert(0, j)
                marked[j] = True
                for k, val in clock[j].items():
                    if known[e].get(k, -1) < val:
                        known[e][k] = val
            clock[i] = dict(known[e])
        else:
            clock[i] = {}
        clock[i][key(i)] = i
    count, value = {e: 0 for e in ENG_SEM}, [None] * n
    waited = {}
    for i, op in enumerate(ops):
        if op["sem"]:
            value[i] = op["sem"]
        elif marked[i]:
            count[op["e"]] += 1
            value[i] = (ENG_SEM[op["e"]], count[op["e"]])
        if op["e"] == "x":
            continue
        for j in waits[i]:
            queue[op["e"]].wait_ge(T.sem[value[j][0]], value[j][1])
            waited[value[j][0]] = 1
        ins = op["f"]()
        if marked[i] and not op["sem"]:
            ins.then_inc(T.sem[value[i][0]], 1)
    for op in ops:
        if op["sem"] and op["sem"][0] not in waited:
            g.wait_ge(T.sem[op["sem"][0]], op["sem"][1])
